import numpy as np, ml_dtypes
CORES = [2,6,10,14,18,22,26,30]
N = 8
BF = ml_dtypes.bfloat16
def gentries(a):
    return np.ascontiguousarray(a.reshape(8, 16, -1).transpose(0, 2, 1)).reshape(8, -1)
def gtable(e):
    e = np.asarray(e); return np.ascontiguousarray(e.reshape(8, -1, 16).transpose(0, 2, 1)).reshape(128, -1).astype(np.int32)
H, W, P, F, S, R, CAP = 16, 32, 512, 8, 8, 9, 128
def near(rng, e):
    c = 2 + np.arange(F) + np.add.accumulate(e, axis=-1); n = np.concatenate([np.zeros((N, 8, 1), np.int64), np.ones((N, 8, 1), np.int64), c], axis=-1)
    j = np.maximum(np.arange(F) + 1 - rng.integers(0, 3, e.shape), 0)
    return np.minimum(c - np.take_along_axis(n, j, -1), R)
def near3(rng, e):
    return np.stack([near(rng, e) for k in range(3)], axis=-1)
def parts(rng):
    e = rng.choice(np.array([0, 0, 0, 1, 1, 2]), (N, 8, F)); op = rng.choice(np.array([0, 0, 1, 1, 2]), (N, 8, F))
    rel = np.where(rng.random((N, 8, F, 3)) < 0.6, near3(rng, e), rng.integers(1, R + 1, (N, 8, F, 3)))
    sh = rng.choice(np.array([0.0, 0.1, 0.45]), (N, 8, F, 1)); sd = rng.choice(np.array([0.2, 0.35, 0.5]), (N, 8, F, 1)); z = (N, 8, F, P)
    ia = np.where(rng.random(z) < sh, S, rng.integers(0, S, z)); ib = np.where(rng.random(z) < sh, S, rng.integers(0, S, z))
    ia = np.where(rng.random(z) < sd, S + 1, ia); z = (N, 8, F, 2, P); b = np.arange(P)
    vy = np.where(rng.random(z) < 0.15, rng.integers(-H, H + 1, z), rng.integers(0, H, z) - b // W)
    vx = np.where(rng.random(z) < 0.15, rng.integers(-W, W + 1, z), rng.integers(0, W, z) - b % W)
    z = (N, 8, 16, F, P); res = np.where(rng.random(z) < 0.05, rng.integers(-255, 256, z), rng.integers(-48, 49, z))
    return e, op, rel, ia, ib, vy, vx, res, rng.integers(0, 256, (N, 8, 16, 2, P))
def keep(rng, ia, ib, top):
    w = np.concatenate([ia == S, (ib == S) & (ia <= S)], axis=-1); o = np.argsort(rng.random(w.shape), axis=-1)
    s = np.take_along_axis(w, o, -1); over = s & (np.add.accumulate(s.astype(np.int64), axis=-1) > CAP)
    cut = np.zeros(w.shape, bool); np.put_along_axis(cut, o, over, -1); new = rng.integers(0, top, w.shape)
    return np.where(cut[..., :P], new[..., :P], ia), np.where(cut[..., P:], new[..., P:], ib)
def gts(a):
    return np.stack([gtable(np.ascontiguousarray(v).reshape(8, -1)) for v in a])
def pack(rng, e, op, rel, ia, ib, vy, vx, res, pic, top=S):
    ia, ib = keep(rng, ia, ib, top)
    return {"res": np.ascontiguousarray(res).reshape(N, 128, F * P).astype(np.float32).astype(BF), "pic0": np.ascontiguousarray(pic).reshape(N, 128, 2 * P).astype(np.float32).astype(BF),
            "ia": gts(ia), "ib": gts(ib), "vy": gts(vy), "vx": gts(vx), "gaps": e.astype(np.int32), "cmd": op.astype(np.int32), "rel": np.ascontiguousarray(rel).reshape(N, 8, 3 * F).astype(np.int32)}
def setup_inputs(rng):
    return pack(rng, *parts(rng))
def setup_inputs_spread(rng):
    e, op, rel, ia, ib, vy, vx, res, pic = parts(rng)
    res = np.clip(np.rint((2 * rng.random(res.shape) - 1) * np.exp2(8 * rng.random((N, 8, 1, F, P)))), -255, 255).astype(np.int64)
    pic = np.minimum((rng.random(pic.shape) * np.exp2(8 * rng.random((N, 8, 1, 2, P)))).astype(np.int64), 255); pic = np.where(rng.random((N, 8, 16, 1, P)) < 0.5, pic, 255 - pic)
    big = rng.random((N, 8, F, 2, P))
    vy = np.where(big < 0.5, vy, np.rint((2 * rng.random(vy.shape) - 1) * H * np.exp2(-6 * rng.random(vy.shape))).astype(np.int64))
    vx = np.where(big < 0.5, vx, np.rint((2 * rng.random(vx.shape) - 1) * W * np.exp2(-6 * rng.random(vx.shape))).astype(np.int64))
    return pack(rng, e, op, rel, ia, ib, vy, vx, res, pic)
def setup_inputs_ends(rng):
    e, op, rel, ia, ib, vy, vx, res, pic = parts(rng); z = ia.shape
    e = np.where(rng.random(e.shape) < 0.35, 2, 0); op = rng.choice(np.array([0, 0, 2, 2, 1]), e.shape); rel = np.where(rng.random(rel.shape) < 0.5, 1, R)
    e[:, 0, 1] = 2; e[:, 0, 2] = 0; op[:, 0, 2] = 2; op[:, 0, 1] = 0
    ia = np.where(rng.random(z) < 0.15, rng.integers(0, S + 1, z), np.where(rng.random(z) < 0.5, S + 1, 0)); ib = np.where(rng.random(z) < 0.5, S, 0)
    vy = np.where(rng.random(vy.shape) < 0.2, vy, np.where(rng.random(vy.shape) < 0.5, H, -H)); vx = np.where(rng.random(vx.shape) < 0.2, vx, np.where(rng.random(vx.shape) < 0.5, W, -W))
    res = np.where(rng.random(res.shape) < 0.65, np.where(rng.random(res.shape) < 0.5, 255, -255), rng.integers(-64, 65, res.shape)); pic = np.where(rng.random(pic.shape) < 0.5, 255, 0)
    e[:, 6:] = 0; op[:, 6:] = 0; rel[:, 6:, :, 1:] = 1
    ia[:, 6:, :, P - 1] = 0; ib[:, 6:, :, P - 1] = 0; vy[:, 6:, :, :, P - 1] = H; vx[:, 6:, :, :, P - 1] = W
    pic[:, 6, :, :, P - 1] = 0; pic[:, 7, :, :, P - 1] = 255
    res[:, 6, :, :, P - 1] = np.tile(np.array([0, 1, 255, -255]), 4)[:, None]; res[:, 7, :, :, P - 1] = np.tile(np.array([0, -1, -255, 255]), 4)[:, None]
    return pack(rng, e, op, rel, ia, ib, vy, vx, res, pic, 1)
def roles():
    return (np.arange(8)[None, :] + np.arange(N)[:, None]) % 8
def setup_inputs_corners(rng):
    e, op, rel, ia, ib, vy, vx, res, pic = parts(rng); k = roles(); b = np.arange(P)
    e[k == 0] = 0; op[k == 0] = 0; e[k == 1] = 2; op[k == 2] = 1; e[k == 3] = 0; op[k == 3] = 2
    nr = near3(rng, e); m = (k == 1) | (k == 2) | (k == 4); rel[m] = nr[m]
    rel[..., 2] = np.where(rng.random((N, 8, F)) < 0.3, rel[..., 1], rel[..., 2]); rel[..., 0] = np.where(rng.random((N, 8, F)) < 0.3, rel[..., 1], rel[..., 0])
    x = rel[..., 0]; x = np.where((k == 3)[..., None], rng.integers(1, 3, x.shape), x); rel[..., 0] = x
    m = (k == 0)[..., None, None]; ia = np.where(m & (ia > S), rng.integers(0, S, ia.shape), ia)
    m = (k == 4)[..., None, None]; late = np.arange(F)[:, None] >= 1
    ia = np.where(m & late, S + 1, np.where(m, rng.integers(0, S, ia.shape), ia))
    m = (k == 5)[..., None, None, None]; z = (N, 8, F, 2, 1)
    vy = np.where(m, rng.choice(np.array([0, H - 1]), z) - b // W, vy); vx = np.where(m, rng.choice(np.array([0, W - 1]), z) - b % W, vx)
    m = (k == 5)[..., None, None]; ib = np.where(m, S, ib); ia = np.where(m, rng.integers(0, S, ia.shape), ia)
    m = (k == 6)[..., None, None, None]; vy = np.where(m, np.where(rng.random(vy.shape) < 0.5, H, -H), vy); vx = np.where(m, np.where(rng.random(vx.shape) < 0.5, W, -W), vx)
    m = (k == 6)[..., None, None]; ia = np.where(m & (ia == S), 0, ia); ib = np.where(m & (ib == S), S - 1, ib)
    m = (k == 7)[..., None, None]; n = CAP - (np.arange(F)[:, None] & 1)
    ia = np.where(m, np.where(b < n, S, rng.integers(0, S, ia.shape)), ia); ib = np.where(m, rng.integers(0, S, ib.shape), ib)
    return pack(rng, e, op, rel, ia, ib, vy, vx, res, pic)
def setup_inputs_calm(rng):
    e, op, rel, ia, ib, vy, vx, res, pic = parts(rng); k = roles(); e0, op0 = e, op; odd = (np.arange(N)[:, None] & 1) == 1
    e = np.zeros(e.shape, np.int64); op = np.zeros(op.shape, np.int64); x = rng.integers(1, 4, e.shape)
    op[k < 2] = 2; x[k == 0] = 1; x[k == 1] = 2
    e[k == 3, 0] = 1; op[k == 3, 0] = 1; x[k == 3, 0] = 4; op[k == 3, F - 1] = 2; e[k == 4, 0] = 2
    e[k == 5, 0] = 2; e[k == 5, 1] = 2; op[k == 5, 2:] = 2
    op[k == 6] = 1; x[k == 6] = 1; e[k == 6, 1] = 1
    m = (k == 6) & odd; e[m] = 0; e[m, 0] = min(S - F, 2); x[m, :F - 1] = 2; e[m, F - 1] = 2
    for t, (o, v) in enumerate(((1, 1), (1, 2), (2, 3))):
        op[k == 2, t] = o; x[k == 2, t] = v
    m = (k == 2) & odd
    for t, (o, v) in enumerate(((1, 1), (2, 2), (0, 3))):
        op[m, t] = o; x[m, t] = v
    e[k == 7] = e0[k == 7]; op[k == 7] = op0[k == 7]
    rel = np.where(rng.random(rel.shape) < 0.7, near3(rng, e), rng.integers(1, 4, rel.shape)); rel[..., 0] = x
    rel[k == 3, 1, 1:] = 2; rel[k == 6, F - 1, 1:] = rng.integers(2, R + 1, (N, 2))
    vy = rng.integers(-3, 4, vy.shape); vx = rng.integers(-3, 4, vx.shape)
    return pack(rng, e, op, rel, ia, ib, vy, vx, res, pic)
def check_inputs(d):
    bad = []
    for k, lo, hi in (("res", -255, 255), ("pic0", 0, 255), ("ia", 0, S + 1), ("ib", 0, S), ("vy", -H, H), ("vx", -W, W), ("gaps", 0, 2), ("cmd", 0, 2), ("rel", 1, R)):
        v = np.asarray(d[k]).astype(np.float64)
        if not (np.min(v) >= lo and np.max(v) <= hi): bad.append("range of " + k)
        if np.any(v != np.rint(v)): bad.append("whole numbers in " + k)
    a, b = [np.stack([gentries(v) for v in np.asarray(d[k])]).reshape(N, 8, F, P) for k in ("ia", "ib")]
    if np.max(np.sum((a == S).astype(np.int64) + ((b == S) & (a <= S)), axis=-1)) > CAP: bad.append("view blocks of a frame and group")
    return bad
def insert(h, n):
    if len(h) == S: del h[min(k for k in h if not h[k])]
    h[n] = False
def step(h, nxt, cur, first, e, op, x, m0, m1):
    if not first: insert(h, cur)
    for k in range(e): insert(h, nxt + k)
    cur = nxt + e
    if op == 1 and cur - x in h: h[cur - x] = True
    if op == 2 and cur - x in h and len(h) > 2: del h[cur - x]
    key = {n: (63 - n if h[n] else 64 + n) + 128 * (n == cur - m0) + 256 * (n == cur - m1) for n in h}
    return sorted(h, key=lambda n: -key[n]), cur + 1, cur
def reference(res, pic0, ia, ib, vy, vx, gaps, cmd, rel):
    M = 3 * F + 2
    rs = res.astype(np.float32).astype(np.int64).reshape(N, 8, 16, F, P); st = pic0.astype(np.float32).astype(np.int64).reshape(N, 8, 16, 2, P)
    la, lb = [np.stack([gentries(v) for v in a]).astype(np.int64).reshape(N, 8, F, P) for a in (ia, ib)]
    ly, lx = [np.stack([gentries(v) for v in a]).astype(np.int64).reshape(N, 8, F, 2, P) for a in (vy, vx)]
    by = np.arange(P) // W; bx = np.arange(P) % W; g8 = np.arange(8); y = np.zeros((N, 8, 16, F, P), np.int64)
    pics = np.full((N, 8, 16, M + 2, P), 128, np.int32); pics[:, :, :, 0:2] = st
    mq = np.full((N, 8, M, P), -1, np.int64); my = np.zeros((N, 8, M, P), np.int64); mx = np.zeros((N, 8, M, P), np.int64)
    held = [[{0: False, 1: False} for g in range(8)] for r in range(N)]; nxt = np.full((N, 8), 2); cur = np.zeros((N, 8), np.int64)
    for f in range(F):
        for r in range(N):
            q = (r - 1) % N; src = (g8 + f) % 8
            pics[r, :, :, M + 1] = st[q, src, :, 1] if f == 0 else y[q, src, :, f - 1]
            A = np.full((8, S + 1), M, np.int64); A[:, S] = M + 1; here = np.zeros((8, M), bool)
            for g in range(8):
                lst, a, b = step(held[r][g], int(nxt[r, g]), int(cur[r, g]), f == 0, int(gaps[r, g, f]), int(cmd[r, g, f]), int(rel[r, g, 3 * f]), int(rel[r, g, 3 * f + 1]), int(rel[r, g, 3 * f + 2]))
                nxt[r, g] = a; cur[r, g] = b; A[g, :len(lst)] = lst; here[g, lst] = True
            B = np.array(A); B[:, 0] = A[:, 1]; B[:, 1] = A[:, 0]; c = B[:, 0]
            ja = la[r, :, f]; direct = ja == S + 1
            na = np.take_along_axis(A, np.where(direct, 0, ja), 1); nb = np.take_along_axis(B, lb[r, :, f], 1)
            n = mq[r, g8, c]; wy = my[r, g8, c]; wx = mx[r, g8, c]; ay = wy >> 1; ax = wx >> 1
            ok = (n >= 0) & np.take_along_axis(here, np.maximum(n, 0), 1)
            na = np.where(direct, np.where(ok, n, A[:, :1]), na); nb = np.where(direct, c[:, None], nb)
            uy = np.where(direct, ay, ly[r, :, f, 0]); ux = np.where(direct, ax, lx[r, :, f, 0])
            ty = np.where(direct, ay - wy, ly[r, :, f, 1]); tx = np.where(direct, ax - wx, lx[r, :, f, 1])
            flat = pics[r].reshape(8, 16, (M + 2) * P)
            i = na * P + np.clip(by + uy, 0, H - 1) * W + np.clip(bx + ux, 0, W - 1); j = nb * P + np.clip(by + ty, 0, H - 1) * W + np.clip(bx + tx, 0, W - 1)
            s = np.take_along_axis(flat, i[:, None, :], 2) + np.take_along_axis(flat, j[:, None, :], 2) + 1
            v = np.clip((s >> 1) + rs[r, :, :, f], 0, 255)
            y[r, :, :, f] = v
            for g in range(8):
                k = cur[r, g]; pics[r, g, :, k] = v[g]; mq[r, g, k] = np.where(na[g] < M, na[g], -1); my[r, g, k] = uy[g]; mx[r, g, k] = ux[g]
    return {"y": y.reshape(N, 128, F * P).astype(np.float32).astype(BF)}

@@ -1,0 +1,529 @@
+import numpy as np
+from concourse.mybir import AluOpType as A, AxisListType, ActivationFunctionType as AF
+
+F = 8
+P = 512
+CUTS = [0, 192, 384, 512]
+SEND_AFTER = [2]
+LOOK = {0: (2, 4), 2: (4, 6), 4: (6, 8)}
+VEC = {1: (2, 4), 2: (4, 6), 4: (6, 8)}
+BIG = 12582912.0
+NN = 26
+
+f32, bf, i32, u16 = "float32", "bfloat16", "int32", "uint16"
+SB_ = {
+    "W": ([128, 16 * P], bf), "RES": ([128, F * P], bf), "SND": ([128, F * P], bf),
+    "GP": ([128, P], bf), "GQ": ([128, P], bf), "RR": ([128, P], bf),
+    "IA": ([128, 256], i32), "IB": ([128, 256], i32), "VY": ([128, 8, 2, 32], i32), "VX": ([128, 8, 2, 32], i32),
+    "CT": ([8, 48], i32), "CB": ([8, 48], bf), "RT": ([64, 3], i32), "RTB": ([64, 3], bf),
+    "ONE": ([128, 256], bf), "MR": ([1, 256], bf), "J": ([128, 256], bf), "JH": ([128, 256], bf), "N15": ([128, 128], bf), "I32": ([128, 128], bf),
+    "E8": ([8, 128], bf), "E8B": ([8, 128], bf), "SEL": ([64, 128], bf), "BO": ([128, 128], f32),
+    "LA": ([128, 128], bf), "LB": ([128, 128], bf), "LS": ([128, 128], bf),
+    "PI": ([128, 8], i32), "PC": ([128, 24], f32), "F8": ([128, 8], f32), "F96": ([128, 96], f32), "EF": ([128, 8], f32),
+    "ACT": ([128, 8], f32), "CMP": ([128, 16], f32),
+    "JL": ([128, 26], f32), "JI": ([128, 26], i32), "JU": ([128, 26], u16), "NR": ([128, 416], f32),
+    "KC": ([128, 156], bf), "KT": ([128, 78], f32), "DA": ([128, 40], f32), "IDF": ([128, 128], f32), "POW": ([128, P], bf), "DL": ([128, 96], f32),
+    "RA": ([128, 24], f32), "RB": ([128, 16], f32), "RL": ([128, 96], f32),
+    "CS": ([128, 24], f32), "CL": ([128, 8, 3, 4], f32), "TB": ([128, 24], f32), "TL": ([128, 96], f32), "LU": ([128, 96], u16),
+    "C1": ([128, 8, 192], i32), "BY": ([128, 64], bf), "BX": ([128, 64], bf),
+    "ZR": ([128, 104], f32), "GA": ([128, 8], f32), "INI": ([128, 8], f32), "NE": ([128, 16], f32), "N99": ([128, 16], f32),
+    "SM": ([128, 16], f32), "TT": ([128, 8], f32), "TG": ([128, 16], f32), "EQ": ([128, 416], bf),
+    "M2": ([128, 8, 2, NN], bf), "M1": ([128, 208], bf), "K2": ([128, 52], f32),
+    "X": ([128, 52], f32), "Q": ([128, 52], f32), "PRD": ([128, 52], f32), "AA": ([128, NN], f32), "BB": ([128, NN], f32),
+    "EE": ([128, 8, NN], f32), "EQC": ([128, NN], bf), "H": ([128, NN], bf),
+    "Y": ([128, 104], f32), "R": ([128, 104], f32), "PP": ([128, 104], f32), "P2": ([128, 52], f32), "RK": ([128, NN], f32),
+    "RAB": ([128, 2, NN], f32), "EW": ([128, 2, 3, NN], f32), "EP": ([128, 156], f32),
+    "IDX": ([128, 8, 2, 32], bf), "H1": ([128, 8, 2, 32], bf), "H2": ([128, 8, 2, 32], bf), "HB": ([128, 8, 2, 32], bf),
+    "Z1": ([128, P], bf), "Z2": ([128, P], bf), "NVY": ([128, 8, 2, 32], bf), "NVX": ([128, 8, 2, 32], bf), "THR": ([128, 256], f32),
+    "MK": ([128, 8, 160], f32), "U1": ([128, P], f32), "U2": ([128, P], f32), "XI": ([128, 8, 2, 32], i32),
+    "SS": ([128, 8, 2, 32], i32), "REC": ([128, 11 * 160], i32), "G": ([128, 192], i32), "MW": ([128, 160], i32),
+    "HY": ([128, 64], i32), "HX": ([128, 64], i32), "CY": ([128, 64], i32), "CX": ([128, 64], i32),
+    "S1": ([128, 64], i32), "S2": ([128, 64], i32), "OFF": ([128, F * 64], u16),
+}
+PS_ = ["PA", "PB", "PU", "XY", "XX", "PM", "PN", "PW"]
+SCRATCH = {k: ("sbuf", v[0], v[1]) for k, v in SB_.items()}
+SCRATCH.update({k: ("psum", [128, P], f32) for k in PS_})
+DMAS = ["ctl", "rt_", "pic", "ia_", "ib_", "vy_", "vx_", "nul", "res0", "res1", "res2"] + ["out%d" % f for f in range(F + 3)]
+SEMAPHORES = ["dve", "act", "pe", "pool"] + DMAS + ["arr%d" % f for f in range(F)] + ["snt%d" % f for f in range(F)]
+
+PSLOT = [4, 3, 2, 1, 0, 9, 8, 10]
+
+
+def wbase(f):
+    return max(0, 5 - f)
+
+
+def build(T, nxt):
+    ops = []
+    cache = {}
+    al = slice(None)
+
+    def S(name, *ix, parts=al):
+        shape = SCRATCH[name][1]
+        if name not in cache:
+            cache[name] = np.arange(int(np.prod(shape[1:]))).reshape(shape[1:])
+        el = np.asarray(cache[name][ix] if ix else cache[name]).ravel()
+        return (T[name][(parts,) + ix], name, el)
+
+    def C(name, a, b=None, st=None):
+        return S(name, slice(a, a + 1 if b is None else b, st))
+
+    def IND(win, off):
+        return (win[0].indirect(off[0]), win[1], win[2], off)
+
+    def val(x):
+        return x[0] if isinstance(x, tuple) else x
+
+    def add(q, fn, outs, ins, waits=(), sem=None):
+        rd = []
+        for x in ins:
+            if isinstance(x, tuple):
+                rd.append((x[1], x[2]))
+                if len(x) > 3:
+                    rd.append((x[3][1], x[3][2]))
+        ops.append((q, fn, rd, [(x[1], x[2]) for x in outs], list(waits), sem))
+
+    def ts(o, i, s1, op0, s2=None, op1=None, waits=()):
+        if op1 is None:
+            add("dve", lambda e: e.tensor_scalar(o[0], i[0], val(s1), None, op0), [o], [i, s1], waits)
+        else:
+            add("dve", lambda e: e.tensor_scalar(o[0], i[0], val(s1), val(s2), op0, op1), [o], [i, s1, s2], waits)
+
+    def tt(o, a, b, op):
+        add("dve", lambda e: e.tensor_tensor(o[0], a[0], b[0], op), [o], [a, b])
+
+    def cp(o, i):
+        add("dve", lambda e: e.tensor_copy(o[0], i[0]), [o], [i])
+
+    def ms(o, c):
+        add("dve", lambda e: e.memset(o[0], c), [o], [])
+
+    def red(o, i):
+        add("dve", lambda e: e.tensor_reduce(o[0], i[0], AxisListType.X, A.add), [o], [i])
+
+    def scan(o, d0, d1, ini):
+        add("dve", lambda e: e.tensor_tensor_scan(o[0], d0[0], d1[0], val(ini), A.add, A.add), [o], [d0, d1, ini])
+
+    def act(o, i, func=AF.Identity, bias=0.0, scale=1.0, waits=()):
+        add("act", lambda e: e.activation(o[0], i[0], func, bias=val(bias), scale=val(scale)), [o], [i, bias, scale], waits)
+
+    def mm(o, l, r, st, sp):
+        add("pe", lambda e: e.matmul(o[0], l[0], r[0], st, sp), [o], [l, r])
+
+    def iota(o, pat, base, cm=0):
+        if SCRATCH[o[1]][2] == i32:
+            add("pool", lambda e: e.iota(o[0], pat, base, cm), [o], [])
+        else:
+            add("pool", lambda e: e.iota(o[0], pat, base, cm, allow_small_or_imprecise_dtypes=True), [o], [])
+
+    def sel(name, pat):
+        o = S(name)
+        n, w = SCRATCH[name][1]
+        i = S("ONE", slice(0, w), parts=slice(0, n))
+        add("pool", lambda e: e.affine_select(o[0], i[0], pat, A.is_equal, 0.0, 0, -1), [o], [i])
+
+    def dma(q, o, i, sem, waits=()):
+        add(q, lambda e: e.dma_start(val(o), val(i)), [o] if isinstance(o, tuple) else [], [i], waits, sem)
+
+    def send(o, i, k):
+        add("pool", lambda e: e.remote_dma(o[0], i[0], T.sem["arr%d" % k], T.sem["snt%d" % k], nxt[1], nxt[0], nxt[2]),
+            [], [i], (), "remote")
+
+    neng = bin(nxt[2]).count("1")
+    narr = nxt[3]
+    nsend = len(SEND_AFTER)
+    col = lambda k: C("PC", k)
+    FP, HALF, G16, G31, NH, KA, KB, SC, W16, H5, CN, CH, CQ, KCB, WS, T0, T1, T2, T3 = range(19)
+
+    dma("sync", C("CT", 0, 8), T.gaps[:], "ctl")
+    dma("scalar", C("CT", 32, 40), T.cmd[:], "ctl")
+    dma("sync", C("CT", 8, 32), T.rel[:], "ctl")
+    dma("scalar", C("CT", 40, 48), T.cmd[:], "ctl")
+    dma("sync", S("IA"), T.ia[:], "ia_")
+    dma("scalar", S("IB"), T.ib[:], "ib_")
+    dma("sync", C("W", 5 * P, 7 * P), T.pic0[:], "pic")
+    dma("sync", S("RT"), T.rel[:], "rt_")
+    dma("sync", S("VY"), T.vy[:], "vy_")
+    dma("sync", S("VX"), T.vx[:], "vx_")
+    dma("sync", C("RES", 0, P), T.res[:, 0:P], "res0")
+    dma("sync", C("RES", P, 3 * P), T.res[:, P:3 * P], "res1")
+
+    ms(S("ONE"), 1.0)
+    iota(C("PI", 0), [[0, 1]], 0, 1)
+    iota(S("F8"), [[1, 8]], 0)
+    sel("E8", [[1, 8], [0, 16]])
+    iota(S("JL"), [[16, 26]], 0, 1)
+    sel("J", [[0, 2], [1, 128]])
+    iota(S("NR"), [[0, 16], [-1, NN]], -1)
+    sel("E8B", [[1, 8], [100, 2], [0, 8]])
+    sel("SEL", [[8, 8], [0, 2], [1, 8]])
+    send(C("W", 8 * P, 9 * P), C("W", 6 * P, 7 * P), 0)
+    iota(S("BY"), [[0, 2], [32, 16], [0, 2]], 0)
+    iota(S("BX"), [[0, 32], [16, 2]], 0, 1)
+    iota(S("C1", al, slice(0, 64)), [[8192, 8], [0, 64]], 0)
+    iota(S("C1", al, slice(64, 128)), [[0, 16], [32, 16], [0, 2]], 0)
+    iota(S("C1", al, slice(128, 192)), [[0, 256], [16, 2]], 0, 1)
+    iota(S("F96"), [[1, 8], [0, 12]], 0)
+    for s, b in enumerate((0, 32, 96)):
+        iota(S("CL", al, s), [[0, 16], [16, 2]], b, 1)
+    ms(S("ZR"), 0.0)
+    ts(C("PI", 1), C("PI", 0), 7, A.bitwise_and)
+    ts(C("PI", 2), C("PI", 0), 3, A.arith_shift_right, 1, A.bitwise_and)
+    ts(C("PI", 3), C("PI", 0), 112, A.bitwise_and)
+    ms(S("MR"), BIG)
+    cp(C("PC", 0, 3), C("PI", 1, 4))
+    ms(C("W", 7 * P, 8 * P), 128.0)
+    ts(S("ACT"), S("F8"), col(FP), A.is_le)
+    ts(S("JL"), S("JL"), col(G16), A.subtract, 12.5, A.subtract)
+    ms(S("HB", al, 0), 0.0)
+    ts(C("CMP", 0, 8), S("ACT"), 7.0, A.mult, -5.0, A.add)
+    ts(S("JL"), S("JL"), 1.0 / NN, A.mult)
+    ts(C("CMP", 8, 16), S("ACT"), 6.0, A.mult, -5.0, A.add)
+    cp(S("JI"), S("JL"))
+    for k, sc, bi in ((NH, -1.0, 1.0), (KA, 6.0, 1.0), (KB, -2.0, 4.0), (SC, 2.0, 1.0), (W16, -16.0, 16.0), (H5, 0.3125, 0.0),
+                      (CN, 0.5, -0.5), (CH, 0.5, 0.0), (CQ, -0.5, 0.5)):
+        act(col(k), col(HALF), scale=sc, bias=bi)
+    act(col(G31), col(G16), bias=31.0)
+    act(col(T0), col(FP), AF.Relu, scale=-1.0, bias=5.0)
+    act(col(T1), col(FP), AF.Sign, bias=-4.5)
+    act(S("EF"), S("F8"), AF.Abs, scale=-1.0, bias=col(FP))
+    act(col(T2), col(T0), scale=-1.0, bias=23.0)
+    act(col(T3), col(T1), scale=5.0, bias=2.0)
+    act(S("EF"), S("EF"), AF.Relu, scale=-1.0, bias=1.0)
+    act(col(KCB), col(T2), scale=col(HALF), bias=-16.0)
+    act(col(T0), col(FP), scale=-1.0, bias=col(T3))
+    ID = C("J", 0, 128)
+    act(S("N15"), ID, scale=-1.5)
+    act(col(WS), col(T0), scale=col(NH))
+
+    cp(S("CB"), S("CT"))
+    mm(C("PM", 0, 48), S("E8"), S("CB"), True, True)
+    cp(S("JU"), S("JI"))
+    ND = C("PN", 0, 256)
+    tt(S("GA"), C("PM", 0, 8), S("ACT"), A.mult)
+    tt(S("NE"), C("PM", 32, 48), S("CMP"), A.not_equal)
+    ts(C("SM", 0), C("PM", 0), 1.0, A.is_lt, -99.0, A.mult)
+    scan(S("INI"), S("GA"), S("ACT"), -25.0)
+    ts(S("N99"), S("NE"), -99.0, A.mult)
+    tt(S("TT"), S("INI"), C("PM", 8, 32, 3), A.subtract)
+    ts(ND, S("IA"), 8.0, A.is_le)
+    tt(C("TG", 1, 8), C("TT", 1, 8), C("N99", 1, 8), A.add)
+    ts(C("TG", 0), C("N99", 0), C("TT", 0), A.add, C("SM", 0), A.add)
+    tt(C("TG", 8, 16), S("TT"), C("N99", 8, 16), A.add)
+    tt(S("IDX", al, 0), S("IA"), ND, A.mult)
+    tt(S("EQ"), IND(C("TG", 0, 16), C("JU", 0, 26)), S("NR"), A.is_equal)
+    tt(S("IDX", al, 1), S("IB"), ND, A.mult)
+    cp(S("RTB"), S("RT"))
+    CP = C("INI", 7)
+    NR = C("NR", 0, NN)
+    E = lambda k: S("EE", k)
+    act(S("KT"), C("NR", 0, 78), AF.Relu, scale=-1.0, bias=-24.0)
+    mm(C("PU", 0, 208), ID, C("EQ", 0, 208), True, False)
+    mm(C("PU", 0, 208), ID, C("EQ", 208, 416), False, True)
+    act(S("M2", slice(2, 8), 0), C("EQ", 52, 208), scale=-99.0, bias=99.0)
+    act(S("M2", slice(2, 8), 1), C("EQ", 260, 416), scale=108.0, bias=-99.0)
+    act(C("M1", 52, 208), C("PU", 52, 208), scale=-9.0, bias=9.0)
+    act(S("H1"), S("IDX"), AF.Sign, bias=-2.5)
+    mm(C("PW", 0, 3), S("SEL"), S("RTB"), True, True)
+    mm(C("XY", 0, 128), S("E8"), S("E8"), True, True)
+    mm(C("XX", 0, 128), S("E8"), S("E8B"), True, True)
+    act(S("H2"), S("IDX"), AF.Sign, bias=-5.5)
+    act(S("HB", al, 1), S("H1", al, 1), scale=0.5, bias=-0.5)
+    act(C("SM", 1, 3), C("PW", 1, 3), scale=-1.0, bias=CP)
+    for bank in ("PA", "PB"):
+        mm(S(bank), ID, S("IDX"), True, False)
+        mm(S(bank), S("N15"), S("H1"), False, False)
+        mm(S(bank), S("N15"), S("H2"), False, bank == "PA")
+    mm(S("PB"), ID, S("HB"), False, True)
+    act(E(4), NR, AF.Relu, scale=-1.0, bias=CP)
+    act(E(3), NR, AF.Abs, scale=-1.0, bias=CP)
+    act(E(0), NR, AF.Abs, scale=-1.0, bias=C("SM", 1))
+    act(E(1), NR, AF.Abs, scale=-1.0, bias=C("SM", 2))
+    act(S("LA"), C("XY", 0, 128), scale=col(W16))
+    act(E(4), E(4), AF.Sign)
+    act(S("EQC"), E(3), AF.Relu, scale=-1.0, bias=1.0)
+    act(S("EE", slice(0, 2)), S("EE", slice(0, 2)), AF.Relu, scale=-1.0, bias=1.0)
+    act(S("LS"), C("XY", 0, 128), scale=col(WS))
+    act(S("BO"), C("XY", 0, 128))
+    act(S("LB"), C("XX", 0, 128), scale=col(W16))
+    act(S("I32"), ID, scale=32.0)
+    act(C("KC", 0, 78), S("KT"), scale=-1.0, bias=-16.0)
+    act(C("KC", 78, 156), S("KT"), scale=-1.0, bias=col(KCB))
+    act(S("Z1"), S("PA"), AF.Relu, bias=-4.0)
+    act(S("Z2"), S("PB"), AF.Abs, bias=-3.0)
+    act(S("Z1"), S("Z1"), scale=-127.0 / 16384, bias=1.0 / 128)
+    act(S("Z2"), S("Z2"), AF.Relu, scale=-127.0 / 128, bias=127.0 / 128)
+    act(C("DA", 0, 8), S("EF"), scale=0.5)
+    act(C("DA", 8, 16), S("EF"), scale=col(CN))
+    act(C("DA", 16, 24), S("EF"), scale=col(CH))
+    act(C("DA", 24, 32), S("EF"), scale=col(CQ))
+    act(C("DA", 32, 40), S("EF"), scale=col(CN))
+    act(S("IDF"), ID)
+    act(C("CS", 0, 8), S("F8"), scale=4194304.0, bias=7.0 * 16513 * 512 + 4194304.0)
+    act(C("CS", 8, 16), S("F8"), scale=0.0)
+    act(C("CS", 16, 24), S("F8"), scale=4194304.0, bias=4194304.0)
+    act(S("JH"), S("J"), scale=0.5)
+    act(S("DL"), S("F96"), AF.Abs, scale=-1.0, bias=col(FP))
+    for s in range(5, 9):
+        dma("sync", C("REC", 160 * s, 160 * s + 160), S("C1", 0, slice(32, 192)), "nul")
+    dma("sync", C("RES", 3 * P, F * P), T.res[:, 3 * P:F * P], "res2", [("snt0", neng)])
+
+    def vec_dve(f0, f1):
+        fs = slice(f0, f1)
+        nd = C("PN", 32 * f0, 32 * f1)
+        return [lambda n=n, i=i: tt(S("N" + n, fs, i), S(n, fs, i), nd, A.mult) for n in ("VY", "VX") for i in (0, 1)]
+
+    def vec_pe(f0, f1):
+        for bank, w, n, b in (("XY", S("I32"), "NVY", "BY"), ("XX", ID, "NVX", "BX")):
+            mm(C(bank, 64 * f0, 64 * f1), w, S(n, slice(f0, f1)), True, False)
+            for k in range(f0, f1):
+                mm(C(bank, 64 * k, 64 * k + 64), ID, S(b), False, k == f1 - 1)
+
+    U, L = C("X", NN, 2 * NN), C("X", 0, NN)
+    QS = C("Q", NN, 2 * NN)
+    tt(S("K2"), C("EQ", 0, 52), C("EQ", 208, 260), A.is_equal)
+    tt(S("AA"), C("EQ", 208, 234), C("EQ", 26, 52), A.is_gt)
+    tt(S("BB"), C("K2", 0, NN), C("EQ", 234, 260), A.mult)
+    tt(U, C("K2", 0, NN), C("K2", NN, 52), A.mult)
+    tt(L, S("AA"), S("BB"), A.add)
+    fill = vec_dve(0, 2) + [
+        lambda: tt(E(2), E(0), E(1), A.is_gt),
+        lambda: tt(E(5), E(2), E(1), A.is_equal),
+        lambda: tt(E(6), E(4), E(5), A.mult),
+    ]
+    for f in range(2, F):
+        fill.pop(0)()
+        scan(S("Q"), S("X"), C("ZR", 0, 52), C("INI", f))
+        tt(S("PRD"), S("X"), S("M2", f), A.mult)
+        tt(S("AA"), U, C("M1", f * NN, (f + 1) * NN), A.mult)
+        tt(S("BB"), C("PRD", 0, NN), C("PRD", NN, 2 * NN), A.add)
+        tt(U, S("AA"), QS, A.is_gt)
+        tt(L, S("BB"), QS, A.is_gt)
+        if f == 5:
+            vec_pe(0, 2)
+            mm(S("PW"), ID, S("Z1"), True, False)
+            mm(S("PW"), ID, S("Z2"), False, True)
+            act(S("POW"), S("PW"))
+    fill.pop(0)()
+    tt(S("H"), U, L, A.add)
+    tt(C("Y", 52, 78), U, E(6), A.mult)
+    tt(C("Y", 78, 104), L, E(5), A.mult)
+    tt(C("Y", 0, 26), S("H"), E(1), A.mult)
+    tt(C("Y", 26, 52), S("H"), E(2), A.mult)
+    D = C("PM", 64, 220)
+    mm(D, ID, S("KC"), True, False)
+    for k in range(6):
+        d = C("PM", 64 + NN * k, 64 + NN * k + NN)
+        mm(d, S("LS"), S("EQC"), False, False)
+    for k in range(6):
+        d = C("PM", 64 + NN * k, 64 + NN * k + NN)
+        mm(d, S("LA" if k < 3 else "LB"), S("H"), False, k == 5)
+    scan(C("PU", 256, 360), S("Y"), S("ZR"), 0.0)
+    ts(C("PU", 384, 448), C("XY", 0, 64), 0.0, A.max, 480.0, A.min)
+    ts(C("SM", 3), C("PU", 359), C("PU", 333), A.add, 1.0, A.add)
+    ts(S("CX"), C("XX", 0, 64), col(G16), A.max, col(G31), A.min)
+    ts(C("PU", 334, 360), C("PU", 334, 360), -1.0, A.mult, C("SM", 3), A.add)
+    tt(C("PU", 448, 512), C("PU", 384, 448), S("CX"), A.add)
+    tt(S("PP"), S("Y"), C("PU", 256, 360), A.mult)
+    tt(S("P2"), C("PP", 0, 52), C("PP", 52, 104), A.add)
+    tt(S("RK"), C("P2", 0, NN), C("P2", NN, 52), A.add)
+    ts(S("RAB", 0), S("RK"), col(KA), A.subtract)
+    ts(S("RAB", 1), S("RK"), col(KB), A.subtract, col(SC), A.mult)
+    for k in range(3):
+        ts(S("EW", al, k), S("RAB"), float(k), A.is_equal, 512.0 * 128 ** k, A.mult)
+    tt(S("EP"), S("EW"), D, A.mult)
+    red(C("SM", 4), C("EP", 0, 78))
+    red(C("SM", 5), C("EP", 78, 156))
+    mm(C("PM", 256, 280), S("IDF"), S("CS"), True, False)
+    ts(S("RA"), C("DA", 0, 24), C("SM", 4), A.mult)
+    ts(S("RB"), C("DA", 24, 40), C("SM", 5), A.mult)
+    mm(C("PM", 256, 280), S("BO"), S("RA"), False, False)
+    mm(C("PM", 264, 280), S("BO"), S("RB"), False, True)
+    r0 = 160 * PSLOT[0]
+    cp(C("REC", r0 + 32, r0 + 96), C("XY", 0, 64))
+    cp(C("REC", r0 + 96, r0 + 160), C("XX", 0, 64))
+    act(S("DL"), S("DL"), AF.Relu, scale=-1.0, bias=1.0)
+    act(S("THR"), ND, scale=1000000.0)
+    act(S("DL"), S("DL"), scale=col(H5))
+    for k in range(4):
+        sg = 1.0 if k % 2 else -1.0
+        act(S("MK", slice(1, 8), slice(32 * k + 32, 32 * k + 64)), C("PN", 32, 256), scale=sg, bias=-sg)
+
+    def look_act(f0, f1):
+        for f in range(f0, f1):
+            act(C("U1", 64 * f, 64 * f + 64), S("H1", f), scale=C("TB", 8 + f), bias=C("TB", f))
+            act(C("U2", 64 * f, 64 * f + 64), S("H2", f), scale=C("TB", 16 + f))
+        mm(C("PW", 64 * f0, 64 * f1), S("IDF"), C("U1", 64 * f0, 64 * f1), True, False)
+        mm(C("PW", 64 * f0, 64 * f1), S("IDF"), C("U2", 64 * f0, 64 * f1), False, True)
+
+    def look_dve(f0, f1):
+        tt(S("XI", slice(f0, f1)), C("PW", 64 * f0, 64 * f1), C("POW", 64 * f0, 64 * f1), A.mult)
+        ts(S("C1", slice(f0, f1), slice(32, 64)), S("XI", slice(f0, f1), 0), 65024, A.bitwise_and)
+        ts(S("SS", slice(f0, f1), 1), S("XI", slice(f0, f1), 1), 7680, A.bitwise_and)
+
+    def motion(f):
+        r = 160 * PSLOT[f]
+        ry, rx = C("REC", r + 32, r + 96), C("REC", r + 96, r + 160)
+        xy, xx = C("XY", 64 * f, 64 * f + 64), C("XX", 64 * f, 64 * f + 64)
+        if f > 0:
+            win = C("REC", 160 * wbase(f), 160 * (8 if f < 6 else 10))
+            tt(S("G"), IND(win, C("LU", 12 * f, 12 * f + 12)), S("C1", f), A.subtract)
+            tt(S("MK", f, slice(0, 32)), C("G", 0, 32), C("THR", 32 * f, 32 * f + 32), A.is_ge)
+            tt(S("MW"), C("G", 32, 192), S("MK", f), A.mult)
+            ts(S("HY"), C("MW", 32, 96), 1, A.arith_shift_right, -32, A.bitwise_and)
+            ts(S("HX"), C("MW", 96, 160), 1, A.arith_shift_right)
+            tt(C("REC", r, r + 32), C("MW", 0, 32), S("C1", f, slice(32, 64)), A.add)
+            tt(ry, S("HY"), xy, A.add)
+            tt(rx, S("HX"), xx, A.add)
+            ts(S("SS", f, 0), C("REC", r, r + 32), 7680, A.bitwise_and)
+            ts(CY, ry, 0.0, A.max, 480.0, A.min)
+            ts(S("CX"), rx, col(G16), A.max, col(G31), A.min)
+            tt(S1, CY, S("SS", f), A.add)
+            tt(S("S2"), S1, S("CX"), A.add)
+        else:
+            tt(S("S2"), C("PU", 448, 512), S("SS", f), A.add)
+        ts(C("OFF", 64 * f, 64 * f + 64), S("S2"), col(G16), A.subtract, float(-P * wbase(f)), A.add)
+
+    banks = ["PA", "PB", "PU"]
+    pieces = list(zip(CUTS[:-1], CUTS[1:]))
+    row1 = S("ONE", slice(0, 128), parts=slice(0, 1))
+
+    def pixels_front(f):
+        s = 16 * ((f + 1) % 8)
+        win = C("W", P * wbase(f), P * (9 + f))
+        aw = [("arr%d" % f, narr * (nsend if f else 1))]
+        for h, (a, b) in enumerate(pieces):
+            mm(C(banks[h], 0, b - a), C("J", s, s + 128), C("RES", f * P + a, f * P + b), True, False)
+        for a, b in pieces:
+            act(C("GP", a, b), IND(win, C("OFF", 64 * f + a // 16, 64 * f + b // 16)), AF.Relu, waits=aw)
+            ts(C("GQ", a, b), IND(win, C("OFF", 64 * f + 32 + a // 16, 64 * f + 32 + b // 16)), 0.0, A.max, -127.5, A.add, aw)
+        sent = 0
+        for h, (a, b) in enumerate(pieces):
+            ps = C(banks[h], 0, b - a)
+            out = C("SND", f * P + a, f * P + b)
+            mm(ps, C("JH", s, s + 128), C("GQ", a, b), False, False)
+            mm(ps, C("JH", s, s + 128), C("GP", a, b), False, False)
+            mm(ps, row1, C("MR", 0, b - a), False, True)
+            if f == F - 1:
+                act(C("RR", a, b), ps, AF.Relu, bias=64.0 - BIG)
+                ts(out, C("RR", a, b), 255.0, A.min)
+                dma("sync", T.y[:, f * P + a:f * P + b], out, "out%d" % (f + h))
+                continue
+            ts(out, ps, 64.0 - BIG, A.add, 255.0, A.min)
+            if h in SEND_AFTER:
+                send(C("W", (9 + f) * P + sent, (9 + f) * P + b), C("SND", f * P + sent, f * P + b), f + 1)
+                sent = b
+
+    def pixels_back(f):
+        s = 128 - 16 * (f + 1)
+        own = C("W", PSLOT[f] * P, PSLOT[f] * P + P)
+        mm(S("PU"), C("J", s, s + 128), C("SND", f * P, f * P + P), True, True)
+        act(own, S("PU"), AF.Relu)
+        dma("sync", T.y[:, f * P:f * P + P], own, "out%d" % f, [("snt%d" % (f + 1), neng * nsend)])
+
+    CY, S1 = C("PN", 256, 320), C("PN", 320, 384)
+    ts(C("U2", 0, 64), S("H2", 0), C("PM", 272), A.mult)
+    ts(C("U1", 0, 64), S("H1", 0), C("PM", 264), A.mult, C("PM", 256), A.add)
+    tt(C("U1", 0, 64), C("U1", 0, 64), C("U2", 0, 64), A.add)
+    act(S("RL"), S("DL"), scale=C("SM", 5))
+    act(S("TB"), C("PM", 256, 280))
+    tt(S("XI", 0), C("U1", 0, 64), C("PW", 0, 64), A.mult)
+    ts(S("SS", 0), S("XI", 0), 7680, A.bitwise_and)
+    motion(0)
+    mm(C("PM", 280, 376), S("BO"), S("RL"), True, True)
+    ts(C("REC", r0, r0 + 32), S("XI", 0, 0), 65024, A.bitwise_and)
+    for f in range(F):
+        pixels_front(f)
+        if f == F - 1:
+            break
+        if f == 0:
+            look_act(1, 2)
+            tt(S("TL"), C("PM", 280, 376), S("CL"), A.add)
+            ts(S("LU"), S("TL"), col(G16), A.subtract)
+            look_dve(1, 2)
+        pixels_back(f)
+        if f in LOOK:
+            look_act(*LOOK[f])
+        if f in VEC:
+            for k in vec_dve(*VEC[f]):
+                k()
+            vec_pe(*VEC[f])
+        if f - 1 in LOOK:
+            look_dve(*LOOK[f - 1])
+        motion(f + 1)
+    return ops, neng, narr
+
+
+def emit(g, T, ops, neng, narr):
+    eng = {"dve": g.vector, "act": g.scalar, "pe": g.tensor, "pool": g, "sync": g.sync, "scalar": g.scalar}
+    queue = {"scalar": "act"}
+    total = {}
+    for o in ops:
+        if o[5] in DMAS:
+            total[o[5]] = total.get(o[5], 0) + 16
+    count = {"dve": 0, "act": 0, "pe": 0, "pool": 0}
+    seen = {q: {} for q in ("dve", "act", "pe", "pool", "sync")}
+    known = {}
+    acc = {}
+    waited = {}
+    for q0, fn, rd, wr, waits, sem in ops:
+        q = queue.get(q0, q0)
+        need = {}
+        for s, v in waits:
+            need[s] = max(need.get(s, 0), v)
+        for name, el, w in [(n, e, False) for n, e in rd] + [(n, e, True) for n, e in wr]:
+            lo, hi = int(el.min()), int(el.max())
+            for pq, pw, plo, phi, pel, tok, pdma in acc.get(name, ()):
+                if sem is not None and tok[0] == sem:
+                    continue
+                same = pq == q and not pdma and sem is None
+                box = plo <= hi and lo <= phi
+                if name in PS_ and not same:
+                    hit = True
+                elif not (w or pw) or not box:
+                    hit = False
+                elif same and q == "pe":
+                    hit = False
+                elif same and w:
+                    hit = bool(np.intersect1d(el, pel).size)
+                else:
+                    hit = True
+                if hit:
+                    need[tok[0]] = max(need.get(tok[0], 0), tok[1])
+        for s, v in sorted(need.items(), key=lambda x: -x[1]):
+            if seen[q].get(s, 0) < v:
+                eng[q].wait_ge(T.sem[s], v)
+                waited[s] = max(waited.get(s, 0), v)
+                seen[q][s] = v
+                for s2, v2 in known.get((s, v), {}).items():
+                    seen[q][s2] = max(seen[q].get(s2, 0), v2)
+        ins = fn(eng[q0]) if fn else None
+        if sem == "remote":
+            continue
+        if sem is None:
+            count[q] += 1
+            tok = (q, count[q])
+            ins.then_inc(T.sem[q], 1)
+            known[tok] = dict(seen[q])
+        else:
+            tok = (sem, total[sem])
+            ins.then_inc(T.sem[sem], 16)
+        for name, el, w in [(n, e, False) for n, e in rd] + [(n, e, True) for n, e in wr]:
+            acc.setdefault(name, []).append((q, w, int(el.min()), int(el.max()), el, tok, sem is not None))
+    last = dict(total)
+    last.update(count)
+    for s, v in last.items():
+        if waited.get(s, 0) < v:
+            g.sync.wait_ge(T.sem[s], v)
+
+
+def rank_program(g, core, T, topo):
+    rank = T.rank_of(core)
+    if rank is None:
+        return
+    n = len(T.cores)
+    dst, src = T.cores[(rank + 1) % n], T.cores[(rank - 1) % n]
+    rid, pid, _ = topo.addr(dst)
+    nxt = (rid, pid, topo.mask(core, dst), len(topo.engines(src, core)))
+    ops, neng, narr = build(T, nxt)
+    emit(g, T, ops, neng, narr)

@@ -3,10 +3,9 @@ from concourse.mybir import AluOpType as A, AxisListType, ActivationFunctionType
 
 F = 8
 P = 512
-CUTS = [0, 192, 384, 512]
-SEND_AFTER = [2]
-LOOK = {0: (2, 4), 2: (4, 6), 4: (6, 8)}
-VEC = {1: (2, 4), 2: (4, 6), 4: (6, 8)}
+CUTS = [0, 160, 320, 448, 512]
+LOOK = {0: (3, 5), 2: (5, 8)}
+MASK = {0: (3, 5), 1: (5, 8)}
 BIG = 12582912.0
 NN = 26
 
@@ -16,7 +15,7 @@ SB_ = {
     "GP": ([128, P], bf), "GQ": ([128, P], bf), "RR": ([128, P], bf),
     "IA": ([128, 256], i32), "IB": ([128, 256], i32), "VY": ([128, 8, 2, 32], i32), "VX": ([128, 8, 2, 32], i32),
     "CT": ([8, 48], i32), "CB": ([8, 48], bf), "RT": ([64, 3], i32), "RTB": ([64, 3], bf),
-    "ONE": ([128, 256], bf), "MR": ([1, 256], bf), "J": ([128, 256], bf), "JH": ([128, 256], bf), "N15": ([128, 128], bf), "I32": ([128, 128], bf),
+    "ONE": ([128, 256], bf), "MR": ([1, 256], bf), "MZ": ([1, 256], bf), "M64": ([1, 256], bf), "J": ([128, 256], bf), "JH": ([128, 256], bf), "IW": ([128, 128], bf), "C7": ([1, 128], bf), "JM": ([128, 256], bf), "JN": ([128, 256], bf), "YO": ([128, 7 * P], bf), "N15": ([128, 128], bf), "I32": ([128, 128], bf),
     "E8": ([8, 128], bf), "E8B": ([8, 128], bf), "SEL": ([64, 128], bf), "BO": ([128, 128], f32),
     "LA": ([128, 128], bf), "LB": ([128, 128], bf), "LS": ([128, 128], bf),
     "PI": ([128, 8], i32), "PC": ([128, 24], f32), "F8": ([128, 8], f32), "F96": ([128, 96], f32), "EF": ([128, 8], f32),
@@ -29,12 +28,12 @@ SB_ = {
     "ZR": ([128, 104], f32), "GA": ([128, 8], f32), "INI": ([128, 8], f32), "NE": ([128, 16], f32), "N99": ([128, 16], f32),
     "SM": ([128, 16], f32), "TT": ([128, 8], f32), "TG": ([128, 16], f32), "EQ": ([128, 416], bf),
     "M2": ([128, 8, 2, NN], bf), "M1": ([128, 208], bf), "K2": ([128, 52], f32),
-    "X": ([128, 52], f32), "Q": ([128, 52], f32), "PRD": ([128, 52], f32), "AA": ([128, NN], f32), "BB": ([128, NN], f32),
+    "X": ([128, 52], f32), "X2": ([128, 52], f32), "MV": ([128, 52], f32), "Q": ([128, 52], f32), "PRD": ([128, 52], f32), "AA": ([128, NN], f32), "BB": ([128, NN], f32),
     "EE": ([128, 8, NN], f32), "EQC": ([128, NN], bf), "H": ([128, NN], bf),
     "Y": ([128, 104], f32), "R": ([128, 104], f32), "PP": ([128, 104], f32), "P2": ([128, 52], f32), "RK": ([128, NN], f32),
     "RAB": ([128, 2, NN], f32), "EW": ([128, 2, 3, NN], f32), "EP": ([128, 156], f32),
     "IDX": ([128, 8, 2, 32], bf), "H1": ([128, 8, 2, 32], bf), "H2": ([128, 8, 2, 32], bf), "HB": ([128, 8, 2, 32], bf),
-    "Z1": ([128, P], bf), "Z2": ([128, P], bf), "NVY": ([128, 8, 2, 32], bf), "NVX": ([128, 8, 2, 32], bf), "THR": ([128, 256], f32),
+    "Z1": ([128, P], bf), "Z2": ([128, P], bf), "NVY": ([128, 8, 2, 32], bf), "NVX": ([128, 8, 2, 32], bf), "THR": ([128, 256], f32), "NDS": ([128, 8, 32], bf),
     "MK": ([128, 8, 160], f32), "U1": ([128, P], f32), "U2": ([128, P], f32), "XI": ([128, 8, 2, 32], i32),
     "SS": ([128, 8, 2, 32], i32), "REC": ([128, 11 * 160], i32), "G": ([128, 192], i32), "MW": ([128, 160], i32),
     "HY": ([128, 64], i32), "HX": ([128, 64], i32), "CY": ([128, 64], i32), "CX": ([128, 64], i32),
@@ -43,7 +42,7 @@ SB_ = {
 PS_ = ["PA", "PB", "PU", "XY", "XX", "PM", "PN", "PW"]
 SCRATCH = {k: ("sbuf", v[0], v[1]) for k, v in SB_.items()}
 SCRATCH.update({k: ("psum", [128, P], f32) for k in PS_})
-DMAS = ["ctl", "rt_", "pic", "ia_", "ib_", "vy_", "vx_", "nul", "res0", "res1", "res2"] + ["out%d" % f for f in range(F + 3)]
+DMAS = ["ctl", "rt_", "pic", "pi0", "ia_", "ib_", "vy_", "vx_", "nul", "res0", "res2", "res3", "res4", "res5", "res6", "res7"] + ["out%d" % f for f in range(F + 3)]
 SEMAPHORES = ["dve", "act", "pe", "pool"] + DMAS + ["arr%d" % f for f in range(F)] + ["snt%d" % f for f in range(F)]
 
 PSLOT = [4, 3, 2, 1, 0, 9, 8, 10]
@@ -129,9 +128,9 @@ def build(T, nxt):
         add("pool", lambda e: e.remote_dma(o[0], i[0], T.sem["arr%d" % k], T.sem["snt%d" % k], nxt[1], nxt[0], nxt[2]),
             [], [i], (), "remote")
 
+    WIDE = max(b - a for a, b in zip(CUTS[:-1], CUTS[1:]))
     neng = bin(nxt[2]).count("1")
     narr = nxt[3]
-    nsend = len(SEND_AFTER)
     col = lambda k: C("PC", k)
     FP, HALF, G16, G31, NH, KA, KB, SC, W16, H5, CN, CH, CQ, KCB, WS, T0, T1, T2, T3 = range(19)
 
@@ -141,12 +140,12 @@ def build(T, nxt):
     dma("scalar", C("CT", 40, 48), T.cmd[:], "ctl")
     dma("sync", S("IA"), T.ia[:], "ia_")
     dma("scalar", S("IB"), T.ib[:], "ib_")
-    dma("sync", C("W", 5 * P, 7 * P), T.pic0[:], "pic")
-    dma("sync", S("RT"), T.rel[:], "rt_")
+    dma("sync", C("YO", 6 * P, 7 * P), T.pic0[:, P:2 * P], "pic")
+    dma("scalar", S("RT"), T.rel[:], "rt_")
     dma("sync", S("VY"), T.vy[:], "vy_")
     dma("sync", S("VX"), T.vx[:], "vx_")
-    dma("sync", C("RES", 0, P), T.res[:, 0:P], "res0")
-    dma("sync", C("RES", P, 3 * P), T.res[:, P:3 * P], "res1")
+    dma("sync", C("YO", 5 * P, 6 * P), T.pic0[:, 0:P], "pi0")
+    dma("sync", C("RES", 0, 2 * P), T.res[:, 0:2 * P], "res0")
 
     ms(S("ONE"), 1.0)
     iota(C("PI", 0), [[0, 1]], 0, 1)
@@ -155,31 +154,27 @@ def build(T, nxt):
     iota(S("JL"), [[16, 26]], 0, 1)
     sel("J", [[0, 2], [1, 128]])
     iota(S("NR"), [[0, 16], [-1, NN]], -1)
-    sel("E8B", [[1, 8], [100, 2], [0, 8]])
+    send(C("YO", 4 * P, 5 * P), C("YO", 6 * P, 7 * P), 0)
     sel("SEL", [[8, 8], [0, 2], [1, 8]])
-    send(C("W", 8 * P, 9 * P), C("W", 6 * P, 7 * P), 0)
+    sel("E8B", [[1, 8], [100, 2], [0, 8]])
     iota(S("BY"), [[0, 2], [32, 16], [0, 2]], 0)
     iota(S("BX"), [[0, 32], [16, 2]], 0, 1)
-    iota(S("C1", al, slice(0, 64)), [[8192, 8], [0, 64]], 0)
-    iota(S("C1", al, slice(64, 128)), [[0, 16], [32, 16], [0, 2]], 0)
-    iota(S("C1", al, slice(128, 192)), [[0, 256], [16, 2]], 0, 1)
-    iota(S("F96"), [[1, 8], [0, 12]], 0)
-    for s, b in enumerate((0, 32, 96)):
-        iota(S("CL", al, s), [[0, 16], [16, 2]], b, 1)
     ms(S("ZR"), 0.0)
     ts(C("PI", 1), C("PI", 0), 7, A.bitwise_and)
     ts(C("PI", 2), C("PI", 0), 3, A.arith_shift_right, 1, A.bitwise_and)
     ts(C("PI", 3), C("PI", 0), 112, A.bitwise_and)
-    ms(S("MR"), BIG)
+    ms(S("C7"), 1.0 / 128)
+    ms(C("MV", NN, 2 * NN), 0.0)
     cp(C("PC", 0, 3), C("PI", 1, 4))
-    ms(C("W", 7 * P, 8 * P), 128.0)
+    ms(C("RR", 0, 256), 0.0)
     ts(S("ACT"), S("F8"), col(FP), A.is_le)
     ts(S("JL"), S("JL"), col(G16), A.subtract, 12.5, A.subtract)
-    ms(S("HB", al, 0), 0.0)
     ts(C("CMP", 0, 8), S("ACT"), 7.0, A.mult, -5.0, A.add)
     ts(S("JL"), S("JL"), 1.0 / NN, A.mult)
     ts(C("CMP", 8, 16), S("ACT"), 6.0, A.mult, -5.0, A.add)
     cp(S("JI"), S("JL"))
+    ms(S("HB", al, 0), 0.0)
+    cp(S("JU"), S("JI"))
     for k, sc, bi in ((NH, -1.0, 1.0), (KA, 6.0, 1.0), (KB, -2.0, 4.0), (SC, 2.0, 1.0), (W16, -16.0, 16.0), (H5, 0.3125, 0.0),
                       (CN, 0.5, -0.5), (CH, 0.5, 0.0), (CQ, -0.5, 0.5)):
         act(col(k), col(HALF), scale=sc, bias=bi)
@@ -195,21 +190,29 @@ def build(T, nxt):
     ID = C("J", 0, 128)
     act(S("N15"), ID, scale=-1.5)
     act(col(WS), col(T0), scale=col(NH))
+    iota(S("F96"), [[1, 8], [0, 12]], 0)
+    iota(S("C1", al, slice(0, 64)), [[8192, 8], [0, 64]], 0)
+    iota(S("C1", al, slice(64, 128)), [[0, 16], [32, 16], [0, 2]], 0)
+    iota(S("C1", al, slice(128, 192)), [[0, 256], [16, 2]], 0, 1)
+    for name, v in (("JN", -1.0), ("JH", 0.5), ("JM", -0.5)):
+        add("pool", lambda e, name=name, v=v: e.affine_select(T[name][:], T.RR[:, 0:256], [[0, 2], [1, 128]], A.not_equal, v, 0, -1),
+            [S(name)], [C("RR", 0, 256)])
+    for s, b in enumerate((0, 32, 96)):
+        iota(S("CL", al, s), [[0, 16], [16, 2]], b, 1)
 
     cp(S("CB"), S("CT"))
     mm(C("PM", 0, 48), S("E8"), S("CB"), True, True)
-    cp(S("JU"), S("JI"))
     ND = C("PN", 0, 256)
+    ms(C("W", 7 * P, 8 * P), 127.0)
     tt(S("GA"), C("PM", 0, 8), S("ACT"), A.mult)
-    tt(S("NE"), C("PM", 32, 48), S("CMP"), A.not_equal)
-    ts(C("SM", 0), C("PM", 0), 1.0, A.is_lt, -99.0, A.mult)
+    tt(S("NE"), C("PM", 32, 48), S("CMP"), A.is_equal)
     scan(S("INI"), S("GA"), S("ACT"), -25.0)
-    ts(S("N99"), S("NE"), -99.0, A.mult)
+    ts(C("SM", 0), C("PM", 0), 1.0, A.is_ge)
     tt(S("TT"), S("INI"), C("PM", 8, 32, 3), A.subtract)
     ts(ND, S("IA"), 8.0, A.is_le)
-    tt(C("TG", 1, 8), C("TT", 1, 8), C("N99", 1, 8), A.add)
-    ts(C("TG", 0), C("N99", 0), C("TT", 0), A.add, C("SM", 0), A.add)
-    tt(C("TG", 8, 16), S("TT"), C("N99", 8, 16), A.add)
+    tt(C("TG", 1, 8), C("TT", 1, 8), C("NE", 1, 8), A.mult)
+    ts(C("TG", 0), C("NE", 0), C("TT", 0), A.mult, C("SM", 0), A.mult)
+    tt(C("TG", 8, 16), S("TT"), C("NE", 8, 16), A.mult)
     tt(S("IDX", al, 0), S("IA"), ND, A.mult)
     tt(S("EQ"), IND(C("TG", 0, 16), C("JU", 0, 26)), S("NR"), A.is_equal)
     tt(S("IDX", al, 1), S("IB"), ND, A.mult)
@@ -218,9 +221,21 @@ def build(T, nxt):
     NR = C("NR", 0, NN)
     E = lambda k: S("EE", k)
     act(S("KT"), C("NR", 0, 78), AF.Relu, scale=-1.0, bias=-24.0)
+    act(C("DA", 0, 8), S("EF"), scale=0.5)
+    act(C("DA", 8, 16), S("EF"), scale=col(CN))
+    act(C("DA", 16, 24), S("EF"), scale=col(CH))
+    act(C("DA", 24, 32), S("EF"), scale=col(CQ))
+    act(C("DA", 32, 40), S("EF"), scale=col(CN))
+    act(S("IDF"), ID)
+    act(C("CS", 0, 8), S("F8"), scale=4194304.0, bias=7.0 * 16513 * 512 + 4194304.0)
+    act(C("CS", 8, 16), S("F8"), scale=0.0)
+    act(C("CS", 16, 24), S("F8"), scale=4194304.0, bias=4194304.0)
+    for name, v in (("MR", BIG), ("MZ", -BIG), ("M64", 64.0)):
+        act(C(name, 0, WIDE), S("ONE", slice(0, WIDE), parts=slice(0, 1)), scale=v)
+
     mm(C("PU", 0, 208), ID, C("EQ", 0, 208), True, False)
     mm(C("PU", 0, 208), ID, C("EQ", 208, 416), False, True)
-    act(S("M2", slice(2, 8), 0), C("EQ", 52, 208), scale=-99.0, bias=99.0)
+    act(S("M2", slice(2, 8), 0), C("EQ", 52, 208), scale=-1.0, bias=1.0)
     act(S("M2", slice(2, 8), 1), C("EQ", 260, 416), scale=108.0, bias=-99.0)
     act(C("M1", 52, 208), C("PU", 52, 208), scale=-9.0, bias=9.0)
     act(S("H1"), S("IDX"), AF.Sign, bias=-2.5)
@@ -251,27 +266,24 @@ def build(T, nxt):
     act(C("KC", 78, 156), S("KT"), scale=-1.0, bias=col(KCB))
     act(S("Z1"), S("PA"), AF.Relu, bias=-4.0)
     act(S("Z2"), S("PB"), AF.Abs, bias=-3.0)
-    act(S("Z1"), S("Z1"), scale=-127.0 / 16384, bias=1.0 / 128)
+    act(S("IW"), ID, scale=-127.0 / 16384)
     act(S("Z2"), S("Z2"), AF.Relu, scale=-127.0 / 128, bias=127.0 / 128)
-    act(C("DA", 0, 8), S("EF"), scale=0.5)
-    act(C("DA", 8, 16), S("EF"), scale=col(CN))
-    act(C("DA", 16, 24), S("EF"), scale=col(CH))
-    act(C("DA", 24, 32), S("EF"), scale=col(CQ))
-    act(C("DA", 32, 40), S("EF"), scale=col(CN))
-    act(S("IDF"), ID)
-    act(C("CS", 0, 8), S("F8"), scale=4194304.0, bias=7.0 * 16513 * 512 + 4194304.0)
-    act(C("CS", 8, 16), S("F8"), scale=0.0)
-    act(C("CS", 16, 24), S("F8"), scale=4194304.0, bias=4194304.0)
-    act(S("JH"), S("J"), scale=0.5)
+    act(C("W", 5 * P, 7 * P), C("YO", 5 * P, 7 * P), scale=-1.0, bias=255.0)
     act(S("DL"), S("F96"), AF.Abs, scale=-1.0, bias=col(FP))
     for s in range(5, 9):
         dma("sync", C("REC", 160 * s, 160 * s + 160), S("C1", 0, slice(32, 192)), "nul")
-    dma("sync", C("RES", 3 * P, F * P), T.res[:, 3 * P:F * P], "res2", [("snt0", neng)])
+    dma("sync", C("RES", 2 * P, 3 * P), T.res[:, 2 * P:3 * P], "res2", [("snt0", neng)])
 
     def vec_dve(f0, f1):
         fs = slice(f0, f1)
         nd = C("PN", 32 * f0, 32 * f1)
         return [lambda n=n, i=i: tt(S("N" + n, fs, i), S(n, fs, i), nd, A.mult) for n in ("VY", "VX") for i in (0, 1)]
+
+    def masks(f0, f1):
+        act(C("THR", 32 * f0, 32 * f1), S("NDS", slice(f0, f1)), scale=1000000.0)
+        for k in range(4):
+            sg = 1.0 if k % 2 else -1.0
+            act(S("MK", slice(f0, f1), slice(32 * k + 32, 32 * k + 64)), S("NDS", slice(f0, f1)), scale=sg, bias=-sg)
 
     def vec_pe(f0, f1):
         for bank, w, n, b in (("XY", S("I32"), "NVY", "BY"), ("XX", ID, "NVX", "BX")):
@@ -282,31 +294,37 @@ def build(T, nxt):
     U, L = C("X", NN, 2 * NN), C("X", 0, NN)
     QS = C("Q", NN, 2 * NN)
     tt(S("K2"), C("EQ", 0, 52), C("EQ", 208, 260), A.is_equal)
-    tt(S("AA"), C("EQ", 208, 234), C("EQ", 26, 52), A.is_gt)
-    tt(S("BB"), C("K2", 0, NN), C("EQ", 234, 260), A.mult)
+    tt(L, C("EQ", 208, 234), C("EQ", 26, 52), A.is_gt)
+    tt(C("MV", 0, NN), C("K2", 0, NN), C("EQ", 234, 260), A.mult)
     tt(U, C("K2", 0, NN), C("K2", NN, 52), A.mult)
-    tt(L, S("AA"), S("BB"), A.add)
-    fill = vec_dve(0, 2) + [
+    fill = vec_dve(0, 3) + [
         lambda: tt(E(2), E(0), E(1), A.is_gt),
         lambda: tt(E(5), E(2), E(1), A.is_equal),
         lambda: tt(E(6), E(4), E(5), A.mult),
     ]
     for f in range(2, F):
+        now, new = ("X", "X2")[f % 2], ("X2", "X")[f % 2]
+        scan(S("Q"), S(now), S("MV"), C("INI", f))
+        tt(S("BB"), C(now, 0, NN), C("MV", 0, NN), A.add)
+        tt(S("AA"), C(now, NN, 2 * NN), C("M1", f * NN, (f + 1) * NN), A.mult)
+        tt(C("PRD", 0, NN), C(now, NN, 2 * NN), S("M2", f, 1), A.mult)
         fill.pop(0)()
-        scan(S("Q"), S("X"), C("ZR", 0, 52), C("INI", f))
-        tt(S("PRD"), S("X"), S("M2", f), A.mult)
-        tt(S("AA"), U, C("M1", f * NN, (f + 1) * NN), A.mult)
-        tt(S("BB"), C("PRD", 0, NN), C("PRD", NN, 2 * NN), A.add)
-        tt(U, S("AA"), QS, A.is_gt)
-        tt(L, S("BB"), QS, A.is_gt)
+        tt(C(new, 0, NN), S("BB"), S("M2", f, 0), A.mult)
+        tt(C(new, NN, 2 * NN), S("AA"), QS, A.is_gt)
+        tt(C("MV", 0, NN), C("PRD", 0, NN), QS, A.is_gt)
         if f == 5:
-            vec_pe(0, 2)
-            mm(S("PW"), ID, S("Z1"), True, False)
+            act(S("NDS"), ND)
+            vec_pe(0, 3)
+            mm(S("PW"), S("IW"), S("Z1"), True, False)
+            for k in (0, 256):
+                mm(C("PW", k, k + 256), S("C7"), S("ONE", parts=slice(0, 1)), False, False)
             mm(S("PW"), ID, S("Z2"), False, True)
             act(S("POW"), S("PW"))
     fill.pop(0)()
-    tt(S("H"), U, L, A.add)
+    tt(S("BB"), L, C("MV", 0, NN), A.add)
+    L = S("BB")
     tt(C("Y", 52, 78), U, E(6), A.mult)
+    tt(S("H"), U, L, A.add)
     tt(C("Y", 78, 104), L, E(5), A.mult)
     tt(C("Y", 0, 26), S("H"), E(1), A.mult)
     tt(C("Y", 26, 52), S("H"), E(2), A.mult)
@@ -325,6 +343,7 @@ def build(T, nxt):
     ts(C("PU", 334, 360), C("PU", 334, 360), -1.0, A.mult, C("SM", 3), A.add)
     tt(C("PU", 448, 512), C("PU", 384, 448), S("CX"), A.add)
     tt(S("PP"), S("Y"), C("PU", 256, 360), A.mult)
+    r0 = 160 * PSLOT[0]
     tt(S("P2"), C("PP", 0, 52), C("PP", 52, 104), A.add)
     tt(S("RK"), C("P2", 0, NN), C("P2", NN, 52), A.add)
     ts(S("RAB", 0), S("RK"), col(KA), A.subtract)
@@ -339,118 +358,151 @@ def build(T, nxt):
     ts(S("RB"), C("DA", 24, 40), C("SM", 5), A.mult)
     mm(C("PM", 256, 280), S("BO"), S("RA"), False, False)
     mm(C("PM", 264, 280), S("BO"), S("RB"), False, True)
-    r0 = 160 * PSLOT[0]
+    masks(1, 3)
     cp(C("REC", r0 + 32, r0 + 96), C("XY", 0, 64))
     cp(C("REC", r0 + 96, r0 + 160), C("XX", 0, 64))
     act(S("DL"), S("DL"), AF.Relu, scale=-1.0, bias=1.0)
-    act(S("THR"), ND, scale=1000000.0)
     act(S("DL"), S("DL"), scale=col(H5))
-    for k in range(4):
-        sg = 1.0 if k % 2 else -1.0
-        act(S("MK", slice(1, 8), slice(32 * k + 32, 32 * k + 64)), C("PN", 32, 256), scale=sg, bias=-sg)
+    act(C("W", 8 * P, 9 * P), C("YO", 4 * P, 5 * P), scale=-1.0, bias=255.0, waits=[("arr0", narr)])
 
     def look_act(f0, f1):
         for f in range(f0, f1):
             act(C("U1", 64 * f, 64 * f + 64), S("H1", f), scale=C("TB", 8 + f), bias=C("TB", f))
             act(C("U2", 64 * f, 64 * f + 64), S("H2", f), scale=C("TB", 16 + f))
+
+    def look_pe(f0, f1):
         mm(C("PW", 64 * f0, 64 * f1), S("IDF"), C("U1", 64 * f0, 64 * f1), True, False)
         mm(C("PW", 64 * f0, 64 * f1), S("IDF"), C("U2", 64 * f0, 64 * f1), False, True)
 
     def look_dve(f0, f1):
-        tt(S("XI", slice(f0, f1)), C("PW", 64 * f0, 64 * f1), C("POW", 64 * f0, 64 * f1), A.mult)
-        ts(S("C1", slice(f0, f1), slice(32, 64)), S("XI", slice(f0, f1), 0), 65024, A.bitwise_and)
-        ts(S("SS", slice(f0, f1), 1), S("XI", slice(f0, f1), 1), 7680, A.bitwise_and)
+        return [
+            lambda: tt(S("XI", slice(f0, f1)), C("PW", 64 * f0, 64 * f1), C("POW", 64 * f0, 64 * f1), A.mult),
+            lambda: (ts(S("C1", slice(f0, f1), slice(32, 64)), S("XI", slice(f0, f1), 0), 65024, A.bitwise_and),
+                     ts(S("SS", slice(f0, f1), 1), S("XI", slice(f0, f1), 1), 7680, A.bitwise_and)),
+        ]
 
-    def motion(f):
+    def record(f):
         r = 160 * PSLOT[f]
-        ry, rx = C("REC", r + 32, r + 96), C("REC", r + 96, r + 160)
-        xy, xx = C("XY", 64 * f, 64 * f + 64), C("XX", 64 * f, 64 * f + 64)
-        if f > 0:
-            win = C("REC", 160 * wbase(f), 160 * (8 if f < 6 else 10))
-            tt(S("G"), IND(win, C("LU", 12 * f, 12 * f + 12)), S("C1", f), A.subtract)
-            tt(S("MK", f, slice(0, 32)), C("G", 0, 32), C("THR", 32 * f, 32 * f + 32), A.is_ge)
-            tt(S("MW"), C("G", 32, 192), S("MK", f), A.mult)
-            ts(S("HY"), C("MW", 32, 96), 1, A.arith_shift_right, -32, A.bitwise_and)
-            ts(S("HX"), C("MW", 96, 160), 1, A.arith_shift_right)
-            tt(C("REC", r, r + 32), C("MW", 0, 32), S("C1", f, slice(32, 64)), A.add)
-            tt(ry, S("HY"), xy, A.add)
-            tt(rx, S("HX"), xx, A.add)
-            ts(S("SS", f, 0), C("REC", r, r + 32), 7680, A.bitwise_and)
-            ts(CY, ry, 0.0, A.max, 480.0, A.min)
-            ts(S("CX"), rx, col(G16), A.max, col(G31), A.min)
-            tt(S1, CY, S("SS", f), A.add)
-            tt(S("S2"), S1, S("CX"), A.add)
-        else:
-            tt(S("S2"), C("PU", 448, 512), S("SS", f), A.add)
-        ts(C("OFF", 64 * f, 64 * f + 64), S("S2"), col(G16), A.subtract, float(-P * wbase(f)), A.add)
+        win = C("REC", 160 * wbase(f), 160 * (8 if f < 6 else 10))
+        return [
+            lambda: tt(S("G"), IND(win, C("LU", 12 * f, 12 * f + 12)), S("C1", f), A.subtract),
+            lambda: tt(S("MK", f, slice(0, 32)), C("G", 0, 32), C("THR", 32 * f, 32 * f + 32), A.is_ge),
+            lambda: tt(S("MW"), C("G", 32, 192), S("MK", f), A.mult),
+            lambda: (ts(S("HY"), C("MW", 32, 96), 1, A.arith_shift_right, -32, A.bitwise_and),
+                     ts(S("HX"), C("MW", 96, 160), 1, A.arith_shift_right),
+                     tt(C("REC", r, r + 32), C("MW", 0, 32), S("C1", f, slice(32, 64)), A.add)),
+            lambda: (tt(C("REC", r + 32, r + 96), S("HY"), C("XY", 64 * f, 64 * f + 64), A.add),
+                     tt(C("REC", r + 96, r + 160), S("HX"), C("XX", 64 * f, 64 * f + 64), A.add)),
+        ]
 
-    banks = ["PA", "PB", "PU"]
+    def offsets(f):
+        r = 160 * PSLOT[f]
+        CY, S1 = C("PM", 376, 440), C("PM", 440, 504)
+        return [
+            lambda: (ts(S("SS", f, 0), C("REC", r, r + 32), 7680, A.bitwise_and),
+                     ts(CY, C("REC", r + 32, r + 96), 0.0, A.max, 480.0, A.min),
+                     ts(S("CX"), C("REC", r + 96, r + 160), col(G16), A.max, col(G31), A.min)),
+            lambda: tt(S1, CY, S("SS", f), A.add),
+            lambda: tt(S("S2"), S1, S("CX"), A.add),
+            lambda: ts(C("OFF", 64 * f, 64 * f + 64), S("S2"), col(G16), A.subtract, float(-P * wbase(f)), A.add),
+        ]
+
+    def weave(a, b):
+        for k in range(max(len(a), len(b))):
+            for x in (a, b):
+                if k < len(x):
+                    x[k]()
+
     pieces = list(zip(CUTS[:-1], CUTS[1:]))
+
+    def bank(h):
+        name, at = (("PA", 0), ("PB", 0), ("PU", 0), ("PN", 384))[h]
+        return C(name, at, at + pieces[h][1] - pieces[h][0])
+
     row1 = S("ONE", slice(0, 128), parts=slice(0, 1))
 
     def pixels_front(f):
         s = 16 * ((f + 1) % 8)
         win = C("W", P * wbase(f), P * (9 + f))
-        aw = [("arr%d" % f, narr * (nsend if f else 1))]
+        aw = [("arr%d" % f, narr)] if f else []
+        last = f == F - 1
         for h, (a, b) in enumerate(pieces):
-            mm(C(banks[h], 0, b - a), C("J", s, s + 128), C("RES", f * P + a, f * P + b), True, False)
+            mm(bank(h), C("J" if last else "JN", s, s + 128), C("RES", f * P + a, f * P + b), True, False)
+            if last:
+                mm(bank(h), row1, C("M64", 0, b - a), False, False)
         for a, b in pieces:
-            act(C("GP", a, b), IND(win, C("OFF", 64 * f + a // 16, 64 * f + b // 16)), AF.Relu, waits=aw)
-            ts(C("GQ", a, b), IND(win, C("OFF", 64 * f + 32 + a // 16, 64 * f + 32 + b // 16)), 0.0, A.max, -127.5, A.add, aw)
-        sent = 0
+            act(C("GP", a, b), IND(win, C("OFF", 64 * f + a // 16, 64 * f + b // 16)), AF.Relu, scale=-1.0, bias=255.0, waits=aw)
+            ts(C("GQ", a, b), IND(win, C("OFF", 64 * f + 32 + a // 16, 64 * f + 32 + b // 16)), 255.0, A.min, -127.5, A.add, aw)
         for h, (a, b) in enumerate(pieces):
-            ps = C(banks[h], 0, b - a)
+            mm(bank(h), C("JM" if last else "JH", s, s + 128), C("GQ", a, b), False, False)
+            mm(bank(h), C("JH" if last else "JM", s, s + 128), C("GP", a, b), False, False)
+            mm(bank(h), row1, C("MR", 0, b - a), False, not last)
+            if last:
+                mm(bank(h), row1, C("MZ", 0, b - a), False, True)
+        for h, (a, b) in enumerate(pieces):
             out = C("SND", f * P + a, f * P + b)
-            mm(ps, C("JH", s, s + 128), C("GQ", a, b), False, False)
-            mm(ps, C("JH", s, s + 128), C("GP", a, b), False, False)
-            mm(ps, row1, C("MR", 0, b - a), False, True)
-            if f == F - 1:
-                act(C("RR", a, b), ps, AF.Relu, bias=64.0 - BIG)
-                ts(out, C("RR", a, b), 255.0, A.min)
-                dma("sync", T.y[:, f * P + a:f * P + b], out, "out%d" % (f + h))
-                continue
-            ts(out, ps, 64.0 - BIG, A.add, 255.0, A.min)
-            if h in SEND_AFTER:
-                send(C("W", (9 + f) * P + sent, (9 + f) * P + b), C("SND", f * P + sent, f * P + b), f + 1)
-                sent = b
+            if last:
+                ts(out, bank(h), 0.0, A.max, 255.0, A.min)
+                if h % 2:
+                    a = pieces[h - 1][0]
+                    dma("sync" if h == 1 else "scalar", T.y[:, f * P + a:f * P + b], C("SND", f * P + a, f * P + b), "out%d" % (f + h // 2))
+            elif h % 2:
+                act(out, bank(h), AF.Relu, bias=191.0 - BIG)
+            else:
+                ts(out, bank(h), 191.0 - BIG, A.add, 0.0, A.max)
+        if not last:
+            send(C("W", (9 + f) * P, (10 + f) * P), C("SND", f * P, f * P + P), f + 1)
 
     def pixels_back(f):
         s = 128 - 16 * (f + 1)
-        own = C("W", PSLOT[f] * P, PSLOT[f] * P + P)
         mm(S("PU"), C("J", s, s + 128), C("SND", f * P, f * P + P), True, True)
-        act(own, S("PU"), AF.Relu)
-        dma("sync", T.y[:, f * P:f * P + P], own, "out%d" % f, [("snt%d" % (f + 1), neng * nsend)])
+        act(C("W", PSLOT[f] * P, PSLOT[f] * P + P), S("PU"))
+        act(C("YO", f * P, f * P + P), S("PU"), AF.Relu, scale=-1.0, bias=255.0)
+        if f < 5:
+            k = f + 3
+            add("sync", lambda e: e.dma_start(T.RES[:, k * P:k * P + P], T.res[:, k * P:k * P + P]),
+                [C("RES", k * P, k * P + P)], [C("YO", f * P, f * P + P)], (), "res%d" % k)
+        dma("sync", T.y[:, f * P:f * P + P], C("YO", f * P, f * P + P), "out%d" % f, [("snt%d" % (f + 1), neng)])
 
-    CY, S1 = C("PN", 256, 320), C("PN", 320, 384)
-    ts(C("U2", 0, 64), S("H2", 0), C("PM", 272), A.mult)
+    ts(C("PU", 0, 64), S("H2", 0), C("PM", 272), A.mult)
     ts(C("U1", 0, 64), S("H1", 0), C("PM", 264), A.mult, C("PM", 256), A.add)
-    tt(C("U1", 0, 64), C("U1", 0, 64), C("U2", 0, 64), A.add)
+    tt(C("U1", 0, 64), C("U1", 0, 64), C("PU", 0, 64), A.add)
     act(S("RL"), S("DL"), scale=C("SM", 5))
     act(S("TB"), C("PM", 256, 280))
     tt(S("XI", 0), C("U1", 0, 64), C("PW", 0, 64), A.mult)
     ts(S("SS", 0), S("XI", 0), 7680, A.bitwise_and)
-    motion(0)
     mm(C("PM", 280, 376), S("BO"), S("RL"), True, True)
     ts(C("REC", r0, r0 + 32), S("XI", 0, 0), 65024, A.bitwise_and)
+    tt(S("S2"), C("PU", 448, 512), S("SS", 0), A.add)
+    offsets(0)[3]()
+    look_act(1, 3)
+    look_pe(1, 2)
     for f in range(F):
         pixels_front(f)
         if f == F - 1:
             break
+        if f == 1:
+            weave(record(2)[2:], vec_dve(3, 5))
+            vec_pe(3, 5)
         if f == 0:
-            look_act(1, 2)
             tt(S("TL"), C("PM", 280, 376), S("CL"), A.add)
+            look_dve(1, 2)[0]()
+            look_pe(2, 3)
             ts(S("LU"), S("TL"), col(G16), A.subtract)
-            look_dve(1, 2)
+            look_dve(1, 2)[1]()
+            weave(record(1), look_dve(2, 3))
         pixels_back(f)
+        if f == 2:
+            weave(vec_dve(5, 8), [])
+            vec_pe(5, 8)
         if f in LOOK:
             look_act(*LOOK[f])
-        if f in VEC:
-            for k in vec_dve(*VEC[f]):
-                k()
-            vec_pe(*VEC[f])
-        if f - 1 in LOOK:
-            look_dve(*LOOK[f - 1])
-        motion(f + 1)
+            look_pe(*LOOK[f])
+        if f in MASK:
+            masks(*MASK[f])
+        ahead = look_dve(*LOOK[f - 1]) if f - 1 in LOOK else []
+        ahead += record(f + 2)[:5 if f else 2] if f + 2 < F else []
+        weave(offsets(f + 1), ahead)
     return ops, neng, narr
 
 

@@ -1,48 +1,45 @@
+import math
 import numpy as np
 from concourse.mybir import AluOpType as A, AxisListType, ActivationFunctionType as AF
 
 F = 8
 P = 512
 CUTS = [0, 160, 320, 448, 512]
-LOOK = {0: (3, 5), 2: (5, 8)}
-MASK = {0: (3, 5), 1: (5, 8)}
+SENDS = (1, 3)
 BIG = 12582912.0
 NN = 26
+N2 = 2 * NN
+RW = 96
 
 f32, bf, i32, u16 = "float32", "bfloat16", "int32", "uint16"
 SB_ = {
-    "W": ([128, 16 * P], bf), "RES": ([128, F * P], bf), "SND": ([128, F * P], bf),
-    "GP": ([128, P], bf), "GQ": ([128, P], bf), "RR": ([128, P], bf),
+    "W": ([128, 16 * P], bf), "RES": ([128, F * P], bf), "SND": ([128, F * P], bf), "YO": ([128, 7 * P], bf),
+    "GP": ([128, P], bf), "GQ": ([128, P], bf),
     "IA": ([128, 256], i32), "IB": ([128, 256], i32), "VY": ([128, 8, 2, 32], i32), "VX": ([128, 8, 2, 32], i32),
-    "CT": ([8, 48], i32), "CB": ([8, 48], bf), "RT": ([64, 3], i32), "RTB": ([64, 3], bf),
-    "ONE": ([128, 256], bf), "MR": ([1, 256], bf), "MZ": ([1, 256], bf), "M64": ([1, 256], bf), "J": ([128, 256], bf), "JH": ([128, 256], bf), "IW": ([128, 128], bf), "C7": ([1, 128], bf), "JM": ([128, 256], bf), "JN": ([128, 256], bf), "YO": ([128, 7 * P], bf), "N15": ([128, 128], bf), "I32": ([128, 128], bf),
-    "E8": ([8, 128], bf), "E8B": ([8, 128], bf), "SEL": ([64, 128], bf), "BO": ([128, 128], f32),
+    "CT": ([128, 8], i32), "EB": ([128, 8], bf), "CA": ([128, 4], f32), "CF": ([128, 4], f32),
+    "ONE": ([128, 256], bf), "MR": ([1, 256], bf), "MZ": ([1, 256], bf), "MQ": ([1, 256], bf), "M128": ([1, 256], bf),
+    "J": ([128, 256], bf), "JH": ([128, 256], bf), "JM": ([128, 256], bf), "N15": ([128, 128], bf), "I32": ([128, 128], bf),
+    "E8": ([8, 128], bf), "EA": ([8, 128], bf), "BO": ([128, 128], f32), "IDF": ([128, 128], f32),
+    "L0": ([128, 128], bf), "LE": ([128, 128], bf), "LT": ([128, 128], bf), "M": ([128, 128], bf), "TR": ([NN, 256], bf),
     "LA": ([128, 128], bf), "LB": ([128, 128], bf), "LS": ([128, 128], bf),
-    "PI": ([128, 8], i32), "PC": ([128, 24], f32), "F8": ([128, 8], f32), "F96": ([128, 96], f32), "EF": ([128, 8], f32),
-    "ACT": ([128, 8], f32), "CMP": ([128, 16], f32),
-    "JL": ([128, 26], f32), "JI": ([128, 26], i32), "JU": ([128, 26], u16), "NR": ([128, 416], f32),
-    "KC": ([128, 156], bf), "KT": ([128, 78], f32), "DA": ([128, 40], f32), "IDF": ([128, 128], f32), "POW": ([128, P], bf), "DL": ([128, 96], f32),
-    "RA": ([128, 24], f32), "RB": ([128, 16], f32), "RL": ([128, 96], f32),
-    "CS": ([128, 24], f32), "CL": ([128, 8, 3, 4], f32), "TB": ([128, 24], f32), "TL": ([128, 96], f32), "LU": ([128, 96], u16),
-    "C1": ([128, 8, 192], i32), "BY": ([128, 64], bf), "BX": ([128, 64], bf),
-    "ZR": ([128, 104], f32), "GA": ([128, 8], f32), "INI": ([128, 8], f32), "NE": ([128, 16], f32), "N99": ([128, 16], f32),
-    "SM": ([128, 16], f32), "TT": ([128, 8], f32), "TG": ([128, 16], f32), "EQ": ([128, 416], bf),
-    "M2": ([128, 8, 2, NN], bf), "M1": ([128, 208], bf), "K2": ([128, 52], f32),
-    "X": ([128, 52], f32), "X2": ([128, 52], f32), "MV": ([128, 52], f32), "Q": ([128, 52], f32), "PRD": ([128, 52], f32), "AA": ([128, NN], f32), "BB": ([128, NN], f32),
-    "EE": ([128, 8, NN], f32), "EQC": ([128, NN], bf), "H": ([128, NN], bf),
-    "Y": ([128, 104], f32), "R": ([128, 104], f32), "PP": ([128, 104], f32), "P2": ([128, 52], f32), "RK": ([128, NN], f32),
-    "RAB": ([128, 2, NN], f32), "EW": ([128, 2, 3, NN], f32), "EP": ([128, 156], f32),
-    "IDX": ([128, 8, 2, 32], bf), "H1": ([128, 8, 2, 32], bf), "H2": ([128, 8, 2, 32], bf), "HB": ([128, 8, 2, 32], bf),
-    "Z1": ([128, P], bf), "Z2": ([128, P], bf), "NVY": ([128, 8, 2, 32], bf), "NVX": ([128, 8, 2, 32], bf), "THR": ([128, 256], f32), "NDS": ([128, 8, 32], bf),
-    "MK": ([128, 8, 160], f32), "U1": ([128, P], f32), "U2": ([128, P], f32), "XI": ([128, 8, 2, 32], i32),
-    "SS": ([128, 8, 2, 32], i32), "REC": ([128, 11 * 160], i32), "G": ([128, 192], i32), "MW": ([128, 160], i32),
-    "HY": ([128, 64], i32), "HX": ([128, 64], i32), "CY": ([128, 64], i32), "CX": ([128, 64], i32),
-    "S1": ([128, 64], i32), "S2": ([128, 64], i32), "OFF": ([128, F * 64], u16),
+    "PI": ([128, 8], i32), "PC": ([128, 24], f32), "F8": ([128, 8], f32), "F48": ([128, 48], f32), "EF": ([128, 8], f32), "TG": ([128, 6], bf),
+    "NR": ([128, N2], bf), "OM": ([128, N2], bf), "OR": ([128, N2], bf), "E0": ([128, N2], bf), "EM": ([128, 3, N2], bf), "EQC": ([128, N2], bf),
+    "GEN": ([128, N2], bf), "TA": ([128, 8, NN], f32), "X": ([128, 2, 56], bf), "Z": ([128, 56], f32), "LM": ([128, N2], bf),
+    "HH": ([128, N2], bf), "LD": ([128, NN], bf), "Y": ([128, 3 * N2], bf), "ZR": ([128, 256], bf), "WK": ([128, 4], bf), "PP": ([128, 104], bf),
+    "EW": ([128, 6, N2], bf), "DS": ([128, 104], f32), "EP": ([128, 104], f32),
+    "KC": ([128, 104], bf), "KT": ([128, N2], f32), "DA": ([128, 40], f32), "DL": ([128, 48], f32),
+    "RA": ([128, 24], f32), "RB": ([128, 16], f32), "RL": ([128, 48], f32), "CS": ([128, 24], f32), "CL": ([128, 48], f32),
+    "TB": ([128, 24], f32), "LU": ([128, 48], u16), "SM": ([128, 8], f32),
+    "IDX": ([128, 2, 8, 32], bf), "H1": ([128, 2, 8, 32], bf), "H2": ([128, 2, 8, 32], bf), "FX": ([128, 2, 256], bf), "POW": ([128, 8, 2, 32], bf),
+    "NV": ([128, 8, 2, 32, 2], bf), "BI": ([128, 2, 32], f32), "BT": ([128, 32, 2], bf), "BM": ([128, 2, 64], bf),
+    "MK": ([128, 8, RW], bf), "U1": ([128, 8, 64], f32), "U2": ([128, 8, 64], f32), "XI": ([128, 8, 2, 32], i32), "A0": ([128, 8, 32], i32),
+    "SS": ([128, 2, 64], i32), "REC": ([128, 11 * RW], i32), "G": ([128, RW], f32), "H": ([128, 128], bf), "CC": ([128, 128], bf),
+    "S2": ([128, 64], i32), "OFF": ([128, F * 64], u16),
 }
 PS_ = ["PA", "PB", "PU", "XY", "XX", "PM", "PN", "PW"]
 SCRATCH = {k: ("sbuf", v[0], v[1]) for k, v in SB_.items()}
 SCRATCH.update({k: ("psum", [128, P], f32) for k in PS_})
-DMAS = ["ctl", "rt_", "pic", "pi0", "ia_", "ib_", "vy_", "vx_", "nul", "res0", "res2", "res3", "res4", "res5", "res6", "res7"] + ["out%d" % f for f in range(F + 3)]
+DMAS = ["ctl", "pic", "pi0", "ia_", "ib_", "vy_", "vx_", "res0", "res2", "res3", "res4", "res5", "res6", "res7"] + ["out%d" % f for f in range(F + 3)]
 SEMAPHORES = ["dve", "act", "pe", "pool"] + DMAS + ["arr%d" % f for f in range(F)] + ["snt%d" % f for f in range(F)]
 
 PSLOT = [4, 3, 2, 1, 0, 9, 8, 10]
@@ -64,8 +61,8 @@ def build(T, nxt):
         el = np.asarray(cache[name][ix] if ix else cache[name]).ravel()
         return (T[name][(parts,) + ix], name, el)
 
-    def C(name, a, b=None, st=None):
-        return S(name, slice(a, a + 1 if b is None else b, st))
+    def C(name, a, b=None, st=None, parts=al):
+        return S(name, slice(a, a + 1 if b is None else b, st), parts=parts)
 
     def IND(win, off):
         return (win[0].indirect(off[0]), win[1], win[2], off)
@@ -97,8 +94,8 @@ def build(T, nxt):
     def ms(o, c):
         add("dve", lambda e: e.memset(o[0], c), [o], [])
 
-    def red(o, i):
-        add("dve", lambda e: e.tensor_reduce(o[0], i[0], AxisListType.X, A.add), [o], [i])
+    def red(o, i, op=A.add):
+        add("dve", lambda e: e.tensor_reduce(o[0], i[0], AxisListType.X, op), [o], [i])
 
     def scan(o, d0, d1, ini):
         add("dve", lambda e: e.tensor_tensor_scan(o[0], d0[0], d1[0], val(ini), A.add, A.add), [o], [d0, d1, ini])
@@ -109,17 +106,21 @@ def build(T, nxt):
     def mm(o, l, r, st, sp):
         add("pe", lambda e: e.matmul(o[0], l[0], r[0], st, sp), [o], [l, r])
 
+    def mms(*steps):
+        for k, (o, l, r) in enumerate(steps):
+            mm(o, l, r, k == 0, k == len(steps) - 1)
+
     def iota(o, pat, base, cm=0):
         if SCRATCH[o[1]][2] == i32:
             add("pool", lambda e: e.iota(o[0], pat, base, cm), [o], [])
         else:
             add("pool", lambda e: e.iota(o[0], pat, base, cm, allow_small_or_imprecise_dtypes=True), [o], [])
 
-    def sel(name, pat):
+    def sel(name, pat, src="ONE", op=A.is_equal, fill=0.0, cm=-1):
         o = S(name)
         n, w = SCRATCH[name][1]
-        i = S("ONE", slice(0, w), parts=slice(0, n))
-        add("pool", lambda e: e.affine_select(o[0], i[0], pat, A.is_equal, 0.0, 0, -1), [o], [i])
+        i = S(src, slice(0, w), parts=slice(0, n))
+        add("pool", lambda e: e.affine_select(o[0], i[0], pat, op, fill, 0, cm), [o], [i])
 
     def dma(q, o, i, sem, waits=()):
         add(q, lambda e: e.dma_start(val(o), val(i)), [o] if isinstance(o, tuple) else [], [i], waits, sem)
@@ -128,317 +129,296 @@ def build(T, nxt):
         add("pool", lambda e: e.remote_dma(o[0], i[0], T.sem["arr%d" % k], T.sem["snt%d" % k], nxt[1], nxt[0], nxt[2]),
             [], [i], (), "remote")
 
+    def weave(*chains):
+        for k in range(max(len(x) for x in chains)):
+            for x in chains:
+                if k < len(x):
+                    x[k]()
+
     WIDE = max(b - a for a, b in zip(CUTS[:-1], CUTS[1:]))
     neng = bin(nxt[2]).count("1")
     narr = nxt[3]
     col = lambda k: C("PC", k)
-    FP, HALF, G16, G31, NH, KA, KB, SC, W16, H5, CN, CH, CQ, KCB, WS, T0, T1, T2, T3 = range(19)
+    FP, HALF, G16, F0, NG, NH, KA, W16, H5, CN, CH, CQ, KCB, WS, T0, T1, T2, T3 = range(18)
+    D_, R_ = slice(0, NN), slice(NN, N2)
 
-    dma("sync", C("CT", 0, 8), T.gaps[:], "ctl")
-    dma("scalar", C("CT", 32, 40), T.cmd[:], "ctl")
-    dma("sync", C("CT", 8, 32), T.rel[:], "ctl")
-    dma("scalar", C("CT", 40, 48), T.cmd[:], "ctl")
+    for h, q in enumerate(("sync", "scalar")):
+        pp = slice(64 * h, 64 * h + 64)
+        dma(q, C("CT", 0, parts=pp), T.gaps[:], "ctl")
+        dma(q, C("CT", 1, parts=pp), T.cmd[:], "ctl")
+        dma(q, C("CT", 2, 5, parts=pp), T.rel[:], "ctl")
     dma("sync", S("IA"), T.ia[:], "ia_")
     dma("scalar", S("IB"), T.ib[:], "ib_")
-    dma("sync", C("YO", 6 * P, 7 * P), T.pic0[:, P:2 * P], "pic")
-    dma("scalar", S("RT"), T.rel[:], "rt_")
+    dma("sync", C("W", 6 * P, 7 * P), T.pic0[:, P:2 * P], "pic")
     dma("sync", S("VY"), T.vy[:], "vy_")
     dma("sync", S("VX"), T.vx[:], "vx_")
-    dma("sync", C("YO", 5 * P, 6 * P), T.pic0[:, 0:P], "pi0")
+    dma("sync", C("W", 5 * P, 6 * P), T.pic0[:, 0:P], "pi0")
     dma("sync", C("RES", 0, 2 * P), T.res[:, 0:2 * P], "res0")
 
     ms(S("ONE"), 1.0)
     iota(C("PI", 0), [[0, 1]], 0, 1)
+    iota(S("NR", R_), [[1, NN]], -1)
+    sel("L0", [[0, 2], [1, 64]], op=A.is_ge)
+    sel("LE", [[0, 2], [-8, 8], [0, 8]], "L0", A.is_ge, cm=1)
     iota(S("F8"), [[1, 8]], 0)
-    sel("E8", [[1, 8], [0, 16]])
-    iota(S("JL"), [[16, 26]], 0, 1)
+    sel("LT", [[0, 2], [1, 64]], "LE", A.is_gt)
     sel("J", [[0, 2], [1, 128]])
-    iota(S("NR"), [[0, 16], [-1, NN]], -1)
-    send(C("YO", 4 * P, 5 * P), C("YO", 6 * P, 7 * P), 0)
-    sel("SEL", [[8, 8], [0, 2], [1, 8]])
-    sel("E8B", [[1, 8], [100, 2], [0, 8]])
-    iota(S("BY"), [[0, 2], [32, 16], [0, 2]], 0)
-    iota(S("BX"), [[0, 32], [16, 2]], 0, 1)
+    sel("EA", [[0, 2], [1, 8], [0, 8]])
+    sel("E8", [[1, 8], [0, 16]])
+    send(C("W", 8 * P, 9 * P), C("W", 6 * P, 7 * P), 0)
     ms(S("ZR"), 0.0)
+    sel("N15", [[1, 128]], "ZR", A.not_equal, -1.5)
+    iota(S("BI", 0), [[1, 16], [0, 2]], 0)
+    iota(S("BI", 1), [[0, 16], [16, 2]], 0, 1)
+    iota(S("F48"), [[1, 8], [0, 6]], 0)
+    sel("I32", [[1, 128]], "ZR", A.not_equal, 32.0)
+    iota(S("CL"), [[0, 8], [16, 6]], 0, 1)
+    for name in ("JH", "JM"):
+        sel(name, [[0, 2], [1, 128]], "ZR", A.not_equal, 0.5 if name == "JH" else -0.5)
     ts(C("PI", 1), C("PI", 0), 7, A.bitwise_and)
-    ts(C("PI", 2), C("PI", 0), 3, A.arith_shift_right, 1, A.bitwise_and)
+    ts(C("PI", 2), C("PI", 0), 6, A.arith_shift_right)
     ts(C("PI", 3), C("PI", 0), 112, A.bitwise_and)
-    ms(S("C7"), 1.0 / 128)
-    ms(C("MV", NN, 2 * NN), 0.0)
+    ms(S("H"), 192.0)
     cp(C("PC", 0, 3), C("PI", 1, 4))
-    ms(C("RR", 0, 256), 0.0)
-    ts(S("ACT"), S("F8"), col(FP), A.is_le)
-    ts(S("JL"), S("JL"), col(G16), A.subtract, 12.5, A.subtract)
-    ts(C("CMP", 0, 8), S("ACT"), 7.0, A.mult, -5.0, A.add)
-    ts(S("JL"), S("JL"), 1.0 / NN, A.mult)
-    ts(C("CMP", 8, 16), S("ACT"), 6.0, A.mult, -5.0, A.add)
-    cp(S("JI"), S("JL"))
-    ms(S("HB", al, 0), 0.0)
-    cp(S("JU"), S("JI"))
-    for k, sc, bi in ((NH, -1.0, 1.0), (KA, 6.0, 1.0), (KB, -2.0, 4.0), (SC, 2.0, 1.0), (W16, -16.0, 16.0), (H5, 0.3125, 0.0),
-                      (CN, 0.5, -0.5), (CH, 0.5, 0.0), (CQ, -0.5, 0.5)):
+    ms(C("REC", 5 * RW, 9 * RW), 0)
+    ms(C("W", 7 * P, 8 * P), 128.0)
+    ms(C("MR", 0, WIDE), BIG)
+    ms(C("MQ", 0, WIDE), -0.25)
+    ms(C("CS", 8, 16), 0.0)
+    ms(C("LB", 64, 128), 0.0)
+    act(S("NR", D_), S("NR", R_), scale=-1.0, bias=23.0)
+    act(col(F0), col(FP), AF.Relu, scale=-1.0, bias=1.0)
+    for k, sc, bi in ((NH, -1.0, 1.0), (KA, 6.0, 1.0), (W16, -16.0, 16.0), (CN, 0.5, -0.5), (CH, 0.5, 0.0), (CQ, -0.5, 0.5)):
         act(col(k), col(HALF), scale=sc, bias=bi)
-    act(col(G31), col(G16), bias=31.0)
+    act(S("WK"), C("F8", 0, 4), AF.Exp, scale=7 * math.log(2), bias=9 * math.log(2))
+    ID = C("J", 0, 128)
+
+    CS_ = C("PM", 0)
+    ND = C("XX", 0, 256)
+    ts(C("EB", 0), C("CT", 0), 1.0, A.add)
+    ts(C("CA", 0), C("CT", 1), 1.0, A.not_equal, 64.0, A.mult)
+    ts(C("CA", 1), C("CT", 1), 2.0, A.not_equal, 64.0, A.mult)
+    ts(C("CA", 2), C("CT", 0), col(F0), A.is_lt, 64.0, A.mult)
+    mm(CS_, S("LE"), C("EB", 0), True, True)
+    ts(C("CF", 2), C("CT", 2), C("CA", 0), A.add)
+    ts(C("CF", 3), C("CT", 2), C("CA", 1), A.add, C("CA", 2), A.add)
+    cp(C("CF", 0, 2), C("CT", 3, 5))
+    ts(S("OM"), S("NR"), C("CF", 2), A.add, CS_, A.is_equal)
+    ts(S("OR"), S("NR"), C("CF", 3), A.add, CS_, A.is_equal)
+    GM, LTC, LTG, UP, U, SU, OS, SV = [S("TA", k) for k in range(8)]
+    ts(GM, S("NR", D_), C("CF", 2), A.add, CS_, A.is_ge)
+    ts(LTC, S("NR", D_), CS_, A.is_lt)
+    TT = C("PA", 0, N2)
+    mms((TT, S("LT"), S("OM")), (TT, S("LT"), S("OR")))
+    top = slice(0, NN)
+    mm(C("PB", 0, 128, parts=top), S("OR", D_), S("LT"), True, True)
+    mm(C("PB", 128, 256, parts=top), S("OM", D_), ID, True, True)
+    mm(C("PU", 128, 128 + NN), S("LE"), S("OR", R_), True, True)
+    ts(S("E0"), S("NR"), C("CF", 0), A.add, CS_, A.is_equal)
+    tt(LTG, GM, LTC, A.min)
+    ts(S("EM", 0), S("NR"), C("CF", 1), A.add, CS_, A.is_equal)
+    act(S("TR"), C("PB", 0, 256, parts=top))
+    mm(C("PU", 0, 128), C("TR", 128, 256), C("TR", 0, 128), True, True)
+    tt(UP, C("PA", 0, NN), LTG, A.is_lt)
+    tt(S("X", 0, slice(0, N2)), TT, S("OM"), A.is_lt)
+    red(C("SM", 0), UP)
+    red(S("X", 0, slice(N2, N2 + 1)), S("X", 0, D_), A.max)
+    tt(U, C("PA", 0, NN), LTC, A.is_lt)
+    tt(S("M"), C("PU", 0, 128), S("LT"), A.is_lt)
+    XW = slice(0, N2 + 1)
+    ts(S("Z", XW), S("X", 0, XW), -99.0, A.mult, C("SM", 0), A.add)
+
     act(col(T0), col(FP), AF.Relu, scale=-1.0, bias=5.0)
     act(col(T1), col(FP), AF.Sign, bias=-4.5)
-    act(S("EF"), S("F8"), AF.Abs, scale=-1.0, bias=col(FP))
+    act(S("KT"), S("NR"), AF.Relu, scale=-1.0, bias=1.0)
     act(col(T2), col(T0), scale=-1.0, bias=23.0)
     act(col(T3), col(T1), scale=5.0, bias=2.0)
-    act(S("EF"), S("EF"), AF.Relu, scale=-1.0, bias=1.0)
+    act(C("KC", 0, N2), S("KT"), scale=-1.0, bias=-16.0)
     act(col(KCB), col(T2), scale=col(HALF), bias=-16.0)
     act(col(T0), col(FP), scale=-1.0, bias=col(T3))
-    ID = C("J", 0, 128)
-    act(S("N15"), ID, scale=-1.5)
+    act(S("EF"), S("F8"), AF.Abs, scale=-1.0, bias=col(FP))
+    act(C("KC", N2, 2 * N2), S("KT"), scale=-1.0, bias=col(KCB))
     act(col(WS), col(T0), scale=col(NH))
-    iota(S("F96"), [[1, 8], [0, 12]], 0)
-    iota(S("C1", al, slice(0, 64)), [[8192, 8], [0, 64]], 0)
-    iota(S("C1", al, slice(64, 128)), [[0, 16], [32, 16], [0, 2]], 0)
-    iota(S("C1", al, slice(128, 192)), [[0, 256], [16, 2]], 0, 1)
-    for name, v in (("JN", -1.0), ("JH", 0.5), ("JM", -0.5)):
-        add("pool", lambda e, name=name, v=v: e.affine_select(T[name][:], T.RR[:, 0:256], [[0, 2], [1, 128]], A.not_equal, v, 0, -1),
-            [S(name)], [C("RR", 0, 256)])
-    for s, b in enumerate((0, 32, 96)):
-        iota(S("CL", al, s), [[0, 16], [16, 2]], b, 1)
+    act(S("EF"), S("EF"), AF.Relu, scale=-1.0, bias=1.0)
+    act(S("TG"), C("F8", 0, 6), bias=col(KA))
+    act(col(NG), col(G16), scale=-1.0)
+    act(C("TG", 3), col(HALF), scale=-2.0, bias=4.0)
 
-    cp(S("CB"), S("CT"))
-    mm(C("PM", 0, 48), S("E8"), S("CB"), True, True)
-    ND = C("PN", 0, 256)
-    ms(C("W", 7 * P, 8 * P), 127.0)
-    tt(S("GA"), C("PM", 0, 8), S("ACT"), A.mult)
-    tt(S("NE"), C("PM", 32, 48), S("CMP"), A.is_equal)
-    scan(S("INI"), S("GA"), S("ACT"), -25.0)
-    ts(C("SM", 0), C("PM", 0), 1.0, A.is_ge)
-    tt(S("TT"), S("INI"), C("PM", 8, 32, 3), A.subtract)
-    ts(ND, S("IA"), 8.0, A.is_le)
-    tt(C("TG", 1, 8), C("TT", 1, 8), C("NE", 1, 8), A.mult)
-    ts(C("TG", 0), C("NE", 0), C("TT", 0), A.mult, C("SM", 0), A.mult)
-    tt(C("TG", 8, 16), S("TT"), C("NE", 8, 16), A.mult)
-    tt(S("IDX", al, 0), S("IA"), ND, A.mult)
-    tt(S("EQ"), IND(C("TG", 0, 16), C("JU", 0, 26)), S("NR"), A.is_equal)
-    tt(S("IDX", al, 1), S("IB"), ND, A.mult)
-    cp(S("RTB"), S("RT"))
-    CP = C("INI", 7)
-    NR = C("NR", 0, NN)
-    E = lambda k: S("EE", k)
-    act(S("KT"), C("NR", 0, 78), AF.Relu, scale=-1.0, bias=-24.0)
-    act(C("DA", 0, 8), S("EF"), scale=0.5)
-    act(C("DA", 8, 16), S("EF"), scale=col(CN))
-    act(C("DA", 16, 24), S("EF"), scale=col(CH))
-    act(C("DA", 24, 32), S("EF"), scale=col(CQ))
-    act(C("DA", 32, 40), S("EF"), scale=col(CN))
-    act(S("IDF"), ID)
-    act(C("CS", 0, 8), S("F8"), scale=4194304.0, bias=7.0 * 16513 * 512 + 4194304.0)
-    act(C("CS", 8, 16), S("F8"), scale=0.0)
-    act(C("CS", 16, 24), S("F8"), scale=4194304.0, bias=4194304.0)
-    for name, v in (("MR", BIG), ("MZ", -BIG), ("M64", 64.0)):
-        act(C(name, 0, WIDE), S("ONE", slice(0, WIDE), parts=slice(0, 1)), scale=v)
-
-    mm(C("PU", 0, 208), ID, C("EQ", 0, 208), True, False)
-    mm(C("PU", 0, 208), ID, C("EQ", 208, 416), False, True)
-    act(S("M2", slice(2, 8), 0), C("EQ", 52, 208), scale=-1.0, bias=1.0)
-    act(S("M2", slice(2, 8), 1), C("EQ", 260, 416), scale=108.0, bias=-99.0)
-    act(C("M1", 52, 208), C("PU", 52, 208), scale=-9.0, bias=9.0)
-    act(S("H1"), S("IDX"), AF.Sign, bias=-2.5)
-    mm(C("PW", 0, 3), S("SEL"), S("RTB"), True, True)
-    mm(C("XY", 0, 128), S("E8"), S("E8"), True, True)
-    mm(C("XX", 0, 128), S("E8"), S("E8B"), True, True)
-    act(S("H2"), S("IDX"), AF.Sign, bias=-5.5)
-    act(S("HB", al, 1), S("H1", al, 1), scale=0.5, bias=-0.5)
-    act(C("SM", 1, 3), C("PW", 1, 3), scale=-1.0, bias=CP)
-    for bank in ("PA", "PB"):
-        mm(S(bank), ID, S("IDX"), True, False)
-        mm(S(bank), S("N15"), S("H1"), False, False)
-        mm(S(bank), S("N15"), S("H2"), False, bank == "PA")
-    mm(S("PB"), ID, S("HB"), False, True)
-    act(E(4), NR, AF.Relu, scale=-1.0, bias=CP)
-    act(E(3), NR, AF.Abs, scale=-1.0, bias=CP)
-    act(E(0), NR, AF.Abs, scale=-1.0, bias=C("SM", 1))
-    act(E(1), NR, AF.Abs, scale=-1.0, bias=C("SM", 2))
-    act(S("LA"), C("XY", 0, 128), scale=col(W16))
-    act(E(4), E(4), AF.Sign)
-    act(S("EQC"), E(3), AF.Relu, scale=-1.0, bias=1.0)
-    act(S("EE", slice(0, 2)), S("EE", slice(0, 2)), AF.Relu, scale=-1.0, bias=1.0)
-    act(S("LS"), C("XY", 0, 128), scale=col(WS))
-    act(S("BO"), C("XY", 0, 128))
-    act(S("LB"), C("XX", 0, 128), scale=col(W16))
-    act(S("I32"), ID, scale=32.0)
-    act(C("KC", 0, 78), S("KT"), scale=-1.0, bias=-16.0)
-    act(C("KC", 78, 156), S("KT"), scale=-1.0, bias=col(KCB))
-    act(S("Z1"), S("PA"), AF.Relu, bias=-4.0)
-    act(S("Z2"), S("PB"), AF.Abs, bias=-3.0)
-    act(S("IW"), ID, scale=-127.0 / 16384)
-    act(S("Z2"), S("Z2"), AF.Relu, scale=-127.0 / 128, bias=127.0 / 128)
-    act(C("W", 5 * P, 7 * P), C("YO", 5 * P, 7 * P), scale=-1.0, bias=255.0)
-    act(S("DL"), S("F96"), AF.Abs, scale=-1.0, bias=col(FP))
-    for s in range(5, 9):
-        dma("sync", C("REC", 160 * s, 160 * s + 160), S("C1", 0, slice(32, 192)), "nul")
-    dma("sync", C("RES", 2 * P, 3 * P), T.res[:, 2 * P:3 * P], "res2", [("snt0", neng)])
-
-    def vec_dve(f0, f1):
+    def vec(f0, f1):
         fs = slice(f0, f1)
-        nd = C("PN", 32 * f0, 32 * f1)
-        return [lambda n=n, i=i: tt(S("N" + n, fs, i), S(n, fs, i), nd, A.mult) for n in ("VY", "VX") for i in (0, 1)]
+        nd = C("XX", 32 * f0, 32 * f1)
+        return [lambda n=n, i=i: tt(S("NV", fs, i, al, n), S(("VY", "VX")[n], fs, i), nd, A.mult) for n in (0, 1) for i in (0, 1)]
 
-    def masks(f0, f1):
-        act(C("THR", 32 * f0, 32 * f1), S("NDS", slice(f0, f1)), scale=1000000.0)
-        for k in range(4):
-            sg = 1.0 if k % 2 else -1.0
-            act(S("MK", slice(f0, f1), slice(32 * k + 32, 32 * k + 64)), S("NDS", slice(f0, f1)), scale=sg, bias=-sg)
-
-    def vec_pe(f0, f1):
-        for bank, w, n, b in (("XY", S("I32"), "NVY", "BY"), ("XX", ID, "NVX", "BX")):
-            mm(C(bank, 64 * f0, 64 * f1), w, S(n, slice(f0, f1)), True, False)
-            for k in range(f0, f1):
-                mm(C(bank, 64 * k, 64 * k + 64), ID, S(b), False, k == f1 - 1)
-
-    U, L = C("X", NN, 2 * NN), C("X", 0, NN)
-    QS = C("Q", NN, 2 * NN)
-    tt(S("K2"), C("EQ", 0, 52), C("EQ", 208, 260), A.is_equal)
-    tt(L, C("EQ", 208, 234), C("EQ", 26, 52), A.is_gt)
-    tt(C("MV", 0, NN), C("K2", 0, NN), C("EQ", 234, 260), A.mult)
-    tt(U, C("K2", 0, NN), C("K2", NN, 52), A.mult)
-    fill = vec_dve(0, 3) + [
-        lambda: tt(E(2), E(0), E(1), A.is_gt),
-        lambda: tt(E(5), E(2), E(1), A.is_equal),
-        lambda: tt(E(6), E(4), E(5), A.mult),
+    v01 = vec(0, 2)
+    fill = [
+        [lambda: ts(ND, S("IA"), 8.0, A.is_le)],
+        [lambda: tt(S("IDX", 0), S("IA"), ND, A.mult)],
+        [lambda: tt(S("IDX", 1), S("IB"), ND, A.mult)],
+        [lambda: scan(SU, U, C("ZR", 0, NN), 0.0), lambda: tt(OS, S("OM", D_), S("OR", D_), A.add),
+         lambda: ts(S("EQC"), S("NR"), CS_, A.is_equal), lambda: tt(OS, U, OS, A.is_gt)],
+        [lambda: ts(S("FX", 0), S("IDX", 1), 0.0, A.is_equal), lambda: ts(OS, OS, -99.0, A.mult),
+         lambda: ts(S("FX", 1), S("IDX", 1), 1.0, A.is_equal, -1.0, A.mult), lambda: tt(SV, SU, OS, A.add)],
+        [lambda: tt(S("EM", 1), S("E0"), S("EM", 0), A.is_gt), lambda: ts(S("GEN", D_), S("NR", D_), CS_, A.is_ge),
+         lambda: ts(S("GEN", R_), C("PU", 128, 128 + NN), 0.0, A.is_equal), lambda: tt(S("EM", 2), S("EM", 1), S("EM", 0), A.is_equal)],
     ]
-    for f in range(2, F):
-        now, new = ("X", "X2")[f % 2], ("X2", "X")[f % 2]
-        scan(S("Q"), S(now), S("MV"), C("INI", f))
-        tt(S("BB"), C(now, 0, NN), C("MV", 0, NN), A.add)
-        tt(S("AA"), C(now, NN, 2 * NN), C("M1", f * NN, (f + 1) * NN), A.mult)
-        tt(C("PRD", 0, NN), C(now, NN, 2 * NN), S("M2", f, 1), A.mult)
-        fill.pop(0)()
-        tt(C(new, 0, NN), S("BB"), S("M2", f, 0), A.mult)
-        tt(C(new, NN, 2 * NN), S("AA"), QS, A.is_gt)
-        tt(C("MV", 0, NN), C("PRD", 0, NN), QS, A.is_gt)
-        if f == 5:
-            act(S("NDS"), ND)
-            vec_pe(0, 3)
-            mm(S("PW"), S("IW"), S("Z1"), True, False)
-            for k in (0, 256):
-                mm(C("PW", k, k + 256), S("C7"), S("ONE", parts=slice(0, 1)), False, False)
-            mm(S("PW"), ID, S("Z2"), False, True)
-            act(S("POW"), S("PW"))
-    fill.pop(0)()
-    tt(S("BB"), L, C("MV", 0, NN), A.add)
-    L = S("BB")
-    tt(C("Y", 52, 78), U, E(6), A.mult)
-    tt(S("H"), U, L, A.add)
-    tt(C("Y", 78, 104), L, E(5), A.mult)
-    tt(C("Y", 0, 26), S("H"), E(1), A.mult)
-    tt(C("Y", 26, 52), S("H"), E(2), A.mult)
-    D = C("PM", 64, 220)
-    mm(D, ID, S("KC"), True, False)
-    for k in range(6):
-        d = C("PM", 64 + NN * k, 64 + NN * k + NN)
-        mm(d, S("LS"), S("EQC"), False, False)
-    for k in range(6):
-        d = C("PM", 64 + NN * k, 64 + NN * k + NN)
-        mm(d, S("LA" if k < 3 else "LB"), S("H"), False, k == 5)
-    scan(C("PU", 256, 360), S("Y"), S("ZR"), 0.0)
-    ts(C("PU", 384, 448), C("XY", 0, 64), 0.0, A.max, 480.0, A.min)
-    ts(C("SM", 3), C("PU", 359), C("PU", 333), A.add, 1.0, A.add)
-    ts(S("CX"), C("XX", 0, 64), col(G16), A.max, col(G31), A.min)
-    ts(C("PU", 334, 360), C("PU", 334, 360), -1.0, A.mult, C("SM", 3), A.add)
-    tt(C("PU", 448, 512), C("PU", 384, 448), S("CX"), A.add)
-    tt(S("PP"), S("Y"), C("PU", 256, 360), A.mult)
-    r0 = 160 * PSLOT[0]
-    tt(S("P2"), C("PP", 0, 52), C("PP", 52, 104), A.add)
-    tt(S("RK"), C("P2", 0, NN), C("P2", NN, 52), A.add)
-    ts(S("RAB", 0), S("RK"), col(KA), A.subtract)
-    ts(S("RAB", 1), S("RK"), col(KB), A.subtract, col(SC), A.mult)
+    LAM = C("PN", N2)
+    for t in range(6):
+        mm(C("PN", 0, N2 + 1), S("M"), S("X", t % 2, XW), True, True)
+        for x in fill[t]:
+            x()
+        if t == 1:
+            mm(C("PW", 0, 128), S("EA"), S("EA"), True, True)
+            mm(C("PW", 128, 256), S("EA"), S("E8"), True, True)
+            act(S("LA"), C("PW", 0, 128), scale=col(W16))
+            act(S("LS"), C("PW", 0, 128), scale=col(WS))
+            act(C("LB", 0, 64), C("PW", 0, 64), scale=col(W16))
+        if t == 2:
+            act(S("H1"), S("IDX"), AF.Sign, bias=-2.5)
+            act(S("H2"), S("IDX"), AF.Sign, bias=-5.5)
+            act(S("BO"), C("PW", 128, 256))
+        if t == 3:
+            mm(S("PA"), ID, S("IDX"), True, False)
+        if t == 4:
+            for i in (0, 1):
+                mm(C("PA", 256, 512), ID, S("FX", i), False, False)
+        if t == 5:
+            ts(S("HH", D_), SV, LAM, A.add, -91.0, A.is_le)
+            tt(S("LM"), C("PN", 0, N2), S("OR"), A.is_gt)
+        ts(S("X", (t + 1) % 2, XW), S("Z", XW), LAM, A.add, -91.0, A.is_le)
+    act(S("BT", al, 0), S("BI", 0))
+    act(S("BT", al, 1), S("BI", 1), bias=col(NG))
+    DD = lambda a, n=N2: C("PB", 256 + a, 256 + a + n)
+    for k, x in enumerate(((DD(0, 2 * N2), ID, S("KC")), (DD(0), S("LS"), S("EQC")), (DD(N2), S("LS"), S("EQC")), (DD(0), S("LA"), S("GEN")), (DD(N2), S("LB"), S("GEN")))):
+        mm(*x, k == 0, False)
+    mm(S("PA"), S("N15"), S("H1"), False, False)
+    tt(S("HH", R_), S("X", 0, R_), S("LM", R_), A.add)
+    tt(S("LD"), S("X", 0, D_), S("LM", D_), A.add)
+    v01[0]()
     for k in range(3):
-        ts(S("EW", al, k), S("RAB"), float(k), A.is_equal, 512.0 * 128 ** k, A.mult)
-    tt(S("EP"), S("EW"), D, A.mult)
-    red(C("SM", 4), C("EP", 0, 78))
-    red(C("SM", 5), C("EP", 78, 156))
-    mm(C("PM", 256, 280), S("IDF"), S("CS"), True, False)
+        tt(C("Y", N2 * k, N2 * k + N2), S("HH"), S("EM", k), A.mult)
+    for k, x in enumerate(((DD(0, NN), S("LA"), S("HH", D_)), (DD(N2, NN), S("LB"), S("HH", D_)), (DD(0, NN), S("LA"), S("LD")), (DD(N2, NN), S("LB"), S("LD")))):
+        mm(*x, False, k == 3)
+    mm(S("PA"), S("N15"), S("H2"), False, True)
+    for i in (0, 1):
+        act(S("BM", i), S("BT"), bias=-192.0)
+    act(S("DS"), DD(0, 2 * N2))
+    v01[1]()
+    scan(C("XY", 256, 256 + 156), S("Y"), C("ZR", 0, 156), 0.0)
+    v01[2]()
+    tt(S("PP"), C("Y", N2, 3 * N2), C("XY", 256 + N2, 256 + 156), A.mult)
+    v01[3]()
+    RK = C("PM", 96, 96 + N2)
+    mms((RK, ID, C("Y", 0, N2)), (RK, ID, C("PP", 0, N2)), (RK, ID, C("PP", N2, 2 * N2)))
+    for k, sc in enumerate((0.5, col(CN), col(CH), col(CQ), col(CN))):
+        ts(C("DA", 8 * k, 8 * k + 8), S("EF"), sc, A.mult)
+    act(C("CS", 0, 8), S("F8"), scale=4194304.0, bias=7.0 * 16513 * 512 + 4194304.0)
+    act(C("CS", 16, 24), S("F8"), scale=4194304.0, bias=4194304.0)
+    act(S("IDF"), ID)
+    for i in (0, 1):
+        act(S("POW", al, i), C("PA", 256 * i, 256 * i + 256), AF.Exp, scale=-7 * math.log(2), bias=21 * math.log(2))
+
+    def places(f):
+        pos = C("XY", 128 * (f % 2), 128 * (f % 2) + 128)
+        mms((pos, ID, S("NV", f)), (pos, ID, S("BM")), (pos, ID, S("H")))
+
+    def clamps(f):
+        a = 128 * (f % 2)
+        ts(C("CC", 0, 64), C("XY", a, a + 128, 2), 0.0, A.max, 15.0, A.min)
+        ts(C("CC", 64, 128), C("XY", a + 1, a + 128, 2), 0.0, A.max, 31.0, A.min)
+        mms((C("PM", 384, 448), S("I32"), C("CC", 0, 64)), (C("PM", 384, 448), ID, C("CC", 64, 128)))
+
+    def keep(f):
+        r, a = RW * PSLOT[f], 128 * (f % 2)
+        tt(C("REC", r + 32, r + RW), C("XY", a, a + 64), S("BT"), A.subtract)
+
+    places(0)
+    for k in range(6):
+        ts(S("EW", k), RK, C("TG", k), A.is_equal, C("WK", k % 3), A.mult)
+        o = C("PN", 64 + N2 * (k // 3), 64 + N2 * (k // 3) + N2)
+        mm(o, ID, S("EW", k), k % 3 == 0, k % 3 == 2)
+    clamps(0)
+    tt(S("EP"), C("PN", 64, 64 + 2 * N2), S("DS"), A.mult)
+    keep(0)
+    red(C("SM", 4), C("EP", 0, N2))
+    red(C("SM", 5), C("EP", N2, 2 * N2))
+    TBP = lambda a, b=None: C("PU", 256 + a, None if b is None else 256 + b)
+    mm(TBP(0, 24), S("IDF"), S("CS"), True, False)
     ts(S("RA"), C("DA", 0, 24), C("SM", 4), A.mult)
     ts(S("RB"), C("DA", 24, 40), C("SM", 5), A.mult)
-    mm(C("PM", 256, 280), S("BO"), S("RA"), False, False)
-    mm(C("PM", 264, 280), S("BO"), S("RB"), False, True)
-    masks(1, 3)
-    cp(C("REC", r0 + 32, r0 + 96), C("XY", 0, 64))
-    cp(C("REC", r0 + 96, r0 + 160), C("XX", 0, 64))
-    act(S("DL"), S("DL"), AF.Relu, scale=-1.0, bias=1.0)
-    act(S("DL"), S("DL"), scale=col(H5))
-    act(C("W", 8 * P, 9 * P), C("YO", 4 * P, 5 * P), scale=-1.0, bias=255.0, waits=[("arr0", narr)])
+    mm(TBP(0, 24), S("BO"), S("RA"), False, False)
+    mm(TBP(8, 24), S("BO"), S("RB"), False, True)
+    ts(S("DL"), S("F48"), col(FP), A.is_equal, col(CH), A.mult)
+    ts(S("RL"), S("DL"), C("SM", 5), A.mult, RW / 256.0, A.mult)
+    act(S("CL"), S("CL"), bias=col(NG))
 
-    def look_act(f0, f1):
-        for f in range(f0, f1):
-            act(C("U1", 64 * f, 64 * f + 64), S("H1", f), scale=C("TB", 8 + f), bias=C("TB", f))
-            act(C("U2", 64 * f, 64 * f + 64), S("H2", f), scale=C("TB", 16 + f))
+    def masks(f0, f1):
+        fs, nd = slice(f0, f1), C("XX", 32 * f0, 32 * f1)
+        act(S("MK", fs, slice(0, 32)), nd, scale=-129.0, bias=129.0)
+        for k in (32, 33):
+            act(S("MK", fs, slice(k, RW, 2)), nd, scale=-1.0, bias=1.0)
 
-    def look_pe(f0, f1):
-        mm(C("PW", 64 * f0, 64 * f1), S("IDF"), C("U1", 64 * f0, 64 * f1), True, False)
-        mm(C("PW", 64 * f0, 64 * f1), S("IDF"), C("U2", 64 * f0, 64 * f1), False, True)
+    def look(f):
+        act(S("U1", f), S("H1", al, f), scale=C("TB", 8 + f), bias=C("TB", f))
+        act(S("U2", f), S("H2", al, f), scale=C("TB", 16 + f))
+        o = C("PW", 64 * f, 64 * f + 64)
+        mms((o, S("IDF"), S("U1", f)), (o, S("IDF"), S("U2", f)))
 
-    def look_dve(f0, f1):
+    def entries(f):
         return [
-            lambda: tt(S("XI", slice(f0, f1)), C("PW", 64 * f0, 64 * f1), C("POW", 64 * f0, 64 * f1), A.mult),
-            lambda: (ts(S("C1", slice(f0, f1), slice(32, 64)), S("XI", slice(f0, f1), 0), 65024, A.bitwise_and),
-                     ts(S("SS", slice(f0, f1), 1), S("XI", slice(f0, f1), 1), 7680, A.bitwise_and)),
+            lambda: tt(S("XI", f), C("PW", 64 * f, 64 * f + 64), S("POW", f), A.mult),
+            lambda: ts(S("A0", f), S("XI", f, 0), 65024, A.bitwise_and),
+            lambda: ts(S("A0", f), S("A0", f), (16 * f - 1) * 65536.0, A.add),
         ]
 
     def record(f):
-        r = 160 * PSLOT[f]
-        win = C("REC", 160 * wbase(f), 160 * (8 if f < 6 else 10))
+        r = RW * PSLOT[f]
+        win = C("REC", RW * wbase(f), RW * (8 if f < 6 else 10))
         return [
-            lambda: tt(S("G"), IND(win, C("LU", 12 * f, 12 * f + 12)), S("C1", f), A.subtract),
-            lambda: tt(S("MK", f, slice(0, 32)), C("G", 0, 32), C("THR", 32 * f, 32 * f + 32), A.is_ge),
-            lambda: tt(S("MW"), C("G", 32, 192), S("MK", f), A.mult),
-            lambda: (ts(S("HY"), C("MW", 32, 96), 1, A.arith_shift_right, -32, A.bitwise_and),
-                     ts(S("HX"), C("MW", 96, 160), 1, A.arith_shift_right),
-                     tt(C("REC", r, r + 32), C("MW", 0, 32), S("C1", f, slice(32, 64)), A.add)),
-            lambda: (tt(C("REC", r + 32, r + 96), S("HY"), C("XY", 64 * f, 64 * f + 64), A.add),
-                     tt(C("REC", r + 96, r + 160), S("HX"), C("XX", 64 * f, 64 * f + 64), A.add)),
+            lambda: (tt(S("G"), IND(win, C("LU", 6 * f, 6 * f + 6)), S("MK", f), A.mult),
+                     act(C("H", 0, 64), C("G", 32, RW), scale=0.5, bias=191.75),
+                     act(C("H", 64, 128), C("G", 32, RW), scale=-0.5, bias=191.75)),
+            lambda: tt(S("XI", f, 0), C("G", 0, 32), S("A0", f), A.max),
+            lambda: (ts(C("REC", r, r + 32), S("XI", f, 0), 65024, A.bitwise_and),
+                     ts(S("SS", f % 2), S("XI", f), 7680, A.bitwise_and)),
         ]
 
     def offsets(f):
-        r = 160 * PSLOT[f]
-        CY, S1 = C("PM", 376, 440), C("PM", 440, 504)
         return [
-            lambda: (ts(S("SS", f, 0), C("REC", r, r + 32), 7680, A.bitwise_and),
-                     ts(CY, C("REC", r + 32, r + 96), 0.0, A.max, 480.0, A.min),
-                     ts(S("CX"), C("REC", r + 96, r + 160), col(G16), A.max, col(G31), A.min)),
-            lambda: tt(S1, CY, S("SS", f), A.add),
-            lambda: tt(S("S2"), S1, S("CX"), A.add),
-            lambda: ts(C("OFF", 64 * f, 64 * f + 64), S("S2"), col(G16), A.subtract, float(-P * wbase(f)), A.add),
+            lambda: tt(S("S2"), C("PM", 384, 448), S("SS", f % 2), A.add),
+            lambda: ts(C("OFF", 64 * f, 64 * f + 64), S("S2"), float(-P * wbase(f)), A.add),
         ]
-
-    def weave(a, b):
-        for k in range(max(len(a), len(b))):
-            for x in (a, b):
-                if k < len(x):
-                    x[k]()
 
     pieces = list(zip(CUTS[:-1], CUTS[1:]))
 
     def bank(h):
-        name, at = (("PA", 0), ("PB", 0), ("PU", 0), ("PN", 384))[h]
+        name, at = (("PA", 0), ("PB", 0), ("PU", 0), ("PN", 320))[h]
         return C(name, at, at + pieces[h][1] - pieces[h][0])
 
     row1 = S("ONE", slice(0, 128), parts=slice(0, 1))
 
+    def pixels_start(f):
+        s = 16 * ((f + 1) % 8)
+        for h, (a, b) in enumerate(pieces):
+            mm(bank(h), C("J", s, s + 128), C("RES", f * P + a, f * P + b), True, False)
+            mm(bank(h), row1, C("MQ", 0, b - a), False, False)
+            if f == F - 1:
+                mm(bank(h), row1, C("M128", 0, b - a), False, False)
+
     def pixels_front(f):
         s = 16 * ((f + 1) % 8)
         win = C("W", P * wbase(f), P * (9 + f))
-        aw = [("arr%d" % f, narr)] if f else []
+        aw = [("arr%d" % f, narr * (len(SENDS) if f else 1))]
         last = f == F - 1
-        for h, (a, b) in enumerate(pieces):
-            mm(bank(h), C("J" if last else "JN", s, s + 128), C("RES", f * P + a, f * P + b), True, False)
-            if last:
-                mm(bank(h), row1, C("M64", 0, b - a), False, False)
         for a, b in pieces:
             act(C("GP", a, b), IND(win, C("OFF", 64 * f + a // 16, 64 * f + b // 16)), AF.Relu, scale=-1.0, bias=255.0, waits=aw)
-            ts(C("GQ", a, b), IND(win, C("OFF", 64 * f + 32 + a // 16, 64 * f + 32 + b // 16)), 255.0, A.min, -127.5, A.add, aw)
+            ts(C("GQ", a, b), IND(win, C("OFF", 64 * f + 32 + a // 16, 64 * f + 32 + b // 16)), 255.0, A.min, waits=aw)
         for h, (a, b) in enumerate(pieces):
-            mm(bank(h), C("JM" if last else "JH", s, s + 128), C("GQ", a, b), False, False)
-            mm(bank(h), C("JH" if last else "JM", s, s + 128), C("GP", a, b), False, False)
+            mm(bank(h), C("JH", s, s + 128), C("GQ", a, b), False, False)
+            mm(bank(h), C("JM", s, s + 128), C("GP", a, b), False, False)
             mm(bank(h), row1, C("MR", 0, b - a), False, not last)
             if last:
                 mm(bank(h), row1, C("MZ", 0, b - a), False, True)
+        sent = 0
         for h, (a, b) in enumerate(pieces):
             out = C("SND", f * P + a, f * P + b)
             if last:
@@ -446,63 +426,88 @@ def build(T, nxt):
                 if h % 2:
                     a = pieces[h - 1][0]
                     dma("sync" if h == 1 else "scalar", T.y[:, f * P + a:f * P + b], C("SND", f * P + a, f * P + b), "out%d" % (f + h // 2))
-            elif h % 2:
-                act(out, bank(h), AF.Relu, bias=191.0 - BIG)
+                continue
+            if h % 2:
+                act(out, bank(h), AF.Relu, bias=128.0 - BIG)
             else:
-                ts(out, bank(h), 191.0 - BIG, A.add, 0.0, A.max)
-        if not last:
-            send(C("W", (9 + f) * P, (10 + f) * P), C("SND", f * P, f * P + P), f + 1)
+                ts(out, bank(h), 128.0 - BIG, A.add, 0.0, A.max)
+            if h in SENDS:
+                send(C("W", (9 + f) * P + sent, (9 + f) * P + b), C("SND", f * P + sent, f * P + b), f + 1)
+                sent = b
 
-    def pixels_back(f):
+    def turn_back(f):
         s = 128 - 16 * (f + 1)
         mm(S("PU"), C("J", s, s + 128), C("SND", f * P, f * P + P), True, True)
-        act(C("W", PSLOT[f] * P, PSLOT[f] * P + P), S("PU"))
-        act(C("YO", f * P, f * P + P), S("PU"), AF.Relu, scale=-1.0, bias=255.0)
+
+    def copy_back(f):
+        own = C("W", PSLOT[f] * P, PSLOT[f] * P + P)
+        act(own, S("PU"))
         if f < 5:
             k = f + 3
             add("sync", lambda e: e.dma_start(T.RES[:, k * P:k * P + P], T.res[:, k * P:k * P + P]),
-                [C("RES", k * P, k * P + P)], [C("YO", f * P, f * P + P)], (), "res%d" % k)
-        dma("sync", T.y[:, f * P:f * P + P], C("YO", f * P, f * P + P), "out%d" % f, [("snt%d" % (f + 1), neng)])
+                [C("RES", k * P, k * P + P)], [own], (), "res%d" % k)
 
-    ts(C("PU", 0, 64), S("H2", 0), C("PM", 272), A.mult)
-    ts(C("U1", 0, 64), S("H1", 0), C("PM", 264), A.mult, C("PM", 256), A.add)
-    tt(C("U1", 0, 64), C("U1", 0, 64), C("PU", 0, 64), A.add)
-    act(S("RL"), S("DL"), scale=C("SM", 5))
-    act(S("TB"), C("PM", 256, 280))
-    tt(S("XI", 0), C("U1", 0, 64), C("PW", 0, 64), A.mult)
+    def store(f):
+        ts(C("YO", f * P, f * P + P), C("W", PSLOT[f] * P, PSLOT[f] * P + P), 255.0, A.min)
+        dma("sync", T.y[:, f * P:f * P + P], C("YO", f * P, f * P + P), "out%d" % f, [("snt%d" % (f + 1), neng * len(SENDS))])
+
+    dma("sync", C("RES", 2 * P, 3 * P), T.res[:, 2 * P:3 * P], "res2", [("snt0", neng)])
+    r0 = RW * PSLOT[0]
+    ts(S("U2", 0), S("H2", al, 0), TBP(16), A.mult)
+    ts(S("U1", 0), S("H1", al, 0), TBP(8), A.mult, TBP(0), A.add)
+    act(S("TB"), TBP(0, 24))
+    mms((C("PM", 280, 328), S("IDF"), S("CL")), (C("PM", 280, 328), S("BO"), S("RL")))
+    tt(S("U1", 0), S("U1", 0), S("U2", 0), A.add)
+    masks(1, 3)
+    look(1)
+    tt(S("XI", 0), S("U1", 0), S("POW", 0), A.mult)
+    cp(S("LU"), C("PM", 280, 328))
     ts(S("SS", 0), S("XI", 0), 7680, A.bitwise_and)
-    mm(C("PM", 280, 376), S("BO"), S("RL"), True, True)
     ts(C("REC", r0, r0 + 32), S("XI", 0, 0), 65024, A.bitwise_and)
-    tt(S("S2"), C("PU", 448, 512), S("SS", 0), A.add)
-    offsets(0)[3]()
-    look_act(1, 3)
-    look_pe(1, 2)
+    weave(offsets(0))
+    entries(1)[0]()
+    look(2)
     for f in range(F):
+        pixels_start(f)
         pixels_front(f)
         if f == F - 1:
             break
-        if f == 1:
-            weave(record(2)[2:], vec_dve(3, 5))
-            vec_pe(3, 5)
+        turn_back(f)
         if f == 0:
-            tt(S("TL"), C("PM", 280, 376), S("CL"), A.add)
-            look_dve(1, 2)[0]()
-            look_pe(2, 3)
-            ts(S("LU"), S("TL"), col(G16), A.subtract)
-            look_dve(1, 2)[1]()
-            weave(record(1), look_dve(2, 3))
-        pixels_back(f)
-        if f == 2:
-            weave(vec_dve(5, 8), [])
-            vec_pe(5, 8)
-        if f in LOOK:
-            look_act(*LOOK[f])
-            look_pe(*LOOK[f])
-        if f in MASK:
-            masks(*MASK[f])
-        ahead = look_dve(*LOOK[f - 1]) if f - 1 in LOOK else []
-        ahead += record(f + 2)[:5 if f else 2] if f + 2 < F else []
-        weave(offsets(f + 1), ahead)
+            e1, r1 = entries(1), record(1)
+            weave(e1[1:], r1[:1])
+            copy_back(f)
+            places(1)
+            weave(r1[1:], entries(2))
+            keep(1)
+            clamps(1)
+            weave(vec(2, 4))
+        g = f + 2
+        if g < F:
+            r = record(g)
+            weave(r[:1], offsets(f + 1)[:1])
+            if f:
+                copy_back(f)
+            weave(r[1:], offsets(f + 1)[1:])
+            places(g)
+            if g + 1 < F:
+                look(g + 1)
+            if f == 0:
+                masks(3, 8)
+            if f == 1:
+                for name, v in (("MZ", -BIG), ("M128", 128.0)):
+                    act(C(name, 0, WIDE), S("ONE", slice(0, WIDE), parts=slice(0, 1)), scale=v)
+            if f in (1, 2):
+                weave(vec(2 * f + 2, 2 * f + 4))
+            keep(g)
+            clamps(g)
+            store(f)
+            if g + 1 < F:
+                weave(entries(g + 1))
+        else:
+            copy_back(f)
+            weave(offsets(f + 1))
+            store(f)
     return ops, neng, narr
 
 

@@ -360,6 +360,8 @@ def build(T, nxt):
     def look(f):
         act(S("U1", f), S("H1", al, f), scale=C("TB", 8 + f), bias=C("TB", f))
         act(S("U2", f), S("H2", al, f), scale=C("TB", 16 + f))
+
+    def look_sum(f):
         o = C("PW", 64 * f, 64 * f + 64)
         mms((o, S("IDF"), S("U1", f)), (o, S("IDF"), S("U2", f)))
 
@@ -398,7 +400,8 @@ def build(T, nxt):
 
     def pixels_start(f):
         s = 16 * ((f + 1) % 8)
-        for h, (a, b) in enumerate(pieces):
+        for h in (0, 1, 3, 2):
+            a, b = pieces[h]
             mm(bank(h), C("J", s, s + 128), C("RES", f * P + a, f * P + b), True, False)
             mm(bank(h), row1, C("MQ", 0, b - a), False, False)
             if f == F - 1:
@@ -458,55 +461,60 @@ def build(T, nxt):
     act(S("TB"), TBP(0, 24))
     mms((C("PM", 280, 328), S("IDF"), S("CL")), (C("PM", 280, 328), S("BO"), S("RL")))
     tt(S("U1", 0), S("U1", 0), S("U2", 0), A.add)
-    masks(1, 3)
     look(1)
+    look(2)
+    masks(1, 3)
+    pixels_start(0)
+    look_sum(1)
     tt(S("XI", 0), S("U1", 0), S("POW", 0), A.mult)
     cp(S("LU"), C("PM", 280, 328))
     ts(S("SS", 0), S("XI", 0), 7680, A.bitwise_and)
     ts(C("REC", r0, r0 + 32), S("XI", 0, 0), 65024, A.bitwise_and)
     weave(offsets(0))
-    entries(1)[0]()
-    look(2)
     for f in range(F):
-        pixels_start(f)
         pixels_front(f)
         if f == F - 1:
             break
         turn_back(f)
         if f == 0:
-            e1, r1 = entries(1), record(1)
-            weave(e1[1:], r1[:1])
+            r1 = record(1)
+            e1 = entries(1)
+            weave(r1[:1], e1[:1])
             copy_back(f)
             places(1)
-            weave(r1[1:], entries(2))
-            keep(1)
+            look_sum(2)
+            weave(e1[1:] + r1[1:], vec(2, 4))
             clamps(1)
-            weave(vec(2, 4))
+            keep(1)
+            weave(entries(2))
         g = f + 2
         if g < F:
             r = record(g)
             weave(r[:1], offsets(f + 1)[:1])
             if f:
                 copy_back(f)
-            weave(r[1:], offsets(f + 1)[1:])
             places(g)
-            if g + 1 < F:
-                look(g + 1)
-            if f == 0:
-                masks(3, 8)
-            if f == 1:
-                for name, v in (("MZ", -BIG), ("M128", 128.0)):
-                    act(C(name, 0, WIDE), S("ONE", slice(0, WIDE), parts=slice(0, 1)), scale=v)
-            if f in (1, 2):
-                weave(vec(2 * f + 2, 2 * f + 4))
+            pixels_start(f + 1)
+            weave((entries(g) if f else []) + r[1:], offsets(f + 1)[1:], vec(2 * f + 2, 2 * f + 4) if f in (1, 2) else [])
             keep(g)
             clamps(g)
-            store(f)
+            if f:
+                store(f - 1)
             if g + 1 < F:
-                weave(entries(g + 1))
+                look(g + 1)
+                look_sum(g + 1)
+            if f == 0:
+                masks(3, 5)
+            if f == 1:
+                masks(5, 8)
+            if f == 2:
+                for name, v in (("MZ", -BIG), ("M128", 128.0)):
+                    act(C(name, 0, WIDE), S("ONE", slice(0, WIDE), parts=slice(0, 1)), scale=v)
         else:
             copy_back(f)
+            pixels_start(f + 1)
             weave(offsets(f + 1))
+            store(f - 1)
             store(f)
     return ops, neng, narr
 

@@ -4,7 +4,8 @@ from concourse.mybir import AluOpType as A, AxisListType, ActivationFunctionType
 
 F = 8
 P = 512
-CUTS = [0, 160, 320, 448, 512]
+CUTS = [0, 128, 288, 448, 512]
+FIN, LASTFIN, GAP = "vsvs", "vssv", 2
 SENDS = (1, 3)
 BIG = 12582912.0
 NN = 26
@@ -18,13 +19,13 @@ SB_ = {
     "IA": ([128, 256], i32), "IB": ([128, 256], i32), "VY": ([128, 8, 2, 32], i32), "VX": ([128, 8, 2, 32], i32),
     "CT": ([128, 8], i32), "EB": ([128, 8], bf), "CA": ([128, 4], f32), "CF": ([128, 4], f32),
     "ONE": ([128, 256], bf), "MR": ([1, 256], bf), "MZ": ([1, 256], bf), "MQ": ([1, 256], bf), "M128": ([1, 256], bf),
-    "J": ([128, 256], bf), "JH": ([128, 256], bf), "JM": ([128, 256], bf), "N15": ([128, 128], bf), "I32": ([128, 128], bf),
+    "ID": ([128, 128], bf), "IK": ([128, 128], bf), "MN": ([128, 128], bf), "NE": ([128, 3 * N2], bf), "J": ([128, 256], bf), "JH": ([128, 256], bf), "JM": ([128, 256], bf), "N15": ([128, 128], bf), "I32": ([128, 128], bf),
     "E8": ([8, 128], bf), "EA": ([8, 128], bf), "BO": ([128, 128], f32), "IDF": ([128, 128], f32),
     "L0": ([128, 128], bf), "LE": ([128, 128], bf), "LT": ([128, 128], bf), "M": ([128, 128], bf), "TR": ([NN, 256], bf),
-    "LA": ([128, 128], bf), "LB": ([128, 128], bf), "LS": ([128, 128], bf),
+    "LA": ([128, 128], bf), "LS": ([128, 128], bf),
     "PI": ([128, 8], i32), "PC": ([128, 24], f32), "F8": ([128, 8], f32), "F48": ([128, 48], f32), "EF": ([128, 8], f32), "TG": ([128, 6], bf),
-    "NR": ([128, N2], bf), "OM": ([128, N2], bf), "OR": ([128, N2], bf), "E0": ([128, N2], bf), "EM": ([128, 3, N2], bf), "EQC": ([128, N2], bf),
-    "GEN": ([128, N2], bf), "TA": ([128, 8, NN], f32), "X": ([128, 2, 56], bf), "Z": ([128, 56], f32), "LM": ([128, N2], bf),
+    "NR": ([128, N2], bf), "OM": ([128, N2], bf), "OR": ([128, N2], bf), "E0": ([128, N2], bf), "EQC": ([128, N2], bf),
+    "GEN": ([128, N2], bf), "TA": ([128, 8, NN], f32), "X": ([128, 2, 56], bf), "Z": ([128, 56], bf), "SV": ([128, NN], bf),
     "HH": ([128, N2], bf), "LD": ([128, NN], bf), "Y": ([128, 3 * N2], bf), "ZR": ([128, 256], bf), "WK": ([128, 4], bf), "PP": ([128, 104], bf),
     "EW": ([128, 6, N2], bf), "DS": ([128, 104], f32), "EP": ([128, 104], f32),
     "KC": ([128, 104], bf), "KT": ([128, N2], f32), "DA": ([128, 40], f32), "DL": ([128, 48], f32),
@@ -39,7 +40,7 @@ SB_ = {
 PS_ = ["PA", "PB", "PU", "XY", "XX", "PM", "PN", "PW"]
 SCRATCH = {k: ("sbuf", v[0], v[1]) for k, v in SB_.items()}
 SCRATCH.update({k: ("psum", [128, P], f32) for k in PS_})
-DMAS = ["ctl", "pic", "pi0", "ia_", "ib_", "vy_", "vx_", "res0", "res2", "res3", "res4", "res5", "res6", "res7"] + ["out%d" % f for f in range(F + 3)]
+DMAS = ["ctl", "pic", "pi0", "ia_", "ib_", "vy_", "vx_", "res0", "res2", "res5"] + ["out%d" % f for f in range(F + 3)]
 SEMAPHORES = ["dve", "act", "pe", "pool"] + DMAS + ["arr%d" % f for f in range(F)] + ["snt%d" % f for f in range(F)]
 
 PSLOT = [4, 3, 2, 1, 0, 9, 8, 10]
@@ -154,27 +155,30 @@ def build(T, nxt):
     dma("sync", S("VX"), T.vx[:], "vx_")
     dma("sync", C("W", 5 * P, 6 * P), T.pic0[:, 0:P], "pi0")
     dma("sync", C("RES", 0, 2 * P), T.res[:, 0:2 * P], "res0")
+    dma("sync", C("RES", 2 * P, 5 * P), T.res[:, 2 * P:5 * P], "res2")
+    dma("sync", C("RES", 5 * P, F * P), T.res[:, 5 * P:F * P], "res5", [("snt0", neng)])
 
     ms(S("ONE"), 1.0)
     iota(C("PI", 0), [[0, 1]], 0, 1)
     iota(S("NR", R_), [[1, NN]], -1)
     sel("L0", [[0, 2], [1, 64]], op=A.is_ge)
     sel("LE", [[0, 2], [-8, 8], [0, 8]], "L0", A.is_ge, cm=1)
-    iota(S("F8"), [[1, 8]], 0)
     sel("LT", [[0, 2], [1, 64]], "LE", A.is_gt)
-    sel("J", [[0, 2], [1, 128]])
+    sel("ID", [[1, 128]])
+    iota(S("F8"), [[1, 8]], 0)
     sel("EA", [[0, 2], [1, 8], [0, 8]])
     sel("E8", [[1, 8], [0, 16]])
-    send(C("W", 8 * P, 9 * P), C("W", 6 * P, 7 * P), 0)
     ms(S("ZR"), 0.0)
+    sel("IK", [[1, 128]], "ZR", A.not_equal, 1024.0)
+    send(C("W", 8 * P, 9 * P), C("W", 6 * P, 7 * P), 0)
     sel("N15", [[1, 128]], "ZR", A.not_equal, -1.5)
     iota(S("BI", 0), [[1, 16], [0, 2]], 0)
     iota(S("BI", 1), [[0, 16], [16, 2]], 0, 1)
     iota(S("F48"), [[1, 8], [0, 6]], 0)
     sel("I32", [[1, 128]], "ZR", A.not_equal, 32.0)
     iota(S("CL"), [[0, 8], [16, 6]], 0, 1)
-    for name in ("JH", "JM"):
-        sel(name, [[0, 2], [1, 128]], "ZR", A.not_equal, 0.5 if name == "JH" else -0.5)
+    for name, v in (("J", 1.0), ("JH", 0.5), ("JM", -0.5)):
+        sel(name, [[0, 2], [1, 128]], "ZR", A.not_equal, v)
     ts(C("PI", 1), C("PI", 0), 7, A.bitwise_and)
     ts(C("PI", 2), C("PI", 0), 6, A.arith_shift_right)
     ts(C("PI", 3), C("PI", 0), 112, A.bitwise_and)
@@ -185,13 +189,12 @@ def build(T, nxt):
     ms(C("MR", 0, WIDE), BIG)
     ms(C("MQ", 0, WIDE), -0.25)
     ms(C("CS", 8, 16), 0.0)
-    ms(C("LB", 64, 128), 0.0)
     act(S("NR", D_), S("NR", R_), scale=-1.0, bias=23.0)
     act(col(F0), col(FP), AF.Relu, scale=-1.0, bias=1.0)
     for k, sc, bi in ((NH, -1.0, 1.0), (KA, 6.0, 1.0), (W16, -16.0, 16.0), (CN, 0.5, -0.5), (CH, 0.5, 0.0), (CQ, -0.5, 0.5)):
         act(col(k), col(HALF), scale=sc, bias=bi)
-    act(S("WK"), C("F8", 0, 4), AF.Exp, scale=7 * math.log(2), bias=9 * math.log(2))
-    ID = C("J", 0, 128)
+    act(S("WK"), C("NR", NN + 1, NN + 5), AF.Exp, scale=7 * math.log(2), bias=9 * math.log(2))
+    ID = S("ID")
 
     CS_ = C("PM", 0)
     ND = C("XX", 0, 256)
@@ -212,12 +215,14 @@ def build(T, nxt):
     mms((TT, S("LT"), S("OM")), (TT, S("LT"), S("OR")))
     top = slice(0, NN)
     mm(C("PB", 0, 128, parts=top), S("OR", D_), S("LT"), True, True)
-    mm(C("PB", 128, 256, parts=top), S("OM", D_), ID, True, True)
+    mm(C("PN", 128, 256, parts=top), S("OM", D_), ID, True, True)
     mm(C("PU", 128, 128 + NN), S("LE"), S("OR", R_), True, True)
-    ts(S("E0"), S("NR"), C("CF", 0), A.add, CS_, A.is_equal)
+    NE = lambda k: C("NE", N2 * k, N2 * k + N2)
+    ts(S("E0"), S("NR"), C("CF", 0), A.add, CS_, A.not_equal)
     tt(LTG, GM, LTC, A.min)
-    ts(S("EM", 0), S("NR"), C("CF", 1), A.add, CS_, A.is_equal)
-    act(S("TR"), C("PB", 0, 256, parts=top))
+    ts(NE(0), S("NR"), C("CF", 1), A.add, CS_, A.not_equal)
+    act(C("TR", 0, 128), C("PB", 0, 128, parts=top))
+    cp(C("TR", 128, 256), C("PN", 128, 256, parts=top))
     mm(C("PU", 0, 128), C("TR", 128, 256), C("TR", 0, 128), True, True)
     tt(UP, C("PA", 0, NN), LTG, A.is_lt)
     tt(S("X", 0, slice(0, N2)), TT, S("OM"), A.is_lt)
@@ -250,76 +255,87 @@ def build(T, nxt):
         return [lambda n=n, i=i: tt(S("NV", fs, i, al, n), S(("VY", "VX")[n], fs, i), nd, A.mult) for n in (0, 1) for i in (0, 1)]
 
     v01 = vec(0, 2)
+    SV = S("SV")
     fill = [
         [lambda: ts(ND, S("IA"), 8.0, A.is_le)],
         [lambda: tt(S("IDX", 0), S("IA"), ND, A.mult)],
         [lambda: tt(S("IDX", 1), S("IB"), ND, A.mult)],
-        [lambda: scan(SU, U, C("ZR", 0, NN), 0.0), lambda: tt(OS, S("OM", D_), S("OR", D_), A.add),
-         lambda: ts(S("EQC"), S("NR"), CS_, A.is_equal), lambda: tt(OS, U, OS, A.is_gt)],
-        [lambda: ts(S("FX", 0), S("IDX", 1), 0.0, A.is_equal), lambda: ts(OS, OS, -99.0, A.mult),
-         lambda: ts(S("FX", 1), S("IDX", 1), 1.0, A.is_equal, -1.0, A.mult), lambda: tt(SV, SU, OS, A.add)],
-        [lambda: tt(S("EM", 1), S("E0"), S("EM", 0), A.is_gt), lambda: ts(S("GEN", D_), S("NR", D_), CS_, A.is_ge),
-         lambda: ts(S("GEN", R_), C("PU", 128, 128 + NN), 0.0, A.is_equal), lambda: tt(S("EM", 2), S("EM", 1), S("EM", 0), A.is_equal)],
+        [lambda: tt(OS, S("OM", D_), S("OR", D_), A.add), lambda: tt(NE(1), S("E0"), NE(0), A.is_ge), lambda: scan(SU, U, C("ZR", 0, NN), 0.0),
+         lambda: tt(OS, U, OS, A.is_gt)],
+        [lambda: tt(NE(2), NE(1), NE(0), A.not_equal), lambda: ts(OS, OS, -99.0, A.mult), lambda: ts(S("EQC"), S("NR"), CS_, A.is_equal),
+         lambda: tt(SV, SU, OS, A.add)],
+        [lambda: ts(S("GEN", D_), S("NR", D_), CS_, A.is_ge), lambda: ts(S("GEN", R_), C("PU", 128, 128 + NN), 0.0, A.is_equal),
+         lambda: ts(S("FX", 0), S("IDX", 1), 0.0, A.is_equal), lambda: ts(S("FX", 1), S("IDX", 1), 1.0, A.is_equal, -1.0, A.mult)],
     ]
     LAM = C("PN", N2)
+    YS = lambda k, h: C("XY", 256 + N2 * k + NN * h, 256 + N2 * k + NN * h + NN)
+    YA = C("XY", 256, 256 + 3 * N2)
     for t in range(6):
         mm(C("PN", 0, N2 + 1), S("M"), S("X", t % 2, XW), True, True)
+        if t == 5:
+            for k in range(3):
+                mm(YS(k, 1), S("MN"), S("X", 1, R_), False, k == 2)
         for x in fill[t]:
             x()
-        if t == 1:
+        if t == 0:
             mm(C("PW", 0, 128), S("EA"), S("EA"), True, True)
             mm(C("PW", 128, 256), S("EA"), S("E8"), True, True)
             act(S("LA"), C("PW", 0, 128), scale=col(W16))
             act(S("LS"), C("PW", 0, 128), scale=col(WS))
-            act(C("LB", 0, 64), C("PW", 0, 64), scale=col(W16))
+            act(S("MN"), S("M"), scale=-256.0)
+        if t == 1:
+            mm(YA, ID, C("ZR", 0, 3 * N2), True, False)
+            for k in range(3):
+                mm(YS(k, 1), ID, S("Z", R_), False, False)
         if t == 2:
+            for k in range(3):
+                mm(YS(k, 1), S("IK"), S("OR", R_), False, False)
             act(S("H1"), S("IDX"), AF.Sign, bias=-2.5)
             act(S("H2"), S("IDX"), AF.Sign, bias=-5.5)
             act(S("BO"), C("PW", 128, 256))
         if t == 3:
             mm(S("PA"), ID, S("IDX"), True, False)
         if t == 4:
-            for i in (0, 1):
-                mm(C("PA", 256, 512), ID, S("FX", i), False, False)
-        if t == 5:
-            ts(S("HH", D_), SV, LAM, A.add, -91.0, A.is_le)
-            tt(S("LM"), C("PN", 0, N2), S("OR"), A.is_gt)
-        ts(S("X", (t + 1) % 2, XW), S("Z", XW), LAM, A.add, -91.0, A.is_le)
-    act(S("BT", al, 0), S("BI", 0))
-    act(S("BT", al, 1), S("BI", 1), bias=col(NG))
-    DD = lambda a, n=N2: C("PB", 256 + a, 256 + a + n)
-    for k, x in enumerate(((DD(0, 2 * N2), ID, S("KC")), (DD(0), S("LS"), S("EQC")), (DD(N2), S("LS"), S("EQC")), (DD(0), S("LA"), S("GEN")), (DD(N2), S("LB"), S("GEN")))):
-        mm(*x, k == 0, False)
-    mm(S("PA"), S("N15"), S("H1"), False, False)
-    tt(S("HH", R_), S("X", 0, R_), S("LM", R_), A.add)
-    tt(S("LD"), S("X", 0, D_), S("LM", D_), A.add)
+            mm(YA, S("IK"), S("NE"), False, False)
+            for k in range(3):
+                mm(YS(k, 0), ID, SV, False, False)
+        if t < 5:
+            ts(S("X", (t + 1) % 2, XW), S("Z", XW), LAM, A.add, -91.0, A.is_le)
+    ts(S("Y"), C("XY", 256, 256 + 3 * N2), LAM, A.add, -91.0, A.is_le)
+    ts(S("HH", D_), SV, LAM, A.add, -91.0, A.is_le)
+    ts(S("HH", R_), S("Z", D_), LAM, A.add, -91.0, A.is_le)
+    scan(C("PU", 300, 300 + 156), S("Y"), C("ZR", 0, 156), 0.0)
+    tt(S("LD"), C("PN", 0, NN), S("OR", D_), A.is_gt)
     v01[0]()
-    for k in range(3):
-        tt(C("Y", N2 * k, N2 * k + N2), S("HH"), S("EM", k), A.mult)
-    for k, x in enumerate(((DD(0, NN), S("LA"), S("HH", D_)), (DD(N2, NN), S("LB"), S("HH", D_)), (DD(0, NN), S("LA"), S("LD")), (DD(N2, NN), S("LB"), S("LD")))):
-        mm(*x, False, k == 3)
-    mm(S("PA"), S("N15"), S("H2"), False, True)
-    for i in (0, 1):
-        act(S("BM", i), S("BT"), bias=-192.0)
-    act(S("DS"), DD(0, 2 * N2))
-    v01[1]()
-    scan(C("XY", 256, 256 + 156), S("Y"), C("ZR", 0, 156), 0.0)
-    v01[2]()
-    tt(S("PP"), C("Y", N2, 3 * N2), C("XY", 256 + N2, 256 + 156), A.mult)
-    v01[3]()
+    tt(S("PP"), C("Y", N2, 3 * N2), C("PU", 300 + N2, 300 + 156), A.mult)
+    weave(v01[1:])
+    DD, D2 = C("PB", 256, 256 + N2), C("PW", 384, 384 + N2)
+    mms((D2, ID, C("KC", N2, 2 * N2)), (D2, S("LS"), S("EQC")))
+    mm(S("PA"), S("N15"), S("H1"), False, False)
+    mms((DD, ID, C("KC", 0, N2)), (DD, S("LS"), S("EQC")), (DD, S("LA"), S("GEN")),
+        *[(C("PB", 256, 256 + NN), S("LA"), x) for x in (S("HH", D_), S("HH", R_), S("LD"))])
     RK = C("PM", 96, 96 + N2)
     mms((RK, ID, C("Y", 0, N2)), (RK, ID, C("PP", 0, N2)), (RK, ID, C("PP", N2, 2 * N2)))
-    for k, sc in enumerate((0.5, col(CN), col(CH), col(CQ), col(CN))):
-        ts(C("DA", 8 * k, 8 * k + 8), S("EF"), sc, A.mult)
+    for i in (0, 1):
+        mm(C("PA", 256, 512), ID, S("FX", i), False, False)
+    lo, hi = slice(0, 64), slice(64, 128)
+    act(S("BT", al, 0), S("BI", 0))
+    act(S("BT", al, 1), S("BI", 1), bias=col(NG))
+    act(C("DS", N2, 2 * N2, parts=hi), C("PW", 384, 384 + N2, parts=hi))
+    act(C("DS", 0, N2), DD)
+    act(C("DS", N2, 2 * N2, parts=lo), C("PB", 256, 256 + N2, parts=lo))
+    for i in (0, 1):
+        act(S("BM", i), S("BT"), bias=-192.0)
     act(C("CS", 0, 8), S("F8"), scale=4194304.0, bias=7.0 * 16513 * 512 + 4194304.0)
     act(C("CS", 16, 24), S("F8"), scale=4194304.0, bias=4194304.0)
     act(S("IDF"), ID)
-    for i in (0, 1):
-        act(S("POW", al, i), C("PA", 256 * i, 256 * i + 256), AF.Exp, scale=-7 * math.log(2), bias=21 * math.log(2))
+    for k, sc in enumerate((0.5, col(CN), col(CH), col(CQ), col(CN))):
+        act(C("DA", 8 * k, 8 * k + 8), S("EF"), scale=sc)
 
-    def places(f):
+    def places(f, parts=(0, 1, 2)):
         pos = C("XY", 128 * (f % 2), 128 * (f % 2) + 128)
-        mms((pos, ID, S("NV", f)), (pos, ID, S("BM")), (pos, ID, S("H")))
+        for k in parts:
+            mm(pos, ID, (S("NV", f), S("BM"), S("H"))[k], k == 0, k == 2)
 
     def clamps(f):
         a = 128 * (f % 2)
@@ -331,23 +347,27 @@ def build(T, nxt):
         r, a = RW * PSLOT[f], 128 * (f % 2)
         tt(C("REC", r + 32, r + RW), C("XY", a, a + 64), S("BT"), A.subtract)
 
-    places(0)
     for k in range(6):
         ts(S("EW", k), RK, C("TG", k), A.is_equal, C("WK", k % 3), A.mult)
         o = C("PN", 64 + N2 * (k // 3), 64 + N2 * (k // 3) + N2)
         mm(o, ID, S("EW", k), k % 3 == 0, k % 3 == 2)
-    clamps(0)
+    ts(S("DL"), S("F48"), col(FP), A.is_equal, col(CH), A.mult)
+    mm(S("PA"), S("N15"), S("H2"), False, True)
+    for fs in (slice(0, 2), slice(2, 8)):
+        for i in (0, 1):
+            act(S("POW", fs, i), C("PA", 256 * i + 32 * fs.start, 256 * i + 32 * fs.stop), AF.Exp, scale=-7 * math.log(2), bias=21 * math.log(2))
     tt(S("EP"), C("PN", 64, 64 + 2 * N2), S("DS"), A.mult)
-    keep(0)
     red(C("SM", 4), C("EP", 0, N2))
     red(C("SM", 5), C("EP", N2, 2 * N2))
     TBP = lambda a, b=None: C("PU", 256 + a, None if b is None else 256 + b)
+    places(0)
     mm(TBP(0, 24), S("IDF"), S("CS"), True, False)
     ts(S("RA"), C("DA", 0, 24), C("SM", 4), A.mult)
     ts(S("RB"), C("DA", 24, 40), C("SM", 5), A.mult)
     mm(TBP(0, 24), S("BO"), S("RA"), False, False)
     mm(TBP(8, 24), S("BO"), S("RB"), False, True)
-    ts(S("DL"), S("F48"), col(FP), A.is_equal, col(CH), A.mult)
+    clamps(0)
+    keep(0)
     ts(S("RL"), S("DL"), C("SM", 5), A.mult, RW / 256.0, A.mult)
     act(S("CL"), S("CL"), bias=col(NG))
 
@@ -362,23 +382,23 @@ def build(T, nxt):
         act(S("U2", f), S("H2", al, f), scale=C("TB", 16 + f))
 
     def look_sum(f):
-        o = C("PW", 64 * f, 64 * f + 64)
+        o = C("PM", 64 * (f % 2), 64 * (f % 2) + 64)
         mms((o, S("IDF"), S("U1", f)), (o, S("IDF"), S("U2", f)))
 
     def entries(f):
         return [
-            lambda: tt(S("XI", f), C("PW", 64 * f, 64 * f + 64), S("POW", f), A.mult),
+            lambda: tt(S("XI", f), C("PM", 64 * (f % 2), 64 * (f % 2) + 64), S("POW", f), A.mult),
             lambda: ts(S("A0", f), S("XI", f, 0), 65024, A.bitwise_and),
-            lambda: ts(S("A0", f), S("A0", f), (16 * f - 1) * 65536.0, A.add),
         ]
 
     def record(f):
         r = RW * PSLOT[f]
         win = C("REC", RW * wbase(f), RW * (8 if f < 6 else 10))
         return [
-            lambda: (tt(S("G"), IND(win, C("LU", 6 * f, 6 * f + 6)), S("MK", f), A.mult),
-                     act(C("H", 0, 64), C("G", 32, RW), scale=0.5, bias=191.75),
+            lambda: tt(S("G"), IND(win, C("LU", 6 * f, 6 * f + 6)), S("MK", f), A.mult),
+            lambda: (act(C("H", 0, 64), C("G", 32, RW), scale=0.5, bias=191.75),
                      act(C("H", 64, 128), C("G", 32, RW), scale=-0.5, bias=191.75)),
+            lambda: act(C("G", 0, 32), C("G", 0, 32), bias=(1 - 16 * f) * 65536.0),
             lambda: tt(S("XI", f, 0), C("G", 0, 32), S("A0", f), A.max),
             lambda: (ts(C("REC", r, r + 32), S("XI", f, 0), 65024, A.bitwise_and),
                      ts(S("SS", f % 2), S("XI", f), 7680, A.bitwise_and)),
@@ -392,22 +412,23 @@ def build(T, nxt):
 
     pieces = list(zip(CUTS[:-1], CUTS[1:]))
 
+    NP = len(pieces)
+
     def bank(h):
-        name, at = (("PA", 0), ("PB", 0), ("PU", 0), ("PN", 320))[h]
-        return C(name, at, at + pieces[h][1] - pieces[h][0])
+        return C(("PA", "PB", "PU", "PN", "PW")[h], 0, pieces[h][1] - pieces[h][0])
 
     row1 = S("ONE", slice(0, 128), parts=slice(0, 1))
 
     def pixels_start(f):
         s = 16 * ((f + 1) % 8)
-        for h in (0, 1, 3, 2):
+        for h in (list(range(2, NP)) + [0, 1] if f else [0, 1, 3, 2, 4][:NP]):
             a, b = pieces[h]
             mm(bank(h), C("J", s, s + 128), C("RES", f * P + a, f * P + b), True, False)
             mm(bank(h), row1, C("MQ", 0, b - a), False, False)
-            if f == F - 1:
+            if f == F - 1 and h == NP - 1:
                 mm(bank(h), row1, C("M128", 0, b - a), False, False)
 
-    def pixels_front(f):
+    def pixels_front(f, gap):
         s = 16 * ((f + 1) % 8)
         win = C("W", P * wbase(f), P * (9 + f))
         aw = [("arr%d" % f, narr * (len(SENDS) if f else 1))]
@@ -415,106 +436,105 @@ def build(T, nxt):
         for a, b in pieces:
             act(C("GP", a, b), IND(win, C("OFF", 64 * f + a // 16, 64 * f + b // 16)), AF.Relu, scale=-1.0, bias=255.0, waits=aw)
             ts(C("GQ", a, b), IND(win, C("OFF", 64 * f + 32 + a // 16, 64 * f + 32 + b // 16)), 255.0, A.min, waits=aw)
+        whole = lambda h: last and h == NP - 1
         for h, (a, b) in enumerate(pieces):
             mm(bank(h), C("JH", s, s + 128), C("GQ", a, b), False, False)
             mm(bank(h), C("JM", s, s + 128), C("GP", a, b), False, False)
-            mm(bank(h), row1, C("MR", 0, b - a), False, not last)
-            if last:
+            mm(bank(h), row1, C("MR", 0, b - a), False, not whole(h))
+            if whole(h):
                 mm(bank(h), row1, C("MZ", 0, b - a), False, True)
         sent = 0
         for h, (a, b) in enumerate(pieces):
             out = C("SND", f * P + a, f * P + b)
-            if last:
+            if h == GAP:
+                gap()
+            if whole(h):
                 ts(out, bank(h), 0.0, A.max, 255.0, A.min)
-                if h % 2:
-                    a = pieces[h - 1][0]
-                    dma("sync" if h == 1 else "scalar", T.y[:, f * P + a:f * P + b], C("SND", f * P + a, f * P + b), "out%d" % (f + h // 2))
-                continue
-            if h % 2:
+            elif (LASTFIN if last else FIN)[h] == "s":
                 act(out, bank(h), AF.Relu, bias=128.0 - BIG)
             else:
                 ts(out, bank(h), 128.0 - BIG, A.add, 0.0, A.max)
-            if h in SENDS:
+            if h in SENDS and last:
+                top = C("SND", f * P + sent, f * P + (a if whole(h) else b))
+                ts(top, top, 255.0, A.min)
+                dma("scalar" if sent else "sync", T.y[:, f * P + sent:f * P + b], C("SND", f * P + sent, f * P + b), "out%d" % (f + (sent > 0)))
+                sent = b
+            elif h in SENDS:
                 send(C("W", (9 + f) * P + sent, (9 + f) * P + b), C("SND", f * P + sent, f * P + b), f + 1)
                 sent = b
 
-    def turn_back(f):
+    halves = ((0, CUTS[SENDS[0] + 1], "PA"), (CUTS[SENDS[0] + 1], P, "PB"))
+
+    def turn_back(f, k):
         s = 128 - 16 * (f + 1)
-        mm(S("PU"), C("J", s, s + 128), C("SND", f * P, f * P + P), True, True)
+        a, b, name = halves[k]
+        mm(C(name, WIDE, WIDE + b - a), C("J", s, s + 128), C("SND", f * P + a, f * P + b), True, True)
 
     def copy_back(f):
-        own = C("W", PSLOT[f] * P, PSLOT[f] * P + P)
-        act(own, S("PU"))
-        if f < 5:
-            k = f + 3
-            add("sync", lambda e: e.dma_start(T.RES[:, k * P:k * P + P], T.res[:, k * P:k * P + P]),
-                [C("RES", k * P, k * P + P)], [own], (), "res%d" % k)
+        for a, b, name in halves:
+            act(C("W", PSLOT[f] * P + a, PSLOT[f] * P + b), C(name, WIDE, WIDE + b - a))
 
     def store(f):
         ts(C("YO", f * P, f * P + P), C("W", PSLOT[f] * P, PSLOT[f] * P + P), 255.0, A.min)
-        dma("sync", T.y[:, f * P:f * P + P], C("YO", f * P, f * P + P), "out%d" % f, [("snt%d" % (f + 1), neng * len(SENDS))])
+        dma("sync", T.y[:, f * P:f * P + P], C("YO", f * P, f * P + P), "out%d" % f, [("snt%d" % k, neng * len(SENDS)) for k in range(f + 1, min(f + 3, F))])
 
-    dma("sync", C("RES", 2 * P, 3 * P), T.res[:, 2 * P:3 * P], "res2", [("snt0", neng)])
     r0 = RW * PSLOT[0]
-    ts(S("U2", 0), S("H2", al, 0), TBP(16), A.mult)
+    masks(1, 3)
+    ts(C("PW", 384, 448), S("H2", al, 0), TBP(16), A.mult)
     ts(S("U1", 0), S("H1", al, 0), TBP(8), A.mult, TBP(0), A.add)
     act(S("TB"), TBP(0, 24))
     mms((C("PM", 280, 328), S("IDF"), S("CL")), (C("PM", 280, 328), S("BO"), S("RL")))
-    tt(S("U1", 0), S("U1", 0), S("U2", 0), A.add)
+    tt(C("PW", 448, 512), S("U1", 0), C("PW", 384, 448), A.add)
     look(1)
     look(2)
-    masks(1, 3)
+    masks(3, 5)
     pixels_start(0)
-    look_sum(1)
-    tt(S("XI", 0), S("U1", 0), S("POW", 0), A.mult)
+    tt(S("XI", 0), C("PW", 448, 512), S("POW", 0), A.mult)
     cp(S("LU"), C("PM", 280, 328))
     ts(S("SS", 0), S("XI", 0), 7680, A.bitwise_and)
     ts(C("REC", r0, r0 + 32), S("XI", 0, 0), 65024, A.bitwise_and)
     weave(offsets(0))
     for f in range(F):
-        pixels_front(f)
+        g = f + 1
+        nop = lambda: None
         if f == F - 1:
+            pixels_front(f, nop)
             break
-        turn_back(f)
+        r = record(g)
+        e = entries(g + 1) if g + 1 < F else [nop] * 2
+        v = vec(2 * f + 2, 2 * f + 4) if f < 3 else [nop] * 4
+        pixels_front(f, r[0])
+        r[1]()
+        r[2]()
         if f == 0:
-            r1 = record(1)
-            e1 = entries(1)
-            weave(r1[:1], e1[:1])
-            copy_back(f)
-            places(1)
+            look_sum(1)
+        places(g, (0, 1))
+        turn_back(f, 0)
+        places(g, (2,))
+        turn_back(f, 1)
+        copy_back(f)
+        if f == 0:
+            weave(entries(1), v[:1])
             look_sum(2)
-            weave(e1[1:] + r1[1:], vec(2, 4))
-            clamps(1)
-            keep(1)
-            weave(entries(2))
-        g = f + 2
-        if g < F:
-            r = record(g)
-            weave(r[:1], offsets(f + 1)[:1])
-            if f:
-                copy_back(f)
-            places(g)
-            pixels_start(f + 1)
-            weave((entries(g) if f else []) + r[1:], offsets(f + 1)[1:], vec(2 * f + 2, 2 * f + 4) if f in (1, 2) else [])
-            keep(g)
-            clamps(g)
-            if f:
-                store(f - 1)
-            if g + 1 < F:
-                look(g + 1)
-                look_sum(g + 1)
-            if f == 0:
-                masks(3, 5)
-            if f == 1:
-                masks(5, 8)
-            if f == 2:
-                for name, v in (("MZ", -BIG), ("M128", 128.0)):
-                    act(C(name, 0, WIDE), S("ONE", slice(0, WIDE), parts=slice(0, 1)), scale=v)
         else:
-            copy_back(f)
-            pixels_start(f + 1)
-            weave(offsets(f + 1))
+            weave(e, v[:1])
             store(f - 1)
+        r[3]()
+        clamps(g)
+        r[4]()
+        pixels_start(g)
+        keep(g)
+        v[1]()
+        weave(offsets(g), v[2:], e if f == 0 else [])
+        if f + 3 < F:
+            look(f + 3)
+            look_sum(f + 3)
+        if f == 3:
+            masks(5, 8)
+        if f == 4:
+            for name, v in (("MZ", -BIG), ("M128", 128.0)):
+                act(C(name, 0, WIDE), S("ONE", slice(0, WIDE), parts=slice(0, 1)), scale=v)
+        if f == F - 2:
             store(f)
     return ops, neng, narr
 

@@ -5,7 +5,8 @@ from concourse.mybir import AluOpType as A, AxisListType, ActivationFunctionType
 F = 8
 P = 512
 CUTS = [0, 128, 288, 448, 512]
-FIN, LASTFIN, GAP = "vsvs", "vssv", 2
+FIN, LASTFIN, GAP = "vsvs", "vvvv", 2
+STORES = (1, 3)
 SENDS = (1, 3)
 BIG = 12582912.0
 NN = 26
@@ -20,9 +21,9 @@ SB_ = {
     "CT": ([128, 8], i32), "EB": ([128, 8], bf), "CA": ([128, 4], f32), "CF": ([128, 4], f32),
     "ONE": ([128, 256], bf), "MR": ([1, 256], bf), "MZ": ([1, 256], bf), "MQ": ([1, 256], bf), "M128": ([1, 256], bf),
     "ID": ([128, 128], bf), "IK": ([128, 128], bf), "MN": ([128, 128], bf), "NE": ([128, 3 * N2], bf), "J": ([128, 256], bf), "JH": ([128, 256], bf), "JM": ([128, 256], bf), "N15": ([128, 128], bf), "I32": ([128, 128], bf),
-    "E8": ([8, 128], bf), "EA": ([8, 128], bf), "BO": ([128, 128], f32), "IDF": ([128, 128], f32),
+    "E8": ([128, 128], bf), "EA": ([128, 128], bf), "BO": ([128, 128], f32), "IDF": ([128, 128], f32),
     "L0": ([128, 128], bf), "LE": ([128, 128], bf), "LT": ([128, 128], bf), "M": ([128, 128], bf), "TR": ([NN, 256], bf),
-    "LA": ([128, 128], bf), "LS": ([128, 128], bf),
+    "LA": ([128, 128], bf),
     "PI": ([128, 8], i32), "PC": ([128, 24], f32), "F8": ([128, 8], f32), "F48": ([128, 48], f32), "EF": ([128, 8], f32), "TG": ([128, 6], bf),
     "NR": ([128, N2], bf), "OM": ([128, N2], bf), "OR": ([128, N2], bf), "E0": ([128, N2], bf), "EQC": ([128, N2], bf),
     "GEN": ([128, N2], bf), "TA": ([128, 8, NN], f32), "X": ([128, 2, 56], bf), "Z": ([128, 56], bf), "SV": ([128, NN], bf),
@@ -35,12 +36,13 @@ SB_ = {
     "NV": ([128, 8, 2, 32, 2], bf), "BI": ([128, 2, 32], f32), "BT": ([128, 32, 2], bf), "BM": ([128, 2, 64], bf),
     "MK": ([128, 8, RW], bf), "U1": ([128, 8, 64], f32), "U2": ([128, 8, 64], f32), "XI": ([128, 8, 2, 32], i32), "A0": ([128, 8, 32], i32),
     "SS": ([128, 2, 64], i32), "REC": ([128, 11 * RW], i32), "G": ([128, RW], f32), "H": ([128, 128], bf), "CC": ([128, 128], bf),
+    "RF": ([1, 128], f32), "C0": ([1, 4], f32), "HF": ([1, 4], bf), "BB": ([128, 128], bf), "W4": ([128, 4], bf), "P0": ([128, 64], bf), "X0": ([128, 64], i32),
     "S2": ([128, 64], i32), "OFF": ([128, F * 64], u16),
 }
 PS_ = ["PA", "PB", "PU", "XY", "XX", "PM", "PN", "PW"]
 SCRATCH = {k: ("sbuf", v[0], v[1]) for k, v in SB_.items()}
 SCRATCH.update({k: ("psum", [128, P], f32) for k in PS_})
-DMAS = ["ctl", "pic", "pi0", "ia_", "ib_", "vy_", "vx_", "res0", "res2", "res5"] + ["out%d" % f for f in range(F + 3)]
+DMAS = ["ctl", "pic", "pi0", "ia_", "ib_", "vy_", "vx_", "res0", "res1", "res3", "vy2", "vx2"] + ["out%d" % f for f in range(F + 3)]
 SEMAPHORES = ["dve", "act", "pe", "pool"] + DMAS + ["arr%d" % f for f in range(F)] + ["snt%d" % f for f in range(F)]
 
 PSLOT = [4, 3, 2, 1, 0, 9, 8, 10]
@@ -126,8 +128,8 @@ def build(T, nxt):
     def dma(q, o, i, sem, waits=()):
         add(q, lambda e: e.dma_start(val(o), val(i)), [o] if isinstance(o, tuple) else [], [i], waits, sem)
 
-    def send(o, i, k):
-        add("pool", lambda e: e.remote_dma(o[0], i[0], T.sem["arr%d" % k], T.sem["snt%d" % k], nxt[1], nxt[0], nxt[2]),
+    def send(o, i, k, mask=nxt[2]):
+        add("pool", lambda e: e.remote_dma(o[0], i[0], T.sem["arr%d" % k], T.sem["snt%d" % k], nxt[1], nxt[0], mask),
             [], [i], (), "remote")
 
     def weave(*chains):
@@ -140,7 +142,7 @@ def build(T, nxt):
     neng = bin(nxt[2]).count("1")
     narr = nxt[3]
     col = lambda k: C("PC", k)
-    FP, HALF, G16, F0, NG, NH, KA, W16, H5, CN, CH, CQ, KCB, WS, T0, T1, T2, T3 = range(18)
+    FP, HALF, G16, GR, NG, F0, KA, W16, H5, CN, CH, CQ, KCB, WS, T0, T1, T2, T3, B0 = range(19)
     D_, R_ = slice(0, NN), slice(NN, N2)
 
     for h, q in enumerate(("sync", "scalar")):
@@ -148,52 +150,66 @@ def build(T, nxt):
         dma(q, C("CT", 0, parts=pp), T.gaps[:], "ctl")
         dma(q, C("CT", 1, parts=pp), T.cmd[:], "ctl")
         dma(q, C("CT", 2, 5, parts=pp), T.rel[:], "ctl")
-    dma("sync", S("IA"), T.ia[:], "ia_")
-    dma("scalar", S("IB"), T.ib[:], "ib_")
     dma("sync", C("W", 6 * P, 7 * P), T.pic0[:, P:2 * P], "pic")
-    dma("sync", S("VY"), T.vy[:], "vy_")
-    dma("sync", S("VX"), T.vx[:], "vx_")
+    dma("scalar", S("IA"), T.ia[:], "ia_")
+    dma("sync", S("IB"), T.ib[:], "ib_")
+    dma("sync", S("VY", slice(0, 2)), T.vy[:, 0:128], "vy_")
+    dma("sync", S("VX", slice(0, 2)), T.vx[:, 0:128], "vx_")
     dma("sync", C("W", 5 * P, 6 * P), T.pic0[:, 0:P], "pi0")
-    dma("sync", C("RES", 0, 2 * P), T.res[:, 0:2 * P], "res0")
-    dma("sync", C("RES", 2 * P, 5 * P), T.res[:, 2 * P:5 * P], "res2")
-    dma("sync", C("RES", 5 * P, F * P), T.res[:, 5 * P:F * P], "res5", [("snt0", neng)])
+    dma("sync", C("RES", 0, P), T.res[:, 0:P], "res0")
+    dma("sync", S("VY", slice(2, 8)), T.vy[:, 128:512], "vy2")
+    dma("sync", S("VX", slice(2, 8)), T.vx[:, 128:512], "vx2")
+    dma("sync", C("RES", P, 3 * P), T.res[:, P:3 * P], "res1")
+    dma("sync", C("RES", 3 * P, F * P), T.res[:, 3 * P:F * P], "res3", [("snt0", neng)])
 
     ms(S("ONE"), 1.0)
     iota(C("PI", 0), [[0, 1]], 0, 1)
     iota(S("NR", R_), [[1, NN]], -1)
     sel("L0", [[0, 2], [1, 64]], op=A.is_ge)
+    iota(S("F8"), [[1, 8]], 0)
     sel("LE", [[0, 2], [-8, 8], [0, 8]], "L0", A.is_ge, cm=1)
     sel("LT", [[0, 2], [1, 64]], "LE", A.is_gt)
     sel("ID", [[1, 128]])
-    iota(S("F8"), [[1, 8]], 0)
-    sel("EA", [[0, 2], [1, 8], [0, 8]])
-    sel("E8", [[1, 8], [0, 16]])
     ms(S("ZR"), 0.0)
-    sel("IK", [[1, 128]], "ZR", A.not_equal, 1024.0)
-    send(C("W", 8 * P, 9 * P), C("W", 6 * P, 7 * P), 0)
-    sel("N15", [[1, 128]], "ZR", A.not_equal, -1.5)
+    iota(S("EA"), [[0, 2], [1, 8], [0, 8]], 0)
+    for k in (0, 1):
+        a, b = k * P // 2, (k + 1) * P // 2
+        send(C("W", 8 * P + a, 8 * P + b), C("W", 6 * P + a, 6 * P + b), 0, nxt[4][k])
     iota(S("BI", 0), [[1, 16], [0, 2]], 0)
     iota(S("BI", 1), [[0, 16], [16, 2]], 0, 1)
+    iota(S("E8"), [[1, 8], [0, 16]], 0)
     iota(S("F48"), [[1, 8], [0, 6]], 0)
-    sel("I32", [[1, 128]], "ZR", A.not_equal, 32.0)
     iota(S("CL"), [[0, 8], [16, 6]], 0, 1)
-    for name, v in (("J", 1.0), ("JH", 0.5), ("JM", -0.5)):
+    for name, v in (("JH", 0.5), ("JM", -0.5)):
         sel(name, [[0, 2], [1, 128]], "ZR", A.not_equal, v)
+    iota(C("REC", 5 * RW, 9 * RW), [[0, 4 * RW]], 0)
     ts(C("PI", 1), C("PI", 0), 7, A.bitwise_and)
     ts(C("PI", 2), C("PI", 0), 6, A.arith_shift_right)
     ts(C("PI", 3), C("PI", 0), 112, A.bitwise_and)
-    ms(S("H"), 192.0)
-    cp(C("PC", 0, 3), C("PI", 1, 4))
-    ms(C("REC", 5 * RW, 9 * RW), 0)
-    ms(C("W", 7 * P, 8 * P), 128.0)
-    ms(C("MR", 0, WIDE), BIG)
-    ms(C("MQ", 0, WIDE), -0.25)
+    ts(C("PI", 4), C("PI", 0), 3, A.arith_shift_right, 7, A.bitwise_and)
     ms(C("CS", 8, 16), 0.0)
+    cp(C("PC", 0, 4), C("PI", 1, 5))
     act(S("NR", D_), S("NR", R_), scale=-1.0, bias=23.0)
     act(col(F0), col(FP), AF.Relu, scale=-1.0, bias=1.0)
-    for k, sc, bi in ((NH, -1.0, 1.0), (KA, 6.0, 1.0), (W16, -16.0, 16.0), (CN, 0.5, -0.5), (CH, 0.5, 0.0), (CQ, -0.5, 0.5)):
+    for k, sc, bi in ((CN, 0.5, -0.5), (CH, 0.5, 0.0), (CQ, -0.5, 0.5), (W16, -16.0, 16.0)):
         act(col(k), col(HALF), scale=sc, bias=bi)
+    act(col(NG), col(G16), scale=-1.0)
     act(S("WK"), C("NR", NN + 1, NN + 5), AF.Exp, scale=7 * math.log(2), bias=9 * math.log(2))
+    act(C("MR", 0, WIDE), C("ONE", 0, WIDE, parts=slice(0, 1)), scale=BIG)
+    ts(col(T0), col(FP), 5.0, A.min, 18.0, A.add)
+    ts(col(T1), col(FP), 5.0, A.is_ge, 10.0, A.mult)
+    ts(col(KA), col(HALF), 6.0, A.mult, 1.0, A.add)
+    ts(col(KCB), col(T0), col(HALF), A.mult, -16.0, A.add)
+    ts(col(T1), col(T1), col(FP), A.subtract, -3.0, A.add)
+    ts(col(B0), col(F0), col(HALF), A.is_gt, 8192.0, A.mult)
+    ts(S("EF"), S("F8"), col(FP), A.is_equal)
+    ts(S("TG"), C("F8", 0, 6), col(KA), A.add)
+    ts(col(WS), col(T1), 1.0 / 16, A.mult)
+    ts(col(B0), col(B0), -8192.0 - 1025 * math.log(4), A.add)
+    ts(C("TG", 3), col(HALF), -2.0, A.mult, 4.0, A.add)
+    ts(C("CS", 0, 8), S("F8"), 4194304.0, A.mult, 7.0 * 16513 * 512 + 4194304.0, A.add)
+    ts(C("CS", 16, 24), S("F8"), 4194304.0, A.mult, 4194304.0, A.add)
+    ms(S("H"), 192.0)
     ID = S("ID")
 
     CS_ = C("PM", 0)
@@ -219,8 +235,11 @@ def build(T, nxt):
     mm(C("PU", 128, 128 + NN), S("LE"), S("OR", R_), True, True)
     NE = lambda k: C("NE", N2 * k, N2 * k + N2)
     ts(S("E0"), S("NR"), C("CF", 0), A.add, CS_, A.not_equal)
+    eye = lambda name, v, a=0: ts(C(name, a, a + 128), ID, v, A.mult)
+    eye("IK", 1024.0)
     tt(LTG, GM, LTC, A.min)
     ts(NE(0), S("NR"), C("CF", 1), A.add, CS_, A.not_equal)
+    eye("N15", -1.5)
     act(C("TR", 0, 128), C("PB", 0, 128, parts=top))
     cp(C("TR", 128, 256), C("PN", 128, 256, parts=top))
     mm(C("PU", 0, 128), C("TR", 128, 256), C("TR", 0, 128), True, True)
@@ -233,21 +252,23 @@ def build(T, nxt):
     XW = slice(0, N2 + 1)
     ts(S("Z", XW), S("X", 0, XW), -99.0, A.mult, C("SM", 0), A.add)
 
-    act(col(T0), col(FP), AF.Relu, scale=-1.0, bias=5.0)
-    act(col(T1), col(FP), AF.Sign, bias=-4.5)
+    one = lambda a, b: C("ONE", a, b, parts=slice(0, 1))
+    act(S("RF"), one(0, 128))
+    act(C("MQ", 0, WIDE), one(0, WIDE), scale=-0.25)
+    act(C("C0", 0), one(0, 1), scale=-(2.0 * (4 ** 8 - 1) / 3 + 3.0 * 4 ** 8))
+    act(S("HF"), C("NR", NN, NN + 4, parts=slice(0, 1)), AF.Abs, bias=-0.5)
     act(S("KT"), S("NR"), AF.Relu, scale=-1.0, bias=1.0)
-    act(col(T2), col(T0), scale=-1.0, bias=23.0)
-    act(col(T3), col(T1), scale=5.0, bias=2.0)
+    act(S("IDF"), ID)
+    act(S("I32"), ID, scale=32.0)
+    act(S("HF"), S("HF"), scale=-0.5, bias=0.75)
     act(C("KC", 0, N2), S("KT"), scale=-1.0, bias=-16.0)
-    act(col(KCB), col(T2), scale=col(HALF), bias=-16.0)
-    act(col(T0), col(FP), scale=-1.0, bias=col(T3))
-    act(S("EF"), S("F8"), AF.Abs, scale=-1.0, bias=col(FP))
     act(C("KC", N2, 2 * N2), S("KT"), scale=-1.0, bias=col(KCB))
-    act(col(WS), col(T0), scale=col(NH))
-    act(S("EF"), S("EF"), AF.Relu, scale=-1.0, bias=1.0)
-    act(S("TG"), C("F8", 0, 6), bias=col(KA))
-    act(col(NG), col(G16), scale=-1.0)
-    act(C("TG", 3), col(HALF), scale=-2.0, bias=4.0)
+
+    def masks(f0, f1):
+        fs, nd = slice(f0, f1), C("XX", 32 * f0, 32 * f1)
+        act(S("MK", fs, slice(0, 32)), nd, scale=-129.0, bias=129.0)
+        for k in (32, 33):
+            act(S("MK", fs, slice(k, RW, 2)), nd, scale=-1.0, bias=1.0)
 
     def vec(f0, f1):
         fs = slice(f0, f1)
@@ -262,14 +283,29 @@ def build(T, nxt):
         [lambda: tt(S("IDX", 1), S("IB"), ND, A.mult)],
         [lambda: tt(OS, S("OM", D_), S("OR", D_), A.add), lambda: tt(NE(1), S("E0"), NE(0), A.is_ge), lambda: scan(SU, U, C("ZR", 0, NN), 0.0),
          lambda: tt(OS, U, OS, A.is_gt)],
-        [lambda: tt(NE(2), NE(1), NE(0), A.not_equal), lambda: ts(OS, OS, -99.0, A.mult), lambda: ts(S("EQC"), S("NR"), CS_, A.is_equal),
+        [lambda: tt(NE(2), NE(1), NE(0), A.not_equal), lambda: ts(OS, OS, -99.0, A.mult), lambda: ts(S("EQC"), S("NR"), CS_, A.is_equal, col(WS), A.mult),
          lambda: tt(SV, SU, OS, A.add)],
         [lambda: ts(S("GEN", D_), S("NR", D_), CS_, A.is_ge), lambda: ts(S("GEN", R_), C("PU", 128, 128 + NN), 0.0, A.is_equal),
-         lambda: ts(S("FX", 0), S("IDX", 1), 0.0, A.is_equal), lambda: ts(S("FX", 1), S("IDX", 1), 1.0, A.is_equal, -1.0, A.mult)],
+         lambda: ts(S("LA"), S("EA"), col(GR), A.is_equal, col(W16), A.mult), lambda: eye("J", 1.0), lambda: eye("J", 1.0, 128)],
     ]
     LAM = C("PN", N2)
     YS = lambda k, h: C("XY", 256 + N2 * k + NN * h, 256 + N2 * k + NN * h + NN)
     YA = C("XY", 256, 256 + 3 * N2)
+    K0, R4, W0 = C("XX", 288, 320), C("PA", 320, 324), C("PU", 480)
+
+    def places_in_word(f0, f1, parts=(0, 1, 2, 3)):
+        fs, n = slice(f0, f1), 32 * (f1 - f0)
+        for k in parts:
+            for i in (0, 1):
+                l, x = ((ID, S("IDX", i, fs)), (ID, S("FX", i, slice(32 * f0, 32 * f1))), (S("N15"), S("H1", i, fs)), (S("N15"), S("H2", i, fs)))[k]
+                j = 1 if k == 1 else i
+                mm(C("PW", n * j, n * j + n), l, x, k == 0 and i == 0, k == 3 and i == 1)
+
+    def power(f0, f1):
+        for i in (0, 1):
+            n = 32 * (f1 - f0)
+            act(S("POW", slice(f0, f1), i), C("PW", n * i, n * i + n), AF.Exp, scale=-7 * math.log(2), bias=21 * math.log(2))
+
     for t in range(6):
         mm(C("PN", 0, N2 + 1), S("M"), S("X", t % 2, XW), True, True)
         if t == 5:
@@ -278,11 +314,12 @@ def build(T, nxt):
         for x in fill[t]:
             x()
         if t == 0:
-            mm(C("PW", 0, 128), S("EA"), S("EA"), True, True)
-            mm(C("PW", 128, 256), S("EA"), S("E8"), True, True)
-            act(S("LA"), C("PW", 0, 128), scale=col(W16))
-            act(S("LS"), C("PW", 0, 128), scale=col(WS))
             act(S("MN"), S("M"), scale=-256.0)
+            for a in (0, 256):
+                act(C("W", 7 * P + a, 7 * P + a + 256), S("ONE"), scale=128.0)
+            for k, sc in enumerate((0.5, col(CN), col(CH), col(CQ), col(CN))):
+                act(C("DA", 8 * k, 8 * k + 8), S("EF"), scale=sc)
+            mm(W0, S("RF"), C("C0", 0), True, False)
         if t == 1:
             mm(YA, ID, C("ZR", 0, 3 * N2), True, False)
             for k in range(3):
@@ -290,11 +327,16 @@ def build(T, nxt):
         if t == 2:
             for k in range(3):
                 mm(YS(k, 1), S("IK"), S("OR", R_), False, False)
+            masks(1, 8)
             act(S("H1"), S("IDX"), AF.Sign, bias=-2.5)
-            act(S("H2"), S("IDX"), AF.Sign, bias=-5.5)
-            act(S("BO"), C("PW", 128, 256))
+            act(S("BT", al, 0), S("BI", 0))
+            act(S("BT", al, 1), S("BI", 1), bias=col(NG))
+            act(C("P0", 0, 32), S("IDX", 0, 0), AF.Exp, scale=-math.log(4), bias=9 * math.log(2))
+            for i in (0, 1):
+                act(S("BM", i), S("BT"), bias=-192.0)
+            act(S("H2", al, slice(0, 2)), S("IDX", al, slice(0, 2)), AF.Sign, bias=-5.5)
         if t == 3:
-            mm(S("PA"), ID, S("IDX"), True, False)
+            places_in_word(0, 2, (0,))
         if t == 4:
             mm(YA, S("IK"), S("NE"), False, False)
             for k in range(3):
@@ -309,73 +351,45 @@ def build(T, nxt):
     v01[0]()
     tt(S("PP"), C("Y", N2, 3 * N2), C("PU", 300 + N2, 300 + 156), A.mult)
     weave(v01[1:])
-    DD, D2 = C("PB", 256, 256 + N2), C("PW", 384, 384 + N2)
-    mms((D2, ID, C("KC", N2, 2 * N2)), (D2, S("LS"), S("EQC")))
-    mm(S("PA"), S("N15"), S("H1"), False, False)
-    mms((DD, ID, C("KC", 0, N2)), (DD, S("LS"), S("EQC")), (DD, S("LA"), S("GEN")),
+    ts(S("FX", 0), S("IDX", 1), 0.0, A.is_equal)
+    ts(S("FX", 1), S("IDX", 1), 1.0, A.is_equal, -1.0, A.mult)
+    ts(S("BB"), S("E8"), col(GR), A.is_equal)
+    row1 = S("ONE", slice(0, 128), parts=slice(0, 1))
+    DD, D2 = C("PB", 256, 256 + N2), C("PB", 320, 320 + N2)
+    mms((D2, ID, C("KC", N2, 2 * N2)), (D2, S("LA"), S("EQC")))
+    four = lambda name, k: C(name, N2 * k + NN - 2, N2 * k + NN + 2)
+    mm(R4, row1, S("HF"), True, False)
+    for l, k in ((ID, 0), (S("IK"), 0), (S("IK"), 1), (S("IK"), 2)):
+        mm(R4, l, four("Y", k), False, False)
+    mms((DD, ID, C("KC", 0, N2)), (DD, S("LA"), S("EQC")), (DD, S("LA"), S("GEN")),
         *[(C("PB", 256, 256 + NN), S("LA"), x) for x in (S("HH", D_), S("HH", R_), S("LD"))])
+    for k in (0, 1):
+        mm(R4, ID, four("PP", k), False, k == 1)
     RK = C("PM", 96, 96 + N2)
     mms((RK, ID, C("Y", 0, N2)), (RK, ID, C("PP", 0, N2)), (RK, ID, C("PP", N2, 2 * N2)))
-    for i in (0, 1):
-        mm(C("PA", 256, 512), ID, S("FX", i), False, False)
+    mms((K0, ID, S("IDX", 1, 0)), *[(K0, ID, S("FX", i, slice(0, 32))) for i in (0, 1)])
     lo, hi = slice(0, 64), slice(64, 128)
-    act(S("BT", al, 0), S("BI", 0))
-    act(S("BT", al, 1), S("BI", 1), bias=col(NG))
-    act(C("DS", N2, 2 * N2, parts=hi), C("PW", 384, 384 + N2, parts=hi))
+    act(S("W4"), R4, AF.Exp, scale=math.log(4), bias=col(B0))
+    act(C("DS", N2, 2 * N2, parts=hi), C("PB", 320, 320 + N2, parts=hi))
+    act(C("P0", 32, 64), K0, AF.Exp, scale=-math.log(4), bias=9 * math.log(2))
     act(C("DS", 0, N2), DD)
     act(C("DS", N2, 2 * N2, parts=lo), C("PB", 256, 256 + N2, parts=lo))
-    for i in (0, 1):
-        act(S("BM", i), S("BT"), bias=-192.0)
-    act(C("CS", 0, 8), S("F8"), scale=4194304.0, bias=7.0 * 16513 * 512 + 4194304.0)
-    act(C("CS", 16, 24), S("F8"), scale=4194304.0, bias=4194304.0)
-    act(S("IDF"), ID)
-    for k, sc in enumerate((0.5, col(CN), col(CH), col(CQ), col(CN))):
-        act(C("DA", 8 * k, 8 * k + 8), S("EF"), scale=sc)
 
     def places(f, parts=(0, 1, 2)):
         pos = C("XY", 128 * (f % 2), 128 * (f % 2) + 128)
         for k in parts:
             mm(pos, ID, (S("NV", f), S("BM"), S("H"))[k], k == 0, k == 2)
 
-    def clamps(f):
+    def clamps(f, now=True):
         a = 128 * (f % 2)
         ts(C("CC", 0, 64), C("XY", a, a + 128, 2), 0.0, A.max, 15.0, A.min)
         ts(C("CC", 64, 128), C("XY", a + 1, a + 128, 2), 0.0, A.max, 31.0, A.min)
-        mms((C("PM", 384, 448), S("I32"), C("CC", 0, 64)), (C("PM", 384, 448), ID, C("CC", 64, 128)))
+        total = lambda: mms((C("PM", 384, 448), S("I32"), C("CC", 0, 64)), (C("PM", 384, 448), ID, C("CC", 64, 128)))
+        return total() if now else total
 
     def keep(f):
         r, a = RW * PSLOT[f], 128 * (f % 2)
         tt(C("REC", r + 32, r + RW), C("XY", a, a + 64), S("BT"), A.subtract)
-
-    for k in range(6):
-        ts(S("EW", k), RK, C("TG", k), A.is_equal, C("WK", k % 3), A.mult)
-        o = C("PN", 64 + N2 * (k // 3), 64 + N2 * (k // 3) + N2)
-        mm(o, ID, S("EW", k), k % 3 == 0, k % 3 == 2)
-    ts(S("DL"), S("F48"), col(FP), A.is_equal, col(CH), A.mult)
-    mm(S("PA"), S("N15"), S("H2"), False, True)
-    for fs in (slice(0, 2), slice(2, 8)):
-        for i in (0, 1):
-            act(S("POW", fs, i), C("PA", 256 * i + 32 * fs.start, 256 * i + 32 * fs.stop), AF.Exp, scale=-7 * math.log(2), bias=21 * math.log(2))
-    tt(S("EP"), C("PN", 64, 64 + 2 * N2), S("DS"), A.mult)
-    red(C("SM", 4), C("EP", 0, N2))
-    red(C("SM", 5), C("EP", N2, 2 * N2))
-    TBP = lambda a, b=None: C("PU", 256 + a, None if b is None else 256 + b)
-    places(0)
-    mm(TBP(0, 24), S("IDF"), S("CS"), True, False)
-    ts(S("RA"), C("DA", 0, 24), C("SM", 4), A.mult)
-    ts(S("RB"), C("DA", 24, 40), C("SM", 5), A.mult)
-    mm(TBP(0, 24), S("BO"), S("RA"), False, False)
-    mm(TBP(8, 24), S("BO"), S("RB"), False, True)
-    clamps(0)
-    keep(0)
-    ts(S("RL"), S("DL"), C("SM", 5), A.mult, RW / 256.0, A.mult)
-    act(S("CL"), S("CL"), bias=col(NG))
-
-    def masks(f0, f1):
-        fs, nd = slice(f0, f1), C("XX", 32 * f0, 32 * f1)
-        act(S("MK", fs, slice(0, 32)), nd, scale=-129.0, bias=129.0)
-        for k in (32, 33):
-            act(S("MK", fs, slice(k, RW, 2)), nd, scale=-1.0, bias=1.0)
 
     def look(f):
         act(S("U1", f), S("H1", al, f), scale=C("TB", 8 + f), bias=C("TB", f))
@@ -417,27 +431,26 @@ def build(T, nxt):
     def bank(h):
         return C(("PA", "PB", "PU", "PN", "PW")[h], 0, pieces[h][1] - pieces[h][0])
 
-    row1 = S("ONE", slice(0, 128), parts=slice(0, 1))
-
-    def pixels_start(f):
+    def pixels_start(f, order=(2, 3, 0, 1)):
         s = 16 * ((f + 1) % 8)
-        for h in (list(range(2, NP)) + [0, 1] if f else [0, 1, 3, 2, 4][:NP]):
+        for h in order:
             a, b = pieces[h]
             mm(bank(h), C("J", s, s + 128), C("RES", f * P + a, f * P + b), True, False)
             mm(bank(h), row1, C("MQ", 0, b - a), False, False)
-            if f == F - 1 and h == NP - 1:
+            if f == F - 1 and LASTFIN[h] == "v":
                 mm(bank(h), row1, C("M128", 0, b - a), False, False)
 
-    def pixels_front(f, gap):
+    def pixels_front(f, gap, after=None):
         s = 16 * ((f + 1) % 8)
         win = C("W", P * wbase(f), P * (9 + f))
         aw = [("arr%d" % f, narr * (len(SENDS) if f else 1))]
         last = f == F - 1
-        for a, b in pieces:
+        whole = lambda h: last and LASTFIN[h] == "v"
+        for h, (a, b) in enumerate(pieces):
             act(C("GP", a, b), IND(win, C("OFF", 64 * f + a // 16, 64 * f + b // 16)), AF.Relu, scale=-1.0, bias=255.0, waits=aw)
             ts(C("GQ", a, b), IND(win, C("OFF", 64 * f + 32 + a // 16, 64 * f + 32 + b // 16)), 255.0, A.min, waits=aw)
-        whole = lambda h: last and h == NP - 1
-        for h, (a, b) in enumerate(pieces):
+            if after:
+                after[h]()
             mm(bank(h), C("JH", s, s + 128), C("GQ", a, b), False, False)
             mm(bank(h), C("JM", s, s + 128), C("GP", a, b), False, False)
             mm(bank(h), row1, C("MR", 0, b - a), False, not whole(h))
@@ -446,19 +459,20 @@ def build(T, nxt):
         sent = 0
         for h, (a, b) in enumerate(pieces):
             out = C("SND", f * P + a, f * P + b)
-            if h == GAP:
-                gap()
+            gap[h]()
             if whole(h):
                 ts(out, bank(h), 0.0, A.max, 255.0, A.min)
             elif (LASTFIN if last else FIN)[h] == "s":
                 act(out, bank(h), AF.Relu, bias=128.0 - BIG)
             else:
                 ts(out, bank(h), 128.0 - BIG, A.add, 0.0, A.max)
-            if h in SENDS and last:
-                top = C("SND", f * P + sent, f * P + (a if whole(h) else b))
-                ts(top, top, 255.0, A.min)
-                dma("scalar" if sent else "sync", T.y[:, f * P + sent:f * P + b], C("SND", f * P + sent, f * P + b), "out%d" % (f + (sent > 0)))
-                sent = b
+            if last:
+                if not whole(h):
+                    ts(out, out, 255.0, A.min)
+                if h in STORES:
+                    k = STORES.index(h)
+                    dma(("sync", "scalar")[k % 2], T.y[:, f * P + sent:f * P + b], C("SND", f * P + sent, f * P + b), "out%d" % (f + k))
+                    sent = b
             elif h in SENDS:
                 send(C("W", (9 + f) * P + sent, (9 + f) * P + b), C("SND", f * P + sent, f * P + b), f + 1)
                 sent = b
@@ -479,58 +493,83 @@ def build(T, nxt):
         dma("sync", T.y[:, f * P:f * P + P], C("YO", f * P, f * P + P), "out%d" % f, [("snt%d" % k, neng * len(SENDS)) for k in range(f + 1, min(f + 3, F))])
 
     r0 = RW * PSLOT[0]
-    masks(1, 3)
-    ts(C("PW", 384, 448), S("H2", al, 0), TBP(16), A.mult)
-    ts(S("U1", 0), S("H1", al, 0), TBP(8), A.mult, TBP(0), A.add)
-    act(S("TB"), TBP(0, 24))
+    TBP = lambda a, b=None: C("XX", 256 + a, None if b is None else 256 + b)
+    places(0)
+    for k in range(6):
+        ts(S("EW", k), RK, C("TG", k), A.is_equal, C("WK", k % 3), A.mult)
+    for k in range(4):
+        mm(W0, S("BB"), C("W4", k), False, k == 3)
+    for k in range(6):
+        o = C("PN", 64 + N2 * (k // 3), 64 + N2 * (k // 3) + N2)
+        mm(o, ID, S("EW", k), k % 3 == 0, k % 3 == 2)
+    ts(S("DL"), S("F48"), col(FP), A.is_equal, col(CH), A.mult)
+    a = clamps(0, False)
+    ts(S("X0"), S("P0"), W0, A.mult, -1.0, A.mult)
+    a()
+    ts(S("SS", 0), S("X0"), 1536, A.bitwise_and)
+    tt(S("EP"), C("PN", 64, 64 + 2 * N2), S("DS"), A.mult)
+    keep(0)
+    tt(S("S2"), C("PM", 384, 448), S("SS", 0), A.add)
+    red(C("SM", 4), C("EP", 0, N2))
+    red(C("SM", 5), C("EP", N2, 2 * N2))
+    cp(C("OFF", 0, 64), S("S2"))
+    ts(S("RA"), C("DA", 0, 24), C("SM", 4), A.mult)
+    ts(S("RB"), C("DA", 24, 40), C("SM", 5), A.mult)
+    act(S("BO"), S("BB"))
+    act(S("H2", al, slice(2, 8)), S("IDX", al, slice(2, 8)), AF.Sign, bias=-5.5)
+    places_in_word(0, 2, (1, 2, 3))
+    act(S("CL"), S("CL"), bias=col(NG))
+    ts(S("RL"), S("DL"), C("SM", 5), A.mult, RW / 256.0, A.mult)
+    pixels_start(0, (0, 2))
+    mms((TBP(0, 24), S("IDF"), S("CS")), (TBP(0, 24), S("BO"), S("RA")), (TBP(8, 24), S("BO"), S("RB")))
+    pixels_start(0, (1, 3))
     mms((C("PM", 280, 328), S("IDF"), S("CL")), (C("PM", 280, 328), S("BO"), S("RL")))
-    tt(C("PW", 448, 512), S("U1", 0), C("PW", 384, 448), A.add)
-    look(1)
-    look(2)
-    masks(3, 5)
-    pixels_start(0)
-    tt(S("XI", 0), C("PW", 448, 512), S("POW", 0), A.mult)
-    cp(S("LU"), C("PM", 280, 328))
-    ts(S("SS", 0), S("XI", 0), 7680, A.bitwise_and)
-    ts(C("REC", r0, r0 + 32), S("XI", 0, 0), 65024, A.bitwise_and)
-    weave(offsets(0))
+    first = [
+        lambda: power(0, 2),
+        lambda: (ts(S("U2", 0, slice(0, 32)), S("H2", 0, 0), TBP(16), A.mult), ts(S("U1", 0, slice(0, 32)), S("H1", 0, 0), TBP(8), A.mult, TBP(0), A.add)),
+        lambda: (tt(S("U1", 0, slice(0, 32)), S("U1", 0, slice(0, 32)), S("U2", 0, slice(0, 32)), A.add), act(S("TB"), TBP(0, 24))),
+        lambda: tt(S("XI", 0, 0), S("U1", 0, slice(0, 32)), S("POW", 0, 0), A.mult),
+    ]
     for f in range(F):
         g = f + 1
         nop = lambda: None
         if f == F - 1:
-            pixels_front(f, nop)
+            pixels_front(f, [nop] * 4)
             break
         r = record(g)
-        e = entries(g + 1) if g + 1 < F else [nop] * 2
+        e = entries(g)
         v = vec(2 * f + 2, 2 * f + 4) if f < 3 else [nop] * 4
-        pixels_front(f, r[0])
-        r[1]()
-        r[2]()
         if f == 0:
+            pixels_front(f, [lambda: (cp(S("LU"), C("PM", 280, 328)), ts(C("REC", r0, r0 + 32), S("XI", 0, 0), 65024, A.bitwise_and)), lambda: look(1), r[0], nop], first)
             look_sum(1)
-        places(g, (0, 1))
+            weave(r[1:3], e)
+        else:
+            pixels_front(f, [lambda: (r[0](), e[0]()), nop, e[1], r[1]])
+            r[2]()
+        if f:
+            places(g)
         turn_back(f, 0)
-        places(g, (2,))
+        if f == 0:
+            places(g)
         turn_back(f, 1)
         copy_back(f)
-        if f == 0:
-            weave(entries(1), v[:1])
-            look_sum(2)
-        else:
-            weave(e, v[:1])
-            store(f - 1)
-        r[3]()
         clamps(g)
-        r[4]()
-        pixels_start(g)
+        r[3]()
         keep(g)
+        v[0]()
+        r[4]()
+        if f in (0, 2):
+            places_in_word(*((2, 5) if f == 0 else (5, 8)))
+        pixels_start(g)
         v[1]()
-        weave(offsets(g), v[2:], e if f == 0 else [])
-        if f + 3 < F:
-            look(f + 3)
-            look_sum(f + 3)
-        if f == 3:
-            masks(5, 8)
+        weave(offsets(g), v[2:])
+        if f:
+            store(f - 1)
+        if f + 2 < F:
+            look(f + 2)
+            look_sum(f + 2)
+        if f in (0, 2):
+            power(*((2, 5) if f == 0 else (5, 8)))
         if f == 4:
             for name, v in (("MZ", -BIG), ("M128", 128.0)):
                 act(C(name, 0, WIDE), S("ONE", slice(0, WIDE), parts=slice(0, 1)), scale=v)
@@ -609,6 +648,8 @@ def rank_program(g, core, T, topo):
     n = len(T.cores)
     dst, src = T.cores[(rank + 1) % n], T.cores[(rank - 1) % n]
     rid, pid, _ = topo.addr(dst)
-    nxt = (rid, pid, topo.mask(core, dst), len(topo.engines(src, core)))
+    eng = topo.engines(core, dst)
+    half = [sum(1 << e for e in part) for part in (eng[:len(eng) // 2], eng[len(eng) // 2:])]
+    nxt = (rid, pid, topo.mask(core, dst), len(topo.engines(src, core)), half)
     ops, neng, narr = build(T, nxt)
     emit(g, T, ops, neng, narr)

@@ -4,26 +4,28 @@ from concourse.mybir import AluOpType as A, AxisListType, ActivationFunctionType
 
 F = 8
 P = 512
-CUTS = [0, 128, 288, 448, 512]
-FIN, LASTFIN, GAP = "vsvs", "vvvv", 2
-STORES = (1, 3)
+CUTS = [0, 160, 288, 416, 512]
+CUTS0 = [0, 256, 512]
+FIN = "vsvs"
 SENDS = (1, 3)
-BIG = 12582912.0
+BIG = 8388608.0
 NN = 26
 N2 = 2 * NN
+N0 = 12
 RW = 96
 
-f32, bf, i32, u16 = "float32", "bfloat16", "int32", "uint16"
+f32, bf, i32, u16, f16 = "float32", "bfloat16", "int32", "uint16", "float16"
 SB_ = {
     "W": ([128, 16 * P], bf), "RES": ([128, F * P], bf), "SND": ([128, F * P], bf), "YO": ([128, 7 * P], bf),
-    "GP": ([128, P], bf), "GQ": ([128, P], bf),
+    "GP": ([128, P], bf), "GQ": ([128, P], f16), "G0": ([128, P], bf), "M4": ([1, 128], bf),
     "IA": ([128, 256], i32), "IB": ([128, 256], i32), "VY": ([128, 8, 2, 32], i32), "VX": ([128, 8, 2, 32], i32),
     "CT": ([128, 8], i32), "EB": ([128, 8], bf), "CA": ([128, 4], f32), "CF": ([128, 4], f32),
-    "ONE": ([128, 256], bf), "MR": ([1, 256], bf), "MZ": ([1, 256], bf), "MQ": ([1, 256], bf), "M128": ([1, 256], bf),
-    "ID": ([128, 128], bf), "IK": ([128, 128], bf), "MN": ([128, 128], bf), "NE": ([128, 3 * N2], bf), "J": ([128, 256], bf), "JH": ([128, 256], bf), "JM": ([128, 256], bf), "N15": ([128, 128], bf), "I32": ([128, 128], bf),
+    "ONE": ([128, 256], bf), "MR": ([1, 192], bf), "MZ": ([1, 192], bf), "MQ": ([1, 128], bf), "MB": ([1, 2, 128], bf),
+    "ID": ([128, 128], bf), "IK": ([128, 128], bf), "MN": ([128, 128], bf), "NE": ([128, 3 * N2], bf), "J": ([128, 256], bf),
+    "JH": ([128, 256], bf), "JM": ([128, 256], bf), "N15": ([128, 128], bf), "I32": ([128, 128], bf),
     "E8": ([128, 128], bf), "EA": ([128, 128], bf), "BO": ([128, 128], f32), "IDF": ([128, 128], f32),
     "L0": ([128, 128], bf), "LE": ([128, 128], bf), "LT": ([128, 128], bf), "M": ([128, 128], bf), "TR": ([NN, 256], bf),
-    "LA": ([128, 128], bf),
+    "LA": ([128, 128], bf), "BLK": ([128, 128], bf), "SEL": ([128, 128], bf),
     "PI": ([128, 8], i32), "PC": ([128, 24], f32), "F8": ([128, 8], f32), "F48": ([128, 48], f32), "EF": ([128, 8], f32), "TG": ([128, 6], bf),
     "NR": ([128, N2], bf), "OM": ([128, N2], bf), "OR": ([128, N2], bf), "E0": ([128, N2], bf), "EQC": ([128, N2], bf),
     "GEN": ([128, N2], bf), "TA": ([128, 8, NN], f32), "X": ([128, 2, 56], bf), "Z": ([128, 56], bf), "SV": ([128, NN], bf),
@@ -32,20 +34,24 @@ SB_ = {
     "KC": ([128, 104], bf), "KT": ([128, N2], f32), "DA": ([128, 40], f32), "DL": ([128, 48], f32),
     "RA": ([128, 24], f32), "RB": ([128, 16], f32), "RL": ([128, 48], f32), "CS": ([128, 24], f32), "CL": ([128, 48], f32),
     "TB": ([128, 24], f32), "LU": ([128, 48], u16), "SM": ([128, 8], f32),
+    "HB": ([128, 32], f32), "HI": ([128, 32], i32), "BITS": ([128, 32], bf), "XH": ([128, 64], bf), "VI": ([128, 64], bf),
+    "TN": ([128, N0], bf), "K5": ([128, 5, N0], bf), "GK": ([128, 2, N0], bf), "AB": ([128, 3, 64], bf),
     "IDX": ([128, 2, 8, 32], bf), "H1": ([128, 2, 8, 32], bf), "H2": ([128, 2, 8, 32], bf), "FX": ([128, 2, 256], bf), "POW": ([128, 8, 2, 32], bf),
-    "NV": ([128, 8, 2, 32, 2], bf), "BI": ([128, 2, 32], f32), "BT": ([128, 32, 2], bf), "BM": ([128, 2, 64], bf),
+    "NV": ([128, 8, 2, 32, 2], bf), "BI": ([128, 2, 32], f32), "BT": ([128, 32, 2], bf), "BQ": ([128, 64], bf),
     "MK": ([128, 8, RW], bf), "U1": ([128, 8, 64], f32), "U2": ([128, 8, 64], f32), "XI": ([128, 8, 2, 32], i32), "A0": ([128, 8, 32], i32),
-    "SS": ([128, 2, 64], i32), "REC": ([128, 11 * RW], i32), "G": ([128, RW], f32), "H": ([128, 128], bf), "CC": ([128, 128], bf),
-    "RF": ([1, 128], f32), "C0": ([1, 4], f32), "HF": ([1, 4], bf), "BB": ([128, 128], bf), "W4": ([128, 4], bf), "P0": ([128, 64], bf), "X0": ([128, 64], i32),
-    "S2": ([128, 64], i32), "OFF": ([128, F * 64], u16),
+    "SS": ([128, 2, 64], i32), "RE": ([128, 11 * 32], i32), "RV": ([128, 11 * 64], bf), "GE": ([128, 32], f32), "GV": ([128, 64], bf),
+    "CC": ([128, 128], bf), "BB": ([128, 128], bf), "S2": ([128, 64], i32), "OFF": ([128, F * 64], u16),
 }
 PS_ = ["PA", "PB", "PU", "XY", "XX", "PM", "PN", "PW"]
 SCRATCH = {k: ("sbuf", v[0], v[1]) for k, v in SB_.items()}
 SCRATCH.update({k: ("psum", [128, P], f32) for k in PS_})
-DMAS = ["ctl", "pic", "pi0", "ia_", "ib_", "vy_", "vx_", "res0", "res1", "res3", "vy2", "vx2"] + ["out%d" % f for f in range(F + 3)]
+DMAS = ["ctl", "pic", "pi0", "ia_", "ib_", "vy_", "vx_", "res0", "res1", "res3", "res5", "vy2", "vx2"] + ["out%d" % f for f in range(F + 1)]
 SEMAPHORES = ["dve", "act", "pe", "pool"] + DMAS + ["arr%d" % f for f in range(F)] + ["snt%d" % f for f in range(F)]
 
 PSLOT = [4, 3, 2, 1, 0, 9, 8, 10]
+
+CYC, WAKE, LAND, HOP, COL, EARLY = 0.0009, 0.24, 1.2, 1.2, 0.001, 2.0
+WIDTH = {f32: 4, i32: 4, bf: 2, u16: 2, f16: 2}
 
 
 def wbase(f):
@@ -73,14 +79,25 @@ def build(T, nxt):
     def val(x):
         return x[0] if isinstance(x, tuple) else x
 
-    def add(q, fn, outs, ins, waits=(), sem=None):
+    def add(q, fn, outs, ins, waits=(), sem=None, rate=None):
         rd = []
         for x in ins:
             if isinstance(x, tuple):
                 rd.append((x[1], x[2]))
                 if len(x) > 3:
                     rd.append((x[3][1], x[3][2]))
-        ops.append((q, fn, rd, [(x[1], x[2]) for x in outs], list(waits), sem))
+        full = [x for x in list(outs) + list(ins) if isinstance(x, tuple)]
+        n = len(full[0][2])
+        width = [WIDTH[SCRATCH[x[1]][2]] for x in full if len(x[2]) == n]
+        if any(len(x) > 3 for x in full):
+            cost = 0.06 + 1.5 * CYC * n
+        elif sem is not None:
+            cost = 0.15 + (rate or 0) if q == "pool" else n * width[0] / 2500.0
+        elif q == "dve":
+            cost = CYC * max(64, len(full[-1][2]) if rate == 0 else n * (rate or (0.5 if max(width) == 2 else 1)))
+        else:
+            cost = {"act": 0.03 + CYC * n, "pe": CYC * max(64, n) * (0.5 if width[-1] == 2 else 2), "pool": 0.15 + 2 * CYC * n}[q] + (rate or 0)
+        ops.append((q, fn, rd, [(x[1], x[2]) for x in outs], list(waits), sem, cost))
 
     def ts(o, i, s1, op0, s2=None, op1=None, waits=()):
         if op1 is None:
@@ -89,22 +106,23 @@ def build(T, nxt):
             add("dve", lambda e: e.tensor_scalar(o[0], i[0], val(s1), val(s2), op0, op1), [o], [i, s1, s2], waits)
 
     def tt(o, a, b, op):
-        add("dve", lambda e: e.tensor_tensor(o[0], a[0], b[0], op), [o], [a, b])
+        add("dve", lambda e: e.tensor_tensor(o[0], a[0], b[0], op), [o], [a, b], rate=1 if a[1] in PS_ or b[1] in PS_ else 2)
 
-    def cp(o, i):
-        add("dve", lambda e: e.tensor_copy(o[0], i[0]), [o], [i])
+    def cp(o, i, waits=()):
+        add("dve", lambda e: e.tensor_copy(o[0], i[0]), [o], [i], waits)
 
     def ms(o, c):
         add("dve", lambda e: e.memset(o[0], c), [o], [])
 
     def red(o, i, op=A.add):
-        add("dve", lambda e: e.tensor_reduce(o[0], i[0], AxisListType.X, op), [o], [i])
+        add("dve", lambda e: e.tensor_reduce(o[0], i[0], AxisListType.X, op), [o], [i], rate=0)
 
     def scan(o, d0, d1, ini):
         add("dve", lambda e: e.tensor_tensor_scan(o[0], d0[0], d1[0], val(ini), A.add, A.add), [o], [d0, d1, ini])
 
-    def act(o, i, func=AF.Identity, bias=0.0, scale=1.0, waits=()):
-        add("act", lambda e: e.activation(o[0], i[0], func, bias=val(bias), scale=val(scale)), [o], [i, bias, scale], waits)
+    def act(o, i, func=AF.Identity, bias=0.0, scale=1.0, waits=(), first=False):
+        add("act", lambda e: e.activation(o[0], i[0], func, bias=val(bias), scale=val(scale)), [o], [i, bias, scale], waits,
+            rate=1.3 if first else None)
 
     def mm(o, l, r, st, sp):
         add("pe", lambda e: e.matmul(o[0], l[0], r[0], st, sp), [o], [l, r])
@@ -128,22 +146,17 @@ def build(T, nxt):
     def dma(q, o, i, sem, waits=()):
         add(q, lambda e: e.dma_start(val(o), val(i)), [o] if isinstance(o, tuple) else [], [i], waits, sem)
 
-    def send(o, i, k, mask=nxt[2]):
+    def send(o, i, k, mask=nxt[2], first=False):
         add("pool", lambda e: e.remote_dma(o[0], i[0], T.sem["arr%d" % k], T.sem["snt%d" % k], nxt[1], nxt[0], mask),
-            [], [i], (), "remote")
+            [], [i], (), k, rate=1.0 if first else None)
 
-    def weave(*chains):
-        for k in range(max(len(x) for x in chains)):
-            for x in chains:
-                if k < len(x):
-                    x[k]()
-
-    WIDE = max(b - a for a, b in zip(CUTS[:-1], CUTS[1:]))
     neng = bin(nxt[2]).count("1")
     narr = nxt[3]
+    sent = lambda k: ("snt%d" % k, neng * (len(SENDS) if k else 1))
     col = lambda k: C("PC", k)
-    FP, HALF, G16, GR, NG, F0, KA, W16, H5, CN, CH, CQ, KCB, WS, T0, T1, T2, T3, B0 = range(19)
+    PF, FP, HALF, G16, GR, NG, F0, KA, W16, CN, CH, CQ, KCB, WS, T0, T1, T2, L2, W7, CL0, CL1 = range(21)
     D_, R_ = slice(0, NN), slice(NN, N2)
+    one = lambda a, b: C("ONE", a, b, parts=slice(0, 1))
 
     for h, q in enumerate(("sync", "scalar")):
         pp = slice(64 * h, 64 * h + 64)
@@ -157,63 +170,89 @@ def build(T, nxt):
     dma("sync", S("VX", slice(0, 2)), T.vx[:, 0:128], "vx_")
     dma("sync", C("W", 5 * P, 6 * P), T.pic0[:, 0:P], "pi0")
     dma("sync", C("RES", 0, P), T.res[:, 0:P], "res0")
-    dma("sync", S("VY", slice(2, 8)), T.vy[:, 128:512], "vy2")
-    dma("sync", S("VX", slice(2, 8)), T.vx[:, 128:512], "vx2")
-    dma("sync", C("RES", P, 3 * P), T.res[:, P:3 * P], "res1")
-    dma("sync", C("RES", 3 * P, F * P), T.res[:, 3 * P:F * P], "res3", [("snt0", neng)])
 
     ms(S("ONE"), 1.0)
+    ms(S("ZR"), 0.0)
+    for a in (0, 256):
+        act(C("W", 7 * P + a, 7 * P + a + 256), S("ONE"), scale=128.0)
     iota(C("PI", 0), [[0, 1]], 0, 1)
     iota(S("NR", R_), [[1, NN]], -1)
     sel("L0", [[0, 2], [1, 64]], op=A.is_ge)
-    iota(S("F8"), [[1, 8]], 0)
-    sel("LE", [[0, 2], [-8, 8], [0, 8]], "L0", A.is_ge, cm=1)
-    sel("LT", [[0, 2], [1, 64]], "LE", A.is_gt)
     sel("ID", [[1, 128]])
-    ms(S("ZR"), 0.0)
+    sel("LE", [[0, 2], [-8, 8], [0, 8]], "L0", A.is_ge, cm=1)
+    iota(S("HB"), [[1, 32]], 0)
+    sel("LT", [[0, 2], [1, 64]], "LE", A.is_gt)
     iota(S("EA"), [[0, 2], [1, 8], [0, 8]], 0)
     for k in (0, 1):
         a, b = k * P // 2, (k + 1) * P // 2
-        send(C("W", 8 * P + a, 8 * P + b), C("W", 6 * P + a, 6 * P + b), 0, nxt[4][k])
+        send(C("W", 8 * P + a, 8 * P + b), C("W", 6 * P + a, 6 * P + b), 0, nxt[4][k], k == 0)
+    dma("sync", C("RES", P, 3 * P), T.res[:, P:3 * P], "res1", [sent(0)])
+    dma("sync", S("VY", slice(2, 8)), T.vy[:, 128:512], "vy2")
+    dma("sync", S("VX", slice(2, 8)), T.vx[:, 128:512], "vx2")
+    iota(S("E8"), [[1, 8], [0, 16]], 0)
     iota(S("BI", 0), [[1, 16], [0, 2]], 0)
     iota(S("BI", 1), [[0, 16], [16, 2]], 0, 1)
-    iota(S("E8"), [[1, 8], [0, 16]], 0)
-    iota(S("F48"), [[1, 8], [0, 6]], 0)
-    iota(S("CL"), [[0, 8], [16, 6]], 0, 1)
-    for name, v in (("JH", 0.5), ("JM", -0.5)):
-        sel(name, [[0, 2], [1, 128]], "ZR", A.not_equal, v)
-    iota(C("REC", 5 * RW, 9 * RW), [[0, 4 * RW]], 0)
+    iota(S("F8"), [[1, 8]], 0)
+    for a, k in ((0, 2), (16, 4)):
+        iota(C("F48", a, a + 8 * k), [[1, 8], [0, k]], 0)
+        iota(C("CL", a, a + 8 * k), [[0, 8], [16, k]], 0, 1)
+    iota(C("RE", 5 * 32, 9 * 32), [[0, 4 * 32]], 0)
+    act(C("RV", 5 * 64, 9 * 64), S("ZR"))
     ts(C("PI", 1), C("PI", 0), 7, A.bitwise_and)
     ts(C("PI", 2), C("PI", 0), 6, A.arith_shift_right)
     ts(C("PI", 3), C("PI", 0), 112, A.bitwise_and)
     ts(C("PI", 4), C("PI", 0), 3, A.arith_shift_right, 7, A.bitwise_and)
-    ms(C("CS", 8, 16), 0.0)
-    cp(C("PC", 0, 4), C("PI", 1, 5))
-    act(S("NR", D_), S("NR", R_), scale=-1.0, bias=23.0)
-    act(col(F0), col(FP), AF.Relu, scale=-1.0, bias=1.0)
-    for k, sc, bi in ((CN, 0.5, -0.5), (CH, 0.5, 0.0), (CQ, -0.5, 0.5), (W16, -16.0, 16.0)):
+    cp(C("PC", 0, 5), C("PI", 0, 5))
+    ts(S("NR", D_), S("NR", R_), -1.0, A.mult, 23.0, A.add)
+    ts(col(F0), col(FP), 0.0, A.is_equal)
+    for k, sc, bi in ((CN, 0.5, -0.5), (CH, 0.5, 0.0), (CQ, -0.5, 0.5), (W16, -16.0, 16.0), (KA, 6.0, 1.0), (CL0, 1.0 / 16, 0.0), (CL1, 1.0 / 8, 0.0)):
         act(col(k), col(HALF), scale=sc, bias=bi)
     act(col(NG), col(G16), scale=-1.0)
-    act(S("WK"), C("NR", NN + 1, NN + 5), AF.Exp, scale=7 * math.log(2), bias=9 * math.log(2))
-    act(C("MR", 0, WIDE), C("ONE", 0, WIDE, parts=slice(0, 1)), scale=BIG)
+    act(S("WK"), C("NR", NN + 1, NN + 5), AF.Exp, scale=7 * math.log(2), bias=9 * math.log(2), first=True)
+    act(C("WK", 3), col(FP), AF.Exp, scale=-math.log(2), bias=7 * math.log(2))
+    for o, v in ((S("MR"), 151.0 * 256), (S("MQ"), 217.0), (S("MB", 0), 1.5 * BIG), (S("MB", 1), -1.5 * BIG), (S("MZ"), -BIG), (S("M4"), 0.25)):
+        act(o, one(0, len(o[2])), scale=v)
     ts(col(T0), col(FP), 5.0, A.min, 18.0, A.add)
     ts(col(T1), col(FP), 5.0, A.is_ge, 10.0, A.mult)
-    ts(col(KA), col(HALF), 6.0, A.mult, 1.0, A.add)
-    ts(col(KCB), col(T0), col(HALF), A.mult, -16.0, A.add)
-    ts(col(T1), col(T1), col(FP), A.subtract, -3.0, A.add)
-    ts(col(B0), col(F0), col(HALF), A.is_gt, 8192.0, A.mult)
+    act(col(KCB), col(T0), scale=col(HALF), bias=-16.0)
+    act(col(T2), col(FP), scale=-1.0, bias=col(T1))
+    act(col(WS), col(T2), scale=1.0 / 16, bias=-3.0 / 16)
+    ts(col(L2), col(FP), 2.0, A.is_lt)
+    ts(col(W7), col(FP), 7.0, A.not_equal, col(W16), A.mult)
     ts(S("EF"), S("F8"), col(FP), A.is_equal)
-    ts(S("TG"), C("F8", 0, 6), col(KA), A.add)
-    ts(col(WS), col(T1), 1.0 / 16, A.mult)
-    ts(col(B0), col(B0), -8192.0 - 1025 * math.log(4), A.add)
-    ts(C("TG", 3), col(HALF), -2.0, A.mult, 4.0, A.add)
-    ts(C("CS", 0, 8), S("F8"), 4194304.0, A.mult, 7.0 * 16513 * 512 + 4194304.0, A.add)
-    ts(C("CS", 16, 24), S("F8"), 4194304.0, A.mult, 4194304.0, A.add)
-    ms(S("H"), 192.0)
+    act(S("TG"), C("F8", 0, 6), bias=col(KA))
+    act(C("TG", 3), col(HALF), scale=-2.0, bias=4.0)
+    act(C("CS", 0, 8), S("F8"), scale=4194304.0, bias=7.0 * 16513 * 512 + 4194304.0)
+    act(C("CS", 8, 16), S("F8"), scale=0.0)
+    act(C("CS", 16, 24), S("F8"), scale=4194304.0, bias=4194304.0)
     ID = S("ID")
+    for o, v in ((S("IK"), 1024.0), (S("N15"), -1.5), (C("J", 0, 128), 1.0), (C("J", 128, 256), 1.0), (S("IDF"), 1.0), (S("I32"), 32.0)):
+        act(o, ID, scale=v)
+    ts(S("JH"), S("J"), 0.5, A.mult)
+    ts(S("JM"), S("J"), -0.5, A.mult)
+    ts(S("SEL"), S("E8"), 8.0, A.mult, col(PF), A.is_equal)
+    ts(S("BB"), S("E8"), col(GR), A.is_equal)
+    act(S("BO"), S("BB"))
+    ts(S("LA"), S("EA"), col(GR), A.is_equal, col(W16), A.mult)
+    ts(S("BLK"), S("EA"), col(GR), A.is_equal, col(W7), A.mult)
+    ts(S("HI"), S("HB"), C("WK", 3), A.mult)
+    ts(S("HI"), S("HI"), 32, A.bitwise_and)
+    ts(S("BITS"), S("HI"), 1.0 / 32, A.mult, col(L2), A.max)
+    act(S("KT"), S("NR"), AF.Relu, scale=-1.0, bias=1.0)
+    act(C("KC", 0, N2), S("KT"), scale=-1.0, bias=-16.0)
+    act(C("KC", N2, 2 * N2), S("KT"), scale=-1.0, bias=col(KCB))
+    for k, sc in enumerate((0.5, col(CN), col(CH), col(CQ), col(CN))):
+        act(C("DA", 8 * k, 8 * k + 8), S("EF"), scale=sc)
+    for a, b, k in ((0, 16, CL0), (16, 48, CL1)):
+        ts(C("DL", a, b), C("F48", a, b), col(FP), A.is_equal, col(k), A.mult)
+    act(S("CL"), S("CL"), bias=col(NG))
+    act(S("BT", al, 0), S("BI", 0))
+    act(S("BT", al, 1), S("BI", 1), bias=col(NG))
+    act(S("BQ"), S("BT"), bias=-0.25)
+    row1 = one(0, 128)
+    FXL = (ID, C("JM", 0, 128))
 
     CS_ = C("PM", 0)
-    ND = C("XX", 0, 256)
     ts(C("EB", 0), C("CT", 0), 1.0, A.add)
     ts(C("CA", 0), C("CT", 1), 1.0, A.not_equal, 64.0, A.mult)
     ts(C("CA", 1), C("CT", 1), 2.0, A.not_equal, 64.0, A.mult)
@@ -224,7 +263,7 @@ def build(T, nxt):
     cp(C("CF", 0, 2), C("CT", 3, 5))
     ts(S("OM"), S("NR"), C("CF", 2), A.add, CS_, A.is_equal)
     ts(S("OR"), S("NR"), C("CF", 3), A.add, CS_, A.is_equal)
-    GM, LTC, LTG, UP, U, SU, OS, SV = [S("TA", k) for k in range(8)]
+    GM, LTC, LTG, UP, U, SU, OS, OT = [S("TA", k) for k in range(8)]
     ts(GM, S("NR", D_), C("CF", 2), A.add, CS_, A.is_ge)
     ts(LTC, S("NR", D_), CS_, A.is_lt)
     TT = C("PA", 0, N2)
@@ -232,37 +271,102 @@ def build(T, nxt):
     top = slice(0, NN)
     mm(C("PB", 0, 128, parts=top), S("OR", D_), S("LT"), True, True)
     mm(C("PN", 128, 256, parts=top), S("OM", D_), ID, True, True)
-    mm(C("PU", 128, 128 + NN), S("LE"), S("OR", R_), True, True)
     NE = lambda k: C("NE", N2 * k, N2 * k + N2)
     ts(S("E0"), S("NR"), C("CF", 0), A.add, CS_, A.not_equal)
-    eye = lambda name, v, a=0: ts(C(name, a, a + 128), ID, v, A.mult)
-    eye("IK", 1024.0)
-    tt(LTG, GM, LTC, A.min)
     ts(NE(0), S("NR"), C("CF", 1), A.add, CS_, A.not_equal)
-    eye("N15", -1.5)
+    ts(S("EQC"), S("NR"), CS_, A.is_equal, col(WS), A.mult)
+    ts(S("GEN", D_), S("NR", D_), CS_, A.is_ge)
+    tt(LTG, GM, LTC, A.min)
     act(C("TR", 0, 128), C("PB", 0, 128, parts=top))
     cp(C("TR", 128, 256), C("PN", 128, 256, parts=top))
+    mm(C("PU", 128, 128 + NN), S("LE"), S("OR", R_), True, True)
     mm(C("PU", 0, 128), C("TR", 128, 256), C("TR", 0, 128), True, True)
     tt(UP, C("PA", 0, NN), LTG, A.is_lt)
     tt(S("X", 0, slice(0, N2)), TT, S("OM"), A.is_lt)
-    red(C("SM", 0), UP)
-    red(S("X", 0, slice(N2, N2 + 1)), S("X", 0, D_), A.max)
     tt(U, C("PA", 0, NN), LTC, A.is_lt)
-    tt(S("M"), C("PU", 0, 128), S("LT"), A.is_lt)
-    XW = slice(0, N2 + 1)
-    ts(S("Z", XW), S("X", 0, XW), -99.0, A.mult, C("SM", 0), A.add)
 
-    one = lambda a, b: C("ONE", a, b, parts=slice(0, 1))
-    act(S("RF"), one(0, 128))
-    act(C("MQ", 0, WIDE), one(0, WIDE), scale=-0.25)
-    act(C("C0", 0), one(0, 1), scale=-(2.0 * (4 ** 8 - 1) / 3 + 3.0 * 4 ** 8))
-    act(S("HF"), C("NR", NN, NN + 4, parts=slice(0, 1)), AF.Abs, bias=-0.5)
-    act(S("KT"), S("NR"), AF.Relu, scale=-1.0, bias=1.0)
-    act(S("IDF"), ID)
-    act(S("I32"), ID, scale=32.0)
-    act(S("HF"), S("HF"), scale=-0.5, bias=0.75)
-    act(C("KC", 0, N2), S("KT"), scale=-1.0, bias=-16.0)
-    act(C("KC", N2, 2 * N2), S("KT"), scale=-1.0, bias=col(KCB))
+    N0_ = slice(NN - N0, NN)
+    act(S("TN"), S("NR", N0_), scale=-1.0, bias=C("EB", 0))
+    for k, (c, v) in enumerate(((C("CF", 2), -8.0), (C("CF", 3), -256.0), (C("CF", 0), 16.0), (C("CF", 1), 32.0))):
+        ts(S("K5", k), S("TN"), c, A.is_equal, v, A.mult)
+    ts(S("K5", 4), S("TN"), 1.0, A.is_ge, 128.0, A.mult)
+    KEY = C("PA", 64, 64 + N0)
+    mms((KEY, S("SEL"), S("NR", N0_)), *[(KEY, S("SEL"), S("K5", k)) for k in range(5)])
+    for k in (0, 1):
+        ts(S("GK", k), KEY, C("PA", 64 + N0 - 1 - k), A.is_gt)
+        red(C("SM", 2 + k), S("GK", k))
+
+    red(C("SM", 0), UP)
+    CAND = S("X", 0, slice(N2, N2 + 1))
+    red(CAND, S("X", 0, D_), A.max)
+    tt(S("M"), C("PU", 0, 128), S("LT"), A.is_lt)
+    ts(S("GEN", R_), C("PU", 128, 128 + NN), 0.0, A.is_equal)
+    XW = slice(0, N2 + 1)
+    act(S("Z", XW), S("X", 0, XW), scale=-99.0, bias=C("SM", 0))
+    act(S("MN"), S("M"), scale=-256.0)
+    ts(C("XH", 0, 32), S("BITS"), CAND, A.mult)
+    ts(C("XH", 32, 64), S("BITS"), CAND, A.mult, -1.0, A.mult)
+    HY, CNT, LT_, LAM = C("PN", 0, 64), C("PN", 64, 96), C("PN", 96, 97 + N2), C("PN", 96 + N2)
+    mms((HY, S("IK"), S("XH")), (HY, S("M"), S("XH")))
+    ts(C("VI", 0, 32), C("PN", 0, 32), C("Z", N2), A.add, 933.0, A.is_gt)
+    ts(C("VI", 32, 64), C("PN", 32, 64), C("Z", N2), A.subtract, 91.0, A.is_ge)
+    mms((CNT, ID, C("XH", 32, 64)), (CNT, S("BLK"), C("VI", 0, 32)), (CNT, S("BLK"), C("VI", 32, 64)))
+    red(C("SM", 1), CNT, A.min)
+    ts(S("X", 1, XW), S("X", 0, XW), C("SM", 1), A.mult, -1.0, A.mult)
+    mm(LT_, S("M"), S("X", 1, XW), True, True)
+
+    SV = S("SV")
+    tt(OS, S("OM", D_), S("OR", D_), A.add)
+    tt(NE(1), S("E0"), NE(0), A.is_ge)
+    scan(SU, U, C("ZR", 0, NN), 0.0)
+    tt(OT, U, OS, A.is_gt)
+    tt(NE(2), NE(1), NE(0), A.not_equal)
+    act(OS, OT, scale=-99.0)
+    tt(SV, SU, OS, A.add)
+    YS = lambda k, h: C("PW", N2 * k + NN * h, N2 * k + NN * h + NN)
+    YA = C("PW", 0, 3 * N2)
+    mms((YA, S("IK"), S("NE")), *[(YS(k, 1), S("IK"), S("OR", R_)) for k in range(3)], *[(YS(k, 1), ID, S("Z", R_)) for k in range(3)],
+        *[(YS(k, 0), ID, SV) for k in range(3)], *[(YS(k, 1), S("MN"), S("X", 1, R_)) for k in range(3)])
+    ts(S("Y"), YA, LAM, A.add, -91.0, A.is_le)
+    ts(S("HH", D_), SV, LAM, A.add, -91.0, A.is_le)
+    ts(S("HH", R_), S("Z", D_), LAM, A.add, -91.0, A.is_le)
+    tt(S("LD"), C("PN", 96, 96 + NN), S("OR", D_), A.is_gt)
+    scan(C("PU", 300, 300 + 156), S("Y"), C("ZR", 0, 156), 0.0)
+    tt(S("PP"), C("Y", N2, 3 * N2), C("PU", 300 + N2, 300 + 156), A.mult)
+    DD, D2 = C("PW", 256, 256 + N2), C("PW", 320, 320 + N2)
+    mms((D2, ID, C("KC", N2, 2 * N2)), (D2, S("LA"), S("EQC")))
+    mms((DD, ID, C("KC", 0, N2)), (DD, S("LA"), S("EQC")), (DD, S("LA"), S("GEN")),
+        *[(C("PW", 256, 256 + NN), S("LA"), x) for x in (S("HH", D_), S("HH", R_), S("LD"))])
+    RK = C("PU", 200, 200 + N2)
+    mms((RK, ID, C("Y", 0, N2)), (RK, ID, C("PP", 0, N2)), (RK, ID, C("PP", N2, 2 * N2)))
+    lo, hi = slice(0, 64), slice(64, 128)
+    act(C("DS", N2, 2 * N2, parts=hi), C("PW", 320, 320 + N2, parts=hi))
+    act(C("DS", 0, N2), DD)
+    act(C("DS", N2, 2 * N2, parts=lo), C("PW", 256, 256 + N2, parts=lo))
+    for k in range(6):
+        ts(S("EW", k), RK, C("TG", k), A.is_equal, C("WK", k % 3), A.mult)
+    for k in range(6):
+        o = C("PN", 160 + N2 * (k // 3), 160 + N2 * (k // 3) + N2)
+        mm(o, ID, S("EW", k), k % 3 == 0, k % 3 == 2)
+    for k in (0, 1):
+        tt(C("EP", N2 * k, N2 * k + N2), C("PN", 160 + N2 * k, 160 + N2 * k + N2), C("DS", N2 * k, N2 * k + N2), A.mult)
+        red(C("SM", 4 + k), C("EP", N2 * k, N2 * k + N2))
+    ts(S("RA"), C("DA", 0, 24), C("SM", 4), A.mult)
+    ts(S("RB"), C("DA", 24, 40), C("SM", 5), A.mult)
+    act(S("RL"), S("DL"), scale=C("SM", 5))
+    TBP = lambda a, b=None: C("PM", 200 + a, None if b is None else 200 + b)
+    mms((TBP(0, 24), S("IDF"), S("CS")), (TBP(0, 24), S("BO"), S("RA")), (TBP(8, 24), S("BO"), S("RB")))
+    mms((C("PU", 0, 48), S("IDF"), S("CL")), (C("PU", 0, 48), S("BO"), S("RL")))
+
+    def lists(f0, f1):
+        fs, cs, nd = slice(f0, f1), slice(32 * f0, 32 * f1), C("XX", 32 * f0, 32 * f1)
+        ts(nd, S("IA", cs), 8.0, A.is_le)
+        tt(S("IDX", 0, fs), S("IA", cs), nd, A.mult)
+        tt(S("IDX", 1, fs), S("IB", cs), nd, A.mult)
+        act(S("FX", 0, cs), S("IDX", 1, fs), AF.Relu, scale=-3.0, bias=3.0)
+        act(S("FX", 1, cs), S("IDX", 1, fs), AF.Relu, scale=-2.0, bias=4.0)
+        act(S("H1", al, fs), S("IDX", al, fs), AF.Sign, bias=-2.5)
+        act(S("H2", al, fs), S("IDX", al, fs), AF.Sign, bias=-5.5)
 
     def masks(f0, f1):
         fs, nd = slice(f0, f1), C("XX", 32 * f0, 32 * f1)
@@ -271,314 +375,251 @@ def build(T, nxt):
             act(S("MK", fs, slice(k, RW, 2)), nd, scale=-1.0, bias=1.0)
 
     def vec(f0, f1):
-        fs = slice(f0, f1)
-        nd = C("XX", 32 * f0, 32 * f1)
-        return [lambda n=n, i=i: tt(S("NV", fs, i, al, n), S(("VY", "VX")[n], fs, i), nd, A.mult) for n in (0, 1) for i in (0, 1)]
+        fs, nd = slice(f0, f1), C("XX", 32 * f0, 32 * f1)
+        for n in (0, 1):
+            for i in (0, 1):
+                tt(S("NV", fs, i, al, n), S(("VY", "VX")[n], fs, i), nd, A.mult)
 
-    v01 = vec(0, 2)
-    SV = S("SV")
-    fill = [
-        [lambda: ts(ND, S("IA"), 8.0, A.is_le)],
-        [lambda: tt(S("IDX", 0), S("IA"), ND, A.mult)],
-        [lambda: tt(S("IDX", 1), S("IB"), ND, A.mult)],
-        [lambda: tt(OS, S("OM", D_), S("OR", D_), A.add), lambda: tt(NE(1), S("E0"), NE(0), A.is_ge), lambda: scan(SU, U, C("ZR", 0, NN), 0.0),
-         lambda: tt(OS, U, OS, A.is_gt)],
-        [lambda: tt(NE(2), NE(1), NE(0), A.not_equal), lambda: ts(OS, OS, -99.0, A.mult), lambda: ts(S("EQC"), S("NR"), CS_, A.is_equal, col(WS), A.mult),
-         lambda: tt(SV, SU, OS, A.add)],
-        [lambda: ts(S("GEN", D_), S("NR", D_), CS_, A.is_ge), lambda: ts(S("GEN", R_), C("PU", 128, 128 + NN), 0.0, A.is_equal),
-         lambda: ts(S("LA"), S("EA"), col(GR), A.is_equal, col(W16), A.mult), lambda: eye("J", 1.0), lambda: eye("J", 1.0, 128)],
-    ]
-    LAM = C("PN", N2)
-    YS = lambda k, h: C("XY", 256 + N2 * k + NN * h, 256 + N2 * k + NN * h + NN)
-    YA = C("XY", 256, 256 + 3 * N2)
-    K0, R4, W0 = C("XX", 288, 320), C("PA", 320, 324), C("PU", 480)
-
-    def places_in_word(f0, f1, parts=(0, 1, 2, 3)):
+    def power(f0, f1, name, a):
         fs, n = slice(f0, f1), 32 * (f1 - f0)
-        for k in parts:
-            for i in (0, 1):
-                l, x = ((ID, S("IDX", i, fs)), (ID, S("FX", i, slice(32 * f0, 32 * f1))), (S("N15"), S("H1", i, fs)), (S("N15"), S("H2", i, fs)))[k]
-                j = 1 if k == 1 else i
-                mm(C("PW", n * j, n * j + n), l, x, k == 0 and i == 0, k == 3 and i == 1)
-
-    def power(f0, f1):
+        o = lambda i: C(name, a + n * i, a + n * i + n)
+        mms(*[(o(i), ID, S("IDX", i, fs)) for i in (0, 1)], *[(o(1), FXL[i], S("FX", i, slice(32 * f0, 32 * f1))) for i in (0, 1)],
+            *[(o(i), S("N15"), S(h, i, fs)) for h in ("H1", "H2") for i in (0, 1)])
         for i in (0, 1):
-            n = 32 * (f1 - f0)
-            act(S("POW", slice(f0, f1), i), C("PW", n * i, n * i + n), AF.Exp, scale=-7 * math.log(2), bias=21 * math.log(2))
+            act(S("POW", fs, i), o(i), AF.Exp, scale=-7 * math.log(2), bias=21 * math.log(2))
 
-    for t in range(6):
-        mm(C("PN", 0, N2 + 1), S("M"), S("X", t % 2, XW), True, True)
-        if t == 5:
-            for k in range(3):
-                mm(YS(k, 1), S("MN"), S("X", 1, R_), False, k == 2)
-        for x in fill[t]:
-            x()
-        if t == 0:
-            act(S("MN"), S("M"), scale=-256.0)
-            for a in (0, 256):
-                act(C("W", 7 * P + a, 7 * P + a + 256), S("ONE"), scale=128.0)
-            for k, sc in enumerate((0.5, col(CN), col(CH), col(CQ), col(CN))):
-                act(C("DA", 8 * k, 8 * k + 8), S("EF"), scale=sc)
-            mm(W0, S("RF"), C("C0", 0), True, False)
-        if t == 1:
-            mm(YA, ID, C("ZR", 0, 3 * N2), True, False)
-            for k in range(3):
-                mm(YS(k, 1), ID, S("Z", R_), False, False)
-        if t == 2:
-            for k in range(3):
-                mm(YS(k, 1), S("IK"), S("OR", R_), False, False)
-            masks(1, 8)
-            act(S("H1"), S("IDX"), AF.Sign, bias=-2.5)
-            act(S("BT", al, 0), S("BI", 0))
-            act(S("BT", al, 1), S("BI", 1), bias=col(NG))
-            act(C("P0", 0, 32), S("IDX", 0, 0), AF.Exp, scale=-math.log(4), bias=9 * math.log(2))
-            for i in (0, 1):
-                act(S("BM", i), S("BT"), bias=-192.0)
-            act(S("H2", al, slice(0, 2)), S("IDX", al, slice(0, 2)), AF.Sign, bias=-5.5)
-        if t == 3:
-            places_in_word(0, 2, (0,))
-        if t == 4:
-            mm(YA, S("IK"), S("NE"), False, False)
-            for k in range(3):
-                mm(YS(k, 0), ID, SV, False, False)
-        if t < 5:
-            ts(S("X", (t + 1) % 2, XW), S("Z", XW), LAM, A.add, -91.0, A.is_le)
-    ts(S("Y"), C("XY", 256, 256 + 3 * N2), LAM, A.add, -91.0, A.is_le)
-    ts(S("HH", D_), SV, LAM, A.add, -91.0, A.is_le)
-    ts(S("HH", R_), S("Z", D_), LAM, A.add, -91.0, A.is_le)
-    scan(C("PU", 300, 300 + 156), S("Y"), C("ZR", 0, 156), 0.0)
-    tt(S("LD"), C("PN", 0, NN), S("OR", D_), A.is_gt)
-    v01[0]()
-    tt(S("PP"), C("Y", N2, 3 * N2), C("PU", 300 + N2, 300 + 156), A.mult)
-    weave(v01[1:])
-    ts(S("FX", 0), S("IDX", 1), 0.0, A.is_equal)
-    ts(S("FX", 1), S("IDX", 1), 1.0, A.is_equal, -1.0, A.mult)
-    ts(S("BB"), S("E8"), col(GR), A.is_equal)
-    row1 = S("ONE", slice(0, 128), parts=slice(0, 1))
-    DD, D2 = C("PB", 256, 256 + N2), C("PB", 320, 320 + N2)
-    mms((D2, ID, C("KC", N2, 2 * N2)), (D2, S("LA"), S("EQC")))
-    four = lambda name, k: C(name, N2 * k + NN - 2, N2 * k + NN + 2)
-    mm(R4, row1, S("HF"), True, False)
-    for l, k in ((ID, 0), (S("IK"), 0), (S("IK"), 1), (S("IK"), 2)):
-        mm(R4, l, four("Y", k), False, False)
-    mms((DD, ID, C("KC", 0, N2)), (DD, S("LA"), S("EQC")), (DD, S("LA"), S("GEN")),
-        *[(C("PB", 256, 256 + NN), S("LA"), x) for x in (S("HH", D_), S("HH", R_), S("LD"))])
-    for k in (0, 1):
-        mm(R4, ID, four("PP", k), False, k == 1)
-    RK = C("PM", 96, 96 + N2)
-    mms((RK, ID, C("Y", 0, N2)), (RK, ID, C("PP", 0, N2)), (RK, ID, C("PP", N2, 2 * N2)))
-    mms((K0, ID, S("IDX", 1, 0)), *[(K0, ID, S("FX", i, slice(0, 32))) for i in (0, 1)])
-    lo, hi = slice(0, 64), slice(64, 128)
-    act(S("W4"), R4, AF.Exp, scale=math.log(4), bias=col(B0))
-    act(C("DS", N2, 2 * N2, parts=hi), C("PB", 320, 320 + N2, parts=hi))
-    act(C("P0", 32, 64), K0, AF.Exp, scale=-math.log(4), bias=9 * math.log(2))
-    act(C("DS", 0, N2), DD)
-    act(C("DS", N2, 2 * N2, parts=lo), C("PB", 256, 256 + N2, parts=lo))
-
-    def places(f, parts=(0, 1, 2)):
-        pos = C("XY", 128 * (f % 2), 128 * (f % 2) + 128)
-        for k in parts:
-            mm(pos, ID, (S("NV", f), S("BM"), S("H"))[k], k == 0, k == 2)
-
-    def clamps(f, now=True):
-        a = 128 * (f % 2)
+    def places(f):
+        a, r = 128 * (f % 2), 64 * PSLOT[f]
+        pos, half = C("XY", a, a + 128), [C("XY", a + 64 * i, a + 64 * i + 64) for i in (0, 1)]
+        steps = [(pos, ID, S("NV", f))] + [(h, ID, S("BQ" if f else "BT")) for h in half]
+        if f:
+            steps += [(h, C(l, 0, 128), S("GV")) for h, l in zip(half, ("JH", "JM"))] + [(pos, row1, S("MB", k)) for k in (0, 1)]
+        mms(*steps)
         ts(C("CC", 0, 64), C("XY", a, a + 128, 2), 0.0, A.max, 15.0, A.min)
         ts(C("CC", 64, 128), C("XY", a + 1, a + 128, 2), 0.0, A.max, 31.0, A.min)
-        total = lambda: mms((C("PM", 384, 448), S("I32"), C("CC", 0, 64)), (C("PM", 384, 448), ID, C("CC", 64, 128)))
-        return total() if now else total
+        if f < F - 1:
+            tt(C("RV", r, r + 64), half[0], S("BT"), A.subtract)
 
-    def keep(f):
-        r, a = RW * PSLOT[f], 128 * (f % 2)
-        tt(C("REC", r + 32, r + RW), C("XY", a, a + 64), S("BT"), A.subtract)
-
-    def look(f):
-        act(S("U1", f), S("H1", al, f), scale=C("TB", 8 + f), bias=C("TB", f))
-        act(S("U2", f), S("H2", al, f), scale=C("TB", 16 + f))
-
-    def look_sum(f):
-        o = C("PM", 64 * (f % 2), 64 * (f % 2) + 64)
-        mms((o, S("IDF"), S("U1", f)), (o, S("IDF"), S("U2", f)))
-
-    def entries(f):
-        return [
-            lambda: tt(S("XI", f), C("PM", 64 * (f % 2), 64 * (f % 2) + 64), S("POW", f), A.mult),
-            lambda: ts(S("A0", f), S("XI", f, 0), 65024, A.bitwise_and),
-        ]
+    def words(f):
+        if f < 2:
+            for i in range(f + 1):
+                u1, u2 = [S(u, f, slice(32 * i, 32 * i + 32)) for u in ("U1", "U2")]
+                ts(u2, S("H2", i, f), TBP(16 + f), A.mult)
+                ts(u1, S("H1", i, f), TBP(8 + f), A.mult, TBP(f), A.add)
+                tt(u1, u1, u2, A.add)
+                tt(S("XI", f, i), u1, S("POW", f, i), A.mult)
+        else:
+            act(S("U1", f), S("H1", al, f), scale=C("TB", 8 + f), bias=C("TB", f))
+            act(S("U2", f), S("H2", al, f), scale=C("TB", 16 + f))
+            o = C("PM", 64 * (f % 2), 64 * (f % 2) + 64)
+            mms((o, S("IDF"), S("U1", f)), (o, S("IDF"), S("U2", f)))
+            tt(S("XI", f), o, S("POW", f), A.mult)
 
     def record(f):
-        r = RW * PSLOT[f]
-        win = C("REC", RW * wbase(f), RW * (8 if f < 6 else 10))
-        return [
-            lambda: tt(S("G"), IND(win, C("LU", 6 * f, 6 * f + 6)), S("MK", f), A.mult),
-            lambda: (act(C("H", 0, 64), C("G", 32, RW), scale=0.5, bias=191.75),
-                     act(C("H", 64, 128), C("G", 32, RW), scale=-0.5, bias=191.75)),
-            lambda: act(C("G", 0, 32), C("G", 0, 32), bias=(1 - 16 * f) * 65536.0),
-            lambda: tt(S("XI", f, 0), C("G", 0, 32), S("A0", f), A.max),
-            lambda: (ts(C("REC", r, r + 32), S("XI", f, 0), 65024, A.bitwise_and),
-                     ts(S("SS", f % 2), S("XI", f), 7680, A.bitwise_and)),
-        ]
+        r = 32 * PSLOT[f]
+        win = lambda name, w: C(name, w * wbase(f), w * (8 if f < 6 else 10))
+        ts(S("A0", f), S("XI", f, 0), 65024, A.bitwise_and)
+        ts(S("A0", f), S("A0", f), (16 * f - 1) * 65536.0, A.add)
+        tt(S("GV"), IND(win("RV", 64), C("LU", 16 + 4 * f, 20 + 4 * f)), S("MK", f, slice(32, RW)), A.mult)
+        tt(S("GE"), IND(win("RE", 32), C("LU", 2 * f, 2 * f + 2)), S("MK", f, slice(0, 32)), A.mult)
+        places(f)
+        tt(S("XI", f, 0), S("GE"), S("A0", f), A.max)
+        if f < F - 1:
+            ts(C("RE", r, r + 32), S("XI", f, 0), 65024, A.bitwise_and)
+        ts(S("SS", f % 2), S("XI", f), 7680, A.bitwise_and)
+        tot = C("PM", 384, 448)
+        mms((tot, S("I32"), C("CC", 0, 64)), (tot, ID, C("CC", 64, 128)))
+        tt(S("S2"), tot, S("SS", f % 2), A.add)
+        ts(C("OFF", 64 * f, 64 * f + 64), S("S2"), float(-P * wbase(f)), A.add)
 
-    def offsets(f):
-        return [
-            lambda: tt(S("S2"), C("PM", 384, 448), S("SS", f % 2), A.add),
-            lambda: ts(C("OFF", 64 * f, 64 * f + 64), S("S2"), float(-P * wbase(f)), A.add),
-        ]
-
-    pieces = list(zip(CUTS[:-1], CUTS[1:]))
-
-    NP = len(pieces)
-
-    def bank(h):
-        return C(("PA", "PB", "PU", "PN", "PW")[h], 0, pieces[h][1] - pieces[h][0])
-
-    def pixels_start(f, order=(2, 3, 0, 1)):
-        s = 16 * ((f + 1) % 8)
-        for h in order:
-            a, b = pieces[h]
-            mm(bank(h), C("J", s, s + 128), C("RES", f * P + a, f * P + b), True, False)
-            mm(bank(h), row1, C("MQ", 0, b - a), False, False)
-            if f == F - 1 and LASTFIN[h] == "v":
-                mm(bank(h), row1, C("M128", 0, b - a), False, False)
-
-    def pixels_front(f, gap, after=None):
+    def pixels(f):
+        cuts = CUTS if f else CUTS0
+        pieces = list(zip(cuts[:-1], cuts[1:]))
+        sends = SENDS if f else (0, 1)
+        bank = lambda h: C(("PA", "PB", "PU", "PN")[h], 0, pieces[h][1] - pieces[h][0])
         s = 16 * ((f + 1) % 8)
         win = C("W", P * wbase(f), P * (9 + f))
         aw = [("arr%d" % f, narr * (len(SENDS) if f else 1))]
         last = f == F - 1
-        whole = lambda h: last and LASTFIN[h] == "v"
+        big = BIG if f else 1.5 * BIG
         for h, (a, b) in enumerate(pieces):
+            mm(bank(h), C("J", s, s + 128), C("RES", f * P + a, f * P + b), True, False)
+            if f:
+                mm(bank(h), S("MQ"), C("MR", 0, b - a), False, False)
+        for h, (a, b) in enumerate(pieces):
+            if f == 0:
+                for k, name in enumerate(("GP", "G0")):
+                    for c in (a, a + 128):
+                        (cp if k and c > a else act)(C(name, c, c + 128), IND(win, C("OFF", 32 * k + c // 16, 32 * k + c // 16 + 8)), waits=aw)
+                    mm(bank(h), C("JH", s, s + 128), C(name, a, b), False, False)
+                mm(bank(h), S("M4"), one(0, b - a), False, False)
+                mm(bank(h), S("MB", 0), one(0, b - a), False, True)
+                continue
             act(C("GP", a, b), IND(win, C("OFF", 64 * f + a // 16, 64 * f + b // 16)), AF.Relu, scale=-1.0, bias=255.0, waits=aw)
-            ts(C("GQ", a, b), IND(win, C("OFF", 64 * f + 32 + a // 16, 64 * f + 32 + b // 16)), 255.0, A.min, waits=aw)
-            if after:
-                after[h]()
-            mm(bank(h), C("JH", s, s + 128), C("GQ", a, b), False, False)
+            ts(C("GQ", a, b), IND(win, C("OFF", 64 * f + 32 + a // 16, 64 * f + 32 + b // 16)), 255.0, A.min, 767.5, A.add, waits=aw)
             mm(bank(h), C("JM", s, s + 128), C("GP", a, b), False, False)
-            mm(bank(h), row1, C("MR", 0, b - a), False, not whole(h))
-            if whole(h):
+            mm(bank(h), C("JH", s, s + 128), C("GQ", a, b), False, not last)
+            if last:
                 mm(bank(h), row1, C("MZ", 0, b - a), False, True)
-        sent = 0
+        done, parts = 0, []
         for h, (a, b) in enumerate(pieces):
             out = C("SND", f * P + a, f * P + b)
-            gap[h]()
-            if whole(h):
-                ts(out, bank(h), 0.0, A.max, 255.0, A.min)
-            elif (LASTFIN if last else FIN)[h] == "s":
-                act(out, bank(h), AF.Relu, bias=128.0 - BIG)
-            else:
-                ts(out, bank(h), 128.0 - BIG, A.add, 0.0, A.max)
             if last:
-                if not whole(h):
-                    ts(out, out, 255.0, A.min)
-                if h in STORES:
-                    k = STORES.index(h)
-                    dma(("sync", "scalar")[k % 2], T.y[:, f * P + sent:f * P + b], C("SND", f * P + sent, f * P + b), "out%d" % (f + k))
-                    sent = b
-            elif h in SENDS:
-                send(C("W", (9 + f) * P + sent, (9 + f) * P + b), C("SND", f * P + sent, f * P + b), f + 1)
-                sent = b
-
-    halves = ((0, CUTS[SENDS[0] + 1], "PA"), (CUTS[SENDS[0] + 1], P, "PB"))
-
-    def turn_back(f, k):
+                ts(out, bank(h), 0.0, A.max, 255.0, A.min)
+            elif FIN[h] == "s":
+                act(out, bank(h), AF.Relu, bias=-big)
+            else:
+                ts(out, bank(h), -big, A.add, 0.0, A.max)
+            if h in sends:
+                k = sends.index(h)
+                if last:
+                    dma(("sync", "scalar")[k % 2], T.y[:, f * P + done:f * P + b], C("SND", f * P + done, f * P + b), "out%d" % (f + k))
+                else:
+                    send(C("W", (9 + f) * P + done, (9 + f) * P + b), C("SND", f * P + done, f * P + b), f + 1)
+                parts.append((done, b))
+                done = b
+        if last:
+            return
         s = 128 - 16 * (f + 1)
-        a, b, name = halves[k]
-        mm(C(name, WIDE, WIDE + b - a), C("J", s, s + 128), C("SND", f * P + a, f * P + b), True, True)
-
-    def copy_back(f):
-        for a, b, name in halves:
-            act(C("W", PSLOT[f] * P + a, PSLOT[f] * P + b), C(name, WIDE, WIDE + b - a))
+        for (a, b), name in zip(parts, ("PA", "PB")):
+            back = C(name, P - b + a, P)
+            mm(back, C("J", s, s + 128), C("SND", f * P + a, f * P + b), True, True)
+            act(C("W", PSLOT[f] * P + a, PSLOT[f] * P + b), back)
 
     def store(f):
         ts(C("YO", f * P, f * P + P), C("W", PSLOT[f] * P, PSLOT[f] * P + P), 255.0, A.min)
-        dma("sync", T.y[:, f * P:f * P + P], C("YO", f * P, f * P + P), "out%d" % f, [("snt%d" % k, neng * len(SENDS)) for k in range(f + 1, min(f + 3, F))])
+        dma("sync", T.y[:, f * P:f * P + P], C("YO", f * P, f * P + P), "out%d" % f, [sent(k) for k in range(f + 1, min(f + 3, F))])
 
-    r0 = RW * PSLOT[0]
-    TBP = lambda a, b=None: C("XX", 256 + a, None if b is None else 256 + b)
+    lists(0, 2)
+    vec(0, 2)
+    masks(1, 2)
+    I0, TOT0 = C("XY", 256, 320), C("XY", 448, 512)
+    mms((C("XY", 256, 288), ID, S("IDX", 0, 0)), (C("XY", 288, 320), ID, S("IDX", 1, 0)),
+        *[(C("XY", 288, 320), FXL[i], S("FX", i, slice(0, 32))) for i in (0, 1)])
     places(0)
-    for k in range(6):
-        ts(S("EW", k), RK, C("TG", k), A.is_equal, C("WK", k % 3), A.mult)
-    for k in range(4):
-        mm(W0, S("BB"), C("W4", k), False, k == 3)
-    for k in range(6):
-        o = C("PN", 64 + N2 * (k // 3), 64 + N2 * (k // 3) + N2)
-        mm(o, ID, S("EW", k), k % 3 == 0, k % 3 == 2)
-    ts(S("DL"), S("F48"), col(FP), A.is_equal, col(CH), A.mult)
-    a = clamps(0, False)
-    ts(S("X0"), S("P0"), W0, A.mult, -1.0, A.mult)
-    a()
-    ts(S("SS", 0), S("X0"), 1536, A.bitwise_and)
-    tt(S("EP"), C("PN", 64, 64 + 2 * N2), S("DS"), A.mult)
-    keep(0)
-    tt(S("S2"), C("PM", 384, 448), S("SS", 0), A.add)
-    red(C("SM", 4), C("EP", 0, N2))
-    red(C("SM", 5), C("EP", N2, 2 * N2))
-    cp(C("OFF", 0, 64), S("S2"))
-    ts(S("RA"), C("DA", 0, 24), C("SM", 4), A.mult)
-    ts(S("RB"), C("DA", 24, 40), C("SM", 5), A.mult)
-    act(S("BO"), S("BB"))
-    act(S("H2", al, slice(2, 8)), S("IDX", al, slice(2, 8)), AF.Sign, bias=-5.5)
-    places_in_word(0, 2, (1, 2, 3))
-    act(S("CL"), S("CL"), bias=col(NG))
-    ts(S("RL"), S("DL"), C("SM", 5), A.mult, RW / 256.0, A.mult)
-    pixels_start(0, (0, 2))
-    mms((TBP(0, 24), S("IDF"), S("CS")), (TBP(0, 24), S("BO"), S("RA")), (TBP(8, 24), S("BO"), S("RB")))
-    pixels_start(0, (1, 3))
-    mms((C("PM", 280, 328), S("IDF"), S("CL")), (C("PM", 280, 328), S("BO"), S("RL")))
-    first = [
-        lambda: power(0, 2),
-        lambda: (ts(S("U2", 0, slice(0, 32)), S("H2", 0, 0), TBP(16), A.mult), ts(S("U1", 0, slice(0, 32)), S("H1", 0, 0), TBP(8), A.mult, TBP(0), A.add)),
-        lambda: (tt(S("U1", 0, slice(0, 32)), S("U1", 0, slice(0, 32)), S("U2", 0, slice(0, 32)), A.add), act(S("TB"), TBP(0, 24))),
-        lambda: tt(S("XI", 0, 0), S("U1", 0, slice(0, 32)), S("POW", 0, 0), A.mult),
-    ]
+    for k, (c, v) in enumerate(((C("SM", 2), -2.0 * P), (C("SM", 3), -1.0 * P), (8.0, 1.0 * P))):
+        ts(S("AB", k), I0, c, A.is_equal, v, A.mult)
+    mms((TOT0, S("I32"), C("CC", 0, 64)), (TOT0, ID, C("CC", 64, 128)), *[(TOT0, ID, S("AB", k)) for k in range(3)])
+    ts(C("OFF", 0, 64), TOT0, 2.0 * P, A.add)
+    power(0, 2, "XY", 320)
+    words(0)
+    words(1)
+    cp(S("LU"), C("PU", 0, 48))
+    act(S("TB"), TBP(0, 24))
+    ts(C("RE", 32 * PSLOT[0], 32 * PSLOT[0] + 32), S("XI", 0, 0), 65024, A.bitwise_and)
+    lists(2, 8)
+    masks(2, 8)
+    power(2, 5, "PW", 0)
+    power(5, 8, "PW", 192)
     for f in range(F):
-        g = f + 1
-        nop = lambda: None
-        if f == F - 1:
-            pixels_front(f, [nop] * 4)
-            break
-        r = record(g)
-        e = entries(g)
-        v = vec(2 * f + 2, 2 * f + 4) if f < 3 else [nop] * 4
-        if f == 0:
-            pixels_front(f, [lambda: (cp(S("LU"), C("PM", 280, 328)), ts(C("REC", r0, r0 + 32), S("XI", 0, 0), 65024, A.bitwise_and)), lambda: look(1), r[0], nop], first)
-            look_sum(1)
-            weave(r[1:3], e)
-        else:
-            pixels_front(f, [lambda: (r[0](), e[0]()), nop, e[1], r[1]])
-            r[2]()
-        if f:
-            places(g)
-        turn_back(f, 0)
-        if f == 0:
-            places(g)
-        turn_back(f, 1)
-        copy_back(f)
-        clamps(g)
-        r[3]()
-        keep(g)
-        v[0]()
-        r[4]()
-        if f in (0, 2):
-            places_in_word(*((2, 5) if f == 0 else (5, 8)))
-        pixels_start(g)
-        v[1]()
-        weave(offsets(g), v[2:])
-        if f:
-            store(f - 1)
+        pixels(f)
+        if f in (0, 1):
+            a, b = ((3, 5), (5, 8))[f]
+            dma("sync", C("RES", a * P, b * P), T.res[:, a * P:b * P], "res%d" % a, [sent(f + 1)])
+        if f < 3:
+            vec(2 * f + 2, 2 * f + 4)
+        if f < F - 1:
+            record(f + 1)
         if f + 2 < F:
-            look(f + 2)
-            look_sum(f + 2)
-        if f in (0, 2):
-            power(*((2, 5) if f == 0 else (5, 8)))
-        if f == 4:
-            for name, v in (("MZ", -BIG), ("M128", 128.0)):
-                act(C(name, 0, WIDE), S("ONE", slice(0, WIDE), parts=slice(0, 1)), scale=v)
+            words(f + 2)
+        if 0 < f < F - 1:
+            store(f - 1)
         if f == F - 2:
             store(f)
-    return ops, neng, narr
+    return ops
 
 
-def emit(g, T, ops, neng, narr):
+def schedule(ops):
+    n = len(ops)
+    queue = [{"scalar": "act"}.get(o[0], o[0]) for o in ops]
+    pre = [{} for o in ops]
+    acc, raised = {}, {}
+    for j, (q0, fn, rd, wr, waits, sem, cost) in enumerate(ops):
+        q = queue[j]
+        for s, v in waits:
+            for i in raised.get(int(s[3:]), ()):
+                pre[j][i] = HOP + COL * (P - int(ops[i][2][0][1].min()) % P)
+        for name, el, w in [(a, e, False) for a, e in rd] + [(a, e, True) for a, e in wr]:
+            lo, hi = int(el.min()), int(el.max())
+            for i, pw, plo, phi, pel in acc.get(name, ()):
+                same = queue[i] == q and ops[i][5] is None and sem is None
+                clash = (w or pw) and plo <= hi and lo <= phi
+                if i == j or not (clash or name in PS_ and (not same or q == "pe")):
+                    continue
+                if same and q == "pe":
+                    pre[j].setdefault(i, 0.0)
+                elif not (same and w) or np.intersect1d(el, pel).size:
+                    for k in ([i] if ops[i][5] not in DMAS else [k for k in range(n) if ops[k][5] == ops[i][5]]):
+                        if sem is None or ops[k][5] != sem:
+                            pre[j][k] = WAKE
+            acc.setdefault(name, []).append((j, w, lo, hi, el))
+        if isinstance(sem, int):
+            raised.setdefault(sem, []).append(j)
+    for q in ("sync", "pool"):
+        l = [j for j in range(n) if queue[j] == q]
+        for i, j in zip(l, l[1:]):
+            pre[j].setdefault(i, None)
+    span = [o[6] for o in ops]
+    unit = ["dma" if o[5] in DMAS else q for o, q in zip(ops, queue)]
+    land = [LAND if u == "dma" else 0.0 for u in unit]
+    lag = [{i: (0.0 if land[j] else span[i]) if d is None else span[i] + d + land[j] for i, d in pre[j].items()} for j in range(n)]
+    back = [{} for o in ops]
+    for j in range(n):
+        for i, d in lag[j].items():
+            back[i][j] = d + span[j] - span[i] + (EARLY if ops[i][5] == 1 and unit[j] != "pool" else 0.0)
+
+    def place(edges, rank, first):
+        post = [[] for o in ops]
+        for j in range(n):
+            for i in edges[j]:
+                post[i].append(j)
+        left = [len(e) for e in edges]
+        todo = [(rank[j], j) for j in range(n) if not left[j]]
+        start, busy = [0.0] * n, {u: [] for u in unit}
+        while todo:
+            j = min(todo)[1]
+            todo.remove((rank[j], j))
+            t = max([first[j]] + [start[i] + d for i, d in edges[j].items()])
+            l = busy[unit[j]]
+            k = 0
+            while k < len(l) and l[k][0] < t + span[j] - 1e-9:
+                t = max(t, l[k][1])
+                k += 1
+            l.insert(k, (t, t + span[j]))
+            start[j] = t
+            for k in post[j]:
+                left[k] -= 1
+                if not left[k]:
+                    todo.append((rank[k], k))
+        return start
+
+    def behind(seeds):
+        seen, todo = set(seeds), list(seeds)
+        while todo:
+            for i in pre[todo.pop()]:
+                if i not in seen:
+                    seen.add(i)
+                    todo.append(i)
+        return seen
+
+    first = behind([j for j in range(n) if ("OFF", 64) in [(a, int(e.min())) for a, e in ops[j][3]]])
+    second = behind([j for j in range(n) if ops[j][5] == 1])
+    group = [0 if j in first else 1 if j in second else 2 for j in range(n)]
+    start, best = [float(j) for j in range(n)], None
+    for k in range(3):
+        late = place(back, [-start[j] - span[j] for j in range(n)], [0.0] * n)
+        start = place(lag, [100 * group[j] - late[j] - span[j] for j in range(n)], land)
+        end = max(start[j] + span[j] for j in range(n))
+        if best is None or end < best[0]:
+            best = (end, start)
+    issue = list(best[1])
+    for j in range(n):
+        if land[j]:
+            issue[j] = max([0.0] + [issue[i] if pre[j][i] is None else best[1][i] + d - LAND for i, d in lag[j].items()])
+    return [ops[j] for j in sorted(range(n), key=lambda j: (issue[j], j))]
+
+
+def emit(g, T, ops):
     eng = {"dve": g.vector, "act": g.scalar, "pe": g.tensor, "pool": g, "sync": g.sync, "scalar": g.scalar}
     queue = {"scalar": "act"}
     total = {}
@@ -590,7 +631,7 @@ def emit(g, T, ops, neng, narr):
     known = {}
     acc = {}
     waited = {}
-    for q0, fn, rd, wr, waits, sem in ops:
+    for q0, fn, rd, wr, waits, sem, cost in ops:
         q = queue.get(q0, q0)
         need = {}
         for s, v in waits:
@@ -621,8 +662,8 @@ def emit(g, T, ops, neng, narr):
                 seen[q][s] = v
                 for s2, v2 in known.get((s, v), {}).items():
                     seen[q][s2] = max(seen[q].get(s2, 0), v2)
-        ins = fn(eng[q0]) if fn else None
-        if sem == "remote":
+        ins = fn(eng[q0])
+        if isinstance(sem, int):
             continue
         if sem is None:
             count[q] += 1
@@ -651,5 +692,4 @@ def rank_program(g, core, T, topo):
     eng = topo.engines(core, dst)
     half = [sum(1 << e for e in part) for part in (eng[:len(eng) // 2], eng[len(eng) // 2:])]
     nxt = (rid, pid, topo.mask(core, dst), len(topo.engines(src, core)), half)
-    ops, neng, narr = build(T, nxt)
-    emit(g, T, ops, neng, narr)
+    emit(g, T, schedule(build(T, nxt)))

@@ -1,56 +1,62 @@
-import math
 import numpy as np
 from concourse.mybir import AluOpType as A, AxisListType, ActivationFunctionType as AF
 
 F = 8
 P = 512
 CUTS = [0, 160, 288, 416, 512]
-CUTS0 = [0, 256, 512]
-FIN = "vsvs"
+FIN = ("sssv", "vsvs")
 SENDS = (1, 3)
 BIG = 8388608.0
 NN = 26
 N2 = 2 * NN
+N3 = 3 * N2
 N0 = 12
 RW = 96
+DS_, DB = 261627 / 2.0 ** 18, 509 / 2.0 ** 18
+US, UB = 11629 / 2.0 ** 14, 5725 / 2.0 ** 14
 
 f32, bf, i32, u16, f16 = "float32", "bfloat16", "int32", "uint16", "float16"
 SB_ = {
     "W": ([128, 16 * P], bf), "RES": ([128, F * P], bf), "SND": ([128, F * P], bf), "YO": ([128, 7 * P], bf),
-    "GP": ([128, P], bf), "GQ": ([128, P], f16), "G0": ([128, P], bf), "M4": ([1, 128], bf),
+    "GP": ([128, P], bf), "GQ": ([128, P], f16),
     "IA": ([128, 256], i32), "IB": ([128, 256], i32), "VY": ([128, 8, 2, 32], i32), "VX": ([128, 8, 2, 32], i32),
-    "CT": ([128, 8], i32), "EB": ([128, 8], bf), "CA": ([128, 4], f32), "CF": ([128, 4], f32),
-    "ONE": ([128, 256], bf), "MR": ([1, 192], bf), "MZ": ([1, 192], bf), "MQ": ([1, 128], bf), "MB": ([1, 2, 128], bf),
-    "ID": ([128, 128], bf), "IK": ([128, 128], bf), "MN": ([128, 128], bf), "NE": ([128, 3 * N2], bf), "J": ([128, 256], bf),
-    "JH": ([128, 256], bf), "JM": ([128, 256], bf), "N15": ([128, 128], bf), "I32": ([128, 128], bf),
-    "E8": ([128, 128], bf), "EA": ([128, 128], bf), "BO": ([128, 128], f32), "IDF": ([128, 128], f32),
-    "L0": ([128, 128], bf), "LE": ([128, 128], bf), "LT": ([128, 128], bf), "M": ([128, 128], bf), "TR": ([NN, 256], bf),
-    "LA": ([128, 128], bf), "BLK": ([128, 128], bf), "SEL": ([128, 128], bf),
-    "PI": ([128, 8], i32), "PC": ([128, 24], f32), "F8": ([128, 8], f32), "F48": ([128, 48], f32), "EF": ([128, 8], f32), "TG": ([128, 6], bf),
-    "NR": ([128, N2], bf), "OM": ([128, N2], bf), "OR": ([128, N2], bf), "E0": ([128, N2], bf), "EQC": ([128, N2], bf),
-    "GEN": ([128, N2], bf), "TA": ([128, 8, NN], f32), "X": ([128, 2, 56], bf), "Z": ([128, 56], bf), "SV": ([128, NN], bf),
-    "HH": ([128, N2], bf), "LD": ([128, NN], bf), "Y": ([128, 3 * N2], bf), "ZR": ([128, 256], bf), "WK": ([128, 4], bf), "PP": ([128, 104], bf),
-    "EW": ([128, 6, N2], bf), "DS": ([128, 104], f32), "EP": ([128, 104], f32),
-    "KC": ([128, 104], bf), "KT": ([128, N2], f32), "DA": ([128, 40], f32), "DL": ([128, 48], f32),
+    "CT": ([128, 8], i32), "CB": ([128, 8], bf), "CA": ([128, 8], f32),
+    "ONE": ([128, 128], bf), "MR": ([1, 192], bf), "MZ": ([1, 192], bf), "MQ": ([1, 128], bf), "MB": ([1, 2, 128], bf),
+    "NG": ([1, 128], bf), "CY": ([1, 4 * N2 + 8], bf), "CI": ([1, 2, 64], bf),
+    "VA": ([128, 128], bf), "VN": ([128, 128], bf), "VI_": ([128, 128], bf), "VS": ([128, 128], bf),
+    "GL": ([128, 3, 128], bf), "CW": ([128, 128], bf), "BW": ([128, 128], bf),
+    "J": ([128, 256], bf), "JH": ([128, 256], bf), "JM": ([128, 256], bf), "N15": ([128, 128], bf), "I32": ([128, 128], bf),
+    "BO": ([128, 128], f32), "IDF": ([128, 128], f32), "LE": ([128, 128], bf), "LT": ([128, 128], bf), "M": ([128, 128], bf),
+    "LA": ([128, 128], bf), "SEL": ([128, 2, 128], bf),
+    "PI": ([128, 8], i32), "PC": ([128, 32], f32), "F48": ([128, 48], f32), "EF": ([128, 8], f32),
+    "NR": ([128, N2], bf), "OM": ([128, N2], bf), "OR": ([128, N2], bf), "EQ": ([128, 2, N2], bf), "EQC": ([128, N2], bf),
+    "GEN": ([128, N2], bf), "TA": ([128, 8, 32], bf), "X": ([128, 2, 56], bf), "Z": ([128, 56], bf),
+    "Y": ([128, 2, N3 + 4], bf), "YH": ([128, N2], bf), "RK": ([128, N3], bf), "SQ": ([128, 2, N3], f32), "EW": ([128, 2, N3], bf),
+    "DS": ([128, 104], f32), "EP": ([128, 104], f32), "KT": ([128, N2], bf),
+    "DA": ([128, 40], f32), "DL": ([128, 48], f32),
     "RA": ([128, 24], f32), "RB": ([128, 16], f32), "RL": ([128, 48], f32), "CS": ([128, 24], f32), "CL": ([128, 48], f32),
-    "TB": ([128, 24], f32), "LU": ([128, 48], u16), "SM": ([128, 8], f32),
-    "HB": ([128, 32], f32), "HI": ([128, 32], i32), "BITS": ([128, 32], bf), "XH": ([128, 64], bf), "VI": ([128, 64], bf),
-    "TN": ([128, N0], bf), "K5": ([128, 5, N0], bf), "GK": ([128, 2, N0], bf), "AB": ([128, 3, 64], bf),
-    "IDX": ([128, 2, 8, 32], bf), "H1": ([128, 2, 8, 32], bf), "H2": ([128, 2, 8, 32], bf), "FX": ([128, 2, 256], bf), "POW": ([128, 8, 2, 32], bf),
-    "NV": ([128, 8, 2, 32, 2], bf), "BI": ([128, 2, 32], f32), "BT": ([128, 32, 2], bf), "BQ": ([128, 64], bf),
-    "MK": ([128, 8, RW], bf), "U1": ([128, 8, 64], f32), "U2": ([128, 8, 64], f32), "XI": ([128, 8, 2, 32], i32), "A0": ([128, 8, 32], i32),
+    "TB": ([128, 24], f32), "LU": ([128, 48], u16), "SM": ([128, 16], f32), "SH": ([128, 8], bf),
+    "HB": ([128, 32], bf), "HI": ([128, 32], i32), "BITS": ([128, 32], bf), "XH": ([128, 32], bf), "VI": ([128, 64], bf),
+    "KS": ([128, 3, 16], f32), "JK": ([128, 8, 16], bf), "SR": ([128, 16], f32), "AB": ([128, 7, 64], bf), "OK": ([128, 4, 32], bf),
+    "ON": ([128, 64], bf), "PX": ([128, 64], bf), "XB": ([128, 3, 32], f32), "GW": ([128, 64], bf),
+    "IDX": ([128, 2, 8, 32], bf), "H1": ([128, 2, 8, 32], bf), "H2": ([128, 2, 8, 32], bf), "FX": ([128, 2, 256], bf),
+    "PQ": ([128, 2, 8, 32], f32), "POW": ([128, 2, 8, 32], bf),
+    "NV": ([128, 8, 2, 32, 2], bf), "BT": ([128, 32, 2], bf), "BQ": ([128, 64], bf),
+    "MK": ([128, 8, RW], bf), "U0": ([128, 128], f32), "U1": ([128, 8, 64], f32), "U2": ([128, 8, 64], f32), "XI": ([128, 8, 2, 32], i32), "A0": ([128, 8, 32], i32),
     "SS": ([128, 2, 64], i32), "RE": ([128, 11 * 32], i32), "RV": ([128, 11 * 64], bf), "GE": ([128, 32], f32), "GV": ([128, 64], bf),
-    "CC": ([128, 128], bf), "BB": ([128, 128], bf), "S2": ([128, 64], i32), "OFF": ([128, F * 64], u16),
+    "CC": ([128, 128], bf), "S2": ([128, 64], i32), "OFF": ([128, F * 64], u16),
 }
 PS_ = ["PA", "PB", "PU", "XY", "XX", "PM", "PN", "PW"]
 SCRATCH = {k: ("sbuf", v[0], v[1]) for k, v in SB_.items()}
 SCRATCH.update({k: ("psum", [128, P], f32) for k in PS_})
-DMAS = ["ctl", "pic", "pi0", "ia_", "ib_", "vy_", "vx_", "res0", "res1", "res3", "res5", "vy2", "vx2"] + ["out%d" % f for f in range(F + 1)]
+DMAS = ["ctl", "pic", "pi0", "ia_", "ib_", "vy_", "vx_", "ia2", "ib2", "vy2", "vx2", "res0", "res1", "res2", "res3", "res5"] + ["out%d" % f for f in range(F + 1)]
 SEMAPHORES = ["dve", "act", "pe", "pool"] + DMAS + ["arr%d" % f for f in range(F)] + ["snt%d" % f for f in range(F)]
 
 PSLOT = [4, 3, 2, 1, 0, 9, 8, 10]
 
-CYC, WAKE, LAND, HOP, COL, EARLY = 0.0009, 0.24, 1.2, 1.2, 0.001, 2.0
+CYC, WAKE, LAND, HOP, COL = 0.0009, 0.24, 1.2, 1.2, 0.001
+ROUNDS = 1000
+ORDER = []
 WIDTH = {f32: 4, i32: 4, bf: 2, u16: 2, f16: 2}
 
 
@@ -114,15 +120,19 @@ def build(T, nxt):
     def ms(o, c):
         add("dve", lambda e: e.memset(o[0], c), [o], [])
 
-    def red(o, i, op=A.add):
-        add("dve", lambda e: e.tensor_reduce(o[0], i[0], AxisListType.X, op), [o], [i], rate=0)
+    def red(o, i, op=A.add, negate=False):
+        add("dve", lambda e: e.tensor_reduce(o[0], i[0], AxisListType.X, op, negate=negate), [o], [i], rate=0)
 
-    def scan(o, d0, d1, ini):
-        add("dve", lambda e: e.tensor_tensor_scan(o[0], d0[0], d1[0], val(ini), A.add, A.add), [o], [d0, d1, ini])
+    def scan(o, d0, d1, ini, op1=A.add):
+        add("dve", lambda e: e.tensor_tensor_scan(o[0], d0[0], d1[0], val(ini), A.add, op1), [o], [d0, d1, ini])
 
-    def act(o, i, func=AF.Identity, bias=0.0, scale=1.0, waits=(), first=False):
-        add("act", lambda e: e.activation(o[0], i[0], func, bias=val(bias), scale=val(scale)), [o], [i, bias, scale], waits,
-            rate=1.3 if first else None)
+    def act(o, i, func=AF.Identity, bias=0.0, scale=1.0, waits=(), first=False, acc=None):
+        if acc is None:
+            add("act", lambda e: e.activation(o[0], i[0], func, bias=val(bias), scale=val(scale)), [o], [i, bias, scale], waits,
+                rate=1.3 if first else None)
+        else:
+            add("act", lambda e: e.activation(o[0], i[0], func, bias=val(bias), scale=val(scale), accum_out=acc[0]), [o, acc],
+                [i, bias, scale], waits, rate=0.02)
 
     def mm(o, l, r, st, sp):
         add("pe", lambda e: e.matmul(o[0], l[0], r[0], st, sp), [o], [l, r])
@@ -137,11 +147,9 @@ def build(T, nxt):
         else:
             add("pool", lambda e: e.iota(o[0], pat, base, cm, allow_small_or_imprecise_dtypes=True), [o], [])
 
-    def sel(name, pat, src="ONE", op=A.is_equal, fill=0.0, cm=-1):
-        o = S(name)
-        n, w = SCRATCH[name][1]
-        i = S(src, slice(0, w), parts=slice(0, n))
-        add("pool", lambda e: e.affine_select(o[0], i[0], pat, op, fill, 0, cm), [o], [i])
+    def diag(o, v):
+        i = C("J", 0, 128)
+        add("pool", lambda e: e.affine_select(o[0], i[0], [[1, 128]], A.not_equal, v, 0, -1), [o], [i])
 
     def dma(q, o, i, sem, waits=()):
         add(q, lambda e: e.dma_start(val(o), val(i)), [o] if isinstance(o, tuple) else [], [i], waits, sem)
@@ -154,9 +162,13 @@ def build(T, nxt):
     narr = nxt[3]
     sent = lambda k: ("snt%d" % k, neng * (len(SENDS) if k else 1))
     col = lambda k: C("PC", k)
-    PF, FP, HALF, G16, GR, NG, F0, KA, W16, CN, CH, CQ, KCB, WS, T0, T1, T2, L2, W7, CL0, CL1 = range(21)
+    (FP, P71, L16, HALF, W16, F0, NF2, C23, W2, CWB, LB, L2, A5, T0, KCB, SG, T2, WS, CN, CH, CQ, CL0, CL1, SB0, SB1, SC1, L32, K0, K1, KB) = range(30)
     D_, R_ = slice(0, NN), slice(NN, N2)
-    one = lambda a, b: C("ONE", a, b, parts=slice(0, 1))
+    N0_ = slice(NN - N0, NN)
+    lo, hi, row = slice(0, 64), slice(64, 128), slice(0, 1)
+    one = lambda a, b: C("ONE", a, b, parts=row)
+    row1 = one(0, 128)
+    ID, NH = C("J", 0, 128), C("JM", 0, 128)
 
     for h, q in enumerate(("sync", "scalar")):
         pp = slice(64 * h, 64 * h + 64)
@@ -164,199 +176,98 @@ def build(T, nxt):
         dma(q, C("CT", 1, parts=pp), T.cmd[:], "ctl")
         dma(q, C("CT", 2, 5, parts=pp), T.rel[:], "ctl")
     dma("sync", C("W", 6 * P, 7 * P), T.pic0[:, P:2 * P], "pic")
-    dma("scalar", S("IA"), T.ia[:], "ia_")
-    dma("sync", S("IB"), T.ib[:], "ib_")
-    dma("sync", S("VY", slice(0, 2)), T.vy[:, 0:128], "vy_")
-    dma("sync", S("VX", slice(0, 2)), T.vx[:, 0:128], "vx_")
+    dma("sync", C("IA", 0, 96), T.ia[:, 0:96], "ia_")
+    dma("sync", C("IB", 0, 96), T.ib[:, 0:96], "ib_")
+    dma("sync", S("VY", slice(0, 3)), T.vy[:, 0:192], "vy_")
+    dma("sync", S("VX", slice(0, 3)), T.vx[:, 0:192], "vx_")
     dma("sync", C("W", 5 * P, 6 * P), T.pic0[:, 0:P], "pi0")
     dma("sync", C("RES", 0, P), T.res[:, 0:P], "res0")
+    dma("sync", C("RES", P, 2 * P), T.res[:, P:2 * P], "res1", [sent(0)])
+    dma("sync", C("IA", 96, 256), T.ia[:, 96:256], "ia2")
+    dma("sync", C("IB", 96, 256), T.ib[:, 96:256], "ib2")
 
     ms(S("ONE"), 1.0)
-    ms(S("ZR"), 0.0)
-    for a in (0, 256):
-        act(C("W", 7 * P + a, 7 * P + a + 256), S("ONE"), scale=128.0)
     iota(C("PI", 0), [[0, 1]], 0, 1)
-    iota(S("NR", R_), [[1, NN]], -1)
-    sel("L0", [[0, 2], [1, 64]], op=A.is_ge)
-    sel("ID", [[1, 128]])
-    sel("LE", [[0, 2], [-8, 8], [0, 8]], "L0", A.is_ge, cm=1)
+    iota(S("VN"), [[0, 2], [16, 8], [1, 8]], 0, -1)
     iota(S("HB"), [[1, 32]], 0)
-    sel("LT", [[0, 2], [1, 64]], "LE", A.is_gt)
-    iota(S("EA"), [[0, 2], [1, 8], [0, 8]], 0)
+    iota(S("VI_"), [[1, 128]], 0, -1)
+    iota(S("VA"), [[0, 2], [-8, 8], [0, 8]], 0, 1)
+    iota(S("VS"), [[-8, 8], [0, 16]], 0, 1)
     for k in (0, 1):
         a, b = k * P // 2, (k + 1) * P // 2
         send(C("W", 8 * P + a, 8 * P + b), C("W", 6 * P + a, 6 * P + b), 0, nxt[4][k], k == 0)
-    dma("sync", C("RES", P, 3 * P), T.res[:, P:3 * P], "res1", [sent(0)])
-    dma("sync", S("VY", slice(2, 8)), T.vy[:, 128:512], "vy2")
-    dma("sync", S("VX", slice(2, 8)), T.vx[:, 128:512], "vx2")
-    iota(S("E8"), [[1, 8], [0, 16]], 0)
-    iota(S("BI", 0), [[1, 16], [0, 2]], 0)
-    iota(S("BI", 1), [[0, 16], [16, 2]], 0, 1)
-    iota(S("F8"), [[1, 8]], 0)
-    for a, k in ((0, 2), (16, 4)):
-        iota(C("F48", a, a + 8 * k), [[1, 8], [0, k]], 0)
-        iota(C("CL", a, a + 8 * k), [[0, 8], [16, k]], 0, 1)
-    iota(C("RE", 5 * 32, 9 * 32), [[0, 4 * 32]], 0)
-    act(C("RV", 5 * 64, 9 * 64), S("ZR"))
-    ts(C("PI", 1), C("PI", 0), 7, A.bitwise_and)
-    ts(C("PI", 2), C("PI", 0), 6, A.arith_shift_right)
-    ts(C("PI", 3), C("PI", 0), 112, A.bitwise_and)
-    ts(C("PI", 4), C("PI", 0), 3, A.arith_shift_right, 7, A.bitwise_and)
-    cp(C("PC", 0, 5), C("PI", 0, 5))
-    ts(S("NR", D_), S("NR", R_), -1.0, A.mult, 23.0, A.add)
-    ts(col(F0), col(FP), 0.0, A.is_equal)
-    for k, sc, bi in ((CN, 0.5, -0.5), (CH, 0.5, 0.0), (CQ, -0.5, 0.5), (W16, -16.0, 16.0), (KA, 6.0, 1.0), (CL0, 1.0 / 16, 0.0), (CL1, 1.0 / 8, 0.0)):
-        act(col(k), col(HALF), scale=sc, bias=bi)
-    act(col(NG), col(G16), scale=-1.0)
-    act(S("WK"), C("NR", NN + 1, NN + 5), AF.Exp, scale=7 * math.log(2), bias=9 * math.log(2), first=True)
-    act(C("WK", 3), col(FP), AF.Exp, scale=-math.log(2), bias=7 * math.log(2))
-    for o, v in ((S("MR"), 151.0 * 256), (S("MQ"), 217.0), (S("MB", 0), 1.5 * BIG), (S("MB", 1), -1.5 * BIG), (S("MZ"), -BIG), (S("M4"), 0.25)):
-        act(o, one(0, len(o[2])), scale=v)
-    ts(col(T0), col(FP), 5.0, A.min, 18.0, A.add)
-    ts(col(T1), col(FP), 5.0, A.is_ge, 10.0, A.mult)
-    act(col(KCB), col(T0), scale=col(HALF), bias=-16.0)
-    act(col(T2), col(FP), scale=-1.0, bias=col(T1))
-    act(col(WS), col(T2), scale=1.0 / 16, bias=-3.0 / 16)
-    ts(col(L2), col(FP), 2.0, A.is_lt)
-    ts(col(W7), col(FP), 7.0, A.not_equal, col(W16), A.mult)
-    ts(S("EF"), S("F8"), col(FP), A.is_equal)
-    act(S("TG"), C("F8", 0, 6), bias=col(KA))
-    act(C("TG", 3), col(HALF), scale=-2.0, bias=4.0)
-    act(C("CS", 0, 8), S("F8"), scale=4194304.0, bias=7.0 * 16513 * 512 + 4194304.0)
-    act(C("CS", 8, 16), S("F8"), scale=0.0)
-    act(C("CS", 16, 24), S("F8"), scale=4194304.0, bias=4194304.0)
-    ID = S("ID")
-    for o, v in ((S("IK"), 1024.0), (S("N15"), -1.5), (C("J", 0, 128), 1.0), (C("J", 128, 256), 1.0), (S("IDF"), 1.0), (S("I32"), 32.0)):
-        act(o, ID, scale=v)
-    ts(S("JH"), S("J"), 0.5, A.mult)
-    ts(S("JM"), S("J"), -0.5, A.mult)
-    ts(S("SEL"), S("E8"), 8.0, A.mult, col(PF), A.is_equal)
-    ts(S("BB"), S("E8"), col(GR), A.is_equal)
-    act(S("BO"), S("BB"))
-    ts(S("LA"), S("EA"), col(GR), A.is_equal, col(W16), A.mult)
-    ts(S("BLK"), S("EA"), col(GR), A.is_equal, col(W7), A.mult)
-    ts(S("HI"), S("HB"), C("WK", 3), A.mult)
+    for k, v in ((5, 120), (1, 7), (2, 71), (3, 15)):
+        ts(C("PI", k), C("PI", 0), v, A.bitwise_and)
+    ts(col(K0), C("PI", 5), -1532.5, A.add)
+    ts(col(K1), C("PI", 5), -1531.5, A.add)
+    ts(C("PI", 4), C("PI", 0), 6, A.arith_shift_right)
+    cp(C("PC", 0, 4), C("PI", 1, 5))
+    act(col(F0), col(FP), AF.Relu, scale=-1.0, bias=1.0)
+    act(col(NF2), col(FP), scale=-1.0, bias=-2.0)
+    act(col(C23), col(FP), scale=-1.0, bias=23.0)
+    act(col(W16), col(HALF), scale=-16.0, bias=16.0)
+    for k, name in enumerate(("LE", "LT")):
+        ts(S("GL", k), S("VN"), col(K0 + k), A.subtract, 0.125, A.mult)
+        ts(S(name), S("GL", k), 192.0, A.is_equal)
+    ts(S("LA"), S("VA"), col(P71), A.is_equal, col(W16), A.mult)
+    ts(ID, S("VI_"), 0.0, A.is_equal)
+    act(NH, ID, scale=-0.5)
+    act(S("I32"), ID, scale=32.0)
+    for o, v in ((C("J", 128, 256), 1.0), (C("JM", 128, 256), -0.5), (C("JH", 0, 128), 0.5), (C("JH", 128, 256), 0.5), (S("N15"), -3.0)):
+        diag(o, v)
+    act(S("IDF"), ID)
+    for a in range(0, P, 128):
+        act(C("W", 7 * P + a, 7 * P + a + 128), S("ONE"), scale=128.0)
+    for o, v in ((S("MR"), 151.0 * 256), (S("MQ"), 217.0), (S("MB", 0), 1.5 * BIG), (S("MB", 1), -1.5 * BIG),
+                 (S("CY"), 56.0), (C("CY", 1, 1 + N2), 1080.0), (C("CY", 1 + N2, 1 + 2 * N2), 568.0), (S("CI", 0), -11.0), (S("CI", 1), 53.5)):
+        ms(o, v)
+    act(S("NR", R_), C("HB", 0, NN), bias=col(NF2))
+    act(S("NR", D_), C("HB", 0, NN), scale=-1.0, bias=col(C23))
+    ts(C("KT", 0, 8), C("HB", 0, 8), col(FP), A.is_ge, 0.5, A.max)
+    red(col(W2), C("KT", 0, 8), A.mult)
+    ts(S("BW"), S("LA"), col(W2), A.mult, 2.0 ** -17, A.mult)
+    ts(S("CW"), S("VI_"), 0.0, A.is_equal, col(W2), A.mult)
+    CWP = C("PM", 0, 128)
+    mms((CWP, S("ONE"), S("CW")), (CWP, S("I32"), S("LT")))
+    for k in (0, 1):
+        ts(S("SEL", k), S("VS"), float(k), A.is_equal)
+    ts(S("BO"), S("VS"), col(P71), A.is_equal)
+    act(col(LB), col(FP), AF.Abs, bias=-4.25)
+    act(col(L2), col(LB), bias=-2.25)
+    ts(S("HI"), S("HB"), col(W2), A.mult, 128.0, A.mult)
     ts(S("HI"), S("HI"), 32, A.bitwise_and)
     ts(S("BITS"), S("HI"), 1.0 / 32, A.mult, col(L2), A.max)
-    act(S("KT"), S("NR"), AF.Relu, scale=-1.0, bias=1.0)
-    act(C("KC", 0, N2), S("KT"), scale=-1.0, bias=-16.0)
-    act(C("KC", N2, 2 * N2), S("KT"), scale=-1.0, bias=col(KCB))
-    for k, sc in enumerate((0.5, col(CN), col(CH), col(CQ), col(CN))):
+    act(col(SG), col(FP), AF.Sign, bias=-4.5)
+    act(col(T2), col(SG), scale=5.0 / 16, bias=2.0 / 16)
+    act(col(WS), col(FP), scale=-1.0 / 16, bias=col(T2))
+    act(col(A5), col(FP), AF.Relu, scale=-1.0, bias=5.0)
+    act(col(KCB), col(A5), scale=-1.0, bias=7.0)
+    for k, sc, bi in ((CN, 1.0, -1.0), (CQ, -1.0, 1.0), (CL0, 2.0 ** -18, 0.0), (CL1, 2.0 ** -17, 0.0),
+                      (SB0, -6 * DS_, DB - 2 * DS_), (SB1, DS_, DB - 5 * DS_), (SC1, DS_, DS_)):
+        act(col(k), col(HALF), scale=sc, bias=bi)
+    act(S("KT", D_), C("HB", 0, NN), AF.Relu, bias=-23.0)
+    act(S("KT", R_), C("HB", 0, NN), AF.Relu, scale=-1.0, bias=2.0)
+    F8 = C("HB", 0, 8)
+    ts(S("EF"), F8, col(FP), A.is_equal)
+    act(C("CS", 0, 8), F8, scale=256.0, bias=7.0 * 16513 * 512 + 512.0)
+    act(C("CS", 8, 16), F8, scale=0.0)
+    act(C("CS", 16, 24), F8, scale=512.0, bias=512.0)
+    for k, sc in enumerate((0.5, col(CN), col(HALF), col(CQ), col(CN))):
         act(C("DA", 8 * k, 8 * k + 8), S("EF"), scale=sc)
+    for a, k in ((0, 2), (16, 4)):
+        iota(C("F48", a, a + 8 * k), [[1, 8], [0, k]], 0)
+        iota(C("CL", a, a + 8 * k), [[0, 8], [16, k]], 0)
     for a, b, k in ((0, 16, CL0), (16, 48, CL1)):
         ts(C("DL", a, b), C("F48", a, b), col(FP), A.is_equal, col(k), A.mult)
-    act(S("CL"), S("CL"), bias=col(NG))
-    act(S("BT", al, 0), S("BI", 0))
-    act(S("BT", al, 1), S("BI", 1), bias=col(NG))
+    act(S("CL"), S("CL"), bias=col(L16))
+    act(col(L32), col(L16), bias=16.0)
+    for k, c in ((0, L16), (1, L32)):
+        act(S("BT", slice(k, 32, 2), 0), C("HB", 0, 16))
+        act(S("BT", slice(k, 32, 2), 1), C("HB", 0, 16), scale=0.0, bias=col(c))
     act(S("BQ"), S("BT"), bias=-0.25)
-    row1 = one(0, 128)
-    FXL = (ID, C("JM", 0, 128))
-
-    CS_ = C("PM", 0)
-    ts(C("EB", 0), C("CT", 0), 1.0, A.add)
-    ts(C("CA", 0), C("CT", 1), 1.0, A.not_equal, 64.0, A.mult)
-    ts(C("CA", 1), C("CT", 1), 2.0, A.not_equal, 64.0, A.mult)
-    ts(C("CA", 2), C("CT", 0), col(F0), A.is_lt, 64.0, A.mult)
-    mm(CS_, S("LE"), C("EB", 0), True, True)
-    ts(C("CF", 2), C("CT", 2), C("CA", 0), A.add)
-    ts(C("CF", 3), C("CT", 2), C("CA", 1), A.add, C("CA", 2), A.add)
-    cp(C("CF", 0, 2), C("CT", 3, 5))
-    ts(S("OM"), S("NR"), C("CF", 2), A.add, CS_, A.is_equal)
-    ts(S("OR"), S("NR"), C("CF", 3), A.add, CS_, A.is_equal)
-    GM, LTC, LTG, UP, U, SU, OS, OT = [S("TA", k) for k in range(8)]
-    ts(GM, S("NR", D_), C("CF", 2), A.add, CS_, A.is_ge)
-    ts(LTC, S("NR", D_), CS_, A.is_lt)
-    TT = C("PA", 0, N2)
-    mms((TT, S("LT"), S("OM")), (TT, S("LT"), S("OR")))
-    top = slice(0, NN)
-    mm(C("PB", 0, 128, parts=top), S("OR", D_), S("LT"), True, True)
-    mm(C("PN", 128, 256, parts=top), S("OM", D_), ID, True, True)
-    NE = lambda k: C("NE", N2 * k, N2 * k + N2)
-    ts(S("E0"), S("NR"), C("CF", 0), A.add, CS_, A.not_equal)
-    ts(NE(0), S("NR"), C("CF", 1), A.add, CS_, A.not_equal)
-    ts(S("EQC"), S("NR"), CS_, A.is_equal, col(WS), A.mult)
-    ts(S("GEN", D_), S("NR", D_), CS_, A.is_ge)
-    tt(LTG, GM, LTC, A.min)
-    act(C("TR", 0, 128), C("PB", 0, 128, parts=top))
-    cp(C("TR", 128, 256), C("PN", 128, 256, parts=top))
-    mm(C("PU", 128, 128 + NN), S("LE"), S("OR", R_), True, True)
-    mm(C("PU", 0, 128), C("TR", 128, 256), C("TR", 0, 128), True, True)
-    tt(UP, C("PA", 0, NN), LTG, A.is_lt)
-    tt(S("X", 0, slice(0, N2)), TT, S("OM"), A.is_lt)
-    tt(U, C("PA", 0, NN), LTC, A.is_lt)
-
-    N0_ = slice(NN - N0, NN)
-    act(S("TN"), S("NR", N0_), scale=-1.0, bias=C("EB", 0))
-    for k, (c, v) in enumerate(((C("CF", 2), -8.0), (C("CF", 3), -256.0), (C("CF", 0), 16.0), (C("CF", 1), 32.0))):
-        ts(S("K5", k), S("TN"), c, A.is_equal, v, A.mult)
-    ts(S("K5", 4), S("TN"), 1.0, A.is_ge, 128.0, A.mult)
-    KEY = C("PA", 64, 64 + N0)
-    mms((KEY, S("SEL"), S("NR", N0_)), *[(KEY, S("SEL"), S("K5", k)) for k in range(5)])
-    for k in (0, 1):
-        ts(S("GK", k), KEY, C("PA", 64 + N0 - 1 - k), A.is_gt)
-        red(C("SM", 2 + k), S("GK", k))
-
-    red(C("SM", 0), UP)
-    CAND = S("X", 0, slice(N2, N2 + 1))
-    red(CAND, S("X", 0, D_), A.max)
-    tt(S("M"), C("PU", 0, 128), S("LT"), A.is_lt)
-    ts(S("GEN", R_), C("PU", 128, 128 + NN), 0.0, A.is_equal)
-    XW = slice(0, N2 + 1)
-    act(S("Z", XW), S("X", 0, XW), scale=-99.0, bias=C("SM", 0))
-    act(S("MN"), S("M"), scale=-256.0)
-    ts(C("XH", 0, 32), S("BITS"), CAND, A.mult)
-    ts(C("XH", 32, 64), S("BITS"), CAND, A.mult, -1.0, A.mult)
-    HY, CNT, LT_, LAM = C("PN", 0, 64), C("PN", 64, 96), C("PN", 96, 97 + N2), C("PN", 96 + N2)
-    mms((HY, S("IK"), S("XH")), (HY, S("M"), S("XH")))
-    ts(C("VI", 0, 32), C("PN", 0, 32), C("Z", N2), A.add, 933.0, A.is_gt)
-    ts(C("VI", 32, 64), C("PN", 32, 64), C("Z", N2), A.subtract, 91.0, A.is_ge)
-    mms((CNT, ID, C("XH", 32, 64)), (CNT, S("BLK"), C("VI", 0, 32)), (CNT, S("BLK"), C("VI", 32, 64)))
-    red(C("SM", 1), CNT, A.min)
-    ts(S("X", 1, XW), S("X", 0, XW), C("SM", 1), A.mult, -1.0, A.mult)
-    mm(LT_, S("M"), S("X", 1, XW), True, True)
-
-    SV = S("SV")
-    tt(OS, S("OM", D_), S("OR", D_), A.add)
-    tt(NE(1), S("E0"), NE(0), A.is_ge)
-    scan(SU, U, C("ZR", 0, NN), 0.0)
-    tt(OT, U, OS, A.is_gt)
-    tt(NE(2), NE(1), NE(0), A.not_equal)
-    act(OS, OT, scale=-99.0)
-    tt(SV, SU, OS, A.add)
-    YS = lambda k, h: C("PW", N2 * k + NN * h, N2 * k + NN * h + NN)
-    YA = C("PW", 0, 3 * N2)
-    mms((YA, S("IK"), S("NE")), *[(YS(k, 1), S("IK"), S("OR", R_)) for k in range(3)], *[(YS(k, 1), ID, S("Z", R_)) for k in range(3)],
-        *[(YS(k, 0), ID, SV) for k in range(3)], *[(YS(k, 1), S("MN"), S("X", 1, R_)) for k in range(3)])
-    ts(S("Y"), YA, LAM, A.add, -91.0, A.is_le)
-    ts(S("HH", D_), SV, LAM, A.add, -91.0, A.is_le)
-    ts(S("HH", R_), S("Z", D_), LAM, A.add, -91.0, A.is_le)
-    tt(S("LD"), C("PN", 96, 96 + NN), S("OR", D_), A.is_gt)
-    scan(C("PU", 300, 300 + 156), S("Y"), C("ZR", 0, 156), 0.0)
-    tt(S("PP"), C("Y", N2, 3 * N2), C("PU", 300 + N2, 300 + 156), A.mult)
-    DD, D2 = C("PW", 256, 256 + N2), C("PW", 320, 320 + N2)
-    mms((D2, ID, C("KC", N2, 2 * N2)), (D2, S("LA"), S("EQC")))
-    mms((DD, ID, C("KC", 0, N2)), (DD, S("LA"), S("EQC")), (DD, S("LA"), S("GEN")),
-        *[(C("PW", 256, 256 + NN), S("LA"), x) for x in (S("HH", D_), S("HH", R_), S("LD"))])
-    RK = C("PU", 200, 200 + N2)
-    mms((RK, ID, C("Y", 0, N2)), (RK, ID, C("PP", 0, N2)), (RK, ID, C("PP", N2, 2 * N2)))
-    lo, hi = slice(0, 64), slice(64, 128)
-    act(C("DS", N2, 2 * N2, parts=hi), C("PW", 320, 320 + N2, parts=hi))
-    act(C("DS", 0, N2), DD)
-    act(C("DS", N2, 2 * N2, parts=lo), C("PW", 256, 256 + N2, parts=lo))
-    for k in range(6):
-        ts(S("EW", k), RK, C("TG", k), A.is_equal, C("WK", k % 3), A.mult)
-    for k in range(6):
-        o = C("PN", 160 + N2 * (k // 3), 160 + N2 * (k // 3) + N2)
-        mm(o, ID, S("EW", k), k % 3 == 0, k % 3 == 2)
-    for k in (0, 1):
-        tt(C("EP", N2 * k, N2 * k + N2), C("PN", 160 + N2 * k, 160 + N2 * k + N2), C("DS", N2 * k, N2 * k + N2), A.mult)
-        red(C("SM", 4 + k), C("EP", N2 * k, N2 * k + N2))
-    ts(S("RA"), C("DA", 0, 24), C("SM", 4), A.mult)
-    ts(S("RB"), C("DA", 24, 40), C("SM", 5), A.mult)
-    act(S("RL"), S("DL"), scale=C("SM", 5))
-    TBP = lambda a, b=None: C("PM", 200 + a, None if b is None else 200 + b)
-    mms((TBP(0, 24), S("IDF"), S("CS")), (TBP(0, 24), S("BO"), S("RA")), (TBP(8, 24), S("BO"), S("RB")))
-    mms((C("PU", 0, 48), S("IDF"), S("CL")), (C("PU", 0, 48), S("BO"), S("RL")))
+    GM, GEX, U, UT, SU, UP, ROWM, OMW = [S("TA", k, slice(0, n)) for k, n in enumerate((NN, NN, NN, NN, NN, NN, N0, N0))]
+    act(ROWM, C("HB", 0, N0), scale=-2.0 / 256, bias=23.0 / 256)
+    FXL = (ID, NH)
 
     def lists(f0, f1):
         fs, cs, nd = slice(f0, f1), slice(32 * f0, 32 * f1), C("XX", 32 * f0, 32 * f1)
@@ -365,8 +276,8 @@ def build(T, nxt):
         tt(S("IDX", 1, fs), S("IB", cs), nd, A.mult)
         act(S("FX", 0, cs), S("IDX", 1, fs), AF.Relu, scale=-3.0, bias=3.0)
         act(S("FX", 1, cs), S("IDX", 1, fs), AF.Relu, scale=-2.0, bias=4.0)
-        act(S("H1", al, fs), S("IDX", al, fs), AF.Sign, bias=-2.5)
-        act(S("H2", al, fs), S("IDX", al, fs), AF.Sign, bias=-5.5)
+        ts(S("H1", al, fs), S("IDX", al, fs), 2.5, A.is_ge, -0.5, A.add)
+        ts(S("H2", al, fs), S("IDX", al, fs), 5.5, A.is_ge, -0.5, A.add)
 
     def masks(f0, f1):
         fs, nd = slice(f0, f1), C("XX", 32 * f0, 32 * f1)
@@ -385,35 +296,146 @@ def build(T, nxt):
         o = lambda i: C(name, a + n * i, a + n * i + n)
         mms(*[(o(i), ID, S("IDX", i, fs)) for i in (0, 1)], *[(o(1), FXL[i], S("FX", i, slice(32 * f0, 32 * f1))) for i in (0, 1)],
             *[(o(i), S("N15"), S(h, i, fs)) for h in ("H1", "H2") for i in (0, 1)])
-        for i in (0, 1):
-            act(S("POW", fs, i), o(i), AF.Exp, scale=-7 * math.log(2), bias=21 * math.log(2))
+        act(S("PQ", al, fs), C(name, a, a + 2 * n), AF.Square, scale=US, bias=UB - 4 * US)
+        act(S("POW", al, fs), S("PQ", al, fs), bias=2.0 ** -14 - float(np.float32(UB * UB)))
+
+    lists(0, 3)
+    vec(0, 3)
+    masks(1, 3)
+
+    CM, CV, CR = C("CA", 0), C("CA", 1), C("CA", 2)
+    cp(C("CB", 0), C("CT", 0))
+    ts(C("CB", 1, 4), C("CT", 2, 5), -1.0, A.mult)
+    ts(CM, C("CT", 1), 1.0, A.is_equal, 256.0, A.mult)
+    ts(CV, C("CT", 0), col(F0), A.is_ge, 4096.0, A.mult)
+    ts(CR, C("CT", 1), 2.0, A.is_equal, CV, A.mult)
+    TX, TG, TM0, TM1 = C("PA", 0), C("PW", 500), C("PW", 501), C("PW", 502)
+    mms((TX, S("LE"), C("CB", 0)), (TX, ID, C("CB", 1)))
+    mms(*[(t, S("LE"), C("CB", 0)) for t in (TG, TM0, TM1)], (C("PW", 501, 503), ID, C("CB", 2, 4)))
+    OM, OR = lambda h=al: S("OM", h), lambda h=al: S("OR", h)
+    ts(OM(), S("NR"), TX, A.is_equal, CM, A.mult)
+    ts(OR(), S("NR"), TX, A.is_equal, CR, A.mult)
+    ts(S("EQ", 0), S("NR"), TM0, A.is_equal, -512.0, A.mult)
+    ts(S("EQ", 1), S("NR"), TM1, A.is_equal, -1024.0, A.mult)
+    ts(GEX, S("NR", D_), TG, A.is_ge, 2048.0, A.mult)
+    ts(GM, S("NR", D_), TX, A.is_ge, 2.0, A.mult)
+    ts(S("EQC"), S("NR"), TG, A.is_equal, col(WS), A.mult)
+    SS_, R1 = C("PU", 0, NN), C("PB", 0, N2)
+    mms((SS_, S("BW"), OR(D_)), (SS_, ID, OM(D_)))
+    mms((R1, S("LT"), OM()), (R1, NH, OM()), (R1, NH, OM()), (R1, S("LT"), OR()))
+    R2, R3, R4, R5 = [C("PN", NN * k, NN * k + NN) for k in range(4)]
+    mms(*[(r, S(l), x) for r, l in ((R3, "LT"), (R2, "LT"), (R5, "LE")) for x in (OM(D_), OR(D_))], *[(r, ID, GEX) for r in (R3, R2, R5)],
+        (R3, NH, GM), (R4, S("LE"), OR(R_)))
+    RHO, CAND, DN, ZC = [C("SM", k) for k in range(4)]
+    red(RHO, SS_, A.max)
+    ts(S("M"), CWP, 224.0, A.add, RHO, A.is_gt)
+    act(S("X", 0, D_), C("PB", 0, NN), AF.Relu, scale=-1.0 / 256, acc=CAND)
+    act(UP, R3, AF.Relu, scale=-1.0, acc=DN)
+    act(S("X", 0, R_), C("PB", NN, N2), AF.Relu, scale=-1.0 / 256)
+    act(U, R2, AF.Relu, scale=-1.0, bias=1.0)
+    act(UT, R5, AF.Relu, scale=-128.0, bias=128.0)
+    act(S("GEN", R_), R4, AF.Relu, scale=-1.0, bias=1.0)
+    act(S("GEN", D_), GEX, scale=1.0 / 2048)
+
+    last0 = lambda x: S(x[1], *([N0_] if x[1] in ("OM", "OR", "EQC") else [int(x[2][0]) // len(cache[x[1]][0]), N0_]))
+    KEY0, KEY1, OH = C("PA", 16, 16 + N0), C("PU", 64, 64 + N0), C("PU", 80, 80 + N0)
+    same = [C("HB", 0, N0)] + [last0(x) for x in (S("EQ", 0), S("EQ", 1), GEX, OR())]
+    mms(*[(KEY0, S("SEL", 0), x) for x in same + [last0(OM())]])
+    KS = lambda k, a=0, b=N0: S("KS", k, slice(a, b))
+    act(KS(0), KEY0)
+
+    def rank(k, keys, key):
+        act(S("JK", k, slice(0, N0)), keys, AF.Sign, scale=-1.0, bias=key, acc=C("SR", k))
+
+    for n in range(4):
+        rank(n, KS(0), KS(0, N0 - 1 - n, N0 - n))
+    tt(OMW, last0(OM()), ROWM, A.mult)
+    mms((OH, S("SEL", 0), last0(S("EQC"))), *[(KEY1, S("SEL", 1), x) for x in same + [OMW]], *[(KEY1, S("SEL", 0), x) for x in (last0(OR()), OMW)])
+    act(KS(1), KEY1)
+    act(KS(2), OH, AF.Sign)
+    for n in (0, 1):
+        rank(4 + n, KS(1), KS(1, N0 - 1 - n, N0 - n))
+    tt(KS(2), KS(2), KS(1), A.mult)
+    act(S("JK", 7, slice(0, N0)), KS(2), scale=-1.0, acc=C("SR", 8))
+    rank(6, KS(1), C("SR", 8))
+    ISB = C("SR", 9)
+    ts(ISB, C("SR", 6), -9.0, A.is_equal, -512.0, A.mult)
+    ts(C("SR", 12, 16), KS(1, N0 - 4, N0), 2048.0, A.is_lt, ISB, A.mult)
+
+    act(S("Z", slice(0, N2)), S("X", 0, slice(0, N2)), scale=-64.0, bias=DN)
+    act(ZC, CAND, scale=-9.0, bias=DN)
+    ts(S("XH"), S("BITS"), CAND, A.min)
+    HY, CNT, SUC = C("PM", 0, 32), C("PM", 32, 64), C("SH", 0)
+    mms((HY, S("I32"), S("XH")), (HY, S("M"), S("XH")))
+    ts(C("VI", 0, 32), HY, ZC, A.add, 31.0, A.is_gt)
+    ts(C("VI", 32, 64), HY, ZC, A.add, 0.0, A.is_lt)
+    mms((CNT, NH, S("XH")), (CNT, S("LA"), C("VI", 0, 32)), (CNT, S("LA"), C("VI", 32, 64)))
+    red(SUC, CNT, A.min)
+    power(0, 3, "PM", 192)
+    ts(S("X", 1, slice(0, N2)), S("X", 0, slice(0, N2)), SUC, A.mult, 240.0, A.mult)
+
+    scan(SU, U, U, 0.0, A.max)
+    YS = lambda k, h=None: C("PW", 1 + N2 * k + NN * (h or 0), 1 + N2 * k + (N2 if h is None else NN * h + NN))
+    LAM = C("PW", 1 + 4 * N2)
+    short = [YS(k, 0) for k in range(4)]
+    long_ = [(YS(k, 1), R_) for k in range(3)] + [(YS(3, 1), D_)]
+    mms((C("PW", 0, 1 + 4 * N2), row1, C("CY", 0, 1 + 4 * N2)),
+        (YS(0), ID, S("EQ", 1)), (YS(1), ID, S("EQ", 0)), (YS(1), NH, S("EQ", 1)), (YS(2), NH, S("EQ", 0)), (YS(2), NH, S("EQ", 1)),
+        *[(y, ID, OR(h)) for y, h in long_], *[(y, NH, UT) for y in short], *[(y, ID, S("Z", h)) for y, h in long_],
+        *[(y, ID, SU) for y in short], (LAM, S("M"), SUC), (LAM, S("M"), SUC), *[(y, S("M"), S("X", 1, h)) for y, h in long_])
+    ts(S("Y", 0, slice(0, N3)), C("PW", 1, 1 + N3), LAM, A.is_le, -63.0, A.mult)
+    ts(S("Y", 1, slice(0, N3)), C("PW", 0, N3), LAM, A.is_le, 64.0, A.mult)
+    ts(S("YH"), YS(3), LAM, A.is_le)
+    scan(S("RK"), S("Y", 0, slice(0, N3)), S("Y", 1, slice(0, N3)), 64.0)
+    act(S("SQ", 0), S("RK"), AF.Square, scale=DS_, bias=col(SB0))
+    act(S("SQ", 1), S("RK"), AF.Square, scale=col(SC1), bias=col(SB1))
+    for k in (0, 1):
+        act(S("EW", k), S("SQ", k), AF.Relu, scale=-BIG, bias=BIG)
+    DD, D2 = C("PW", 256, 256 + N2), C("PW", 320, 320 + N2)
+    mms(*[(d, l, x) for d in (D2, DD) for l, x in ((NH, S("KT")), (NH, S("KT")), (S("LA"), S("EQC")))], (DD, S("LA"), S("GEN")),
+        *[(C("PW", 256, 256 + NN), S("LA"), S("YH", h)) for h in (D_, R_)])
+    act(C("DS", 0, N2), DD, bias=-16.0)
+    act(C("DS", N2, 2 * N2, parts=hi), C("PW", 320, 320 + N2, parts=hi), bias=C("PC", KCB, parts=hi))
+    act(C("DS", N2, 2 * N2, parts=lo), C("PW", 256, 256 + N2, parts=lo), bias=-16.0)
+    TBP = lambda a, b=None: C("PW", 400 + a, None if b is None else 400 + b)
+    for k in (0, 1):
+        o = C("PM", 64 + N2 * k, 64 + N2 * k + N2)
+        mms(*[(o, ID, S("EW", k, slice(N2 * s, N2 * s + N2))) for s in range(3)])
+    for k in (0, 1):
+        tt(C("EP", N2 * k, N2 * k + N2), C("PM", 64 + N2 * k, 64 + N2 * k + N2), C("DS", N2 * k, N2 * k + N2), A.mult)
+        act(C("DS", N2 * k, N2 * k + N2), C("EP", N2 * k, N2 * k + N2), acc=C("SM", 8 + k))
+    act(S("RA"), C("DA", 0, 24), scale=C("SM", 8))
+    act(S("RB"), C("DA", 24, 40), scale=C("SM", 9))
+    mms((TBP(0, 24), S("IDF"), S("CS")), (TBP(0, 24), S("BO"), S("RA")), (TBP(8, 24), S("BO"), S("RB")))
+
+    def record_lists():
+        iota(C("RE", 5 * 32, 9 * 32), [[0, 4 * 32]], 0)
+        iota(C("RV", 5 * 64, 9 * 64), [[0, 4 * 64]], 0)
+        act(S("RL"), S("DL"), scale=C("SM", 9))
+        mms((C("PM", 448, 496), S("IDF"), S("CL")), (C("PM", 448, 496), S("BO"), S("RL")))
+        cp(S("LU"), C("PM", 448, 496))
 
     def places(f):
         a, r = 128 * (f % 2), 64 * PSLOT[f]
-        pos, half = C("XY", a, a + 128), [C("XY", a + 64 * i, a + 64 * i + 64) for i in (0, 1)]
+        XY, a = ("XX", 256) if f == 1 else ("XY", a)
+        pos, half = C(XY, a, a + 128), [C(XY, a + 64 * i, a + 64 * i + 64) for i in (0, 1)]
         steps = [(pos, ID, S("NV", f))] + [(h, ID, S("BQ" if f else "BT")) for h in half]
         if f:
             steps += [(h, C(l, 0, 128), S("GV")) for h, l in zip(half, ("JH", "JM"))] + [(pos, row1, S("MB", k)) for k in (0, 1)]
         mms(*steps)
-        ts(C("CC", 0, 64), C("XY", a, a + 128, 2), 0.0, A.max, 15.0, A.min)
-        ts(C("CC", 64, 128), C("XY", a + 1, a + 128, 2), 0.0, A.max, 31.0, A.min)
-        if f < F - 1:
+        ts(C("CC", 0, 64), C(XY, a, a + 128, 2), 0.0, A.max, 15.0, A.min)
+        ts(C("CC", 64, 128), C(XY, a + 1, a + 128, 2), 0.0, A.max, 31.0, A.min)
+        if f == 0:
+            act(C("RV", r, r + 64), S("NV", 0, 0))
+        elif f < F - 1:
             tt(C("RV", r, r + 64), half[0], S("BT"), A.subtract)
 
     def words(f):
-        if f < 2:
-            for i in range(f + 1):
-                u1, u2 = [S(u, f, slice(32 * i, 32 * i + 32)) for u in ("U1", "U2")]
-                ts(u2, S("H2", i, f), TBP(16 + f), A.mult)
-                ts(u1, S("H1", i, f), TBP(8 + f), A.mult, TBP(f), A.add)
-                tt(u1, u1, u2, A.add)
-                tt(S("XI", f, i), u1, S("POW", f, i), A.mult)
-        else:
-            act(S("U1", f), S("H1", al, f), scale=C("TB", 8 + f), bias=C("TB", f))
-            act(S("U2", f), S("H2", al, f), scale=C("TB", 16 + f))
-            o = C("PM", 64 * (f % 2), 64 * (f % 2) + 64)
-            mms((o, S("IDF"), S("U1", f)), (o, S("IDF"), S("U2", f)))
-            tt(S("XI", f), o, S("POW", f), A.mult)
+        act(S("U1", f), S("H1", al, f), scale=C("TB", 8 + f), bias=C("TB", f))
+        act(S("U2", f), S("H2", al, f), scale=C("TB", 16 + f))
+        o = C("PM", 192 + 64 * (f % 2), 192 + 64 * (f % 2) + 64)
+        mms((o, S("IDF"), S("U1", f)), (o, S("IDF"), S("U2", f)))
+        tt(S("XI", f), o, S("POW", al, f), A.mult)
 
     def record(f):
         r = 32 * PSLOT[f]
@@ -433,45 +455,33 @@ def build(T, nxt):
         ts(C("OFF", 64 * f, 64 * f + 64), S("S2"), float(-P * wbase(f)), A.add)
 
     def pixels(f):
-        cuts = CUTS if f else CUTS0
-        pieces = list(zip(cuts[:-1], cuts[1:]))
-        sends = SENDS if f else (0, 1)
+        pieces = list(zip(CUTS[:-1], CUTS[1:]))
         bank = lambda h: C(("PA", "PB", "PU", "PN")[h], 0, pieces[h][1] - pieces[h][0])
         s = 16 * ((f + 1) % 8)
         win = C("W", P * wbase(f), P * (9 + f))
         aw = [("arr%d" % f, narr * (len(SENDS) if f else 1))]
         last = f == F - 1
-        big = BIG if f else 1.5 * BIG
         for h, (a, b) in enumerate(pieces):
             mm(bank(h), C("J", s, s + 128), C("RES", f * P + a, f * P + b), True, False)
-            if f:
-                mm(bank(h), S("MQ"), C("MR", 0, b - a), False, False)
+            mm(bank(h), S("MQ"), C("MR", 0, b - a), False, False)
         for h, (a, b) in enumerate(pieces):
-            if f == 0:
-                for k, name in enumerate(("GP", "G0")):
-                    for c in (a, a + 128):
-                        (cp if k and c > a else act)(C(name, c, c + 128), IND(win, C("OFF", 32 * k + c // 16, 32 * k + c // 16 + 8)), waits=aw)
-                    mm(bank(h), C("JH", s, s + 128), C(name, a, b), False, False)
-                mm(bank(h), S("M4"), one(0, b - a), False, False)
-                mm(bank(h), S("MB", 0), one(0, b - a), False, True)
-                continue
             act(C("GP", a, b), IND(win, C("OFF", 64 * f + a // 16, 64 * f + b // 16)), AF.Relu, scale=-1.0, bias=255.0, waits=aw)
             ts(C("GQ", a, b), IND(win, C("OFF", 64 * f + 32 + a // 16, 64 * f + 32 + b // 16)), 255.0, A.min, 767.5, A.add, waits=aw)
             mm(bank(h), C("JM", s, s + 128), C("GP", a, b), False, False)
             mm(bank(h), C("JH", s, s + 128), C("GQ", a, b), False, not last)
             if last:
-                mm(bank(h), row1, C("MZ", 0, b - a), False, True)
+                mm(bank(h), S("NG"), C("MZ", 0, b - a), False, True)
         done, parts = 0, []
         for h, (a, b) in enumerate(pieces):
             out = C("SND", f * P + a, f * P + b)
             if last:
                 ts(out, bank(h), 0.0, A.max, 255.0, A.min)
-            elif FIN[h] == "s":
-                act(out, bank(h), AF.Relu, bias=-big)
+            elif FIN[f > 1][h] == "s":
+                act(out, bank(h), AF.Relu, bias=-BIG)
             else:
-                ts(out, bank(h), -big, A.add, 0.0, A.max)
-            if h in sends:
-                k = sends.index(h)
+                ts(out, bank(h), -BIG, A.add, 0.0, A.max)
+            if h in SENDS:
+                k = SENDS.index(h)
                 if last:
                     dma(("sync", "scalar")[k % 2], T.y[:, f * P + done:f * P + b], C("SND", f * P + done, f * P + b), "out%d" % (f + k))
                 else:
@@ -490,37 +500,77 @@ def build(T, nxt):
         ts(C("YO", f * P, f * P + P), C("W", PSLOT[f] * P, PSLOT[f] * P + P), 255.0, A.min)
         dma("sync", T.y[:, f * P:f * P + P], C("YO", f * P, f * P + P), "out%d" % f, [sent(k) for k in range(f + 1, min(f + 3, F))])
 
-    lists(0, 2)
-    vec(0, 2)
-    masks(1, 2)
-    I0, TOT0 = C("XY", 256, 320), C("XY", 448, 512)
-    mms((C("XY", 256, 288), ID, S("IDX", 0, 0)), (C("XY", 288, 320), ID, S("IDX", 1, 0)),
-        *[(C("XY", 288, 320), FXL[i], S("FX", i, slice(0, 32))) for i in (0, 1)])
+    TOT = C("XY", 448, 512)
+
+    def twice(f, more=()):
+        o = C("XY", 256 + 64 * f, 320 + 64 * f)
+        ob = C("XY", 288 + 64 * f, 320 + 64 * f)
+        mms((o, row1, S("CI", 0)), *[(o, ID, S("IDX", al, f))] * 2,
+            *[(ob, FXL[i], S("FX", i, slice(32 * f, 32 * f + 32))) for i in (0, 1, 0, 1)], *more)
+        return o
+
+    def offsets(f, idx, slots, more=()):
+        act(S("AB", 5 + f), S("IDX", al, f), AF.Relu, scale=512.0 * (f + 1), bias=-3584.0 * (f + 1))
+        for k, (c, v) in enumerate(slots):
+            ts(S("AB", 2 * f + k), idx, C("SR", c), A.is_equal, v * P, A.mult)
+        mms((TOT, ID, S("AB", 5 + f)), (TOT, S("I32"), C("CC", 0, 64)), (TOT, ID, C("CC", 64, 128)), *more,
+            *[(TOT, ID, S("AB", 2 * f + k)) for k in range(len(slots))])
+        ts(C("OFF", 64 * f, 64 * f + 64), TOT, float(P * (7 - wbase(f))), A.add)
+
+    I0 = twice(0)
     places(0)
-    for k, (c, v) in enumerate(((C("SM", 2), -2.0 * P), (C("SM", 3), -1.0 * P), (8.0, 1.0 * P))):
-        ts(S("AB", k), I0, c, A.is_equal, v, A.mult)
-    mms((TOT0, S("I32"), C("CC", 0, 64)), (TOT0, ID, C("CC", 64, 128)), *[(TOT0, ID, S("AB", k)) for k in range(3)])
-    ts(C("OFF", 0, 64), TOT0, 2.0 * P, A.add)
-    power(0, 2, "XY", 320)
-    words(0)
-    words(1)
-    cp(S("LU"), C("PU", 0, 48))
+    offsets(0, I0, ((0, -2.0), (1, -1.0)))
+    IA0, OKS = C("XY", 384, 416), C("XX", 384, 416)
+    mms((IA0, row1, S("CI", 1, slice(0, 32))), (IA0, ID, S("IDX", 0, 0)), (IA0, ID, S("IDX", 0, 0)), (IA0, NH, S("MK", 1, slice(0, 32))))
+    for n in range(4):
+        ts(S("OK", n), IA0, C("SR", n), A.is_equal, C("SR", 15 - n), A.mult)
+    tt(S("GW"), S("NV", 0, 0), S("MK", 1, slice(32, RW)), A.mult)
+    ts(S("GV"), S("GW"), ISB, A.mult, -1.0 / 512, A.mult)
+    places(1)
+    I1 = twice(1, [(C("XY", 320, 352), ID, S("OK", n)) for n in range(4)])
+    mms(*[(OKS, NH, S("OK", n)) for n in range(4)])
+    offsets(1, I1, ((4, -2.0), (5, -1.0), (6, -3.0)), [(C("XY", 448, 480), ID, S("OK", n)) for n in (0, 0, 1)])
+    act(C("ON", 0, 32), OKS, AF.Sign)
+    act(C("ON", 32, 64), OKS, AF.Relu, scale=-1.0, bias=1.0)
+
+    tt(S("PX"), S("POW", 0, slice(0, 2)), S("ON"), A.mult)
+    for f, a, n in ((0, 0, 32), (1, 32, 32), (2, 64, 64)):
+        h = lambda name: S(name, 0 if f < 2 else al, f)
+        ts(C("U0", a, a + n), h("H1"), TBP(8 + f), A.mult, TBP(f), A.add)
+        ts(C("XX", 256 + a, 256 + a + n), h("H2"), TBP(16 + f), A.mult)
     act(S("TB"), TBP(0, 24))
-    ts(C("RE", 32 * PSLOT[0], 32 * PSLOT[0] + 32), S("XI", 0, 0), 65024, A.bitwise_and)
-    lists(2, 8)
-    masks(2, 8)
-    power(2, 5, "PW", 0)
-    power(5, 8, "PW", 192)
+    tt(C("XX", 384, 512), C("XX", 256, 384), S("U0"), A.add)
+    tt(S("XB", slice(0, 2)), C("XX", 384, 448), S("PX"), A.mult)
+    tt(S("XI", 0, 0), C("XX", 384, 416), S("POW", 0, 0), A.mult)
+    tt(S("XI", 2), C("XX", 448, 512), S("POW", al, 2), A.mult)
+    tt(S("XI", 1, 0), S("XB", 0), S("XB", 1), A.max)
+    for f in (1, 0):
+        ts(C("RE", 32 * PSLOT[f], 32 * PSLOT[f] + 32), S("XI", f, 0), 65024, A.bitwise_and)
     for f in range(F):
         pixels(f)
-        if f in (0, 1):
-            a, b = ((3, 5), (5, 8))[f]
+        if f == 1:
+            iota(S("MZ"), [[0, 192]], int(BIG))
+            iota(S("NG"), [[0, 128]], -1)
+        if f == 0:
+            record_lists()
+            dma("sync", C("RES", 2 * P, 3 * P), T.res[:, 2 * P:3 * P], "res2", [sent(1)])
+            dma("sync", S("VY", slice(3, 8)), T.vy[:, 192:512], "vy2")
+            dma("sync", S("VX", slice(3, 8)), T.vx[:, 192:512], "vx2")
+        if f in (1, 2):
+            a, b = ((3, 5), (5, 8))[f - 1]
             dma("sync", C("RES", a * P, b * P), T.res[:, a * P:b * P], "res%d" % a, [sent(f + 1)])
-        if f < 3:
-            vec(2 * f + 2, 2 * f + 4)
-        if f < F - 1:
+        if f == 1:
+            record(2)
+            lists(3, 8)
+            masks(3, 8)
+            power(3, 5, "PW", 0)
+            words(3)
+            power(5, 8, "PW", 192)
+        if f in (1, 2, 3):
+            vec(2 * f + 1, min(2 * f + 3, F))
+        if 1 < f < F - 1:
             record(f + 1)
-        if f + 2 < F:
+        if 1 < f < F - 2:
             words(f + 2)
         if 0 < f < F - 1:
             store(f - 1)
@@ -566,7 +616,7 @@ def schedule(ops):
     back = [{} for o in ops]
     for j in range(n):
         for i, d in lag[j].items():
-            back[i][j] = d + span[j] - span[i] + (EARLY if ops[i][5] == 1 and unit[j] != "pool" else 0.0)
+            back[i][j] = d + span[j] - span[i]
 
     def place(edges, rank, first):
         post = [[] for o in ops]
@@ -593,30 +643,33 @@ def schedule(ops):
                     todo.append((rank[k], k))
         return start
 
-    def behind(seeds):
-        seen, todo = set(seeds), list(seeds)
-        while todo:
-            for i in pre[todo.pop()]:
-                if i not in seen:
-                    seen.add(i)
-                    todo.append(i)
-        return seen
+    group = [0] * n
+    seed = [1]
 
-    first = behind([j for j in range(n) if ("OFF", 64) in [(a, int(e.min())) for a, e in ops[j][3]]])
-    second = behind([j for j in range(n) if ops[j][5] == 1])
-    group = [0 if j in first else 1 if j in second else 2 for j in range(n)]
-    start, best = [float(j) for j in range(n)], None
-    for k in range(3):
-        late = place(back, [-start[j] - span[j] for j in range(n)], [0.0] * n)
-        start = place(lag, [100 * group[j] - late[j] - span[j] for j in range(n)], land)
-        end = max(start[j] + span[j] for j in range(n))
-        if best is None or end < best[0]:
-            best = (end, start)
+    def draw():
+        seed[0] = (seed[0] * 1103515245 + 12345) % 2 ** 31
+        return seed[0] / 2.0 ** 31
+
+    marks = [j for j in range(n) if isinstance(ops[j][5], int) or "OFF" in [a for a, e in ops[j][3]]]
+    worth = lambda start: max(start[j] + span[j] for j in range(n)) + 0.002 * sum(start[j] for j in marks)
+    best = (1e9, [float(j) for j in range(n)], None)
+    for k in range(ROUNDS):
+        if k < 4 or draw() < 0.3:
+            late = place(back, [-best[1][j] - span[j] for j in range(n)], [0.0] * n)
+            rank = [-late[j] - span[j] + 0.1 * draw() for j in range(n)]
+        else:
+            rank, part = list(best[2]), 0.05 * draw()
+            for j in range(n):
+                if draw() < part and best[1][j] < 18:
+                    rank[j] += draw() - 0.5
+        start = place(lag, rank, land)
+        if worth(start) <= best[0]:
+            best = (worth(start), start, rank)
     issue = list(best[1])
     for j in range(n):
         if land[j]:
             issue[j] = max([0.0] + [issue[i] if pre[j][i] is None else best[1][i] + d - LAND for i, d in lag[j].items()])
-    return [ops[j] for j in sorted(range(n), key=lambda j: (issue[j], j))]
+    return sorted(range(n), key=lambda j: (issue[j], j))
 
 
 def emit(g, T, ops):
@@ -692,4 +745,7 @@ def rank_program(g, core, T, topo):
     eng = topo.engines(core, dst)
     half = [sum(1 << e for e in part) for part in (eng[:len(eng) // 2], eng[len(eng) // 2:])]
     nxt = (rid, pid, topo.mask(core, dst), len(topo.engines(src, core)), half)
-    emit(g, T, schedule(build(T, nxt)))
+    ops = build(T, nxt)
+    if not ORDER:
+        ORDER.extend(schedule(ops))
+    emit(g, T, [ops[j] for j in ORDER])

@@ -4,8 +4,9 @@ from concourse.mybir import AluOpType as A, AxisListType, ActivationFunctionType
 F = 8
 P = 512
 CUTS = [0, 160, 288, 416, 512]
-FIN = ("sssv", "vsvs")
+FIN = ("ssvv", "ssss", "vssv")
 SENDS = (1, 3)
+STORES = (1, 2, 3)
 BIG = 8388608.0
 NN = 26
 N2 = 2 * NN
@@ -21,41 +22,41 @@ SB_ = {
     "GP": ([128, P], bf), "GQ": ([128, P], f16),
     "IA": ([128, 256], i32), "IB": ([128, 256], i32), "VY": ([128, 8, 2, 32], i32), "VX": ([128, 8, 2, 32], i32),
     "CT": ([128, 8], i32), "CB": ([128, 8], bf), "CA": ([128, 8], f32),
-    "ONE": ([128, 128], bf), "MR": ([1, 192], bf), "MZ": ([1, 192], bf), "MQ": ([1, 128], bf), "MB": ([1, 2, 128], bf),
-    "NG": ([1, 128], bf), "CY": ([1, 4 * N2 + 8], bf), "CI": ([1, 2, 64], bf),
-    "VA": ([128, 128], bf), "VN": ([128, 128], bf), "VI_": ([128, 128], bf), "VS": ([128, 128], bf),
-    "GL": ([128, 3, 128], bf), "CW": ([128, 128], bf), "BW": ([128, 128], bf),
+    "ONE": ([128, 128], bf), "MR": ([1, 192], bf), "MZ": ([1, 192], bf), "MQ": ([1, 128], bf), "MB": ([1, 3, 128], bf),
+    "NG": ([1, 128], bf), "CY": ([1, 4 * N2 + 8], bf), "CI": ([1, 2, 64], bf), "ONF": ([1, 128], f32),
+    "VA": ([128, 128], bf), "VN": ([128, 128], bf), "VI_": ([128, 128], bf),
+    "GL": ([128, 2, 128], bf), "CW": ([128, 128], bf), "BW": ([128, 128], bf),
     "J": ([128, 256], bf), "JH": ([128, 256], bf), "JM": ([128, 256], bf), "N15": ([128, 128], bf), "I32": ([128, 128], bf),
-    "BO": ([128, 128], f32), "IDF": ([128, 128], f32), "LE": ([128, 128], bf), "LT": ([128, 128], bf), "M": ([128, 128], bf),
-    "LA": ([128, 128], bf), "SEL": ([128, 2, 128], bf),
-    "PI": ([128, 8], i32), "PC": ([128, 32], f32), "F48": ([128, 48], f32), "EF": ([128, 8], f32),
+    "BO": ([128, 8, 2, 8], f32), "IDF": ([128, 128], f32), "LE": ([128, 128], bf), "LT": ([128, 128], bf), "M": ([128, 128], bf),
+    "LA": ([128, 128], bf), "SEL": ([128, 2, 8, 2, 8], bf),
+    "PI": ([128, 8], i32), "PC": ([128, 32], f32), "EF": ([128, 8], f32),
     "NR": ([128, N2], bf), "OM": ([128, N2], bf), "OR": ([128, N2], bf), "EQ": ([128, 2, N2], bf), "EQC": ([128, N2], bf),
     "GEN": ([128, N2], bf), "TA": ([128, 8, 32], bf), "X": ([128, 2, 56], bf), "Z": ([128, 56], bf),
     "Y": ([128, 2, N3 + 4], bf), "YH": ([128, N2], bf), "RK": ([128, N3], bf), "SQ": ([128, 2, N3], f32), "EW": ([128, 2, N3], bf),
-    "DS": ([128, 104], f32), "EP": ([128, 104], f32), "KT": ([128, N2], bf),
-    "DA": ([128, 40], f32), "DL": ([128, 48], f32),
-    "RA": ([128, 24], f32), "RB": ([128, 16], f32), "RL": ([128, 48], f32), "CS": ([128, 24], f32), "CL": ([128, 48], f32),
-    "TB": ([128, 24], f32), "LU": ([128, 48], u16), "SM": ([128, 16], f32), "SH": ([128, 8], bf),
-    "HB": ([128, 32], bf), "HI": ([128, 32], i32), "BITS": ([128, 32], bf), "XH": ([128, 32], bf), "VI": ([128, 64], bf),
+    "DS": ([128, N2], f32), "EP": ([128, 104], f32), "KT": ([128, N2], bf),
+    "DA": ([128, 4, 8], f32), "RA": ([128, 24], f32), "RB": ([128, 16], f32), "CS": ([1, 4, 8], f32), "CL": ([128, 4], f32),
+    "TB": ([128, 32], f32), "LU": ([128, 32], u16), "SM": ([128, 16], f32), "SH": ([128, 8], bf),
+    "HB": ([128, 32], bf), "HI": ([128, 2, 32], bf), "XH": ([128, 32], bf), "VI": ([128, 64], bf),
     "KS": ([128, 3, 16], f32), "JK": ([128, 8, 16], bf), "SR": ([128, 16], f32), "AB": ([128, 7, 64], bf), "OK": ([128, 4, 32], bf),
     "ON": ([128, 64], bf), "PX": ([128, 64], bf), "XB": ([128, 3, 32], f32), "GW": ([128, 64], bf),
-    "IDX": ([128, 2, 8, 32], bf), "H1": ([128, 2, 8, 32], bf), "H2": ([128, 2, 8, 32], bf), "FX": ([128, 2, 256], bf),
+    "IDX": ([128, 8, 2, 32], bf), "H1": ([128, 8, 2, 32], bf), "H2": ([128, 8, 2, 32], bf), "FX": ([128, 2, 256], bf),
     "PQ": ([128, 2, 8, 32], f32), "POW": ([128, 2, 8, 32], bf),
-    "NV": ([128, 8, 2, 32, 2], bf), "BT": ([128, 32, 2], bf), "BQ": ([128, 64], bf),
+    "NV": ([128, 8, 2, 32, 2], bf), "BT": ([128, 32, 2], bf),
     "MK": ([128, 8, RW], bf), "U0": ([128, 128], f32), "U1": ([128, 8, 64], f32), "U2": ([128, 8, 64], f32), "XI": ([128, 8, 2, 32], i32), "A0": ([128, 8, 32], i32),
-    "SS": ([128, 2, 64], i32), "RE": ([128, 11 * 32], i32), "RV": ([128, 11 * 64], bf), "GE": ([128, 32], f32), "GV": ([128, 64], bf),
+    "SS": ([128, 2, 64], i32), "RE": ([128, 11 * 64], i32), "RV": ([128, 11 * 64], bf), "GE": ([128, 32], f32), "GV": ([128, 64], bf),
     "CC": ([128, 128], bf), "S2": ([128, 64], i32), "OFF": ([128, F * 64], u16),
 }
 PS_ = ["PA", "PB", "PU", "XY", "XX", "PM", "PN", "PW"]
 SCRATCH = {k: ("sbuf", v[0], v[1]) for k, v in SB_.items()}
 SCRATCH.update({k: ("psum", [128, P], f32) for k in PS_})
-DMAS = ["ctl", "pic", "pi0", "ia_", "ib_", "vy_", "vx_", "ia2", "ib2", "vy2", "vx2", "res0", "res1", "res2", "res3", "res5"] + ["out%d" % f for f in range(F + 1)]
+DMAS = ["ctl", "pic", "pid", "pi0", "ia_", "ib_", "vy_", "vx_", "ia2", "ib2", "vy1", "vx1", "vy2", "vx2"] + ["res%d" % f for f in range(F)] + ["out%d" % f for f in range(F + 2)]
 SEMAPHORES = ["dve", "act", "pe", "pool"] + DMAS + ["arr%d" % f for f in range(F)] + ["snt%d" % f for f in range(F)]
 
 PSLOT = [4, 3, 2, 1, 0, 9, 8, 10]
 
-CYC, WAKE, LAND, HOP, COL = 0.0009, 0.24, 1.2, 1.2, 0.001
-ROUNDS = 1000
+CYC, WAKE, LAND, HOP, ROWS, COL = 0.0009, 0.24, 1.2, 1.1, 0.25, 0.0003
+SLOWER = ((1.3, 0.06, 0.0), (1.0, 0.0, 1.2))
+ROUNDS = 12000
 ORDER = []
 WIDTH = {f32: 4, i32: 4, bf: 2, u16: 2, f16: 2}
 
@@ -71,6 +72,8 @@ def build(T, nxt):
 
     def S(name, *ix, parts=al):
         shape = SCRATCH[name][1]
+        if name in ("IDX", "H1", "H2"):
+            ix = ix[::-1]
         if name not in cache:
             cache[name] = np.arange(int(np.prod(shape[1:]))).reshape(shape[1:])
         el = np.asarray(cache[name][ix] if ix else cache[name]).ravel()
@@ -147,9 +150,8 @@ def build(T, nxt):
         else:
             add("pool", lambda e: e.iota(o[0], pat, base, cm, allow_small_or_imprecise_dtypes=True), [o], [])
 
-    def diag(o, v):
-        i = C("J", 0, 128)
-        add("pool", lambda e: e.affine_select(o[0], i[0], [[1, 128]], A.not_equal, v, 0, -1), [o], [i])
+    def select(o, i, pat, op, fill, base, cm):
+        add("pool", lambda e: e.affine_select(o[0], i[0], pat, op, fill, base, cm), [o], [i])
 
     def dma(q, o, i, sem, waits=()):
         add(q, lambda e: e.dma_start(val(o), val(i)), [o] if isinstance(o, tuple) else [], [i], waits, sem)
@@ -162,7 +164,7 @@ def build(T, nxt):
     narr = nxt[3]
     sent = lambda k: ("snt%d" % k, neng * (len(SENDS) if k else 1))
     col = lambda k: C("PC", k)
-    (FP, P71, L16, HALF, W16, F0, NF2, C23, W2, CWB, LB, L2, A5, T0, KCB, SG, T2, WS, CN, CH, CQ, CL0, CL1, SB0, SB1, SC1, L32, K0, K1, KB) = range(30)
+    (FP, P71, L16, HALF, W16, F0, NF2, C23, W2, LB, L2, KCB, SG, T2, WS, CA0, CB2, SB0, SB1, SC1, L32, K0, K1, W4, W5) = range(25)
     D_, R_ = slice(0, NN), slice(NN, N2)
     N0_ = slice(NN - N0, NN)
     lo, hi, row = slice(0, 64), slice(64, 128), slice(0, 1)
@@ -175,16 +177,17 @@ def build(T, nxt):
         dma(q, C("CT", 0, parts=pp), T.gaps[:], "ctl")
         dma(q, C("CT", 1, parts=pp), T.cmd[:], "ctl")
         dma(q, C("CT", 2, 5, parts=pp), T.rel[:], "ctl")
-    dma("sync", C("W", 6 * P, 7 * P), T.pic0[:, P:2 * P], "pic")
-    dma("sync", C("IA", 0, 96), T.ia[:, 0:96], "ia_")
-    dma("sync", C("IB", 0, 96), T.ib[:, 0:96], "ib_")
-    dma("sync", S("VY", slice(0, 3)), T.vy[:, 0:192], "vy_")
-    dma("sync", S("VX", slice(0, 3)), T.vx[:, 0:192], "vx_")
+    dma("sync", C("W", 6 * P, 6 * P + P // 2), T.pic0[:, P:P + P // 2], "pic")
+    dma("sync", C("W", 6 * P + P // 2, 7 * P), T.pic0[:, P + P // 2:2 * P], "pid")
+    dma("sync", C("IA", 0, 128), T.ia[:, 0:128], "ia_")
+    dma("sync", C("IB", 0, 128), T.ib[:, 0:128], "ib_")
+    dma("sync", S("VY", slice(0, 2)), T.vy[:, 0:128], "vy_")
+    dma("sync", S("VX", slice(0, 2)), T.vx[:, 0:128], "vx_")
     dma("sync", C("W", 5 * P, 6 * P), T.pic0[:, 0:P], "pi0")
     dma("sync", C("RES", 0, P), T.res[:, 0:P], "res0")
-    dma("sync", C("RES", P, 2 * P), T.res[:, P:2 * P], "res1", [sent(0)])
-    dma("sync", C("IA", 96, 256), T.ia[:, 96:256], "ia2")
-    dma("sync", C("IB", 96, 256), T.ib[:, 96:256], "ib2")
+    dma("sync", S("VY", slice(2, 4)), T.vy[:, 128:256], "vy1", [sent(0)])
+    dma("sync", S("VX", slice(2, 4)), T.vx[:, 128:256], "vx1")
+    dma("sync", C("RES", P, 2 * P), T.res[:, P:2 * P], "res1")
 
     ms(S("ONE"), 1.0)
     iota(C("PI", 0), [[0, 1]], 0, 1)
@@ -192,7 +195,6 @@ def build(T, nxt):
     iota(S("HB"), [[1, 32]], 0)
     iota(S("VI_"), [[1, 128]], 0, -1)
     iota(S("VA"), [[0, 2], [-8, 8], [0, 8]], 0, 1)
-    iota(S("VS"), [[-8, 8], [0, 16]], 0, 1)
     for k in (0, 1):
         a, b = k * P // 2, (k + 1) * P // 2
         send(C("W", 8 * P + a, 8 * P + b), C("W", 6 * P + a, 6 * P + b), 0, nxt[4][k], k == 0)
@@ -213,58 +215,63 @@ def build(T, nxt):
     ts(ID, S("VI_"), 0.0, A.is_equal)
     act(NH, ID, scale=-0.5)
     act(S("I32"), ID, scale=32.0)
-    for o, v in ((C("J", 128, 256), 1.0), (C("JM", 128, 256), -0.5), (C("JH", 0, 128), 0.5), (C("JH", 128, 256), 0.5), (S("N15"), -3.0)):
-        diag(o, v)
+    def diag(name, a, b, v):
+        select(C(name, a, b), C("J", a % 128, a % 128 + b - a), [[1, b - a]], A.not_equal, v, a % 128, -1)
+
+    diag("J", 128, 256, 1.0)
+    select(S("SEL", 1), S("ONE"), [[-8, 8], [0, 16]], A.is_equal, 0.0, -1, 1)
+    for name, a, b, v in (("JM", 128, 160, -0.5), ("JH", 0, 128, 0.5), ("JH", 128, 160, 0.5), ("N15", 0, 128, -3.0)):
+        diag(name, a, b, v)
+    iota(S("CI", 1), [[0, 64]], -16)
+    iota(S("ONF"), [[0, 128]], 1)
+    act(S("MB", 1), row1, scale=-1.5 * BIG)
+    act(S("MB", 2), row1, scale=-0.25)
     act(S("IDF"), ID)
     for a in range(0, P, 128):
         act(C("W", 7 * P + a, 7 * P + a + 128), S("ONE"), scale=128.0)
-    for o, v in ((S("MR"), 151.0 * 256), (S("MQ"), 217.0), (S("MB", 0), 1.5 * BIG), (S("MB", 1), -1.5 * BIG),
-                 (S("CY"), 56.0), (C("CY", 1, 1 + N2), 1080.0), (C("CY", 1 + N2, 1 + 2 * N2), 568.0), (S("CI", 0), -11.0), (S("CI", 1), 53.5)):
+    for o, v in ((S("MR"), 151.0 * 256), (S("MQ"), 217.0), (S("MB", 0), 1.5 * BIG), (S("CY"), 56.0), (C("CY", 1, 1 + N2), 1080.0),
+                 (C("CY", 1 + N2, 1 + 2 * N2), 568.0), (S("CI", 0), -11.0)):
         ms(o, v)
     act(S("NR", R_), C("HB", 0, NN), bias=col(NF2))
     act(S("NR", D_), C("HB", 0, NN), scale=-1.0, bias=col(C23))
     ts(C("KT", 0, 8), C("HB", 0, 8), col(FP), A.is_ge, 0.5, A.max)
     red(col(W2), C("KT", 0, 8), A.mult)
     ts(S("BW"), S("LA"), col(W2), A.mult, 2.0 ** -17, A.mult)
-    ts(S("CW"), S("VI_"), 0.0, A.is_equal, col(W2), A.mult)
+    act(S("CW"), ID, scale=col(W2))
     CWP = C("PM", 0, 128)
     mms((CWP, S("ONE"), S("CW")), (CWP, S("I32"), S("LT")))
-    for k in (0, 1):
-        ts(S("SEL", k), S("VS"), float(k), A.is_equal)
-    ts(S("BO"), S("VS"), col(P71), A.is_equal)
+    for h in (0, 1):
+        ts(S("SEL", 0, al, h), C("VA", 0, 64), 0.0, A.is_equal)
     act(col(LB), col(FP), AF.Abs, bias=-4.25)
     act(col(L2), col(LB), bias=-2.25)
-    ts(S("HI"), S("HB"), col(W2), A.mult, 128.0, A.mult)
-    ts(S("HI"), S("HI"), 32, A.bitwise_and)
-    ts(S("BITS"), S("HI"), 1.0 / 32, A.mult, col(L2), A.max)
+    for k, (v, c) in enumerate(((4.0, 143.0), (2.0, 180.0))):
+        act(col(W4 + k), col(W2), scale=v)
+        act(S("HI", k), S("HB"), scale=col(W4 + k), bias=c - 0.5 + 1.0 / 64)
+    BITS = C("PM", 128, 160)
+    mms((BITS, S("MQ"), one(0, 32)), (BITS, ID, S("HI", 0)), *[(BITS, NH, S("HI", 1))] * 4)
     act(col(SG), col(FP), AF.Sign, bias=-4.5)
     act(col(T2), col(SG), scale=5.0 / 16, bias=2.0 / 16)
     act(col(WS), col(FP), scale=-1.0 / 16, bias=col(T2))
-    act(col(A5), col(FP), AF.Relu, scale=-1.0, bias=5.0)
-    act(col(KCB), col(A5), scale=-1.0, bias=7.0)
-    for k, sc, bi in ((CN, 1.0, -1.0), (CQ, -1.0, 1.0), (CL0, 2.0 ** -18, 0.0), (CL1, 2.0 ** -17, 0.0),
-                      (SB0, -6 * DS_, DB - 2 * DS_), (SB1, DS_, DB - 5 * DS_), (SC1, DS_, DS_)):
-        act(col(k), col(HALF), scale=sc, bias=bi)
+    halves = {KCB: (-16.0, 7.0), SB0: (DB - 2 * DS_, DB - 4 * DS_), SC1: (DS_, 2 * DS_), SB1: (DB - 5 * DS_, DB - 8 * DS_),
+              CA0: (0.0, 2.0 ** -13), CB2: (-16.0, 16.0)}
+    for k, (a, b) in halves.items():
+        act(col(k), col(HALF), scale=b - a, bias=a)
     act(S("KT", D_), C("HB", 0, NN), AF.Relu, bias=-23.0)
     act(S("KT", R_), C("HB", 0, NN), AF.Relu, scale=-1.0, bias=2.0)
     F8 = C("HB", 0, 8)
-    ts(S("EF"), F8, col(FP), A.is_equal)
-    act(C("CS", 0, 8), F8, scale=256.0, bias=7.0 * 16513 * 512 + 512.0)
-    act(C("CS", 8, 16), F8, scale=0.0)
-    act(C("CS", 16, 24), F8, scale=512.0, bias=512.0)
-    for k, sc in enumerate((0.5, col(CN), col(HALF), col(CQ), col(CN))):
-        act(C("DA", 8 * k, 8 * k + 8), S("EF"), scale=sc)
-    for a, k in ((0, 2), (16, 4)):
-        iota(C("F48", a, a + 8 * k), [[1, 8], [0, k]], 0)
-        iota(C("CL", a, a + 8 * k), [[0, 8], [16, k]], 0)
-    for a, b, k in ((0, 16, CL0), (16, 48, CL1)):
-        ts(C("DL", a, b), C("F48", a, b), col(FP), A.is_equal, col(k), A.mult)
-    act(S("CL"), S("CL"), bias=col(L16))
+    act(S("EF"), F8, AF.Abs, scale=-1.0, bias=col(FP))
+    act(S("EF"), S("EF"), AF.Relu, scale=-1.0 / 16, bias=1.0 / 16)
+    iota(S("CS", slice(0, 4, 2)), [[0, 2], [0, 8]], 0)
+    act(S("CS", 1), C("HB", 0, 8, parts=row), scale=0.0, bias=7.0 * 16513 * 512 + 256.0)
+    act(S("CS", 3), C("HB", 0, 8, parts=row), scale=512.0, bias=512.0)
+    for k, c in ((0, CA0), (1, W16), (3, CB2)):
+        act(S("DA", k), S("EF"), scale=col(c))
+    act(S("DA", 2), S("DA", 1), scale=-1.0)
+    act(S("CL"), C("HB", 0, 4), scale=16.0, bias=col(L16))
     act(col(L32), col(L16), bias=16.0)
     for k, c in ((0, L16), (1, L32)):
         act(S("BT", slice(k, 32, 2), 0), C("HB", 0, 16))
         act(S("BT", slice(k, 32, 2), 1), C("HB", 0, 16), scale=0.0, bias=col(c))
-    act(S("BQ"), S("BT"), bias=-0.25)
     GM, GEX, U, UT, SU, UP, ROWM, OMW = [S("TA", k, slice(0, n)) for k, n in enumerate((NN, NN, NN, NN, NN, NN, N0, N0))]
     act(ROWM, C("HB", 0, N0), scale=-2.0 / 256, bias=23.0 / 256)
     FXL = (ID, NH)
@@ -274,16 +281,15 @@ def build(T, nxt):
         ts(nd, S("IA", cs), 8.0, A.is_le)
         tt(S("IDX", 0, fs), S("IA", cs), nd, A.mult)
         tt(S("IDX", 1, fs), S("IB", cs), nd, A.mult)
-        act(S("FX", 0, cs), S("IDX", 1, fs), AF.Relu, scale=-3.0, bias=3.0)
-        act(S("FX", 1, cs), S("IDX", 1, fs), AF.Relu, scale=-2.0, bias=4.0)
-        ts(S("H1", al, fs), S("IDX", al, fs), 2.5, A.is_ge, -0.5, A.add)
-        ts(S("H2", al, fs), S("IDX", al, fs), 5.5, A.is_ge, -0.5, A.add)
+        v = 1.0 if f0 else 2.0
+        act(S("FX", 0, cs), S("IDX", 1, fs), AF.Relu, scale=-3.0 * v, bias=3.0 * v)
+        act(S("FX", 1, cs), S("IDX", 1, fs), AF.Relu, scale=-2.0 * v, bias=4.0 * v)
 
-    def masks(f0, f1):
+    def masks(f0, f1, v=1.0, explicit=0.0, direct=129.0):
         fs, nd = slice(f0, f1), C("XX", 32 * f0, 32 * f1)
-        act(S("MK", fs, slice(0, 32)), nd, scale=-129.0, bias=129.0)
+        act(S("MK", fs, slice(0, 32)), nd, scale=explicit - direct, bias=direct)
         for k in (32, 33):
-            act(S("MK", fs, slice(k, RW, 2)), nd, scale=-1.0, bias=1.0)
+            act(S("MK", fs, slice(k, RW, 2)), nd, scale=-v, bias=v)
 
     def vec(f0, f1):
         fs, nd = slice(f0, f1), C("XX", 32 * f0, 32 * f1)
@@ -291,17 +297,19 @@ def build(T, nxt):
             for i in (0, 1):
                 tt(S("NV", fs, i, al, n), S(("VY", "VX")[n], fs, i), nd, A.mult)
 
-    def power(f0, f1, name, a):
-        fs, n = slice(f0, f1), 32 * (f1 - f0)
+    def power(f0, f1, name, a, m=2):
+        fs, n, ls = slice(f0, f1), 32 * (f1 - f0), slice(0, m)
+        ts(S("H1", ls, fs), S("IDX", ls, fs), 3.0, A.is_ge)
+        ts(S("H2", ls, fs), S("IDX", ls, fs), 6.0, A.is_ge)
         o = lambda i: C(name, a + n * i, a + n * i + n)
-        mms(*[(o(i), ID, S("IDX", i, fs)) for i in (0, 1)], *[(o(1), FXL[i], S("FX", i, slice(32 * f0, 32 * f1))) for i in (0, 1)],
-            *[(o(i), S("N15"), S(h, i, fs)) for h in ("H1", "H2") for i in (0, 1)])
-        act(S("PQ", al, fs), C(name, a, a + 2 * n), AF.Square, scale=US, bias=UB - 4 * US)
-        act(S("POW", al, fs), S("PQ", al, fs), bias=2.0 ** -14 - float(np.float32(UB * UB)))
+        mms(*[(o(i), ID, S("IDX", i, fs)) for i in range(m)], *[(o(1), FXL[i], S("FX", i, slice(32 * f0, 32 * f1))) for i in (0, 1) if m > 1],
+            *[(o(i), S("N15"), S(h, i, fs)) for h in ("H1", "H2") for i in range(m)])
+        act(S("PQ", ls, fs), C(name, a, a + m * n), AF.Square, scale=US, bias=UB - US)
+        act(S("POW", ls, fs), S("PQ", ls, fs), bias=2.0 ** -14 - float(np.float32(UB * UB)))
 
-    lists(0, 3)
-    vec(0, 3)
-    masks(1, 3)
+    lists(0, 2)
+    vec(0, 2)
+    masks(1, 2, -1.0 / 512, 99.0, 0.0)
 
     CM, CV, CR = C("CA", 0), C("CA", 1), C("CA", 2)
     cp(C("CB", 0), C("CT", 0))
@@ -309,9 +317,9 @@ def build(T, nxt):
     ts(CM, C("CT", 1), 1.0, A.is_equal, 256.0, A.mult)
     ts(CV, C("CT", 0), col(F0), A.is_ge, 4096.0, A.mult)
     ts(CR, C("CT", 1), 2.0, A.is_equal, CV, A.mult)
-    TX, TG, TM0, TM1 = C("PA", 0), C("PW", 500), C("PW", 501), C("PW", 502)
+    TX, TG, TM0, TM1 = C("PA", 0), C("XY", 400), C("XY", 401), C("XY", 402)
     mms((TX, S("LE"), C("CB", 0)), (TX, ID, C("CB", 1)))
-    mms(*[(t, S("LE"), C("CB", 0)) for t in (TG, TM0, TM1)], (C("PW", 501, 503), ID, C("CB", 2, 4)))
+    mms(*[(t, S("LE"), C("CB", 0)) for t in (TG, TM0, TM1)], (C("XY", 401, 403), ID, C("CB", 2, 4)))
     OM, OR = lambda h=al: S("OM", h), lambda h=al: S("OR", h)
     ts(OM(), S("NR"), TX, A.is_equal, CM, A.mult)
     ts(OR(), S("NR"), TX, A.is_equal, CR, A.mult)
@@ -323,15 +331,17 @@ def build(T, nxt):
     SS_, R1 = C("PU", 0, NN), C("PB", 0, N2)
     mms((SS_, S("BW"), OR(D_)), (SS_, ID, OM(D_)))
     mms((R1, S("LT"), OM()), (R1, NH, OM()), (R1, NH, OM()), (R1, S("LT"), OR()))
-    R2, R3, R4, R5 = [C("PN", NN * k, NN * k + NN) for k in range(4)]
-    mms(*[(r, S(l), x) for r, l in ((R3, "LT"), (R2, "LT"), (R5, "LE")) for x in (OM(D_), OR(D_))], *[(r, ID, GEX) for r in (R3, R2, R5)],
-        (R3, NH, GM), (R4, S("LE"), OR(R_)))
+    R3 = C("PN", 0, NN)
+    R2, R4, R5 = [C("PB", 64 + NN * k, 64 + NN * k + NN) for k in range(3)]
+    mms((R3, S("LT"), OM(D_)), (R3, S("LT"), OR(D_)), (R3, ID, GEX), (R3, NH, GM))
     RHO, CAND, DN, ZC = [C("SM", k) for k in range(4)]
     red(RHO, SS_, A.max)
     ts(S("M"), CWP, 224.0, A.add, RHO, A.is_gt)
     act(S("X", 0, D_), C("PB", 0, NN), AF.Relu, scale=-1.0 / 256, acc=CAND)
     act(UP, R3, AF.Relu, scale=-1.0, acc=DN)
     act(S("X", 0, R_), C("PB", NN, N2), AF.Relu, scale=-1.0 / 256)
+    mms(*[(r, S(l), x) for r, l in ((R2, "LT"), (R5, "LE")) for x in (OM(D_), OR(D_))], *[(r, ID, GEX) for r in (R2, R5)],
+        (R4, S("LE"), OR(R_)))
     act(U, R2, AF.Relu, scale=-1.0, bias=1.0)
     act(UT, R5, AF.Relu, scale=-128.0, bias=128.0)
     act(S("GEN", R_), R4, AF.Relu, scale=-1.0, bias=1.0)
@@ -350,7 +360,7 @@ def build(T, nxt):
     for n in range(4):
         rank(n, KS(0), KS(0, N0 - 1 - n, N0 - n))
     tt(OMW, last0(OM()), ROWM, A.mult)
-    mms((OH, S("SEL", 0), last0(S("EQC"))), *[(KEY1, S("SEL", 1), x) for x in same + [OMW]], *[(KEY1, S("SEL", 0), x) for x in (last0(OR()), OMW)])
+    mms((OH, S("SEL", 0), last0(S("EQC"))), *[(KEY1, S("SEL", 0), x) for x in (last0(OR()), OMW)], *[(KEY1, S("SEL", 1), x) for x in same + [OMW]])
     act(KS(1), KEY1)
     act(KS(2), OH, AF.Sign)
     for n in (0, 1):
@@ -364,14 +374,66 @@ def build(T, nxt):
 
     act(S("Z", slice(0, N2)), S("X", 0, slice(0, N2)), scale=-64.0, bias=DN)
     act(ZC, CAND, scale=-9.0, bias=DN)
-    ts(S("XH"), S("BITS"), CAND, A.min)
+    ts(S("XH"), BITS, col(L2), A.max, CAND, A.min)
     HY, CNT, SUC = C("PM", 0, 32), C("PM", 32, 64), C("SH", 0)
     mms((HY, S("I32"), S("XH")), (HY, S("M"), S("XH")))
     ts(C("VI", 0, 32), HY, ZC, A.add, 31.0, A.is_gt)
     ts(C("VI", 32, 64), HY, ZC, A.add, 0.0, A.is_lt)
     mms((CNT, NH, S("XH")), (CNT, S("LA"), C("VI", 0, 32)), (CNT, S("LA"), C("VI", 32, 64)))
     red(SUC, CNT, A.min)
-    power(0, 3, "PM", 192)
+
+    def places(f):
+        a, r = 128 * (f % 2), 64 * PSLOT[f]
+        XY = "PM" if f == 1 else "XY"
+        pos, half = C(XY, a, a + 128), [C(XY, a + 64 * i, a + 64 * i + 64) for i in (0, 1)]
+        steps = [(pos, ID, S("NV", f))] + [(h, ID, S("BT")) for h in half]
+        if f:
+            steps += [(pos, row1, S("MB", 2))] + [(h, C(l, 0, 128), S("GV")) for h, l in zip(half, ("JH", "JM"))]
+            steps += [(pos, row1, S("MB", k)) for k in (0, 1)]
+        mms(*steps)
+        ts(C("CC", 0, 64), C(XY, a, a + 128, 2), 0.0, A.max, 15.0, A.min)
+        ts(C("CC", 64, 128), C(XY, a + 1, a + 128, 2), 0.0, A.max, 31.0, A.min)
+        if f == 0:
+            act(C("RV", r, r + 64), S("NV", 0, 0))
+        elif f < F - 1:
+            tt(C("RV", r, r + 64), half[0], S("BT"), A.subtract)
+
+    TOT = C("XY", 448, 512)
+
+    def twice(f, more=()):
+        o = C("XX", 256 + 64 * f, 320 + 64 * f)
+        ob = C("XX", 288 + 64 * f, 320 + 64 * f)
+        mms((o, row1, S("CI", 0)), *[(o, ID, S("IDX", al, f))] * 2,
+            *[(ob, FXL[i], S("FX", i, slice(32 * f, 32 * f + 32))) for i in (0, 1)], *more)
+        return o
+
+    def offsets(f, idx, slots, more=()):
+        act(S("AB", 5 + f), S("IDX", al, f), AF.Relu, scale=512.0 * (f + 1), bias=-3584.0 * (f + 1))
+        for k, (c, v) in enumerate(slots):
+            ts(S("AB", 2 * f + k), idx, C("SR", c), A.is_equal, v * P, A.mult)
+        mms((TOT, ID, S("AB", 5 + f)), (TOT, S("I32"), C("CC", 0, 64)), (TOT, ID, C("CC", 64, 128)), *more,
+            *[(TOT, ID, S("AB", 2 * f + k)) for k in range(len(slots))])
+        ts(C("OFF", 64 * f, 64 * f + 64), TOT, float(P * (7 - wbase(f))), A.add)
+
+    I0 = twice(0)
+    places(0)
+    offsets(0, I0, ((0, -2.0), (1, -1.0)))
+    mm(C("XY", 128, 256), S("LA"), S("SEL", 0), True, True)
+    act(S("BO"), C("XY", 128, 256), scale=1.0 / 16)
+    power(0, 2, "XY", 256, 1)
+    IA0 = S("MK", 1, slice(0, 32))
+    tt(IA0, IA0, S("IDX", 0, 0), A.max)
+    act(S("KS", 0, slice(12, 16)), C("SR", 0, 4), scale=0.5, bias=5.5)
+    for n in range(4):
+        ts(S("OK", n), IA0, S("KS", 0, slice(12 + n, 13 + n)), A.is_equal, C("SR", 15 - n), A.mult)
+    tt(S("GW"), S("NV", 0, 0), S("MK", 1, slice(32, RW)), A.mult)
+    act(S("GV"), S("GW"), scale=ISB)
+    places(1)
+    I1 = twice(1, [(C("XX", 320, 352), ID, S("OK", n)) for n in range(4)])
+    offsets(1, I1, ((4, -2.0), (5, -1.0), (6, -3.0)), [(C("XY", 448, 480), ID, S("OK", n)) for n in (0, 0, 1)])
+    act(C("ON", 0, 32), C("XX", 320, 352), AF.Relu, scale=-1.0 / 512, bias=-11.0 / 512)
+    act(C("ON", 32, 64), C("ON", 0, 32), scale=-1.0, bias=1.0)
+
     ts(S("X", 1, slice(0, N2)), S("X", 0, slice(0, N2)), SUC, A.mult, 240.0, A.mult)
 
     scan(SU, U, U, 0.0, A.max)
@@ -387,63 +449,47 @@ def build(T, nxt):
     ts(S("Y", 1, slice(0, N3)), C("PW", 0, N3), LAM, A.is_le, 64.0, A.mult)
     ts(S("YH"), YS(3), LAM, A.is_le)
     scan(S("RK"), S("Y", 0, slice(0, N3)), S("Y", 1, slice(0, N3)), 64.0)
-    act(S("SQ", 0), S("RK"), AF.Square, scale=DS_, bias=col(SB0))
-    act(S("SQ", 1), S("RK"), AF.Square, scale=col(SC1), bias=col(SB1))
-    for k in (0, 1):
-        act(S("EW", k), S("SQ", k), AF.Relu, scale=-BIG, bias=BIG)
+    wide, rest = slice(0, N3), slice(2 * N2, N3)
+    act(S("SQ", 0), S("RK"), AF.Square, scale=col(SC1), bias=col(SB0))
+    act(S("SQ", 1, rest), S("RK", rest), AF.Square, scale=DS_, bias=col(SB1))
+    for k, c in ((0, wide), (1, rest)):
+        act(S("EW", k, c), S("SQ", k, c), AF.Relu, scale=-BIG, bias=BIG)
     DD, D2 = C("PW", 256, 256 + N2), C("PW", 320, 320 + N2)
+    LAL = C("LA", 0, 64)
     mms(*[(d, l, x) for d in (D2, DD) for l, x in ((NH, S("KT")), (NH, S("KT")), (S("LA"), S("EQC")))], (DD, S("LA"), S("GEN")),
+        (C("PW", 320, 320 + N2, parts=lo), LAL, S("GEN")), (DD, row1, S("CI", 1, slice(0, N2))),
+        *[(C("PW", 320, 320 + NN, parts=lo), LAL, S("YH", h)) for h in (D_, R_)],
         *[(C("PW", 256, 256 + NN), S("LA"), S("YH", h)) for h in (D_, R_)])
-    act(C("DS", 0, N2), DD, bias=-16.0)
-    act(C("DS", N2, 2 * N2, parts=hi), C("PW", 320, 320 + N2, parts=hi), bias=C("PC", KCB, parts=hi))
-    act(C("DS", N2, 2 * N2, parts=lo), C("PW", 256, 256 + N2, parts=lo), bias=-16.0)
+    act(S("DS"), D2, bias=col(KCB))
     TBP = lambda a, b=None: C("PW", 400 + a, None if b is None else 400 + b)
-    for k in (0, 1):
-        o = C("PM", 64 + N2 * k, 64 + N2 * k + N2)
-        mms(*[(o, ID, S("EW", k, slice(N2 * s, N2 * s + N2))) for s in range(3)])
-    for k in (0, 1):
-        tt(C("EP", N2 * k, N2 * k + N2), C("PM", 64 + N2 * k, 64 + N2 * k + N2), C("DS", N2 * k, N2 * k + N2), A.mult)
-        act(C("DS", N2 * k, N2 * k + N2), C("EP", N2 * k, N2 * k + N2), acc=C("SM", 8 + k))
-    act(S("RA"), C("DA", 0, 24), scale=C("SM", 8))
-    act(S("RB"), C("DA", 24, 40), scale=C("SM", 9))
-    mms((TBP(0, 24), S("IDF"), S("CS")), (TBP(0, 24), S("BO"), S("RA")), (TBP(8, 24), S("BO"), S("RB")))
-
-    def record_lists():
-        iota(C("RE", 5 * 32, 9 * 32), [[0, 4 * 32]], 0)
-        iota(C("RV", 5 * 64, 9 * 64), [[0, 4 * 64]], 0)
-        act(S("RL"), S("DL"), scale=C("SM", 9))
-        mms((C("PM", 448, 496), S("IDF"), S("CL")), (C("PM", 448, 496), S("BO"), S("RL")))
-        cp(S("LU"), C("PM", 448, 496))
-
-    def places(f):
-        a, r = 128 * (f % 2), 64 * PSLOT[f]
-        XY, a = ("XX", 256) if f == 1 else ("XY", a)
-        pos, half = C(XY, a, a + 128), [C(XY, a + 64 * i, a + 64 * i + 64) for i in (0, 1)]
-        steps = [(pos, ID, S("NV", f))] + [(h, ID, S("BQ" if f else "BT")) for h in half]
-        if f:
-            steps += [(h, C(l, 0, 128), S("GV")) for h, l in zip(half, ("JH", "JM"))] + [(pos, row1, S("MB", k)) for k in (0, 1)]
-        mms(*steps)
-        ts(C("CC", 0, 64), C(XY, a, a + 128, 2), 0.0, A.max, 15.0, A.min)
-        ts(C("CC", 64, 128), C(XY, a + 1, a + 128, 2), 0.0, A.max, 31.0, A.min)
-        if f == 0:
-            act(C("RV", r, r + 64), S("NV", 0, 0))
-        elif f < F - 1:
-            tt(C("RV", r, r + 64), half[0], S("BT"), A.subtract)
+    o = C("PM", 64, 64 + N2)
+    mms(*[(o, ID, S("EW", 0, slice(N2 * s, N2 * s + N2))) for s in range(3)])
+    tt(C("EP", 0, N2), o, S("DS"), A.mult)
+    tt(C("EP", N2, 2 * N2), DD, S("EW", 1, rest), A.mult)
+    for k, name in enumerate(("RA", "RB")):
+        red(C("SM", 8 + k), C("EP", N2 * k, N2 * k + N2))
+        act(S(name), S("DA", (slice(0, 3), slice(1, 4, 2))[k]), scale=C("SM", 8 + k))
+    mms((TBP(0, 32), S("ONF"), S("CS")), (TBP(16, 32), S("BO"), S("RB")), (TBP(0, 24), S("BO"), S("RA")))
 
     def words(f):
-        act(S("U1", f), S("H1", al, f), scale=C("TB", 8 + f), bias=C("TB", f))
-        act(S("U2", f), S("H2", al, f), scale=C("TB", 16 + f))
+        act(S("U1", f), S("H1", al, f), scale=C("TB", 16 + f), bias=C("TB", 8 + f))
+        act(S("U2", f), S("H2", al, f), scale=C("TB", 24 + f))
         o = C("PM", 192 + 64 * (f % 2), 192 + 64 * (f % 2) + 64)
         mms((o, S("IDF"), S("U1", f)), (o, S("IDF"), S("U2", f)))
         tt(S("XI", f), o, S("POW", al, f), A.mult)
 
+    def columns(f, first):
+        ts(C("LU", 4 * f, 4 * f + 4), S("CL"), first, A.add, -64.0 * wbase(f), A.add)
+
     def record(f):
-        r = 32 * PSLOT[f]
-        win = lambda name, w: C(name, w * wbase(f), w * (8 if f < 6 else 10))
+        r = 64 * PSLOT[f]
+        win = lambda name: C(name, 64 * wbase(f), 64 * (8 if f < 6 else 10))
+        if f > 2:
+            columns(f, C("TB", f))
         ts(S("A0", f), S("XI", f, 0), 65024, A.bitwise_and)
         ts(S("A0", f), S("A0", f), (16 * f - 1) * 65536.0, A.add)
-        tt(S("GV"), IND(win("RV", 64), C("LU", 16 + 4 * f, 20 + 4 * f)), S("MK", f, slice(32, RW)), A.mult)
-        tt(S("GE"), IND(win("RE", 32), C("LU", 2 * f, 2 * f + 2)), S("MK", f, slice(0, 32)), A.mult)
+        tt(S("GV"), IND(win("RV"), C("LU", 4 * f, 4 * f + 4)), S("MK", f, slice(32, RW)), A.mult)
+        tt(S("GE"), IND(win("RE"), C("LU", 4 * f, 4 * f + 2)), S("MK", f, slice(0, 32)), A.mult)
         places(f)
         tt(S("XI", f, 0), S("GE"), S("A0", f), A.max)
         if f < F - 1:
@@ -476,13 +522,13 @@ def build(T, nxt):
             out = C("SND", f * P + a, f * P + b)
             if last:
                 ts(out, bank(h), 0.0, A.max, 255.0, A.min)
-            elif FIN[f > 1][h] == "s":
+            elif FIN[min(f, 2)][h] == "s":
                 act(out, bank(h), AF.Relu, bias=-BIG)
             else:
                 ts(out, bank(h), -BIG, A.add, 0.0, A.max)
-            if h in SENDS:
-                k = SENDS.index(h)
+            if h in (STORES if last else SENDS):
                 if last:
+                    k = STORES.index(h)
                     dma(("sync", "scalar")[k % 2], T.y[:, f * P + done:f * P + b], C("SND", f * P + done, f * P + b), "out%d" % (f + k))
                 else:
                     send(C("W", (9 + f) * P + done, (9 + f) * P + b), C("SND", f * P + done, f * P + b), f + 1)
@@ -500,74 +546,51 @@ def build(T, nxt):
         ts(C("YO", f * P, f * P + P), C("W", PSLOT[f] * P, PSLOT[f] * P + P), 255.0, A.min)
         dma("sync", T.y[:, f * P:f * P + P], C("YO", f * P, f * P + P), "out%d" % f, [sent(k) for k in range(f + 1, min(f + 3, F))])
 
-    TOT = C("XY", 448, 512)
-
-    def twice(f, more=()):
-        o = C("XY", 256 + 64 * f, 320 + 64 * f)
-        ob = C("XY", 288 + 64 * f, 320 + 64 * f)
-        mms((o, row1, S("CI", 0)), *[(o, ID, S("IDX", al, f))] * 2,
-            *[(ob, FXL[i], S("FX", i, slice(32 * f, 32 * f + 32))) for i in (0, 1, 0, 1)], *more)
-        return o
-
-    def offsets(f, idx, slots, more=()):
-        act(S("AB", 5 + f), S("IDX", al, f), AF.Relu, scale=512.0 * (f + 1), bias=-3584.0 * (f + 1))
-        for k, (c, v) in enumerate(slots):
-            ts(S("AB", 2 * f + k), idx, C("SR", c), A.is_equal, v * P, A.mult)
-        mms((TOT, ID, S("AB", 5 + f)), (TOT, S("I32"), C("CC", 0, 64)), (TOT, ID, C("CC", 64, 128)), *more,
-            *[(TOT, ID, S("AB", 2 * f + k)) for k in range(len(slots))])
-        ts(C("OFF", 64 * f, 64 * f + 64), TOT, float(P * (7 - wbase(f))), A.add)
-
-    I0 = twice(0)
-    places(0)
-    offsets(0, I0, ((0, -2.0), (1, -1.0)))
-    IA0, OKS = C("XY", 384, 416), C("XX", 384, 416)
-    mms((IA0, row1, S("CI", 1, slice(0, 32))), (IA0, ID, S("IDX", 0, 0)), (IA0, ID, S("IDX", 0, 0)), (IA0, NH, S("MK", 1, slice(0, 32))))
-    for n in range(4):
-        ts(S("OK", n), IA0, C("SR", n), A.is_equal, C("SR", 15 - n), A.mult)
-    tt(S("GW"), S("NV", 0, 0), S("MK", 1, slice(32, RW)), A.mult)
-    ts(S("GV"), S("GW"), ISB, A.mult, -1.0 / 512, A.mult)
-    places(1)
-    I1 = twice(1, [(C("XY", 320, 352), ID, S("OK", n)) for n in range(4)])
-    mms(*[(OKS, NH, S("OK", n)) for n in range(4)])
-    offsets(1, I1, ((4, -2.0), (5, -1.0), (6, -3.0)), [(C("XY", 448, 480), ID, S("OK", n)) for n in (0, 0, 1)])
-    act(C("ON", 0, 32), OKS, AF.Sign)
-    act(C("ON", 32, 64), OKS, AF.Relu, scale=-1.0, bias=1.0)
-
     tt(S("PX"), S("POW", 0, slice(0, 2)), S("ON"), A.mult)
+    lists(2, 4)
+    vec(2, 4)
+    masks(2, 4)
+    power(2, 4, "XY", 256)
     for f, a, n in ((0, 0, 32), (1, 32, 32), (2, 64, 64)):
         h = lambda name: S(name, 0 if f < 2 else al, f)
-        ts(C("U0", a, a + n), h("H1"), TBP(8 + f), A.mult, TBP(f), A.add)
-        ts(C("XX", 256 + a, 256 + a + n), h("H2"), TBP(16 + f), A.mult)
-    act(S("TB"), TBP(0, 24))
-    tt(C("XX", 384, 512), C("XX", 256, 384), S("U0"), A.add)
-    tt(S("XB", slice(0, 2)), C("XX", 384, 448), S("PX"), A.mult)
-    tt(S("XI", 0, 0), C("XX", 384, 416), S("POW", 0, 0), A.mult)
-    tt(S("XI", 2), C("XX", 448, 512), S("POW", al, 2), A.mult)
+        ts(C("U0", a, a + n), h("H1"), TBP(16 + f), A.mult, TBP(8 + f), A.add)
+        ts(C("PW", 128 + a, 128 + a + n), h("H2"), TBP(24 + f), A.mult)
+    columns(2, TBP(2))
+    for a in (0, 64):
+        tt(C("PW", 256 + a, 320 + a), C("PW", 128 + a, 192 + a), C("U0", a, a + 64), A.add)
+    tt(S("XB", slice(0, 2)), C("PW", 256, 320), S("PX"), A.mult)
+    tt(S("XI", 0, 0), C("PW", 256, 288), S("POW", 0, 0), A.mult)
+    tt(S("XI", 2), C("PW", 320, 384), S("POW", al, 2), A.mult)
+    act(S("TB"), TBP(0, 32))
     tt(S("XI", 1, 0), S("XB", 0), S("XB", 1), A.max)
-    for f in (1, 0):
-        ts(C("RE", 32 * PSLOT[f], 32 * PSLOT[f] + 32), S("XI", f, 0), 65024, A.bitwise_and)
     for f in range(F):
         pixels(f)
+        if f == 0:
+            iota(C("RE", 0, 10 * 64), [[0, 10 * 64]], 0)
+            iota(C("RV", 5 * 64, 9 * 64), [[0, 4 * 64]], 0)
+            diag("JM", 160, 256, -0.5)
+            diag("JH", 160, 256, 0.5)
+            for k in (1, 0):
+                ts(C("RE", 64 * PSLOT[k], 64 * PSLOT[k] + 32), S("XI", k, 0), 65024, A.bitwise_and)
         if f == 1:
             iota(S("MZ"), [[0, 192]], int(BIG))
             iota(S("NG"), [[0, 128]], -1)
+        if f + 2 < F:
+            dma("sync", C("RES", (f + 2) * P, (f + 3) * P), T.res[:, (f + 2) * P:(f + 3) * P], "res%d" % (f + 2), [sent(f + 1)])
         if f == 0:
-            record_lists()
-            dma("sync", C("RES", 2 * P, 3 * P), T.res[:, 2 * P:3 * P], "res2", [sent(1)])
-            dma("sync", S("VY", slice(3, 8)), T.vy[:, 192:512], "vy2")
-            dma("sync", S("VX", slice(3, 8)), T.vx[:, 192:512], "vx2")
-        if f in (1, 2):
-            a, b = ((3, 5), (5, 8))[f - 1]
-            dma("sync", C("RES", a * P, b * P), T.res[:, a * P:b * P], "res%d" % a, [sent(f + 1)])
+            dma("sync", C("IA", 128, 256), T.ia[:, 128:256], "ia2")
+            dma("sync", C("IB", 128, 256), T.ib[:, 128:256], "ib2")
+        if f == 1:
+            dma("sync", S("VY", slice(4, 8)), T.vy[:, 256:512], "vy2")
+            dma("sync", S("VX", slice(4, 8)), T.vx[:, 256:512], "vx2")
         if f == 1:
             record(2)
-            lists(3, 8)
-            masks(3, 8)
-            power(3, 5, "PW", 0)
             words(3)
-            power(5, 8, "PW", 192)
-        if f in (1, 2, 3):
-            vec(2 * f + 1, min(2 * f + 3, F))
+            lists(4, 8)
+            masks(4, 8)
+            power(4, 8, "PW", 0)
+        if f in (2, 3):
+            vec(2 * f, 2 * f + 2)
         if 1 < f < F - 1:
             record(f + 1)
         if 1 < f < F - 2:
@@ -587,8 +610,8 @@ def schedule(ops):
     for j, (q0, fn, rd, wr, waits, sem, cost) in enumerate(ops):
         q = queue[j]
         for s, v in waits:
-            for i in raised.get(int(s[3:]), ()):
-                pre[j][i] = HOP + COL * (P - int(ops[i][2][0][1].min()) % P)
+            for k, i in enumerate(raised.get(int(s[3:]), ())[::-1]):
+                pre[j][i] = HOP + ROWS * (k + 1) + COL * (P - int(ops[i][2][0][1].min()) % P)
         for name, el, w in [(a, e, False) for a, e in rd] + [(a, e, True) for a, e in wr]:
             lo, hi = int(el.min()), int(el.max())
             for i, pw, plo, phi, pel in acc.get(name, ()):
@@ -609,6 +632,10 @@ def schedule(ops):
         l = [j for j in range(n) if queue[j] == q]
         for i, j in zip(l, l[1:]):
             pre[j].setdefault(i, None)
+    for name in ("GP", "GQ"):
+        l = [j for j in range(n) if ops[j][3] and ops[j][3][0][0] == name]
+        for i, j in zip(l, l[1:]):
+            pre[j].setdefault(i, 0.0)
     span = [o[6] for o in ops]
     unit = ["dma" if o[5] in DMAS else q for o, q in zip(ops, queue)]
     land = [LAND if u == "dma" else 0.0 for u in unit]
@@ -618,53 +645,90 @@ def schedule(ops):
         for i, d in lag[j].items():
             back[i][j] = d + span[j] - span[i]
 
-    def place(edges, rank, first):
-        post = [[] for o in ops]
-        for j in range(n):
-            for i in edges[j]:
-                post[i].append(j)
-        left = [len(e) for e in edges]
-        todo = [(rank[j], j) for j in range(n) if not left[j]]
-        start, busy = [0.0] * n, {u: [] for u in unit}
-        while todo:
-            j = min(todo)[1]
-            todo.remove((rank[j], j))
-            t = max([first[j]] + [start[i] + d for i, d in edges[j].items()])
-            l = busy[unit[j]]
-            k = 0
-            while k < len(l) and l[k][0] < t + span[j] - 1e-9:
-                t = max(t, l[k][1])
+    ahead, behind = [list(e.items()) for e in lag], [list(e.items()) for e in back]
+    up = list(range(n))
+    down = up[::-1]
+
+    def place(edges, rank, first, walk):
+        rank = list(rank)
+        for j in walk:
+            for i, d in edges[j]:
+                if rank[i] >= rank[j]:
+                    rank[j] = rank[i] + 1e-7
+        start, busy = [0.0] * n, {u: ([], []) for u in unit}
+        for j in sorted(walk, key=lambda j: rank[j]):
+            t = first[j]
+            for i, d in edges[j]:
+                if start[i] + d > t:
+                    t = start[i] + d
+            a, b = busy[unit[j]]
+            k = len(b)
+            while k and b[k - 1] > t:
+                k -= 1
+            while k < len(a) and a[k] < t + span[j] - 1e-9:
+                t = max(t, b[k])
                 k += 1
-            l.insert(k, (t, t + span[j]))
+            a.insert(k, t)
+            b.insert(k, t + span[j])
             start[j] = t
-            for k in post[j]:
-                left[k] -= 1
-                if not left[k]:
-                    todo.append((rank[k], k))
         return start
 
-    group = [0] * n
     seed = [1]
 
     def draw():
         seed[0] = (seed[0] * 1103515245 + 12345) % 2 ** 31
         return seed[0] / 2.0 ** 31
 
-    marks = [j for j in range(n) if isinstance(ops[j][5], int) or "OFF" in [a for a, e in ops[j][3]]]
-    worth = lambda start: max(start[j] + span[j] for j in range(n)) + 0.002 * sum(start[j] for j in marks)
-    best = (1e9, [float(j) for j in range(n)], None)
+    marks = [j for j in up if isinstance(ops[j][5], int) or "OFF" in [a for a, e in ops[j][3]]]
+    cases = []
+    for engines, waits, writes in SLOWER:
+        more = [writes if isinstance(ops[j][5], int) else 0.0 if land[j] else (engines - 1) * span[j] for j in up]
+        more = [2 * more[j] if unit[j] == "pool" and span[j] > 1 else more[j] for j in up]
+        holds = [more[j] if unit[j] != "pool" or span[j] > 1 else 0.0 for j in up]
+        cases.append(([[(i, d + (holds[i] if unit[j] == "pool" else more[i]) + waits * (pre[j][i] == WAKE)) for i, d in ahead[j]] for j in up],
+                      [span[j] + holds[j] for j in up]))
+
+    def slower(start):
+        total, order = 0.0, sorted(up, key=lambda j: start[j])
+        for edges, takes in cases:
+            at, free = [0.0] * n, {u: 0.0 for u in unit}
+            for j in order:
+                t = max(free[unit[j]], land[j])
+                for i, d in edges[j]:
+                    if at[i] + d > t:
+                        t = at[i] + d
+                at[j] = t
+                free[unit[j]] = t + takes[j]
+            total += 0.5 * max(free.values())
+        return total
+
+    rank = [-s for s in span]
+    for j in down:
+        for i, d in ahead[j]:
+            rank[i] = min(rank[i], rank[j] - d)
+    due = [0.7 - min(rank) + r for r in rank]
+    head = [j for j in up if due[j] < 15]
+    best = now = (1e9, None, rank, 1e9)
     for k in range(ROUNDS):
-        if k < 4 or draw() < 0.3:
-            late = place(back, [-best[1][j] - span[j] for j in range(n)], [0.0] * n)
-            rank = [-late[j] - span[j] + 0.1 * draw() for j in range(n)]
-        else:
-            rank, part = list(best[2]), 0.05 * draw()
-            for j in range(n):
-                if draw() < part and best[1][j] < 18:
-                    rank[j] += draw() - 0.5
-        start = place(lag, rank, land)
-        if worth(start) <= best[0]:
-            best = (worth(start), start, rank)
+        if k == ROUNDS * 2 // 3:
+            best = now = (best[3] + slower(best[1]),) + best[1:]
+        if k and draw() < 0.3:
+            late = place(behind, [-now[1][j] - span[j] for j in up], [0.0] * n, down)
+            rank = [-late[j] - span[j] + 0.1 * draw() for j in up]
+        elif k:
+            rank, early = list(now[2]), [j for j in up if now[1][j] < 17]
+            for m in range(1 + int(0.05 * draw() * len(early))):
+                rank[early[int(draw() * len(early))]] += draw() - 0.5
+        start = place(ahead, rank, land, up)
+        end = max(start[j] + span[j] for j in up) + 0.003 * sum(start[j] for j in marks)
+        end += 0.01 * sum((start[j] - due[j]) ** 2 for j in head if start[j] > due[j])
+        if end > now[3] + 0.25:
+            continue
+        value = end + (slower(start) if k >= ROUNDS * 2 // 3 else 0.0)
+        if value <= now[0] + 0.06 * draw() * (1 - k / ROUNDS):
+            now = (value, start, rank, end)
+        if value < best[0]:
+            best = now
     issue = list(best[1])
     for j in range(n):
         if land[j]:

import numpy as np
from concourse.mybir import AluOpType as A, AxisListType, ActivationFunctionType as AF

F = 8
P = 512
CUTS = [0, 160, 288, 416, 512]
FIN = ("ssvv", "ssss", "vssv")
SENDS = (1, 3)
STORES = (1, 2, 3)
BIG = 8388608.0
NN = 26
N2 = 2 * NN
N3 = 3 * N2
N0 = 12
RW = 96
DS_, DB = 261627 / 2.0 ** 18, 509 / 2.0 ** 18
US, UB = 11629 / 2.0 ** 14, 5725 / 2.0 ** 14

f32, bf, i32, u16, f16 = "float32", "bfloat16", "int32", "uint16", "float16"
SB_ = {
    "W": ([128, 16 * P], bf), "RES": ([128, F * P], bf), "SND": ([128, F * P], bf), "YO": ([128, 7 * P], bf),
    "GP": ([128, P], bf), "GQ": ([128, P], f16),
    "IA": ([128, 256], i32), "IB": ([128, 256], i32), "VY": ([128, 8, 2, 32], i32), "VX": ([128, 8, 2, 32], i32),
    "CT": ([128, 8], i32), "CB": ([128, 8], bf), "CA": ([128, 8], f32),
    "ONE": ([128, 128], bf), "MR": ([1, 192], bf), "MZ": ([1, 192], bf), "MQ": ([1, 128], bf), "MB": ([1, 3, 128], bf),
    "NG": ([1, 128], bf), "CY": ([1, 4 * N2 + 8], bf), "CI": ([1, 2, 64], bf), "ONF": ([1, 128], f32),
    "VA": ([128, 128], bf), "VN": ([128, 128], bf), "VI_": ([128, 128], bf),
    "GL": ([128, 2, 128], bf), "CW": ([128, 128], bf), "BW": ([128, 128], bf),
    "J": ([128, 256], bf), "JH": ([128, 256], bf), "JM": ([128, 256], bf), "N15": ([128, 128], bf), "I32": ([128, 128], bf),
    "BO": ([128, 8, 2, 8], f32), "IDF": ([128, 128], f32), "LE": ([128, 128], bf), "LT": ([128, 128], bf), "M": ([128, 128], bf),
    "LA": ([128, 128], bf), "SEL": ([128, 2, 8, 2, 8], bf),
    "PI": ([128, 8], i32), "PC": ([128, 32], f32), "EF": ([128, 8], f32),
    "NR": ([128, N2], bf), "OM": ([128, N2], bf), "OR": ([128, N2], bf), "EQ": ([128, 2, N2], bf), "EQC": ([128, N2], bf),
    "GEN": ([128, N2], bf), "TA": ([128, 8, 32], bf), "X": ([128, 2, 56], bf), "Z": ([128, 56], bf),
    "Y": ([128, 2, N3 + 4], bf), "YH": ([128, N2], bf), "RK": ([128, N3], bf), "SQ": ([128, 2, N3], f32), "EW": ([128, 2, N3], bf),
    "DS": ([128, N2], f32), "EP": ([128, 104], f32), "KT": ([128, N2], bf),
    "DA": ([128, 4, 8], f32), "RA": ([128, 24], f32), "RB": ([128, 16], f32), "CS": ([1, 4, 8], f32), "CL": ([128, 4], f32),
    "TB": ([128, 32], f32), "LU": ([128, 32], u16), "SM": ([128, 16], f32), "SH": ([128, 8], bf),
    "HB": ([128, 32], bf), "HI": ([128, 2, 32], bf), "XH": ([128, 32], bf), "VI": ([128, 64], bf),
    "KS": ([128, 3, 16], f32), "JK": ([128, 8, 16], bf), "SR": ([128, 16], f32), "AB": ([128, 7, 64], bf), "OK": ([128, 4, 32], bf),
    "ON": ([128, 64], bf), "PX": ([128, 64], bf), "XB": ([128, 3, 32], f32), "GW": ([128, 64], bf),
    "IDX": ([128, 8, 2, 32], bf), "H1": ([128, 8, 2, 32], bf), "H2": ([128, 8, 2, 32], bf), "FX": ([128, 2, 256], bf),
    "PQ": ([128, 2, 8, 32], f32), "POW": ([128, 2, 8, 32], bf),
    "NV": ([128, 8, 2, 32, 2], bf), "BT": ([128, 32, 2], bf),
    "MK": ([128, 8, RW], bf), "U0": ([128, 128], f32), "U1": ([128, 8, 64], f32), "U2": ([128, 8, 64], f32), "XI": ([128, 8, 2, 32], i32), "A0": ([128, 8, 32], i32),
    "SS": ([128, 2, 64], i32), "RE": ([128, 11 * 64], i32), "RV": ([128, 11 * 64], bf), "GE": ([128, 32], f32), "GV": ([128, 64], bf),
    "CC": ([128, 128], bf), "S2": ([128, 64], i32), "OFF": ([128, F * 64], u16),
}
PS_ = ["PA", "PB", "PU", "XY", "XX", "PM", "PN", "PW"]
SCRATCH = {k: ("sbuf", v[0], v[1]) for k, v in SB_.items()}
SCRATCH.update({k: ("psum", [128, P], f32) for k in PS_})
DMAS = ["ctl", "pic", "pid", "pi0", "ia_", "ib_", "vy_", "vx_", "ia2", "ib2", "vy1", "vx1", "vy2", "vx2"] + ["res%d" % f for f in range(F)] + ["out%d" % f for f in range(F + 2)]
SEMAPHORES = ["dve", "act", "pe", "pool"] + DMAS + ["arr%d" % f for f in range(F)] + ["snt%d" % f for f in range(F)]

PSLOT = [4, 3, 2, 1, 0, 9, 8, 10]

CYC, WAKE, LAND, HOP, ROWS, COL = 0.0009, 0.24, 1.2, 1.1, 0.25, 0.0003
SLOWER = ((1.3, 0.06, 0.0), (1.0, 0.0, 1.2))
ROUNDS = 12000
ORDER = []
WIDTH = {f32: 4, i32: 4, bf: 2, u16: 2, f16: 2}


def wbase(f):
    return max(0, 5 - f)


def build(T, nxt):
    ops = []
    cache = {}
    al = slice(None)

    def S(name, *ix, parts=al):
        shape = SCRATCH[name][1]
        if name in ("IDX", "H1", "H2"):
            ix = ix[::-1]
        if name not in cache:
            cache[name] = np.arange(int(np.prod(shape[1:]))).reshape(shape[1:])
        el = np.asarray(cache[name][ix] if ix else cache[name]).ravel()
        return (T[name][(parts,) + ix], name, el)

    def C(name, a, b=None, st=None, parts=al):
        return S(name, slice(a, a + 1 if b is None else b, st), parts=parts)

    def IND(win, off):
        return (win[0].indirect(off[0]), win[1], win[2], off)

    def val(x):
        return x[0] if isinstance(x, tuple) else x

    def add(q, fn, outs, ins, waits=(), sem=None, rate=None):
        rd = []
        for x in ins:
            if isinstance(x, tuple):
                rd.append((x[1], x[2]))
                if len(x) > 3:
                    rd.append((x[3][1], x[3][2]))
        full = [x for x in list(outs) + list(ins) if isinstance(x, tuple)]
        n = len(full[0][2])
        width = [WIDTH[SCRATCH[x[1]][2]] for x in full if len(x[2]) == n]
        if any(len(x) > 3 for x in full):
            cost = 0.06 + 1.5 * CYC * n
        elif sem is not None:
            cost = 0.15 + (rate or 0) if q == "pool" else n * width[0] / 2500.0
        elif q == "dve":
            cost = CYC * max(64, len(full[-1][2]) if rate == 0 else n * (rate or (0.5 if max(width) == 2 else 1)))
        else:
            cost = {"act": 0.03 + CYC * n, "pe": CYC * max(64, n) * (0.5 if width[-1] == 2 else 2), "pool": 0.15 + 2 * CYC * n}[q] + (rate or 0)
        ops.append((q, fn, rd, [(x[1], x[2]) for x in outs], list(waits), sem, cost))

    def ts(o, i, s1, op0, s2=None, op1=None, waits=()):
        if op1 is None:
            add("dve", lambda e: e.tensor_scalar(o[0], i[0], val(s1), None, op0), [o], [i, s1], waits)
        else:
            add("dve", lambda e: e.tensor_scalar(o[0], i[0], val(s1), val(s2), op0, op1), [o], [i, s1, s2], waits)

    def tt(o, a, b, op):
        add("dve", lambda e: e.tensor_tensor(o[0], a[0], b[0], op), [o], [a, b], rate=1 if a[1] in PS_ or b[1] in PS_ else 2)

    def cp(o, i, waits=()):
        add("dve", lambda e: e.tensor_copy(o[0], i[0]), [o], [i], waits)

    def ms(o, c):
        add("dve", lambda e: e.memset(o[0], c), [o], [])

    def red(o, i, op=A.add, negate=False):
        add("dve", lambda e: e.tensor_reduce(o[0], i[0], AxisListType.X, op, negate=negate), [o], [i], rate=0)

    def scan(o, d0, d1, ini, op1=A.add):
        add("dve", lambda e: e.tensor_tensor_scan(o[0], d0[0], d1[0], val(ini), A.add, op1), [o], [d0, d1, ini])

    def act(o, i, func=AF.Identity, bias=0.0, scale=1.0, waits=(), first=False, acc=None):
        if acc is None:
            add("act", lambda e: e.activation(o[0], i[0], func, bias=val(bias), scale=val(scale)), [o], [i, bias, scale], waits,
                rate=1.3 if first else None)
        else:
            add("act", lambda e: e.activation(o[0], i[0], func, bias=val(bias), scale=val(scale), accum_out=acc[0]), [o, acc],
                [i, bias, scale], waits, rate=0.02)

    def mm(o, l, r, st, sp):
        add("pe", lambda e: e.matmul(o[0], l[0], r[0], st, sp), [o], [l, r])

    def mms(*steps):
        for k, (o, l, r) in enumerate(steps):
            mm(o, l, r, k == 0, k == len(steps) - 1)

    def iota(o, pat, base, cm=0):
        if SCRATCH[o[1]][2] == i32:
            add("pool", lambda e: e.iota(o[0], pat, base, cm), [o], [])
        else:
            add("pool", lambda e: e.iota(o[0], pat, base, cm, allow_small_or_imprecise_dtypes=True), [o], [])

    def select(o, i, pat, op, fill, base, cm):
        add("pool", lambda e: e.affine_select(o[0], i[0], pat, op, fill, base, cm), [o], [i])

    def dma(q, o, i, sem, waits=()):
        add(q, lambda e: e.dma_start(val(o), val(i)), [o] if isinstance(o, tuple) else [], [i], waits, sem)

    def send(o, i, k, mask=nxt[2], first=False):
        add("pool", lambda e: e.remote_dma(o[0], i[0], T.sem["arr%d" % k], T.sem["snt%d" % k], nxt[1], nxt[0], mask),
            [], [i], (), k, rate=1.0 if first else None)

    neng = bin(nxt[2]).count("1")
    narr = nxt[3]
    sent = lambda k: ("snt%d" % k, neng * (len(SENDS) if k else 1))
    col = lambda k: C("PC", k)
    (FP, P71, L16, HALF, W16, F0, NF2, C23, W2, LB, L2, KCB, SG, T2, WS, CA0, CB2, SB0, SB1, SC1, L32, K0, K1, W4, W5) = range(25)
    D_, R_ = slice(0, NN), slice(NN, N2)
    N0_ = slice(NN - N0, NN)
    lo, hi, row = slice(0, 64), slice(64, 128), slice(0, 1)
    one = lambda a, b: C("ONE", a, b, parts=row)
    row1 = one(0, 128)
    ID, NH = C("J", 0, 128), C("JM", 0, 128)

    for h, q in enumerate(("sync", "scalar")):
        pp = slice(64 * h, 64 * h + 64)
        dma(q, C("CT", 0, parts=pp), T.gaps[:], "ctl")
        dma(q, C("CT", 1, parts=pp), T.cmd[:], "ctl")
        dma(q, C("CT", 2, 5, parts=pp), T.rel[:], "ctl")
    dma("sync", C("W", 6 * P, 6 * P + P // 2), T.pic0[:, P:P + P // 2], "pic")
    dma("sync", C("W", 6 * P + P // 2, 7 * P), T.pic0[:, P + P // 2:2 * P], "pid")
    dma("sync", C("IA", 0, 128), T.ia[:, 0:128], "ia_")
    dma("sync", C("IB", 0, 128), T.ib[:, 0:128], "ib_")
    dma("sync", S("VY", slice(0, 2)), T.vy[:, 0:128], "vy_")
    dma("sync", S("VX", slice(0, 2)), T.vx[:, 0:128], "vx_")
    dma("sync", C("W", 5 * P, 6 * P), T.pic0[:, 0:P], "pi0")
    dma("sync", C("RES", 0, P), T.res[:, 0:P], "res0")
    dma("sync", S("VY", slice(2, 4)), T.vy[:, 128:256], "vy1", [sent(0)])
    dma("sync", S("VX", slice(2, 4)), T.vx[:, 128:256], "vx1")
    dma("sync", C("RES", P, 2 * P), T.res[:, P:2 * P], "res1")

    ms(S("ONE"), 1.0)
    iota(C("PI", 0), [[0, 1]], 0, 1)
    iota(S("VN"), [[0, 2], [16, 8], [1, 8]], 0, -1)
    iota(S("HB"), [[1, 32]], 0)
    iota(S("VI_"), [[1, 128]], 0, -1)
    iota(S("VA"), [[0, 2], [-8, 8], [0, 8]], 0, 1)
    for k in (0, 1):
        a, b = k * P // 2, (k + 1) * P // 2
        send(C("W", 8 * P + a, 8 * P + b), C("W", 6 * P + a, 6 * P + b), 0, nxt[4][k], k == 0)
    for k, v in ((5, 120), (1, 7), (2, 71), (3, 15)):
        ts(C("PI", k), C("PI", 0), v, A.bitwise_and)
    ts(col(K0), C("PI", 5), -1532.5, A.add)
    ts(col(K1), C("PI", 5), -1531.5, A.add)
    ts(C("PI", 4), C("PI", 0), 6, A.arith_shift_right)
    cp(C("PC", 0, 4), C("PI", 1, 5))
    act(col(F0), col(FP), AF.Relu, scale=-1.0, bias=1.0)
    act(col(NF2), col(FP), scale=-1.0, bias=-2.0)
    act(col(C23), col(FP), scale=-1.0, bias=23.0)
    act(col(W16), col(HALF), scale=-16.0, bias=16.0)
    for k, name in enumerate(("LE", "LT")):
        ts(S("GL", k), S("VN"), col(K0 + k), A.subtract, 0.125, A.mult)
        ts(S(name), S("GL", k), 192.0, A.is_equal)
    ts(S("LA"), S("VA"), col(P71), A.is_equal, col(W16), A.mult)
    ts(ID, S("VI_"), 0.0, A.is_equal)
    act(NH, ID, scale=-0.5)
    act(S("I32"), ID, scale=32.0)
    def diag(name, a, b, v):
        select(C(name, a, b), C("J", a % 128, a % 128 + b - a), [[1, b - a]], A.not_equal, v, a % 128, -1)

    diag("J", 128, 256, 1.0)
    select(S("SEL", 1), S("ONE"), [[-8, 8], [0, 16]], A.is_equal, 0.0, -1, 1)
    for name, a, b, v in (("JM", 128, 160, -0.5), ("JH", 0, 128, 0.5), ("JH", 128, 160, 0.5), ("N15", 0, 128, -3.0)):
        diag(name, a, b, v)
    iota(S("CI", 1), [[0, 64]], -16)
    iota(S("ONF"), [[0, 128]], 1)
    act(S("MB", 1), row1, scale=-1.5 * BIG)
    act(S("MB", 2), row1, scale=-0.25)
    act(S("IDF"), ID)
    for a in range(0, P, 128):
        act(C("W", 7 * P + a, 7 * P + a + 128), S("ONE"), scale=128.0)
    for o, v in ((S("MR"), 151.0 * 256), (S("MQ"), 217.0), (S("MB", 0), 1.5 * BIG), (S("CY"), 56.0), (C("CY", 1, 1 + N2), 1080.0),
                 (C("CY", 1 + N2, 1 + 2 * N2), 568.0), (S("CI", 0), -11.0)):
        ms(o, v)
    act(S("NR", R_), C("HB", 0, NN), bias=col(NF2))
    act(S("NR", D_), C("HB", 0, NN), scale=-1.0, bias=col(C23))
    ts(C("KT", 0, 8), C("HB", 0, 8), col(FP), A.is_ge, 0.5, A.max)
    red(col(W2), C("KT", 0, 8), A.mult)
    ts(S("BW"), S("LA"), col(W2), A.mult, 2.0 ** -17, A.mult)
    act(S("CW"), ID, scale=col(W2))
    CWP = C("PM", 0, 128)
    mms((CWP, S("ONE"), S("CW")), (CWP, S("I32"), S("LT")))
    for h in (0, 1):
        ts(S("SEL", 0, al, h), C("VA", 0, 64), 0.0, A.is_equal)
    act(col(LB), col(FP), AF.Abs, bias=-4.25)
    act(col(L2), col(LB), bias=-2.25)
    for k, (v, c) in enumerate(((4.0, 143.0), (2.0, 180.0))):
        act(col(W4 + k), col(W2), scale=v)
        act(S("HI", k), S("HB"), scale=col(W4 + k), bias=c - 0.5 + 1.0 / 64)
    BITS = C("PM", 128, 160)
    mms((BITS, S("MQ"), one(0, 32)), (BITS, ID, S("HI", 0)), *[(BITS, NH, S("HI", 1))] * 4)
    act(col(SG), col(FP), AF.Sign, bias=-4.5)
    act(col(T2), col(SG), scale=5.0 / 16, bias=2.0 / 16)
    act(col(WS), col(FP), scale=-1.0 / 16, bias=col(T2))
    halves = {KCB: (-16.0, 7.0), SB0: (DB - 2 * DS_, DB - 4 * DS_), SC1: (DS_, 2 * DS_), SB1: (DB - 5 * DS_, DB - 8 * DS_),
              CA0: (0.0, 2.0 ** -13), CB2: (-16.0, 16.0)}
    for k, (a, b) in halves.items():
        act(col(k), col(HALF), scale=b - a, bias=a)
    act(S("KT", D_), C("HB", 0, NN), AF.Relu, bias=-23.0)
    act(S("KT", R_), C("HB", 0, NN), AF.Relu, scale=-1.0, bias=2.0)
    F8 = C("HB", 0, 8)
    act(S("EF"), F8, AF.Abs, scale=-1.0, bias=col(FP))
    act(S("EF"), S("EF"), AF.Relu, scale=-1.0 / 16, bias=1.0 / 16)
    iota(S("CS", slice(0, 4, 2)), [[0, 2], [0, 8]], 0)
    act(S("CS", 1), C("HB", 0, 8, parts=row), scale=0.0, bias=7.0 * 16513 * 512 + 256.0)
    act(S("CS", 3), C("HB", 0, 8, parts=row), scale=512.0, bias=512.0)
    for k, c in ((0, CA0), (1, W16), (3, CB2)):
        act(S("DA", k), S("EF"), scale=col(c))
    act(S("DA", 2), S("DA", 1), scale=-1.0)
    act(S("CL"), C("HB", 0, 4), scale=16.0, bias=col(L16))
    act(col(L32), col(L16), bias=16.0)
    for k, c in ((0, L16), (1, L32)):
        act(S("BT", slice(k, 32, 2), 0), C("HB", 0, 16))
        act(S("BT", slice(k, 32, 2), 1), C("HB", 0, 16), scale=0.0, bias=col(c))
    GM, GEX, U, UT, SU, UP, ROWM, OMW = [S("TA", k, slice(0, n)) for k, n in enumerate((NN, NN, NN, NN, NN, NN, N0, N0))]
    act(ROWM, C("HB", 0, N0), scale=-2.0 / 256, bias=23.0 / 256)
    FXL = (ID, NH)

    def lists(f0, f1):
        fs, cs, nd = slice(f0, f1), slice(32 * f0, 32 * f1), C("XX", 32 * f0, 32 * f1)
        ts(nd, S("IA", cs), 8.0, A.is_le)
        tt(S("IDX", 0, fs), S("IA", cs), nd, A.mult)
        tt(S("IDX", 1, fs), S("IB", cs), nd, A.mult)
        v = 1.0 if f0 else 2.0
        act(S("FX", 0, cs), S("IDX", 1, fs), AF.Relu, scale=-3.0 * v, bias=3.0 * v)
        act(S("FX", 1, cs), S("IDX", 1, fs), AF.Relu, scale=-2.0 * v, bias=4.0 * v)

    def masks(f0, f1, v=1.0, explicit=0.0, direct=129.0):
        fs, nd = slice(f0, f1), C("XX", 32 * f0, 32 * f1)
        act(S("MK", fs, slice(0, 32)), nd, scale=explicit - direct, bias=direct)
        for k in (32, 33):
            act(S("MK", fs, slice(k, RW, 2)), nd, scale=-v, bias=v)

    def vec(f0, f1):
        fs, nd = slice(f0, f1), C("XX", 32 * f0, 32 * f1)
        for n in (0, 1):
            for i in (0, 1):
                tt(S("NV", fs, i, al, n), S(("VY", "VX")[n], fs, i), nd, A.mult)

    def power(f0, f1, name, a, m=2):
        fs, n, ls = slice(f0, f1), 32 * (f1 - f0), slice(0, m)
        ts(S("H1", ls, fs), S("IDX", ls, fs), 3.0, A.is_ge)
        ts(S("H2", ls, fs), S("IDX", ls, fs), 6.0, A.is_ge)
        o = lambda i: C(name, a + n * i, a + n * i + n)
        mms(*[(o(i), ID, S("IDX", i, fs)) for i in range(m)], *[(o(1), FXL[i], S("FX", i, slice(32 * f0, 32 * f1))) for i in (0, 1) if m > 1],
            *[(o(i), S("N15"), S(h, i, fs)) for h in ("H1", "H2") for i in range(m)])
        act(S("PQ", ls, fs), C(name, a, a + m * n), AF.Square, scale=US, bias=UB - US)
        act(S("POW", ls, fs), S("PQ", ls, fs), bias=2.0 ** -14 - float(np.float32(UB * UB)))

    lists(0, 2)
    vec(0, 2)
    masks(1, 2, -1.0 / 512, 99.0, 0.0)

    CM, CV, CR = C("CA", 0), C("CA", 1), C("CA", 2)
    cp(C("CB", 0), C("CT", 0))
    ts(C("CB", 1, 4), C("CT", 2, 5), -1.0, A.mult)
    ts(CM, C("CT", 1), 1.0, A.is_equal, 256.0, A.mult)
    ts(CV, C("CT", 0), col(F0), A.is_ge, 4096.0, A.mult)
    ts(CR, C("CT", 1), 2.0, A.is_equal, CV, A.mult)
    TX, TG, TM0, TM1 = C("PA", 0), C("XY", 400), C("XY", 401), C("XY", 402)
    mms((TX, S("LE"), C("CB", 0)), (TX, ID, C("CB", 1)))
    mms(*[(t, S("LE"), C("CB", 0)) for t in (TG, TM0, TM1)], (C("XY", 401, 403), ID, C("CB", 2, 4)))
    OM, OR = lambda h=al: S("OM", h), lambda h=al: S("OR", h)
    ts(OM(), S("NR"), TX, A.is_equal, CM, A.mult)
    ts(OR(), S("NR"), TX, A.is_equal, CR, A.mult)
    ts(S("EQ", 0), S("NR"), TM0, A.is_equal, -512.0, A.mult)
    ts(S("EQ", 1), S("NR"), TM1, A.is_equal, -1024.0, A.mult)
    ts(GEX, S("NR", D_), TG, A.is_ge, 2048.0, A.mult)
    ts(GM, S("NR", D_), TX, A.is_ge, 2.0, A.mult)
    ts(S("EQC"), S("NR"), TG, A.is_equal, col(WS), A.mult)
    SS_, R1 = C("PU", 0, NN), C("PB", 0, N2)
    mms((SS_, S("BW"), OR(D_)), (SS_, ID, OM(D_)))
    mms((R1, S("LT"), OM()), (R1, NH, OM()), (R1, NH, OM()), (R1, S("LT"), OR()))
    R3 = C("PN", 0, NN)
    R2, R4, R5 = [C("PB", 64 + NN * k, 64 + NN * k + NN) for k in range(3)]
    mms((R3, S("LT"), OM(D_)), (R3, S("LT"), OR(D_)), (R3, ID, GEX), (R3, NH, GM))
    RHO, CAND, DN, ZC = [C("SM", k) for k in range(4)]
    red(RHO, SS_, A.max)
    ts(S("M"), CWP, 224.0, A.add, RHO, A.is_gt)
    act(S("X", 0, D_), C("PB", 0, NN), AF.Relu, scale=-1.0 / 256, acc=CAND)
    act(UP, R3, AF.Relu, scale=-1.0, acc=DN)
    act(S("X", 0, R_), C("PB", NN, N2), AF.Relu, scale=-1.0 / 256)
    mms(*[(r, S(l), x) for r, l in ((R2, "LT"), (R5, "LE")) for x in (OM(D_), OR(D_))], *[(r, ID, GEX) for r in (R2, R5)],
        (R4, S("LE"), OR(R_)))
    act(U, R2, AF.Relu, scale=-1.0, bias=1.0)
    act(UT, R5, AF.Relu, scale=-128.0, bias=128.0)
    act(S("GEN", R_), R4, AF.Relu, scale=-1.0, bias=1.0)
    act(S("GEN", D_), GEX, scale=1.0 / 2048)

    last0 = lambda x: S(x[1], *([N0_] if x[1] in ("OM", "OR", "EQC") else [int(x[2][0]) // len(cache[x[1]][0]), N0_]))
    KEY0, KEY1, OH = C("PA", 16, 16 + N0), C("PU", 64, 64 + N0), C("PU", 80, 80 + N0)
    same = [C("HB", 0, N0)] + [last0(x) for x in (S("EQ", 0), S("EQ", 1), GEX, OR())]
    mms(*[(KEY0, S("SEL", 0), x) for x in same + [last0(OM())]])
    KS = lambda k, a=0, b=N0: S("KS", k, slice(a, b))
    act(KS(0), KEY0)

    def rank(k, keys, key):
        act(S("JK", k, slice(0, N0)), keys, AF.Sign, scale=-1.0, bias=key, acc=C("SR", k))

    for n in range(4):
        rank(n, KS(0), KS(0, N0 - 1 - n, N0 - n))
    tt(OMW, last0(OM()), ROWM, A.mult)
    mms((OH, S("SEL", 0), last0(S("EQC"))), *[(KEY1, S("SEL", 0), x) for x in (last0(OR()), OMW)], *[(KEY1, S("SEL", 1), x) for x in same + [OMW]])
    act(KS(1), KEY1)
    act(KS(2), OH, AF.Sign)
    for n in (0, 1):
        rank(4 + n, KS(1), KS(1, N0 - 1 - n, N0 - n))
    tt(KS(2), KS(2), KS(1), A.mult)
    act(S("JK", 7, slice(0, N0)), KS(2), scale=-1.0, acc=C("SR", 8))
    rank(6, KS(1), C("SR", 8))
    ISB = C("SR", 9)
    ts(ISB, C("SR", 6), -9.0, A.is_equal, -512.0, A.mult)
    ts(C("SR", 12, 16), KS(1, N0 - 4, N0), 2048.0, A.is_lt, ISB, A.mult)

    act(S("Z", slice(0, N2)), S("X", 0, slice(0, N2)), scale=-64.0, bias=DN)
    act(ZC, CAND, scale=-9.0, bias=DN)
    ts(S("XH"), BITS, col(L2), A.max, CAND, A.min)
    HY, CNT, SUC = C("PM", 0, 32), C("PM", 32, 64), C("SH", 0)
    mms((HY, S("I32"), S("XH")), (HY, S("M"), S("XH")))
    ts(C("VI", 0, 32), HY, ZC, A.add, 31.0, A.is_gt)
    ts(C("VI", 32, 64), HY, ZC, A.add, 0.0, A.is_lt)
    mms((CNT, NH, S("XH")), (CNT, S("LA"), C("VI", 0, 32)), (CNT, S("LA"), C("VI", 32, 64)))
    red(SUC, CNT, A.min)

    def places(f):
        a, r = 128 * (f % 2), 64 * PSLOT[f]
        XY = "PM" if f == 1 else "XY"
        pos, half = C(XY, a, a + 128), [C(XY, a + 64 * i, a + 64 * i + 64) for i in (0, 1)]
        steps = [(pos, ID, S("NV", f))] + [(h, ID, S("BT")) for h in half]
        if f:
            steps += [(pos, row1, S("MB", 2))] + [(h, C(l, 0, 128), S("GV")) for h, l in zip(half, ("JH", "JM"))]
            steps += [(pos, row1, S("MB", k)) for k in (0, 1)]
        mms(*steps)
        ts(C("CC", 0, 64), C(XY, a, a + 128, 2), 0.0, A.max, 15.0, A.min)
        ts(C("CC", 64, 128), C(XY, a + 1, a + 128, 2), 0.0, A.max, 31.0, A.min)
        if f == 0:
            act(C("RV", r, r + 64), S("NV", 0, 0))
        elif f < F - 1:
            tt(C("RV", r, r + 64), half[0], S("BT"), A.subtract)

    TOT = C("XY", 448, 512)

    def twice(f, more=()):
        o = C("XX", 256 + 64 * f, 320 + 64 * f)
        ob = C("XX", 288 + 64 * f, 320 + 64 * f)
        mms((o, row1, S("CI", 0)), *[(o, ID, S("IDX", al, f))] * 2,
            *[(ob, FXL[i], S("FX", i, slice(32 * f, 32 * f + 32))) for i in (0, 1)], *more)
        return o

    def offsets(f, idx, slots, more=()):
        act(S("AB", 5 + f), S("IDX", al, f), AF.Relu, scale=512.0 * (f + 1), bias=-3584.0 * (f + 1))
        for k, (c, v) in enumerate(slots):
            ts(S("AB", 2 * f + k), idx, C("SR", c), A.is_equal, v * P, A.mult)
        mms((TOT, ID, S("AB", 5 + f)), (TOT, S("I32"), C("CC", 0, 64)), (TOT, ID, C("CC", 64, 128)), *more,
            *[(TOT, ID, S("AB", 2 * f + k)) for k in range(len(slots))])
        ts(C("OFF", 64 * f, 64 * f + 64), TOT, float(P * (7 - wbase(f))), A.add)

    I0 = twice(0)
    places(0)
    offsets(0, I0, ((0, -2.0), (1, -1.0)))
    mm(C("XY", 128, 256), S("LA"), S("SEL", 0), True, True)
    act(S("BO"), C("XY", 128, 256), scale=1.0 / 16)
    power(0, 2, "XY", 256, 1)
    IA0 = S("MK", 1, slice(0, 32))
    tt(IA0, IA0, S("IDX", 0, 0), A.max)
    act(S("KS", 0, slice(12, 16)), C("SR", 0, 4), scale=0.5, bias=5.5)
    for n in range(4):
        ts(S("OK", n), IA0, S("KS", 0, slice(12 + n, 13 + n)), A.is_equal, C("SR", 15 - n), A.mult)
    tt(S("GW"), S("NV", 0, 0), S("MK", 1, slice(32, RW)), A.mult)
    act(S("GV"), S("GW"), scale=ISB)
    places(1)
    I1 = twice(1, [(C("XX", 320, 352), ID, S("OK", n)) for n in range(4)])
    offsets(1, I1, ((4, -2.0), (5, -1.0), (6, -3.0)), [(C("XY", 448, 480), ID, S("OK", n)) for n in (0, 0, 1)])
    act(C("ON", 0, 32), C("XX", 320, 352), AF.Relu, scale=-1.0 / 512, bias=-11.0 / 512)
    act(C("ON", 32, 64), C("ON", 0, 32), scale=-1.0, bias=1.0)

    ts(S("X", 1, slice(0, N2)), S("X", 0, slice(0, N2)), SUC, A.mult, 240.0, A.mult)

    scan(SU, U, U, 0.0, A.max)
    YS = lambda k, h=None: C("PW", 1 + N2 * k + NN * (h or 0), 1 + N2 * k + (N2 if h is None else NN * h + NN))
    LAM = C("PW", 1 + 4 * N2)
    short = [YS(k, 0) for k in range(4)]
    long_ = [(YS(k, 1), R_) for k in range(3)] + [(YS(3, 1), D_)]
    mms((C("PW", 0, 1 + 4 * N2), row1, C("CY", 0, 1 + 4 * N2)),
        (YS(0), ID, S("EQ", 1)), (YS(1), ID, S("EQ", 0)), (YS(1), NH, S("EQ", 1)), (YS(2), NH, S("EQ", 0)), (YS(2), NH, S("EQ", 1)),
        *[(y, ID, OR(h)) for y, h in long_], *[(y, NH, UT) for y in short], *[(y, ID, S("Z", h)) for y, h in long_],
        *[(y, ID, SU) for y in short], (LAM, S("M"), SUC), (LAM, S("M"), SUC), *[(y, S("M"), S("X", 1, h)) for y, h in long_])
    ts(S("Y", 0, slice(0, N3)), C("PW", 1, 1 + N3), LAM, A.is_le, -63.0, A.mult)
    ts(S("Y", 1, slice(0, N3)), C("PW", 0, N3), LAM, A.is_le, 64.0, A.mult)
    ts(S("YH"), YS(3), LAM, A.is_le)
    scan(S("RK"), S("Y", 0, slice(0, N3)), S("Y", 1, slice(0, N3)), 64.0)
    wide, rest = slice(0, N3), slice(2 * N2, N3)
    act(S("SQ", 0), S("RK"), AF.Square, scale=col(SC1), bias=col(SB0))
    act(S("SQ", 1, rest), S("RK", rest), AF.Square, scale=DS_, bias=col(SB1))
    for k, c in ((0, wide), (1, rest)):
        act(S("EW", k, c), S("SQ", k, c), AF.Relu, scale=-BIG, bias=BIG)
    DD, D2 = C("PW", 256, 256 + N2), C("PW", 320, 320 + N2)
    LAL = C("LA", 0, 64)
    mms(*[(d, l, x) for d in (D2, DD) for l, x in ((NH, S("KT")), (NH, S("KT")), (S("LA"), S("EQC")))], (DD, S("LA"), S("GEN")),
        (C("PW", 320, 320 + N2, parts=lo), LAL, S("GEN")), (DD, row1, S("CI", 1, slice(0, N2))),
        *[(C("PW", 320, 320 + NN, parts=lo), LAL, S("YH", h)) for h in (D_, R_)],
        *[(C("PW", 256, 256 + NN), S("LA"), S("YH", h)) for h in (D_, R_)])
    act(S("DS"), D2, bias=col(KCB))
    TBP = lambda a, b=None: C("PW", 400 + a, None if b is None else 400 + b)
    o = C("PM", 64, 64 + N2)
    mms(*[(o, ID, S("EW", 0, slice(N2 * s, N2 * s + N2))) for s in range(3)])
    tt(C("EP", 0, N2), o, S("DS"), A.mult)
    tt(C("EP", N2, 2 * N2), DD, S("EW", 1, rest), A.mult)
    for k, name in enumerate(("RA", "RB")):
        red(C("SM", 8 + k), C("EP", N2 * k, N2 * k + N2))
        act(S(name), S("DA", (slice(0, 3), slice(1, 4, 2))[k]), scale=C("SM", 8 + k))
    mms((TBP(0, 32), S("ONF"), S("CS")), (TBP(16, 32), S("BO"), S("RB")), (TBP(0, 24), S("BO"), S("RA")))

    def words(f):
        act(S("U1", f), S("H1", al, f), scale=C("TB", 16 + f), bias=C("TB", 8 + f))
        act(S("U2", f), S("H2", al, f), scale=C("TB", 24 + f))
        o = C("PM", 192 + 64 * (f % 2), 192 + 64 * (f % 2) + 64)
        mms((o, S("IDF"), S("U1", f)), (o, S("IDF"), S("U2", f)))
        tt(S("XI", f), o, S("POW", al, f), A.mult)

    def columns(f, first):
        ts(C("LU", 4 * f, 4 * f + 4), S("CL"), first, A.add, -64.0 * wbase(f), A.add)

    def record(f):
        r = 64 * PSLOT[f]
        win = lambda name: C(name, 64 * wbase(f), 64 * (8 if f < 6 else 10))
        if f > 2:
            columns(f, C("TB", f))
        ts(S("A0", f), S("XI", f, 0), 65024, A.bitwise_and)
        ts(S("A0", f), S("A0", f), (16 * f - 1) * 65536.0, A.add)
        tt(S("GV"), IND(win("RV"), C("LU", 4 * f, 4 * f + 4)), S("MK", f, slice(32, RW)), A.mult)
        tt(S("GE"), IND(win("RE"), C("LU", 4 * f, 4 * f + 2)), S("MK", f, slice(0, 32)), A.mult)
        places(f)
        tt(S("XI", f, 0), S("GE"), S("A0", f), A.max)
        if f < F - 1:
            ts(C("RE", r, r + 32), S("XI", f, 0), 65024, A.bitwise_and)
        ts(S("SS", f % 2), S("XI", f), 7680, A.bitwise_and)
        tot = C("PM", 384, 448)
        mms((tot, S("I32"), C("CC", 0, 64)), (tot, ID, C("CC", 64, 128)))
        tt(S("S2"), tot, S("SS", f % 2), A.add)
        ts(C("OFF", 64 * f, 64 * f + 64), S("S2"), float(-P * wbase(f)), A.add)

    def pixels(f):
        pieces = list(zip(CUTS[:-1], CUTS[1:]))
        bank = lambda h: C(("PA", "PB", "PU", "PN")[h], 0, pieces[h][1] - pieces[h][0])
        s = 16 * ((f + 1) % 8)
        win = C("W", P * wbase(f), P * (9 + f))
        aw = [("arr%d" % f, narr * (len(SENDS) if f else 1))]
        last = f == F - 1
        for h, (a, b) in enumerate(pieces):
            mm(bank(h), C("J", s, s + 128), C("RES", f * P + a, f * P + b), True, False)
            mm(bank(h), S("MQ"), C("MR", 0, b - a), False, False)
        for h, (a, b) in enumerate(pieces):
            act(C("GP", a, b), IND(win, C("OFF", 64 * f + a // 16, 64 * f + b // 16)), AF.Relu, scale=-1.0, bias=255.0, waits=aw)
            ts(C("GQ", a, b), IND(win, C("OFF", 64 * f + 32 + a // 16, 64 * f + 32 + b // 16)), 255.0, A.min, 767.5, A.add, waits=aw)
            mm(bank(h), C("JM", s, s + 128), C("GP", a, b), False, False)
            mm(bank(h), C("JH", s, s + 128), C("GQ", a, b), False, not last)
            if last:
                mm(bank(h), S("NG"), C("MZ", 0, b - a), False, True)
        done, parts = 0, []
        for h, (a, b) in enumerate(pieces):
            out = C("SND", f * P + a, f * P + b)
            if last:
                ts(out, bank(h), 0.0, A.max, 255.0, A.min)
            elif FIN[min(f, 2)][h] == "s":
                act(out, bank(h), AF.Relu, bias=-BIG)
            else:
                ts(out, bank(h), -BIG, A.add, 0.0, A.max)
            if h in (STORES if last else SENDS):
                if last:
                    k = STORES.index(h)
                    dma(("sync", "scalar")[k % 2], T.y[:, f * P + done:f * P + b], C("SND", f * P + done, f * P + b), "out%d" % (f + k))
                else:
                    send(C("W", (9 + f) * P + done, (9 + f) * P + b), C("SND", f * P + done, f * P + b), f + 1)
                parts.append((done, b))
                done = b
        if last:
            return
        s = 128 - 16 * (f + 1)
        for (a, b), name in zip(parts, ("PA", "PB")):
            back = C(name, P - b + a, P)
            mm(back, C("J", s, s + 128), C("SND", f * P + a, f * P + b), True, True)
            act(C("W", PSLOT[f] * P + a, PSLOT[f] * P + b), back)

    def store(f):
        ts(C("YO", f * P, f * P + P), C("W", PSLOT[f] * P, PSLOT[f] * P + P), 255.0, A.min)
        dma("sync", T.y[:, f * P:f * P + P], C("YO", f * P, f * P + P), "out%d" % f, [sent(k) for k in range(f + 1, min(f + 3, F))])

    tt(S("PX"), S("POW", 0, slice(0, 2)), S("ON"), A.mult)
    lists(2, 4)
    vec(2, 4)
    masks(2, 4)
    power(2, 4, "XY", 256)
    for f, a, n in ((0, 0, 32), (1, 32, 32), (2, 64, 64)):
        h = lambda name: S(name, 0 if f < 2 else al, f)
        ts(C("U0", a, a + n), h("H1"), TBP(16 + f), A.mult, TBP(8 + f), A.add)
        ts(C("PW", 128 + a, 128 + a + n), h("H2"), TBP(24 + f), A.mult)
    columns(2, TBP(2))
    for a in (0, 64):
        tt(C("PW", 256 + a, 320 + a), C("PW", 128 + a, 192 + a), C("U0", a, a + 64), A.add)
    tt(S("XB", slice(0, 2)), C("PW", 256, 320), S("PX"), A.mult)
    tt(S("XI", 0, 0), C("PW", 256, 288), S("POW", 0, 0), A.mult)
    tt(S("XI", 2), C("PW", 320, 384), S("POW", al, 2), A.mult)
    act(S("TB"), TBP(0, 32))
    tt(S("XI", 1, 0), S("XB", 0), S("XB", 1), A.max)
    for f in range(F):
        pixels(f)
        if f == 0:
            iota(C("RE", 0, 10 * 64), [[0, 10 * 64]], 0)
            iota(C("RV", 5 * 64, 9 * 64), [[0, 4 * 64]], 0)
            diag("JM", 160, 256, -0.5)
            diag("JH", 160, 256, 0.5)
            for k in (1, 0):
                ts(C("RE", 64 * PSLOT[k], 64 * PSLOT[k] + 32), S("XI", k, 0), 65024, A.bitwise_and)
        if f == 1:
            iota(S("MZ"), [[0, 192]], int(BIG))
            iota(S("NG"), [[0, 128]], -1)
        if f + 2 < F:
            dma("sync", C("RES", (f + 2) * P, (f + 3) * P), T.res[:, (f + 2) * P:(f + 3) * P], "res%d" % (f + 2), [sent(f + 1)])
        if f == 0:
            dma("sync", C("IA", 128, 256), T.ia[:, 128:256], "ia2")
            dma("sync", C("IB", 128, 256), T.ib[:, 128:256], "ib2")
        if f == 1:
            dma("sync", S("VY", slice(4, 8)), T.vy[:, 256:512], "vy2")
            dma("sync", S("VX", slice(4, 8)), T.vx[:, 256:512], "vx2")
        if f == 1:
            record(2)
            words(3)
            lists(4, 8)
            masks(4, 8)
            power(4, 8, "PW", 0)
        if f in (2, 3):
            vec(2 * f, 2 * f + 2)
        if 1 < f < F - 1:
            record(f + 1)
        if 1 < f < F - 2:
            words(f + 2)
        if 0 < f < F - 1:
            store(f - 1)
        if f == F - 2:
            store(f)
    return ops


def schedule(ops):
    n = len(ops)
    queue = [{"scalar": "act"}.get(o[0], o[0]) for o in ops]
    pre = [{} for o in ops]
    acc, raised = {}, {}
    for j, (q0, fn, rd, wr, waits, sem, cost) in enumerate(ops):
        q = queue[j]
        for s, v in waits:
            for k, i in enumerate(raised.get(int(s[3:]), ())[::-1]):
                pre[j][i] = HOP + ROWS * (k + 1) + COL * (P - int(ops[i][2][0][1].min()) % P)
        for name, el, w in [(a, e, False) for a, e in rd] + [(a, e, True) for a, e in wr]:
            lo, hi = int(el.min()), int(el.max())
            for i, pw, plo, phi, pel in acc.get(name, ()):
                same = queue[i] == q and ops[i][5] is None and sem is None
                clash = (w or pw) and plo <= hi and lo <= phi
                if i == j or not (clash or name in PS_ and (not same or q == "pe")):
                    continue
                if same and q == "pe":
                    pre[j].setdefault(i, 0.0)
                elif not (same and w) or np.intersect1d(el, pel).size:
                    for k in ([i] if ops[i][5] not in DMAS else [k for k in range(n) if ops[k][5] == ops[i][5]]):
                        if sem is None or ops[k][5] != sem:
                            pre[j][k] = WAKE
            acc.setdefault(name, []).append((j, w, lo, hi, el))
        if isinstance(sem, int):
            raised.setdefault(sem, []).append(j)
    for q in ("sync", "pool"):
        l = [j for j in range(n) if queue[j] == q]
        for i, j in zip(l, l[1:]):
            pre[j].setdefault(i, None)
    for name in ("GP", "GQ"):
        l = [j for j in range(n) if ops[j][3] and ops[j][3][0][0] == name]
        for i, j in zip(l, l[1:]):
            pre[j].setdefault(i, 0.0)
    span = [o[6] for o in ops]
    unit = ["dma" if o[5] in DMAS else q for o, q in zip(ops, queue)]
    land = [LAND if u == "dma" else 0.0 for u in unit]
    lag = [{i: (0.0 if land[j] else span[i]) if d is None else span[i] + d + land[j] for i, d in pre[j].items()} for j in range(n)]
    back = [{} for o in ops]
    for j in range(n):
        for i, d in lag[j].items():
            back[i][j] = d + span[j] - span[i]

    ahead, behind = [list(e.items()) for e in lag], [list(e.items()) for e in back]
    up = list(range(n))
    down = up[::-1]

    def place(edges, rank, first, walk):
        rank = list(rank)
        for j in walk:
            for i, d in edges[j]:
                if rank[i] >= rank[j]:
                    rank[j] = rank[i] + 1e-7
        start, busy = [0.0] * n, {u: ([], []) for u in unit}
        for j in sorted(walk, key=lambda j: rank[j]):
            t = first[j]
            for i, d in edges[j]:
                if start[i] + d > t:
                    t = start[i] + d
            a, b = busy[unit[j]]
            k = len(b)
            while k and b[k - 1] > t:
                k -= 1
            while k < len(a) and a[k] < t + span[j] - 1e-9:
                t = max(t, b[k])
                k += 1
            a.insert(k, t)
            b.insert(k, t + span[j])
            start[j] = t
        return start

    seed = [1]

    def draw():
        seed[0] = (seed[0] * 1103515245 + 12345) % 2 ** 31
        return seed[0] / 2.0 ** 31

    marks = [j for j in up if isinstance(ops[j][5], int) or "OFF" in [a for a, e in ops[j][3]]]
    cases = []
    for engines, waits, writes in SLOWER:
        more = [writes if isinstance(ops[j][5], int) else 0.0 if land[j] else (engines - 1) * span[j] for j in up]
        more = [2 * more[j] if unit[j] == "pool" and span[j] > 1 else more[j] for j in up]
        holds = [more[j] if unit[j] != "pool" or span[j] > 1 else 0.0 for j in up]
        cases.append(([[(i, d + (holds[i] if unit[j] == "pool" else more[i]) + waits * (pre[j][i] == WAKE)) for i, d in ahead[j]] for j in up],
                      [span[j] + holds[j] for j in up]))

    def slower(start):
        total, order = 0.0, sorted(up, key=lambda j: start[j])
        for edges, takes in cases:
            at, free = [0.0] * n, {u: 0.0 for u in unit}
            for j in order:
                t = max(free[unit[j]], land[j])
                for i, d in edges[j]:
                    if at[i] + d > t:
                        t = at[i] + d
                at[j] = t
                free[unit[j]] = t + takes[j]
            total += 0.5 * max(free.values())
        return total

    rank = [-s for s in span]
    for j in down:
        for i, d in ahead[j]:
            rank[i] = min(rank[i], rank[j] - d)
    due = [0.7 - min(rank) + r for r in rank]
    head = [j for j in up if due[j] < 15]
    best = now = (1e9, None, rank, 1e9)
    for k in range(ROUNDS):
        if k == ROUNDS * 2 // 3:
            best = now = (best[3] + slower(best[1]),) + best[1:]
        if k and draw() < 0.3:
            late = place(behind, [-now[1][j] - span[j] for j in up], [0.0] * n, down)
            rank = [-late[j] - span[j] + 0.1 * draw() for j in up]
        elif k:
            rank, early = list(now[2]), [j for j in up if now[1][j] < 17]
            for m in range(1 + int(0.05 * draw() * len(early))):
                rank[early[int(draw() * len(early))]] += draw() - 0.5
        start = place(ahead, rank, land, up)
        end = max(start[j] + span[j] for j in up) + 0.003 * sum(start[j] for j in marks)
        end += 0.01 * sum((start[j] - due[j]) ** 2 for j in head if start[j] > due[j])
        if end > now[3] + 0.25:
            continue
        value = end + (slower(start) if k >= ROUNDS * 2 // 3 else 0.0)
        if value <= now[0] + 0.06 * draw() * (1 - k / ROUNDS):
            now = (value, start, rank, end)
        if value < best[0]:
            best = now
    issue = list(best[1])
    for j in range(n):
        if land[j]:
            issue[j] = max([0.0] + [issue[i] if pre[j][i] is None else best[1][i] + d - LAND for i, d in lag[j].items()])
    return sorted(range(n), key=lambda j: (issue[j], j))


def emit(g, T, ops):
    eng = {"dve": g.vector, "act": g.scalar, "pe": g.tensor, "pool": g, "sync": g.sync, "scalar": g.scalar}
    queue = {"scalar": "act"}
    total = {}
    for o in ops:
        if o[5] in DMAS:
            total[o[5]] = total.get(o[5], 0) + 16
    count = {"dve": 0, "act": 0, "pe": 0, "pool": 0}
    seen = {q: {} for q in ("dve", "act", "pe", "pool", "sync")}
    known = {}
    acc = {}
    waited = {}
    for q0, fn, rd, wr, waits, sem, cost in ops:
        q = queue.get(q0, q0)
        need = {}
        for s, v in waits:
            need[s] = max(need.get(s, 0), v)
        for name, el, w in [(n, e, False) for n, e in rd] + [(n, e, True) for n, e in wr]:
            lo, hi = int(el.min()), int(el.max())
            for pq, pw, plo, phi, pel, tok, pdma in acc.get(name, ()):
                if sem is not None and tok[0] == sem:
                    continue
                same = pq == q and not pdma and sem is None
                box = plo <= hi and lo <= phi
                if name in PS_ and not same:
                    hit = True
                elif not (w or pw) or not box:
                    hit = False
                elif same and q == "pe":
                    hit = False
                elif same and w:
                    hit = bool(np.intersect1d(el, pel).size)
                else:
                    hit = True
                if hit:
                    need[tok[0]] = max(need.get(tok[0], 0), tok[1])
        for s, v in sorted(need.items(), key=lambda x: -x[1]):
            if seen[q].get(s, 0) < v:
                eng[q].wait_ge(T.sem[s], v)
                waited[s] = max(waited.get(s, 0), v)
                seen[q][s] = v
                for s2, v2 in known.get((s, v), {}).items():
                    seen[q][s2] = max(seen[q].get(s2, 0), v2)
        ins = fn(eng[q0])
        if isinstance(sem, int):
            continue
        if sem is None:
            count[q] += 1
            tok = (q, count[q])
            ins.then_inc(T.sem[q], 1)
            known[tok] = dict(seen[q])
        else:
            tok = (sem, total[sem])
            ins.then_inc(T.sem[sem], 16)
        for name, el, w in [(n, e, False) for n, e in rd] + [(n, e, True) for n, e in wr]:
            acc.setdefault(name, []).append((q, w, int(el.min()), int(el.max()), el, tok, sem is not None))
    last = dict(total)
    last.update(count)
    for s, v in last.items():
        if waited.get(s, 0) < v:
            g.sync.wait_ge(T.sem[s], v)


def rank_program(g, core, T, topo):
    rank = T.rank_of(core)
    if rank is None:
        return
    n = len(T.cores)
    dst, src = T.cores[(rank + 1) % n], T.cores[(rank - 1) % n]
    rid, pid, _ = topo.addr(dst)
    eng = topo.engines(core, dst)
    half = [sum(1 << e for e in part) for part in (eng[:len(eng) // 2], eng[len(eng) // 2:])]
    nxt = (rid, pid, topo.mask(core, dst), len(topo.engines(src, core)), half)
    ops = build(T, nxt)
    if not ORDER:
        ORDER.extend(schedule(ops))
    emit(g, T, [ops[j] for j in ORDER])
